import numpy as np, ml_dtypes
CORES = [16,18,20,22]
N = 4
BF = ml_dtypes.bfloat16
S, R, NF, PH, LB, RO = 4096, 4096, 256, 512, 9, 5
def place(s, p):
    return ((s * p >> 4) + s + 37 * p) & (R - 1)
def records(rng):
    st = ((np.arange(8)[None, :] + rng.integers(0, 3, (N, 1))) % 3)[:, :, None, None]
    lo = np.where(st == 0, 0, np.where(st == 1, 64 * rng.integers(0, 4, (N, 8, 1, R)), 200 * (rng.random((N, 8, 1, R)) < 0.35))).astype(np.int32)
    span = np.where(st == 0, 256, np.where(st == 1, 64, 56)).astype(np.float32)
    x = np.minimum(lo + (rng.random((N, 8, 16, R), dtype=np.float32) * span).astype(np.int32), 255)
    u = rng.random((N, 8, 16, 1))
    th = np.where(st == 0, 1000 + 700 * u, np.where(st == 1, 256 + 2000 * u, 450 + 1150 * u)).astype(np.int64)
    return x, th
def parts(rng):
    var = rng.choice(np.array([0.2, 0.35, 0.5]), (N, 8, 1, 1)); emp = rng.choice(np.array([0.2, 0.45, 0.7]), (N, 8, 1, 1))
    tk = rng.integers(0, S, (N, 8, 16, S)) + S * (rng.random((N, 8, 16, S)) < var)
    fr = np.where(rng.random((N, 8, 16, NF)) < emp, -1, rng.integers(0, S * PH, (N, 8, 16, NF)))
    return tk, fr, rng.integers(0, S, (N, 8, NF)), rng.integers(0, NF, (N, 8, NF)), rng.integers(0, S, (N, 8, NF))
def pack(x, tk, fr, th, s, f, c):
    return {"x": np.ascontiguousarray(x.reshape(N, 128, R)).astype(np.float32).astype(BF), "sk": np.ascontiguousarray(tk.reshape(N, 128, S)).astype(np.int32),
            "fr": np.ascontiguousarray(fr.reshape(N, 128, NF)).astype(np.int32), "th": np.ascontiguousarray(th.reshape(N, 128, 1)).astype(np.int32),
            "gs": s.astype(np.int32), "gf": f.astype(np.int32), "gcl": c.astype(np.int32)}
def setup_inputs(rng):
    x, th = records(rng); tk, fr, s, f, c = parts(rng)
    return pack(x, tk, fr, th, s, f, c)
def setup_inputs_spread(rng):
    amp = np.exp2(8 * rng.random((N, 8, 1, R))).astype(np.float32)
    x = np.minimum((rng.random((N, 8, 16, R), dtype=np.float32) * amp).astype(np.int32), 255)
    x = np.where(rng.random((N, 8, 1, R)) < 0.0625, 255 - x, x)
    th = np.minimum(np.exp2(12 * rng.random((N, 8, 16, 1))).astype(np.int64), 4080)
    u = rng.random((N, 8, 16, S)); tk = np.minimum((2 * S * u * np.sqrt(u)).astype(np.int64), 2 * S - 1)
    v = rng.random((N, 8, 16, NF)); fr = np.where(rng.random(v.shape) < 0.3 * rng.random((N, 8, 1, 1)) + 0.1, -1, np.minimum((S * PH * v * v).astype(np.int64), S * PH - 1))
    w = rng.random((3, N, 8, NF)); w = w * w
    return pack(x, tk, fr, th, np.minimum((S * w[0]).astype(np.int64), S - 1), np.minimum((NF * w[1]).astype(np.int64), NF - 1), np.minimum((S * w[2]).astype(np.int64), S - 1))
def setup_inputs_ends(rng):
    one = rng.random((N, 8, 1, R)) < 0.5; each = rng.random((N, 8, 16, R)) < 0.5
    x = 255 * np.where(rng.random((N, 8, 1, R)) < 0.25, each, one).astype(np.int64)
    tk = (2 * S - 1) * rng.integers(0, 2, (N, 8, 16, S)); fr = np.where(rng.integers(0, 2, (N, 8, 16, NF)) == 1, S * PH - 1, -1)
    s = (S - 1) * rng.integers(0, 2, (N, 8, NF)); f = (NF - 1) * rng.integers(0, 2, (N, 8, NF)); c = (S - 1) * rng.integers(0, 2, (N, 8, NF))
    th = np.full((N, 8, 16, 1), 4080, np.int64)
    for a in range(N):
        for g in range(8):
            if g == 7: z = rng.permutation(15)[:9 if a % 2 == 0 else 7]
            else: z = rng.permutation(16)[:16 if g == 6 else 8]
            th[a, g, z, 0] = 0
    s[:, :, NF - 1] = S - 1; f[:, :, NF - 1] = NF - 1; c[:, :, NF - 1] = 0
    tk[::2, :, :, S - 1] = 2 * S - 1; tk[::2, :, :, 0] = 0; tk[:, 7, :, S - 1] = 2 * S - 1; tk[:, 7, :, 0] = 0
    x[..., place(S - 1, PH - 1)] = 255; x[..., place(S - 1, NF - 1)] = 255; x[..., place(0, NF - 1)] = 0
    return pack(x, tk, fr, th, s, f, c)
def setup_inputs_corners(rng):
    x, th = records(rng); tk, fr, s, f, c = parts(rng); i = np.arange(NF); even = i % 2 == 0
    near = np.array([[3, 21], [21, 3], [5, 19], [19, 5], [7, 9], [9, 7]])
    for a in range(N):
        o = rng.permutation(8)
        tk[a, o[0]] = tk[a, o[0]] & (S - 1); fr[a, o[0]] = -1
        tk[a, o[1]] = (tk[a, o[1]] & (S - 1)) + S; fr[a, o[1]] = -1
        tk[a, o[2]] = (tk[a, o[2]] & (S - 1)) + S
        fr[a, o[2]] = PH * rng.integers(0, S, (16, NF)) + np.where(rng.random((16, NF)) < 0.5, i, NF + i)
        f[a, o[3]] = i; fr[a, o[3]] = np.where(i % 2 == 0, -1, rng.integers(0, S * PH, (16, NF)))
        f[a, o[4]] = rng.choice(np.array([0, NF - 1]), NF); s[a, o[4]] = rng.choice(np.array([0, S - 1]), NF); c[a, o[4]] = np.where(rng.random(NF) < 0.5, s[a, o[4]], S - 1 - s[a, o[4]])
        fr[a, o[4]] = np.where(rng.random((16, NF)) < 0.4, -1, PH * rng.choice(np.array([0, S - 1]), (16, NF)) + rng.choice(np.array([0, NF - 1, NF, PH - 1]), (16, NF)))
        th[a, o[5]] = 4080; th[a, o[6]] = 0; th[a, o[7]] = 4080; th[a, o[7], rng.permutation(16)[:8]] = 0
        f[a, o[5]] = np.where(even, i, f[a, o[5]]); c[a, o[5]] = np.where(even, s[a, o[5]], c[a, o[5]]); fr[a, o[5]] = np.where(even, -1, fr[a, o[5]])
        pq = near[rng.integers(0, 6, NF)]
        s[a, o[6]] = np.where(even, S - pq[:, 0], s[a, o[6]]); c[a, o[6]] = np.where(even, S - pq[:, 1], c[a, o[6]])
    return pack(x, tk, fr, th, s, f, c)
def setup_inputs_ties(rng):
    v, th = records(rng); tk, fr, s, f, c = parts(rng)
    x = np.broadcast_to(60 * rng.integers(0, 5, (N, 8, 1, R)), (N, 8, 16, R)).copy()
    th = rng.choice(np.array([959, 960, 961, 1919, 1920, 1921]), (N, 8, 16, 1))
    off = rng.integers(0, 4, (N, 2, 16, R)) * (rng.random((N, 2, 1, R)) < 0.5)
    x[:, 1::4] = np.abs(255 * rng.integers(0, 2, (N, 2, 1, R)) - off)
    lev = np.array([0, 0, 0, 24, 24, 24, 4048, 4056, 4060, 4064, 4078, 4079, 4079, 4079, 4080, 4080])
    th[:, 1::4] = lev[np.argsort(rng.random((N, 2, 16, 1)), axis=2)]
    few = rng.integers(0, S, (N, 4, 3)); which = rng.integers(0, 3, (2, N, 4, NF))
    s[:, ::2] = np.take_along_axis(few, which[0], 2); c[:, ::2] = np.take_along_axis(few, which[1], 2); f[:, ::2] = rng.integers(0, 4, (N, 4, NF))
    return pack(x, tk, fr, th, s, f, c)
def check_inputs(d):
    bad = []
    for k, lo, hi in (("x", 0, 255), ("sk", 0, 2 * S - 1), ("fr", -1, S * PH - 1), ("th", 0, 4080), ("gs", 0, S - 1), ("gf", 0, NF - 1), ("gcl", 0, S - 1)):
        if k not in d: bad.append("no " + k); continue
        v = np.asarray(d[k]).astype(np.float64)
        if not (np.min(v) >= lo and np.max(v) <= hi): bad.append("range of " + k)
        elif np.any(v != np.floor(v)): bad.append("whole numbers in " + k)
    return bad
def reference(x, sk, fr, th, gs, gf, gcl):
    X = x.astype(np.float32).astype(np.int32).reshape(N, 8, 16, R); T = sk.astype(np.int64).reshape(N, 8, 16, S); lim = th.astype(np.int64).reshape(N, 8, 16, 1)
    own = fr.astype(np.int64).reshape(N, 8, 16, NF); F = np.concatenate([own, own], axis=3)
    i = np.arange(NF); mark = np.zeros((N, 8, 16, NF), bool); A = np.zeros((N, NF), np.int64)
    s = gs.astype(np.int64); f = gf.astype(np.int64); c = gcl.astype(np.int64); h = np.zeros_like(s) + i
    s0 = s; f0 = f; c0 = c
    def molecules(a, b):
        v = np.take_along_axis(T, a[:, :, None, :], 3); w = np.take_along_axis(F, b[:, :, None, :], 3)
        return np.where((v >= S) & (w >= 0), w, (v & (S - 1)) * PH + b[:, :, None, :]), (v >= S) & (w < 0)
    def pick(m):
        return np.take_along_axis(X, place(m >> LB, m & (PH - 1)).reshape(N, 8, 1, 16 * NF), 3)
    for rnd in range(RO):
        goal, _ = molecules(s, f); clause, hole = molecules(c, h)
        free = hole & (h == i)[:, :, None, :]; clause = np.where(free, goal, clause)
        D = np.add.reduce(np.abs(pick(goal) - pick(clause)), axis=2).astype(np.int64).reshape(N, 8, 16, NF)
        over = D > lim; clash = np.add.reduce(over.astype(np.int64), axis=2) >= 8 + (A & 1)[:, None, :]
        m = np.argmax(np.where(over, -1, D), axis=2)[:, :, None, :]
        gm = np.take_along_axis(goal, m, 2)[:, :, 0]; cm = np.take_along_axis(clause, m, 2)[:, :, 0]
        dm = np.take_along_axis(D, m, 2)[:, :, 0]; tm = np.take_along_axis(np.broadcast_to(lim, D.shape), m, 2)[:, :, 0]
        save = ~clash & (2 * dm < tm)
        bind = free & ~clash[:, :, None, :]
        own = np.where(mark & clash[:, :, None, :], -1, np.where(bind, goal, own))
        mark = (mark | bind) & ~(clash | save)[:, :, None, :]
        nxt = ((c0 * s0 >> 5) + c0 + 1) & (S - 1)
        s = np.where(clash, s0, gm >> LB); f = np.where(clash, f0, gm & (PH - 1))
        c = np.where(clash, nxt, cm >> LB); h = np.where(clash, i, cm & (PH - 1))
        s0 = np.where(save, s, s0); f0 = np.where(save, f, f0); c0 = np.where(clash, nxt, np.where(save, c, c0))
        A = np.add.reduce(clash.astype(np.int64), axis=1)
        F = np.concatenate([own, F[..., NF:]], axis=3)
        if rnd < RO - 1:
            d = 1 + rnd % (N - 1); col = np.take_along_axis(F, f[:, :, None, :], 3)
            F = np.concatenate([own, np.roll(col, d, axis=0)], axis=3); s = np.roll(s, d, axis=0); f = np.zeros_like(s) + NF + i
    return {"yf": np.where(own < 0, -1, 2 * own + mark).reshape(N, 128, NF).astype(np.float32), "yg": (PH * s + f).astype(np.float32), "yc": (PH * c + h).astype(np.float32),
            "ysg": (PH * s0 + f0).astype(np.float32), "yk": c0.astype(np.float32)}

@@ -1,0 +1,519 @@
+from concourse.mybir import AluOpType, ActivationFunctionType
+
+OP = AluOpType
+AF = ActivationFunctionType
+U = 1 << 22
+NF, RO, N = 256, 5, 4
+H = (0, 1)
+F32, BF, I32, U16 = "float32", "bfloat16", "int32", "uint16"
+SCRATCH = {}
+
+
+def _bufs(where, dtype, text):
+    for w in text.split():
+        n, c = w.split(":")
+        r, c = (c.split("x") if "x" in c else (128, c))
+        SCRATCH[n] = (where, [int(r), int(c)], dtype)
+
+
+_bufs("sbuf", F32, "skv:4096 skt:4096 inf:8x512 ine:8x512 thf:8 tabb:768 tabh:768 j8:8 mske:256 rst:256 idf:128 onef:128 thrt:256 "
+      "iw:16 il:16 lim:16 fb:256 hb:256 tg:256 tc:256 f3p:256 own3:256 x3:256 eqm:256 nov:256 key:256 cnt:256 sm:256 "
+      "cl:16 smx:16 pgc:512 thp:256 clst:32 lsb:32 lh:512 we:16 wf:16 wh:16 sc:32 sv:32 s1:32 s2:32 t1:16 st:16 par:64 "
+      "fot:64x128 oy:256 oy2:256 oz:256 f0:768 f1:768 f2:768 f3:768 f4:768 snd0:256 snd1:256 snd2:256 snd3:256")
+_bufs("sbuf", BF, "idk:128 xr:4096 ub:4096 hi:256 em:256 df:4096 ab:4096 b16:8 idb:128 k0:8 zero:16 rcb:256 oneb:128 krow:128 fr5:256 mk2:256 sel:256 lhb:512")
+_bufs("sbuf", I32, "ski:4096 ini:8x768 fri:256 thi:8 thj:8 pi:256 ci:256 pm:256 cm:256 ps:8 rawg:256 rawc:256 ga:256 ca:256 "
+      "pg:256 qg:256 prg:256 rg:256 pc:256 qc:256 prc:256 rc:256 wi:32 wq:32 s3:32 t4:16 t5:16 t6:16 t7:16 t8:16 fip:64 oi:256 op:256")
+_bufs("sbuf", U16, "ug:256 uc:256 el:16 fl:16 hl:16 sl:160 sarr:80")
+_bufs("psum", F32, "b0:512 b1:512 pe:512 pl:512 pr:512 sr:512 d0:512 d1:512")
+SEMAPHORES = ["sv", "ss", "st", "sg", "rl"] + ["as%d" % t for t in range(4)] + ["ac%d" % t for t in range(4)] + ["d%d" % t for t in range(24)]
+VIEW = {"sks": ("df", 0, 4096), "frs": ("op", 0, 256), "frm": ("oy", 0, 256), "dg": ("oz", 0, 128), "fin": ("lh", 0, 64), "fiq": ("lh", 64, 64), "fim": ("lh", 128, 64)}
+PSUM = [n for n in SCRATCH if SCRATCH[n][0] == "psum"]
+GCH = [(0, 1024), (1024, 2048), (2048, 3072), (3072, 4096)]
+VCH = [(0, 1024), (1024, 2048), (2048, 3072), (3072, 3584), (3584, 4096)]
+PH = [(0, 128), (128, 256)]
+SKW = 512
+KS = (1, 3, 5)
+CYC, CG, FIX, GFIX, SFIX, WAKE, PEC = 0.00083, 1.5, 0.01, 0.05, 0.06, 0.11, 0.00071
+SLACK, OVER, UP, UQ = 0.1, 0.05, 1.5, 3.0
+PREF = {33: 8, 55: -8, 110: 8, 124: -3, 125: -8, 137: 8, 142: -1.5, 146: 1.5, 166: -3, 211: -8, 214: -8, 224: 3,
+        511: -1.5, 512: -3, 527: -3, 581: -3, 605: 3, 622: -3}
+
+
+def rank_program(g, core, T, topo):
+    rank = T.rank_of(core)
+    if rank is None:
+        return
+    Q = {"v": g.vector, "s": g.scalar, "t": g.tensor, "g": g, "y": g.sync}
+    SEM = {"v": "sv", "s": "ss", "t": "st", "g": "sg"}
+    know = {q: {} for q in Q}
+    cnt, snap, nd = {}, {}, [0]
+    prog, boost, mark = [], [0.0], [0]
+
+    def a(n, lo=0, hi=None, st=1, r=None, r0=0):
+        if n in VIEW:
+            b, c, w = VIEW[n]
+            return a(b, c + lo, c + (w if hi is None else hi), st, r, r0)
+        return (n, lo, SCRATCH[n][1][1] if hi is None else hi, st, r0, SCRATCH[n][1][0] if r is None else r)
+
+    def ind(w, o):
+        return ("@", w, o)
+
+    def ap(o):
+        if o[0] == "@":
+            return ap(o[1]).indirect(ap(o[2]))
+        if o[0] == "!":
+            return o[1]
+        b = T[o[0]]
+        return b[o[4]:o[5], o[1]:o[2]] if o[3] == 1 else b[o[4]:o[5], o[1]:o[2]:o[3]]
+
+    def parts(o):
+        return [o[1], o[2]] if o[0] == "@" else [] if o[0] == "!" else [o]
+
+    def flat(reads, writes):
+        return [(k, p) for k, ops in (("r", reads), ("w", writes)) for o in ops for p in parts(o)]
+
+    def size(o):
+        return (o[2][2] - o[2][1]) * 16 if o[0] == "@" else (o[2] - o[1] + o[3] - 1) // o[3]
+
+    def meets(q, acc, lg):
+        for kind, (n, lo, hi, st, r0, r1) in acc:
+            for e in lg.get(n, []):
+                if n in PSUM and e[4] != q:
+                    yield e, kind
+                elif lo < e[1] and e[0] < hi and "w" in (kind, e[2]):
+                    yield e, kind
+                elif n in PSUM and q == "t" and kind == "w" and e[2] == "w":
+                    yield e, kind
+
+    def note(q, acc, lg, ref):
+        for kind, (n, lo, hi, st, r0, r1) in acc:
+            old = lg.get(n, [])
+            if kind == "w" and st == 1 and n not in PSUM:
+                old = [e for e in old if not (lo <= e[0] and e[1] <= hi)]
+            if n in PSUM and kind == "w":
+                old = [e for e in old if e[4] == q and not (st == 1 and lo <= e[0] and e[1] <= hi)]
+            lg[n] = old + [(lo, hi, kind, ref, q)]
+
+    def add(q, call, reads, writes, dur, lat=0.0, kind="c", extra=None):
+        prog.append({"up": boost[0], "id": len(prog) - mark[0], "q": q, "call": call, "acc": flat(reads, writes), "dur": dur, "lat": lat, "kind": kind, "extra": extra})
+
+    def vcost(o, ins, two=False):
+        n = max(size(x) for x in ins)
+        if any(x[0] == "@" for x in ins):
+            return GFIX + CYC * CG * n
+        f = 2.0 if two and not any(x[0] in PSUM for x in ins) else 1.0
+        return FIX + CYC * max(64, n * f)
+
+    def tt(o, x, y, op):
+        add("v", lambda: g.vector.tensor_tensor(ap(o), ap(x), ap(y), op), [x, y], [o], vcost(o, [x, y], True))
+
+    def ts(o, x, s1, op0, s2=None, op1=None):
+        def call():
+            if op1 is None:
+                return g.vector.tensor_scalar(ap(o), ap(x), s1, None, op0)
+            return g.vector.tensor_scalar(ap(o), ap(x), s1, s2, op0, op1)
+        add("v", call, [x], [o], vcost(o, [x]))
+
+    def cp(o, x):
+        add("v", lambda: g.vector.tensor_copy(ap(o), ap(x)), [x], [o], vcost(o, [x]))
+
+    def scan(o, d0, d1, op0, op1):
+        add("v", lambda: g.vector.tensor_tensor_scan(ap(o), ap(d0), ap(d1), 0.0, op0, op1), [d0, d1], [o], vcost(o, [d1]))
+
+    def act(o, x, func, scale=1.0, bias=0.0):
+        rd = [x] + ([scale] if isinstance(scale, tuple) else [])
+
+        def call():
+            return g.scalar.activation(ap(o), ap(x), func, bias, ap(scale) if isinstance(scale, tuple) else scale)
+        add("s", call, rd, [o], SFIX + CYC * size(x) * (CG if x[0] == "@" else 1.0))
+
+    def mm(o, l, r, start=True, stop=True):
+        w = 4 if SCRATCH[l[0]][2] == F32 else 1
+        add("t", lambda: g.tensor.matmul(ap(o), ap(l), ap(r), start, stop), [l, r], [o], 0.03 + PEC * w * max(min(64, size(l)), size(r)))
+
+    def tr(o, x, i):
+        add("t", lambda: g.tensor.transpose(ap(o), ap(x), ap(i)), [x, i], [o], 0.3)
+
+    def iota(o, pat, base, cmul):
+        def call():
+            if SCRATCH[o[0]][2] == I32:
+                return g.iota(ap(o), pat, base, cmul)
+            return g.iota(ap(o), pat, base, cmul, allow_small_or_imprecise_dtypes=True)
+        add("g", call, [], [o], 0.15 + 2 * CYC * size(o))
+
+    def dma(q, out, in_, lat=2.0):
+        add(q, lambda: Q[q].dma_start(ap(out), ap(in_)), [in_], [out], 0.1, lat, "d")
+
+    def dr(x):
+        return ("!", x)
+
+    def send(dst, src, to, rsem):
+        def call():
+            rid, pid, _ = topo.addr(to)
+            g.remote_dma(ap(dst), ap(src), T.sem[rsem], T.sem["rl"], pid, rid, topo.mask(core, to))
+        add("g", call, [src], [], 0.6, 0.0, "r", (rsem, len(topo.engines(core, to))))
+        add("net", None, [], [dst], 0.0, 2.2 + 0.3 * size(dst) / 256, "n", (rsem, len(topo.engines(core, to)), len(prog) - 1))
+
+    boost[0] = 1000.0
+    LD = [("ini", 0, 256, T.gs[:], 0.01), ("ini", 256, 512, T.gf[:], 0.01), ("ini", 512, 768, T.gcl[:], 0.01), ("fri", 0, 256, T.fr[:], 0.15)]
+    LD += [("ski", w, w + SKW, T.sk[:, w:w + SKW], 0.6 * SKW / 512) for w in range(0, 4096, SKW)]
+    LD += [("thi", 0, 1, T.th[:], 0.01), ("xr", 592, 4096, T.x[:, 0:3504], 2.3), ("xr", 0, 592, T.x[:, 3504:4096], 0.4)]
+    came = 0.0
+    for j, (n, lo, hi, src, us) in enumerate(LD):
+        boost[0] -= 10.0
+        came += us
+        dma("ys"[j % 2], a(n, lo, hi), dr(src), 2.0 + came - 0.05 * j)
+    boost[0] = 0.0
+    iota(a("ci"), [[1, 256]], 0, 0)
+    iota(a("pi"), [[0, 256]], 0, 1)
+    iota(a("il"), [[128, 2], [0, 8]], 16, 1)
+    iota(a("tabb", 0, 512), [[1, 512]], 16, 0)
+    iota(a("tabb", 512, 768), [[1, 256]], 16, 0)
+    iota(a("cm"), [[0, 16], [1, 16]], 0, 0)
+    iota(a("tabh", 0, 512), [[0, 512]], 0, 0)
+    iota(a("tabh", 512, 768), [[0, 256]], 1, 0)
+    iota(a("onef"), [[0, 128]], 1, 0)
+    iota(a("oneb"), [[0, 128]], 1, 0)
+    iota(a("zero"), [[0, 16]], 0, 0)
+    iota(a("lim"), [[0, 16]], 8, 0)
+    iota(a("krow", 0, 128, 1, 1), [[0, 8], [-1, 16]], 16, 0)
+    tt(a("idf"), a("pi", 0, 128), a("ci", 0, 128), OP.is_equal)
+    act(a("idb"), a("idf"), AF.Copy)
+    act(a("idk"), a("idf"), AF.Copy, 8192.0)
+    ts(a("ps"), a("pi", 0, 8), 4, OP.arith_shift_right)
+    tt(a("j8"), a("ps"), a("ci", 0, 8), OP.is_equal)
+    ts(a("pm"), a("pi"), 15, OP.bitwise_and)
+    tt(a("mske"), a("pm"), a("cm"), OP.is_equal)
+    cp(a("el"), a("ci", 0, 16))
+    ts(a("inf", 0, 256), a("ini", 0, 256), 1024, OP.mult, 16, OP.add)
+    ts(a("inf", 256, 512), a("ini", 512, 768), 1024, OP.mult, 16, OP.add)
+    tt(a("ine", 0, 256), a("inf", 0, 256), a("ini", 256, 512), OP.add)
+    tt(a("ine", 256, 512), a("inf", 256, 512), a("ci", 0, 256, 1, 8), OP.add)
+    for x in H:
+        for ch in H:
+            mm(a("pl", 16 * x + 8 * ch, 16 * x + 8 * ch + 8), a("ine", 256 * x + 128 * ch, 256 * x + 128 * ch + 128), a("idf", 0, 8, 1, 8))
+    cp(a("lsb"), a("pl", 0, 32))
+    mkA, keep, emhi = a("b1", 0, 256), a("b1", 256, 512), a("pe", 256, 512)
+    pw = (a("pl", 64, 80), a("pl", 80, 96))
+
+    def to_w(x):
+        tt(a("lh", 256 * x, 256 * x + 256), ind(a("lsb", 16 * x, 16 * x + 16), a("el")), a("mske"), OP.mult)
+        for ch in H:
+            mm(a("pl", 64 + 16 * x + 8 * ch, 72 + 16 * x + 8 * ch), a("lh", 256 * x + 128 * ch, 256 * x + 128 * ch + 128), a("j8"))
+
+    def upper(o, x):
+        ts(o, x, 1.0 / 1024, OP.mult, -1.0 / 64, OP.add)
+
+    def goal_lists(t):
+        ts(a("wi", 0, 16), pw[0], -16, OP.add)
+        ts(a("wq", 0, 16), a("wi", 0, 16), 1023, OP.bitwise_and)
+        cp(a("fl"), a("wq", 0, 16))
+        upper(a("sl", 32 * t, 32 * t + 16), pw[0])
+
+    def clause_lists(t):
+        upper(a("sl", 32 * t + 16, 32 * t + 32), pw[1])
+        ts(a("wi", 16, 32), pw[1], -16, OP.add)
+        ts(a("wq", 16, 32), a("wi", 16, 32), 1023, OP.bitwise_and)
+        tt(a("we"), a("wq", 16, 32), a("iw"), OP.is_equal)
+        ts(a("wf"), a("we"), 512, OP.mult)
+        tt(a("wh"), a("wf"), a("wq", 16, 32), OP.add)
+        cp(a("hl"), a("wh"))
+        act(a("hi"), ind(a("tabh"), a("hl")), AF.Identity)
+        act(a("hb"), ind(a("tabb"), a("hl")), AF.Identity)
+
+    def clause_side(t):
+        tt(a("tc"), ind(a("skt"), a("sl", 32 * t + 16, 32 * t + 32)), a("hb"), OP.add)
+        mm(a("d1", 256, 512), a("idb"), a("hi"), True, False)
+        mm(a("d1", 256, 512), a("idb"), a("em"), False, True)
+        act(emhi, a("d1", 256, 512), AF.Relu, 1.0, -1.0)
+
+    def next_saved():
+        upper(a("s3"), a("sv"))
+        tt(a("t4"), a("s3", 0, 16), a("s3", 16, 32), OP.mult)
+        ts(a("t8"), a("s3", 16, 32), 1, OP.add)
+        ts(a("t5"), a("t4"), 5, OP.arith_shift_right)
+        tt(a("t6"), a("t5"), a("t8"), OP.add)
+        ts(a("t7"), a("t6"), 4095, OP.bitwise_and)
+        ts(a("t1"), a("t7"), 1024, OP.mult)
+        tt(a("st"), a("t1"), a("il"), OP.add)
+
+    def own_parts(F):
+        act(a("em"), a(F, 0, 256), AF.Relu, -1.0, 1.0)
+        act(a("f3p"), a(F, 0, 256), AF.Relu, 1.0, -float(U))
+        act(a("own3"), a("f3p"), AF.Identity, 1.0, float(U))
+
+    ts(a("wf"), a("ci", 0, 16), 16, OP.mult)
+    tt(a("iw"), a("wf"), a("pm", 0, 16), OP.add)
+    to_w(0)
+    goal_lists(4)
+    to_w(1)
+    clause_lists(4)
+    act(a("fb"), ind(a("tabb", 0, 512), a("fl")), AF.Identity)
+    ts(a("frs"), a("fri"), 9, OP.arith_shift_right)
+    ts(keep, a("frs"), 512, OP.mult, 16 + U, OP.add)
+    tt(a("x3"), a("fri"), keep, OP.add)
+    ts(a("frm"), a("fri"), 0, OP.is_ge)
+    tt(a("f0", 0, 256), a("x3"), a("frm"), OP.mult)
+    ts(mkA, a("frm"), 2, OP.mult)
+    act(a("f0", 256, 512), a("f0", 0, 256), AF.Identity)
+    own_parts("f0")
+    for j in range(8):
+        s = 512 * j
+        if j in KS:
+            h = a(("pr", "sr")[j % 2])
+            cp(a("skv", s, s + 512), a("ski", s, s + 512))
+            act(a("sks", s, s + 512), a("skv", s, s + 512), AF.Sign, -1.0, 4095.5)
+            mm(h, a("idf"), a("skv", s, s + 512), True, False)
+            mm(h, a("idk"), a("sks", s, s + 512), False, True)
+            act(a("skt", s, s + 512), h, AF.Identity, 1024.0, float(U))
+            continue
+        h = a(("d0", "d1")[j % 2])
+        ts(h, a("ski", s, s + 512), 4096, OP.is_lt, 16384, OP.mult)
+        tt(a("skv", s, s + 512), a("ski", s, s + 512), h, OP.add)
+        act(a("skt", s, s + 512), a("skv", s, s + 512), AF.Identity, 1024.0, -float(U))
+    act(a("b16"), a("j8"), AF.Copy, 16.0)
+    ts(a("k0"), a("pm", 0, 8), 0, OP.is_equal)
+    ts(a("rst"), a("cm"), 0, OP.not_equal)
+    ts(a("thf", 0, 1), a("thi", 0, 1), 16, OP.mult, 16, OP.add)
+    act(a("dg"), a("idf"), AF.Copy, a("thf", 0, 1))
+    mm(a("pr", 0, 128), a("onef"), a("dg"))
+    for ch in H:
+        act(a("thrt", 128 * ch, 128 * ch + 128), a("pr", 0, 128), AF.Copy)
+    ts(a("thj", 0, 1), a("thi", 0, 1), -1, OP.add)
+    ts(a("thj", 1, 2), a("thj", 0, 1), 1, OP.arith_shift_right)
+    ts(a("thf", 1, 2), a("thj", 1, 2), 16, OP.mult, 16, OP.add)
+    act(a("sv"), a("lsb"), AF.Copy)
+    next_saved()
+
+    def places(raw, m, p, q, pr, r, u):
+        for w in PH:
+            ts(a(m, *w), a(raw, *w), U - 1, OP.bitwise_and)
+            ts(a(q, *w), a(raw, *w), 1023, OP.bitwise_and)
+            ts(a(p, *w), a(m, *w), 1.0 / 1024, OP.mult, 592 - 1.0 / 64, OP.add)
+            tt(a(pr, *w), a(p, *w), a(q, *w), OP.mult)
+            ts(a(r, *w), a(pr, *w), 4, OP.arith_shift_right, 4095, OP.bitwise_and)
+            cp(a(u, *w), a(r, *w))
+
+    for t in range(RO):
+        F, last = "f%d" % t, t == RO - 1
+        b = 32 * ((t + 4) % 5)
+        mark[0] = len(prog) - 500 if t else mark[0]
+        if t == 0:
+            clause_side(4)
+        if t == 0:
+            tt(a("tg"), ind(a("skt"), a("sl", b, b + 16)), a("fb"), OP.add)
+            tt(a("rawg"), ind(a(F, 0, 512), a("fl")), a("tg"), OP.max)
+        else:
+            tt(a("tg"), ind(a("skt"), a("sarr", 16 * t, 16 * t + 16)), a("tabb", 256, 512), OP.add)
+            for lo, hi in PH:
+                tt(a("rawg", lo, hi), a(F, 256 + lo, 256 + hi), a("tg", lo, hi), OP.max)
+        boost[0] = UP
+        places("rawg", "ga", "pg", "qg", "prg", "rg", "ug")
+        boost[0] = 0.0
+        for lo, hi in GCH:
+            act(a("ub", lo, hi), ind(a("xr"), a("ug", lo // 16, hi // 16)), AF.Identity)
+        for lo, hi in PH:
+            e = a("b0", lo, hi)
+            tt(e, a("pe", 256 + lo, 256 + hi), a("ga", lo, hi), OP.mult)
+            tt(a(F, 512 + lo, 512 + hi), a("own3", lo, hi), e, OP.add)
+        tt(a("rawc"), ind(a(F), a("hl")), a("tc"), OP.max)
+        places("rawc", "ca", "pc", "qc", "prc", "rc", "uc")
+        for lo, hi in VCH:
+            tt(a("df", lo, hi), ind(a("xr"), a("uc", lo // 16, hi // 16)), a("ub", lo, hi), OP.subtract)
+            act(a("ab", lo, hi), a("df", lo, hi), AF.Abs)
+        for ch in H:
+            D = ("d0", "d1")[ch]
+            mm(a(D, 0, 128), a("oneb", 0, 128, 1, 1), a("krow", 0, 128, 1, 1), True, False)
+            for k in range(16):
+                mm(a(D, k, 128, 16), a("ab", 2048 * ch + k, 2048 * ch + 2048, 16), a("b16"), False, k == 15)
+        mm(a("pr", 256, 512), a("idf"), a(F, 512, 768))
+        tt(a("fr5"), a("rawc"), a("pr", 256, 512), OP.is_equal)
+        tt(a("mk2"), a("fr5"), mkA, OP.max)
+        for ch in H:
+            D, R = a(("d0", "d1")[ch], 0, 128), a(("sr", "pe")[ch], 0, 128)
+            lo, hi, l8 = 128 * ch, 128 * ch + 128, (8 * ch, 8 * ch + 8)
+            tt(a("nov", lo, hi), D, a("thrt", lo, hi), OP.is_le)
+            tt(a("key", lo, hi), a("nov", lo, hi), D, OP.mult)
+            scan(a("cnt", lo, hi), a("rst", lo, hi), a("nov", lo, hi), OP.mult, OP.add)
+            scan(a("sm", lo, hi), a("rst", lo, hi), a("key", lo, hi), OP.mult, OP.max)
+            tt(a("cl", *l8), a("cnt", lo + 15, hi, 16), a("lim", *l8), OP.is_le)
+            tt(a("smx", *l8), a("sm", lo + 15, hi, 16), a("cl", *l8), OP.add)
+            tt(a("sel", lo, hi), ind(a("smx", *l8), a("el", 0, 8)), a("key", lo, hi), OP.is_equal)
+            mm(R, a("sel", lo, hi), a("idb"))
+            tt(a("pgc", lo, hi), a("ga", lo, hi), R, OP.mult)
+            tt(a("pgc", 256 + lo, 256 + hi), a("ca", lo, hi), R, OP.mult)
+        act(a("lhb", 0, 256), ind(a("cl"), a("el")), AF.Identity)
+        for ch in H:
+            mm(a("pr", 128 * ch, 128 * ch + 128), a("lhb", 128 * ch, 128 * ch + 128), a("idb"))
+        tt(keep, a("mk2"), a("pr", 0, 256), OP.is_gt)
+        tt(a("oi") if last else a(F, 0, 256), a(F, 512, 768), keep, OP.mult)
+        if not last:
+            act(a("rcb"), a("pr", 0, 256), AF.Copy)
+        for ch in H:
+            act(a("thp", 128 * ch, 128 * ch + 128), a(("sr", "pe")[ch], 0, 128), AF.Copy, a("thf", 1, 2))
+        tt(a("clst", 0, 16), a("cl"), a("sv", 0, 16), OP.mult)
+        tt(a("clst", 16, 32), a("cl"), a("st"), OP.mult)
+        for x in H:
+            B, c = (("pl", 0), ("d1", 128))[x]
+            mm(a(B, c, c + 16), a("idb"), a("zero"), True, False)
+            mm(a(B, c, c + 8), a("pgc", 256 * x, 256 * x + 128), a("j8"), False, False)
+            mm(a(B, c, c + 16), a("idf"), a("clst", 16 * x, 16 * x + 16), False, False)
+            mm(a(B, c + 8, c + 16), a("pgc", 256 * x + 128, 256 * x + 256), a("j8"), False, True)
+            cp(a("lsb", 16 * x, 16 * x + 16), a(B, c, c + 16))
+        if not last:
+            to = T.cores[(rank + 1 + t % 3) % N]
+            to_w(0)
+            goal_lists(t)
+            send(a("sarr", 16 * t + 16, 16 * t + 32), a("sl", 32 * t, 32 * t + 16), to, "as%d" % t)
+            act(a("snd%d" % t), ind(a(F, 0, 512), a("fl")), AF.Identity)
+            send(a("f%d" % (t + 1), 256, 512), a("snd%d" % t), to, "ac%d" % t)
+            to_w(1)
+        for ch in H:
+            mm(a("pl", 32 + 8 * ch, 40 + 8 * ch), a("thp", 128 * ch, 128 * ch + 128), a("j8"))
+        if not last:
+            for ch in H:
+                mm(a("pl", 48 + 8 * ch, 56 + 8 * ch), a("rcb", 128 * ch, 128 * ch + 128), a("k0"))
+        tt(a("sc", 0, 16), a("smx"), a("pl", 32, 48), OP.is_le)
+        if not last:
+            clause_lists(t)
+            act(a("par", 0, 16), a("pl", 48, 64), AF.Abs, 1.0, -4.0)
+            act(a("par", 16, 32), a("par", 0, 16), AF.Abs, 1.0, -2.0)
+            act(a("par", 32, 48), a("par", 16, 32), AF.Abs, 1.0, -1.0)
+            act(a("lim"), a("par", 32, 48), AF.Identity, 1.0, 7.0)
+            own_parts(F)
+            act(a("f%d" % (t + 1), 0, 256), a(F, 0, 256), AF.Identity)
+            clause_side(t)
+        boost[0] = UQ
+        act(a("lhb", 256, 512), ind(a("sc", 0, 16), a("el")), AF.Identity, -1.0, 1.0)
+        boost[0] = 0.0
+        tt(a("s1"), a("lsb"), a("sv"), OP.subtract)
+        tt(a("sc", 16, 32), a("sc", 0, 16), a("cl"), OP.add)
+        tt(a("s2"), a("s1"), a("sc"), OP.mult)
+        tt(a("sv"), a("sv"), a("s2"), OP.add)
+        boost[0] = UQ
+        for ch in H:
+            mm(a("pr", 256 + 128 * ch, 384 + 128 * ch), a("lhb", 256 + 128 * ch, 384 + 128 * ch), a("idb"))
+        boost[0] = 0.0
+        if not last:
+            next_saved()
+        boost[0] = UQ
+        tt(a("eqm"), a("mk2"), a("pr", 256, 512), OP.is_gt)
+        if last:
+            break
+        tt(mkA, keep, a("eqm"), OP.add)
+        boost[0] = 0.0
+
+    boost[0] = 0.0
+    ts(a("op"), a("oi"), 10, OP.arith_shift_right, 4095, OP.bitwise_and)
+    ts(mkA, a("op"), -512, OP.mult, -16 - U, OP.add)
+    tt(a("oy"), a("oi"), mkA, OP.add)
+    tt(a("oy2"), keep, a("eqm"), OP.subtract)
+    ts(mkA, a("oy"), 2, OP.mult, -1, OP.max)
+    tt(a("oz"), a("oy2"), mkA, OP.add)
+    dma("y", dr(T.yf[:]), a("oz"))
+    cp(a("fin", 0, 32), a("lsb"))
+    cp(a("fin", 32, 64), a("sv"))
+    upper(a("fip"), a("fin"))
+    ts(a("fiq", 0, 48), a("fip", 0, 48), -512, OP.mult, -16, OP.add)
+    tt(a("fim", 0, 48), a("fin", 0, 48), a("fiq", 0, 48), OP.add)
+    cp(a("fim", 48, 64), a("fip", 48, 64))
+    tr(a("pl", 0, 128, 1, 64), a("fim"), a("idf"))
+    cp(a("fot"), a("pl", 0, 128, 1, 64))
+    for j, y in enumerate((T.yg, T.yc, T.ysg, T.yk)):
+        for ch in H:
+            r0 = 16 * j + 8 * ch
+            dma("ys"[(2 * j + ch) % 2], dr(y[:, 128 * ch:128 * ch + 128]), a("fot", 0, 128, 1, r0 + 8, r0))
+
+    lg, n = {}, len(prog)
+    dep, succ = [[] for _ in range(n)], [[] for _ in range(n)]
+    for i, p in enumerate(prog):
+        ds, q = {}, p["q"] if p["kind"] == "c" else "#%d" % i
+        for e, kind in meets(q, p["acc"], lg):
+            ds[e[3]] = 0.0 if (p["q"] == "t" and prog[e[3]]["q"] == "t") else WAKE
+        if p["kind"] == "n":
+            ds[p["extra"][2]] = 0.0
+        note(q, p["acc"], lg, i)
+        dep[i] = sorted(ds.items())
+        for d, w in dep[i]:
+            succ[d].append((i, w))
+    rankp, base = [0.0] * n, [0.0] * n
+    for i in range(n - 1, -1, -1):
+        p = prog[i]
+        base[i] = p["dur"] + p["lat"] + max([w + base[j] for j, w in succ[i]] + [0.0])
+        rankp[i] = base[i] + p["up"] + PREF.get(p["id"], 0.0)
+    free = {q: 0.0 for q in list(Q) + ["net"]}
+    left = [len(d) for d in dep]
+    done = [0.0] * n
+    ready = {q: [] for q in free}
+    for i in range(n):
+        if not left[i]:
+            ready[prog[i]["q"]].append((0.0, i))
+    plan = []
+    for _ in range(n):
+        best = None
+        for q in free:
+            if not ready[q]:
+                continue
+            t0 = max(free[q], min(e for e, i in ready[q])) if q != "net" else min(e for e, i in ready[q])
+            c = max((rankp[i], -i, e) for e, i in ready[q] if e <= t0 + SLACK)
+            i = -c[1]
+            if c[2] > t0:
+                short = [(rankp[k], -k) for e, k in ready[q] if e <= t0 + 1e-9 and t0 + prog[k]["dur"] <= c[2] + OVER]
+                if short:
+                    i = -max(short)[1]
+                else:
+                    t0 = c[2]
+            if best is None or t0 < best[0]:
+                best = (t0, i, q)
+        t0, i, q = best
+        ready[q] = [x for x in ready[q] if x[1] != i]
+        if q != "net":
+            free[q] = t0 + prog[i]["dur"]
+        done[i] = t0 + prog[i]["dur"] + prog[i]["lat"]
+        plan.append(i)
+        for j, w in succ[i]:
+            left[j] -= 1
+            if not left[j]:
+                ready[prog[j]["q"]].append((max(done[d] + w2 for d, w2 in dep[j]), j))
+
+    def wait(q, sem, c):
+        if know[q].get(sem, 0) < c:
+            Q[q].wait_ge(T.sem[sem], c)
+            for k, v in snap.get((sem, c), {}).items():
+                know[q][k] = max(know[q].get(k, 0), v)
+            know[q][sem] = c
+
+    ref = {}
+    for i in plan:
+        p = prog[i]
+        q = p["q"]
+        if p["kind"] != "n":
+            want = {}
+            for d, w in dep[i]:
+                if q == "t" and prog[d]["q"] == "t":
+                    continue
+                sem, c = ref[d]
+                want[sem] = max(want.get(sem, 0), c)
+            for sem in sorted(want, key=lambda s: (s == SEM.get(q), s)):
+                wait(q, sem, want[sem])
+            inst = p["call"]()
+        if p["kind"] == "c":
+            sem = SEM[q]
+            inst.then_inc(T.sem[sem], 1)
+            cnt[sem] = cnt.get(sem, 0) + 1
+        elif p["kind"] == "d":
+            sem = "d%d" % nd[0]
+            nd[0] += 1
+            inst.then_inc(T.sem[sem], 16)
+            cnt[sem] = 16
+        elif p["kind"] == "r":
+            sem = "rl"
+            cnt[sem] = cnt.get(sem, 0) + p["extra"][1]
+        else:
+            sem = p["extra"][0]
+            cnt[sem] = p["extra"][1]
+        ref[i] = (sem, cnt[sem])
+        if p["kind"] != "n":
+            snap[ref[i]] = dict(know[q])
+    for sem in sorted(cnt):
+        g.wait_ge(T.sem[sem], cnt[sem])

@@ -2,7 +2,7 @@ from concourse.mybir import AluOpType, ActivationFunctionType
 
 OP = AluOpType
 AF = ActivationFunctionType
-U = 1 << 22
+U, L, O = 1 << 22, 1 << 23, 592 * 1024
 NF, RO, N = 256, 5, 4
 H = (0, 1)
 F32, BF, I32, U16 = "float32", "bfloat16", "int32", "uint16"
@@ -16,27 +16,38 @@ def _bufs(where, dtype, text):
         SCRATCH[n] = (where, [int(r), int(c)], dtype)
 
 
-_bufs("sbuf", F32, "skv:4096 skt:4096 inf:8x512 ine:8x512 thf:8 tabb:768 tabh:768 j8:8 mske:256 rst:256 idf:128 onef:128 thrt:256 "
-      "iw:16 il:16 lim:16 fb:256 hb:256 tg:256 tc:256 f3p:256 own3:256 x3:256 eqm:256 nov:256 key:256 cnt:256 sm:256 "
-      "cl:16 smx:16 pgc:512 thp:256 clst:32 lsb:32 lh:512 we:16 wf:16 wh:16 sc:32 sv:32 s1:32 s2:32 t1:16 st:16 par:64 "
-      "fot:64x128 oy:256 oy2:256 oz:256 f0:768 f1:768 f2:768 f3:768 f4:768 snd0:256 snd1:256 snd2:256 snd3:256")
-_bufs("sbuf", BF, "idk:128 xr:4096 ub:4096 hi:256 em:256 df:4096 ab:4096 b16:8 idb:128 k0:8 zero:16 rcb:256 oneb:128 krow:128 fr5:256 mk2:256 sel:256 lhb:512")
-_bufs("sbuf", I32, "ski:4096 ini:8x768 fri:256 thi:8 thj:8 pi:256 ci:256 pm:256 cm:256 ps:8 rawg:256 rawc:256 ga:256 ca:256 "
-      "pg:256 qg:256 prg:256 rg:256 pc:256 qc:256 prc:256 rc:256 wi:32 wq:32 s3:32 t4:16 t5:16 t6:16 t7:16 t8:16 fip:64 oi:256 op:256")
-_bufs("sbuf", U16, "ug:256 uc:256 el:16 fl:16 hl:16 sl:160 sarr:80")
-_bufs("psum", F32, "b0:512 b1:512 pe:512 pl:512 pr:512 sr:512 d0:512 d1:512")
-SEMAPHORES = ["sv", "ss", "st", "sg", "rl"] + ["as%d" % t for t in range(4)] + ["ac%d" % t for t in range(4)] + ["d%d" % t for t in range(24)]
-VIEW = {"sks": ("df", 0, 4096), "frs": ("op", 0, 256), "frm": ("oy", 0, 256), "dg": ("oz", 0, 128), "fin": ("lh", 0, 64), "fiq": ("lh", 64, 64), "fim": ("lh", 128, 64)}
+_bufs("sbuf", F32, "skv:4096 skt:4688 tabb:784 j8:8 mske:256 rst:128 idf:128 go:128 gok:128 onef:128 e8:8x128 m16:16x128 vals:8 "
+      "iw:32 iu:32 il:24 lim:8 hb:256 tg:256 tc:256 fu:256 key:256 sm:256 pgc:512 lh:512 we:16 wf:16 sv:32 svs:32 sg1:32 sh:32 mx:32 par:8 "
+      "fim:64 fot:32x256 oz:256 f0:784 f1:784 f2:784 f3:784 f4:784 r0:528 r1:528 r2:528 r3:528")
+_bufs("sbuf", BF, "idk:128 xr:4096 ub:4096 df:4096 ab:4096 bw:24 idb:128 id4:128 idh:128 gou:128 gon:128 oneb:128 crow:2x384 cu:1x256 five:1x128 mtwo:1x128 idu:128 idn:128 idc:128 "
+      "rstb:128 sg:512 cnt:256 sel:256 rs:256 clx:256 sa:256 sb:256")
+_bufs("sbuf", I32, "ski:4096 ini:48 fri:256 thi:8 thj:8 pi:8 ci:40 pm:8 rawg:256 rawc:256 ga:256 ca:256 "
+      "pg:256 qg:256 prg:256 rg:256 pc:256 qc:256 prc:256 rc:256 w:32 w2:32 wq:64 s3:32 t4:24 t5:24 t6:24 t7:24 t8:24 fi:64 fq:64 oi:256")
+_bufs("sbuf", U16, "ug:256 uc:256 el:24 ek:8 gl:320 arr:192")
+_bufs("psum", F32, "d0:512 d1:512 p3:512 ea:512 eb:512 pl:512 fa:512 fb:512")
+SEMAPHORES = ["sv", "ss", "st", "sg", "rl"] + [n + str(t) for n in ("al", "ao", "ag") for t in range(8)] + ["d%d" % t for t in range(32)]
+VIEW = {"sks": ("df", 0, 4096), "frs": ("oi", 0, 256), "frm": ("oz", 0, 256), "o2": ("pg", 0, 256), "oq": ("qg", 0, 256), "o3": ("tg", 0, 256), "fb0": ("key", 0, 256)}
 PSUM = [n for n in SCRATCH if SCRATCH[n][0] == "psum"]
+OWN, GH, F3 = (16, 272), (272, 528), (528, 784)
 GCH = [(0, 1024), (1024, 2048), (2048, 3072), (3072, 4096)]
 VCH = [(0, 1024), (1024, 2048), (2048, 3072), (3072, 3584), (3584, 4096)]
+DCH = [[(0, 128)], [(0, 128)]]
 PH = [(0, 128), (128, 256)]
+ACH = [(0, 1024), (1024, 2048), (2048, 3072), (3072, 3584), (3584, 4096)]
 SKW = 512
 KS = (1, 3, 5)
-CYC, CG, FIX, GFIX, SFIX, WAKE, PEC = 0.00083, 1.5, 0.01, 0.05, 0.06, 0.11, 0.00071
-SLACK, OVER, UP, UQ = 0.1, 0.05, 1.5, 3.0
-PREF = {33: 8, 55: -8, 110: 8, 124: -3, 125: -8, 137: 8, 142: -1.5, 146: 1.5, 166: -3, 211: -8, 214: -8, 224: 3,
-        511: -1.5, 512: -3, 527: -3, 581: -3, 605: 3, 622: -3}
+CYC, CG, FIX, GFIX, SFIX, PEC, PFIX = 0.00085, 1.2, 0.005, 0.05, 0.05, 0.0005, 0.015
+WAKE = {"v": 0.16, "vv": 0.22, "s": 0.24, "t": 0.3, "tt": 0.0, "g": 0.1, "y": 0.2, "net": 0.2, "vg": 0.3}
+RI, RL, RB = 0.25, 1.3, 0.4
+NOWAR = False
+VS = {"y1", "r1"}
+SLACK, OVER, PASSES = 0.1, 0.05, 2
+T0, PERIOD = 8.0, 17.6
+UPS = {"g0": 5.0, "col": 5.0, "u0": 7.3, "u1": 8.7, "c0": 6.0, "g1": 7.0, "w0": 9.9, "w1": 11.3, "c1": 12.7, "u2": 10.2, "a0": 11.6, "w2": 14.0, "a1": 12.8, "u3": 13.7,
+       "d0": 10, "w3": 15.9, "a2": 15.5, "f0": 15, "m0": 15, "w4": 16.8, "a3": 16.8, "a4": 17.6, "d1": 10, "f1": 18, "m1": 18, "l0": 15, "l1": 18, "k0": 20.5, "k1": 21,
+       "fu": 22, "sv": 22, "o0": 17, "o1": 18, "x1": 8.5, "j0": 15, "j1": 21, "col1": 5}
+PLAN = []
+TURNS, STEPS, HEAT, FAR = 12, 40000, 0.2, 40
 
 
 def rank_program(g, core, T, topo):
@@ -47,7 +58,7 @@ def rank_program(g, core, T, topo):
     SEM = {"v": "sv", "s": "ss", "t": "st", "g": "sg"}
     know = {q: {} for q in Q}
     cnt, snap, nd = {}, {}, [0]
-    prog, boost, mark = [], [0.0], [0]
+    prog, boost, mark, seen = [], [0.0], [0, 0], {}
 
     def a(n, lo=0, hi=None, st=1, r=None, r0=0):
         if n in VIEW:
@@ -59,6 +70,8 @@ def rank_program(g, core, T, topo):
         return ("@", w, o)
 
     def ap(o):
+        if not isinstance(o, tuple):
+            return o
         if o[0] == "@":
             return ap(o[1]).indirect(ap(o[2]))
         if o[0] == "!":
@@ -70,7 +83,7 @@ def rank_program(g, core, T, topo):
         return [o[1], o[2]] if o[0] == "@" else [] if o[0] == "!" else [o]
 
     def flat(reads, writes):
-        return [(k, p) for k, ops in (("r", reads), ("w", writes)) for o in ops for p in parts(o)]
+        return [(k, p) for k, ops in (("r", reads), ("w", writes)) for o in ops if isinstance(o, tuple) for p in parts(o)]
 
     def size(o):
         return (o[2][2] - o[2][1]) * 16 if o[0] == "@" else (o[2] - o[1] + o[3] - 1) // o[3]
@@ -91,17 +104,21 @@ def rank_program(g, core, T, topo):
             if kind == "w" and st == 1 and n not in PSUM:
                 old = [e for e in old if not (lo <= e[0] and e[1] <= hi)]
             if n in PSUM and kind == "w":
-                old = [e for e in old if e[4] == q and not (st == 1 and lo <= e[0] and e[1] <= hi)]
+                old = [e for e in old if (q != "t" if e[4] != q else not (st == 1 and lo <= e[0] and e[1] <= hi))]
             lg[n] = old + [(lo, hi, kind, ref, q)]
 
     def add(q, call, reads, writes, dur, lat=0.0, kind="c", extra=None):
-        prog.append({"up": boost[0], "id": len(prog) - mark[0], "q": q, "call": call, "acc": flat(reads, writes), "dur": dur, "lat": lat, "kind": kind, "extra": extra})
+        key = None if boost[0] is None else (mark[1], mark[0])
+        seen[key] = seen.get(key, -1) + 1
+        prog.append({"up": boost[0], "id": key and key + (seen[key],), "q": q, "call": call, "acc": flat(reads, writes), "dur": dur, "lat": lat, "kind": kind, "extra": extra})
 
     def vcost(o, ins, two=False):
         n = max(size(x) for x in ins)
         if any(x[0] == "@" for x in ins):
             return GFIX + CYC * CG * n
         f = 2.0 if two and not any(x[0] in PSUM for x in ins) else 1.0
+        if not two and all(SCRATCH[x[0]][2] in (BF, U16) for x in ins + [o]):
+            f = 0.5
         return FIX + CYC * max(64, n * f)
 
     def tt(o, x, y, op):
@@ -111,35 +128,41 @@ def rank_program(g, core, T, topo):
         def call():
             if op1 is None:
                 return g.vector.tensor_scalar(ap(o), ap(x), s1, None, op0)
-            return g.vector.tensor_scalar(ap(o), ap(x), s1, s2, op0, op1)
-        add("v", call, [x], [o], vcost(o, [x]))
+            return g.vector.tensor_scalar(ap(o), ap(x), s1, ap(s2), op0, op1)
+        add("v", call, [x, s2], [o], vcost(o, [x]))
 
     def cp(o, x):
         add("v", lambda: g.vector.tensor_copy(ap(o), ap(x)), [x], [o], vcost(o, [x]))
 
     def scan(o, d0, d1, op0, op1):
-        add("v", lambda: g.vector.tensor_tensor_scan(ap(o), ap(d0), ap(d1), 0.0, op0, op1), [d0, d1], [o], vcost(o, [d1]))
+        add("v", lambda: g.vector.tensor_tensor_scan(ap(o), ap(d0), ap(d1), 0.0, op0, op1), [d0, d1], [o], vcost(o, [d0, d1]))
 
-    def act(o, x, func, scale=1.0, bias=0.0):
-        rd = [x] + ([scale] if isinstance(scale, tuple) else [])
-
+    def act(o, x, func, scale=1.0, bias=0.0, acc=None):
         def call():
-            return g.scalar.activation(ap(o), ap(x), func, bias, ap(scale) if isinstance(scale, tuple) else scale)
-        add("s", call, rd, [o], SFIX + CYC * size(x) * (CG if x[0] == "@" else 1.0))
+            if acc:
+                return g.scalar.activation(ap(o), ap(x), func, ap(bias), scale, accum_out=ap(acc))
+            return g.scalar.activation(ap(o), ap(x), func, ap(bias), scale)
+        add("s", call, [x, bias], [o, acc], 0.065 + CYC * CG * size(x) if x[0] == "@" else SFIX + CYC * max(64, size(x)))
+
+    def mms(ms):
+        add("t", lambda: [g.tensor.matmul(ap(o), ap(l), ap(r), s0, s1) for o, l, r, s0, s1 in ms][-1], [x for m in ms for x in m[1:3]], [m[0] for m in ms],
+            sum(PFIX + PEC * (4 if SCRATCH[l[0]][2] == F32 else 1) * max(min(64, size(l)), size(r)) for o, l, r, s0, s1 in ms))
 
     def mm(o, l, r, start=True, stop=True):
-        w = 4 if SCRATCH[l[0]][2] == F32 else 1
-        add("t", lambda: g.tensor.matmul(ap(o), ap(l), ap(r), start, stop), [l, r], [o], 0.03 + PEC * w * max(min(64, size(l)), size(r)))
+        mms([(o, l, r, start, stop)])
 
     def tr(o, x, i):
-        add("t", lambda: g.tensor.transpose(ap(o), ap(x), ap(i)), [x, i], [o], 0.3)
+        add("t", lambda: g.tensor.transpose(ap(o), ap(x), ap(i)), [x, i], [o], 0.35)
 
     def iota(o, pat, base, cmul):
         def call():
             if SCRATCH[o[0]][2] == I32:
                 return g.iota(ap(o), pat, base, cmul)
             return g.iota(ap(o), pat, base, cmul, allow_small_or_imprecise_dtypes=True)
-        add("g", call, [], [o], 0.15 + 2 * CYC * size(o))
+        add("g", call, [], [o], 0.14 + 2 * CYC * size(o))
+
+    def pick(o, x, pat, op, base, cmul):
+        add("g", lambda: g.affine_select(ap(o), ap(x), pat, op, 0.0, base, cmul), [x], [o], 0.18 + 2 * CYC * size(o))
 
     def dma(q, out, in_, lat=2.0):
         add(q, lambda: Q[q].dma_start(ap(out), ap(in_)), [in_], [out], 0.1, lat, "d")
@@ -151,330 +174,521 @@ def rank_program(g, core, T, topo):
         def call():
             rid, pid, _ = topo.addr(to)
             g.remote_dma(ap(dst), ap(src), T.sem[rsem], T.sem["rl"], pid, rid, topo.mask(core, to))
-        add("g", call, [src], [], 0.6, 0.0, "r", (rsem, len(topo.engines(core, to))))
-        add("net", None, [], [dst], 0.0, 2.2 + 0.3 * size(dst) / 256, "n", (rsem, len(topo.engines(core, to)), len(prog) - 1))
+        add("g", call, [src], [], RI + (2.0 if rsem == "ag0" else 0.0), 0.0, "r", (rsem, len(topo.engines(core, to))))
+        add("net", None, [], [dst], 0.0, RL + RB * size(dst) / 256, "n", (rsem, len(topo.engines(core, to)), len(prog) - 1))
 
-    boost[0] = 1000.0
-    LD = [("ini", 0, 256, T.gs[:], 0.01), ("ini", 256, 512, T.gf[:], 0.01), ("ini", 512, 768, T.gcl[:], 0.01), ("fri", 0, 256, T.fr[:], 0.15)]
-    LD += [("ski", w, w + SKW, T.sk[:, w:w + SKW], 0.6 * SKW / 512) for w in range(0, 4096, SKW)]
-    LD += [("thi", 0, 1, T.th[:], 0.01), ("xr", 592, 4096, T.x[:, 0:3504], 2.3), ("xr", 0, 592, T.x[:, 3504:4096], 0.4)]
+    boost[0] = None
+    LD = [("ini", 0, 16, T.gs[:], 0.35), ("ini", 16, 32, T.gf[:], 0.35), ("ini", 32, 48, T.gcl[:], 0.35), ("fri", 0, 256, T.fr[:], 0.5)]
+    LD += [("ski", w, w + SKW, T.sk[:, w:w + SKW], 0.7 * SKW / 512) for w in range(0, 4096, SKW)]
+    LD += [("thi", 0, 1, T.th[:], 0.35), ("xr", 592, 4096, T.x[:, 0:3504], 1.6), ("xr", 0, 592, T.x[:, 3504:4096], 0.55)]
     came = 0.0
     for j, (n, lo, hi, src, us) in enumerate(LD):
-        boost[0] -= 10.0
         came += us
-        dma("ys"[j % 2], a(n, lo, hi), dr(src), 2.0 + came - 0.05 * j)
-    boost[0] = 0.0
-    iota(a("ci"), [[1, 256]], 0, 0)
-    iota(a("pi"), [[0, 256]], 0, 1)
-    iota(a("il"), [[128, 2], [0, 8]], 16, 1)
-    iota(a("tabb", 0, 512), [[1, 512]], 16, 0)
-    iota(a("tabb", 512, 768), [[1, 256]], 16, 0)
-    iota(a("cm"), [[0, 16], [1, 16]], 0, 0)
-    iota(a("tabh", 0, 512), [[0, 512]], 0, 0)
-    iota(a("tabh", 512, 768), [[0, 256]], 1, 0)
+        dma("ys"[j % 2], a(n, lo, hi), dr(src), 2.2 + came - 0.05 * j)
+    boost[0] = None
     iota(a("onef"), [[0, 128]], 1, 0)
-    iota(a("oneb"), [[0, 128]], 1, 0)
-    iota(a("zero"), [[0, 16]], 0, 0)
-    iota(a("lim"), [[0, 16]], 8, 0)
-    iota(a("krow", 0, 128, 1, 1), [[0, 8], [-1, 16]], 16, 0)
-    tt(a("idf"), a("pi", 0, 128), a("ci", 0, 128), OP.is_equal)
-    act(a("idb"), a("idf"), AF.Copy)
-    act(a("idk"), a("idf"), AF.Copy, 8192.0)
-    ts(a("ps"), a("pi", 0, 8), 4, OP.arith_shift_right)
-    tt(a("j8"), a("ps"), a("ci", 0, 8), OP.is_equal)
+    pick(a("idf"), a("onef"), [[-1, 128]], OP.is_equal, 0, 1)
+    pick(a("m16"), a("onef", 0, 128, 1, 16), [[0, 8], [1, 16]], OP.is_equal, 0, -1)
+    pick(a("e8"), a("onef", 0, 128, 1, 8), [[1, 8], [0, 16]], OP.is_equal, 0, -1)
+    pick(a("rst"), a("onef"), [[0, 8], [1, 16]], OP.not_equal, 0, 0)
+    iota(a("pi"), [[0, 8]], 0, 1)
+    iota(a("iu"), [[0, 32]], O - L, 0)
+    iota(a("ci", 0, 16), [[16, 2], [1, 8]], 0, 0)
+    iota(a("ci", 16, 24), [[16, 8]], 15, 0)
+    iota(a("ci", 24, 40), [[16, 16]], O - L + 16, 0)
+    iota(a("tabb", 0, 528), [[1, 528]], 0, 0)
+    iota(a("tabb", *F3), [[1, 256]], L + 16, 0)
+    iota(a("skt", 0, 592), [[0, 592]], 0, 0)
+    iota(a("lim"), [[0, 8]], 1, 0)
+    iota(a("five"), [[0, 128]], 5, 0)
+    iota(a("mtwo"), [[0, 128]], -2, 0)
+    iota(a("cu"), [[0, 256]], L, 0)
+    iota(a("vals"), [[0, 8]], 0, 0)
+    iota(a("il"), [[64, 3], [0, 8]], O - L + 16, 1)
+    for t in range(RO):
+        iota(a("f%d" % t, 0, 16), [[0, 16]], 0, 0)
+        if t < RO - 1:
+            iota(a("r%d" % t, 0, 16), [[0, 16]], 0, 0)
+    mm(a("ea", 0, 128), a("e8"), a("e8"))
+    mm(a("ea", 128, 136), a("e8"), a("idf", 0, 8, 1, 8))
+    mm(a("eb", 0, 128), a("m16"), a("m16"))
+    for n, w in (("go", 1.0), ("gok", 1024.0), ("gou", float(L)), ("gon", -2.0 * L)):
+        act(a(n), a("ea", 0, 128), AF.Copy, w)
+    act(a("j8"), a("ea", 128, 136), AF.Copy)
+    for ch in H:
+        act(a("mske", *PH[ch]), a("eb", 0, 128), AF.Copy)
+    for n, w in (("idb", 1.0), ("idk", -10240.0), ("id4", 4.0), ("idh", 0.5), ("idc", -2.0), ("idn", -1.0), ("idu", float(L))):
+        act(a(n), a("idf"), AF.Copy, w)
+    act(a("oneb"), a("onef"), AF.Copy)
     ts(a("pm"), a("pi"), 15, OP.bitwise_and)
-    tt(a("mske"), a("pm"), a("cm"), OP.is_equal)
-    cp(a("el"), a("ci", 0, 16))
-    ts(a("inf", 0, 256), a("ini", 0, 256), 1024, OP.mult, 16, OP.add)
-    ts(a("inf", 256, 512), a("ini", 512, 768), 1024, OP.mult, 16, OP.add)
-    tt(a("ine", 0, 256), a("inf", 0, 256), a("ini", 256, 512), OP.add)
-    tt(a("ine", 256, 512), a("inf", 256, 512), a("ci", 0, 256, 1, 8), OP.add)
-    for x in H:
-        for ch in H:
-            mm(a("pl", 16 * x + 8 * ch, 16 * x + 8 * ch + 8), a("ine", 256 * x + 128 * ch, 256 * x + 128 * ch + 128), a("idf", 0, 8, 1, 8))
-    cp(a("lsb"), a("pl", 0, 32))
-    mkA, keep, emhi = a("b1", 0, 256), a("b1", 256, 512), a("pe", 256, 512)
-    pw = (a("pl", 64, 80), a("pl", 80, 96))
+    cp(a("el"), a("ci", 0, 24))
+    cp(a("ek"), a("pm"))
+    for ch in H:
+        tt(a("iu", 16 * ch + 8, 16 * ch + 16), a("ci", 24 + 8 * ch, 32 + 8 * ch), a("pm"), OP.add)
+    act(a("iw"), a("iu"), AF.Identity, 1.0, float(L - O))
+    EX = ("ea", "eb")
+    fcs, xp, fus = (a("fa", 0, 128), a("fb", 256, 384)), a("fb", 0, 256), a("fa", 256, 512)
 
-    def to_w(x):
-        tt(a("lh", 256 * x, 256 * x + 256), ind(a("lsb", 16 * x, 16 * x + 16), a("el")), a("mske"), OP.mult)
-        for ch in H:
-            mm(a("pl", 64 + 16 * x + 8 * ch, 72 + 16 * x + 8 * ch), a("lh", 256 * x + 128 * ch, 256 * x + 128 * ch + 128), a("j8"))
+    XP = (a("fb", 0, 128), a("eb", 256, 384))
 
-    def upper(o, x):
-        ts(o, x, 1.0 / 1024, OP.mult, -1.0 / 64, OP.add)
+    def to_w(x, ch):
+        c = 256 * x + 128 * ch
+        tt(a("lh", c, c + 128), a("mske", 0, 128), a(EX[x], 128 * ch, 128 * ch + 128), OP.mult)
+        mm(a("pl", 16 * ch + 8 * x, 16 * ch + 8 * x + 8), a("lh", c, c + 128), a("j8"))
 
-    def goal_lists(t):
-        ts(a("wi", 0, 16), pw[0], -16, OP.add)
-        ts(a("wq", 0, 16), a("wi", 0, 16), 1023, OP.bitwise_and)
-        cp(a("fl"), a("wq", 0, 16))
-        upper(a("sl", 32 * t, 32 * t + 16), pw[0])
+    def lists(t, ch, xs):
+        n, l8 = 8 * len(xs), (8 * ch, 8 * ch + 8)
+        c, w = 32 * ch + 16 * xs[0], a("w", 16 * ch + 8 * xs[0], 16 * ch + 8 * xs[0] + n)
+        ts(a("wq", c, c + n), w, 1023, OP.bitwise_and)
+        ts(a("wq", c + n, c + 2 * n), w, 10, OP.arith_shift_right, 8191, OP.bitwise_and)
+        if 1 in xs:
+            h = a("wq", c + n - 8, c + n)
+            tt(a("we", *l8), h, a("iw", 16 * ch + 8, 16 * ch + 16), OP.is_equal)
+            ts(a("wf", *l8), a("we", *l8), 512, OP.mult)
+            tt(h, a("wf", *l8), h, OP.add)
+        cp(a("gl", 64 * t + c, 64 * t + c + 2 * n), a("wq", c, c + 2 * n))
 
-    def clause_lists(t):
-        upper(a("sl", 32 * t + 16, 32 * t + 32), pw[1])
-        ts(a("wi", 16, 32), pw[1], -16, OP.add)
-        ts(a("wq", 16, 32), a("wi", 16, 32), 1023, OP.bitwise_and)
-        tt(a("we"), a("wq", 16, 32), a("iw"), OP.is_equal)
-        ts(a("wf"), a("we"), 512, OP.mult)
-        tt(a("wh"), a("wf"), a("wq", 16, 32), OP.add)
-        cp(a("hl"), a("wh"))
-        act(a("hi"), ind(a("tabh"), a("hl")), AF.Identity)
-        act(a("hb"), ind(a("tabb"), a("hl")), AF.Identity)
+    def hl(t, ch):
+        c = 64 * t + 32 * ch + (16 if ch and t < 4 else 8)
+        return a("gl", c, c + 8)
 
-    def clause_side(t):
-        tt(a("tc"), ind(a("skt"), a("sl", 32 * t + 16, 32 * t + 32)), a("hb"), OP.add)
-        mm(a("d1", 256, 512), a("idb"), a("hi"), True, False)
-        mm(a("d1", 256, 512), a("idb"), a("em"), False, True)
-        act(emhi, a("d1", 256, 512), AF.Relu, 1.0, -1.0)
+    def clause_part(t, F, ch):
+        (lo, hi), c = PH[ch], 64 * t + 32 * ch
+        y = a("p3", 256 + lo, 256 + hi)
+        act(a("hb", lo, hi), ind(a("tabb"), hl(t, ch)), AF.Identity)
+        tt(a("tc", lo, hi), ind(a("skt"), a("gl", c + 24, c + 32)), a("hb", lo, hi), OP.add)
+        if "x" in VS:
+            tt(a("hb", lo, hi), a(F, 16 + lo, 16 + hi), a("tc", lo, hi), OP.min)
+            ts(XP[ch], a("hb", lo, hi), 2 * L, OP.is_lt, 2 * L, OP.mult)
+            return
+        act(a("sb", lo, hi), a(F, 16 + lo, 16 + hi), AF.Sign, 1.0, -1.5 * L)
+        act(a("sa", lo, hi), a("tc", lo, hi), AF.Sign, 1.0, -2.0 * L)
+        mms([(y, a("idb"), a("sb", lo, hi), True, False), (y, a("idb"), a("sa", lo, hi), False, True)])
+        act(XP[ch], y, AF.Relu, -float(L), 2.0 * L)
 
-    def next_saved():
-        upper(a("s3"), a("sv"))
-        tt(a("t4"), a("s3", 0, 16), a("s3", 16, 32), OP.mult)
-        ts(a("t8"), a("s3", 16, 32), 1, OP.add)
-        ts(a("t5"), a("t4"), 5, OP.arith_shift_right)
-        tt(a("t6"), a("t5"), a("t8"), OP.add)
-        ts(a("t7"), a("t6"), 4095, OP.bitwise_and)
-        ts(a("t1"), a("t7"), 1024, OP.mult)
-        tt(a("st"), a("t1"), a("il"), OP.add)
+    def up(name, more=0.0):
+        boost[0], mark[0] = T0 + PERIOD * mark[1] + UPS[name] + more, name
 
-    def own_parts(F):
-        act(a("em"), a(F, 0, 256), AF.Relu, -1.0, 1.0)
-        act(a("f3p"), a(F, 0, 256), AF.Relu, 1.0, -float(U))
-        act(a("own3"), a("f3p"), AF.Identity, 1.0, float(U))
+    def save(sv, out):
+        ts(a("w2"), a("w"), 2 * L - 1, OP.bitwise_and)
+        ts(a("sg1"), a("w2"), L, OP.is_ge, -2 * L, OP.mult)
+        tt(a("sh"), sv, a("sg1"), OP.add)
+        tt(out, a("w2"), a("sh"), OP.max)
 
-    ts(a("wf"), a("ci", 0, 16), 16, OP.mult)
-    tt(a("iw"), a("wf"), a("pm", 0, 16), OP.add)
-    to_w(0)
-    goal_lists(4)
-    to_w(1)
-    clause_lists(4)
-    act(a("fb"), ind(a("tabb", 0, 512), a("fl")), AF.Identity)
-    ts(a("frs"), a("fri"), 9, OP.arith_shift_right)
-    ts(keep, a("frs"), 512, OP.mult, 16 + U, OP.add)
-    tt(a("x3"), a("fri"), keep, OP.add)
-    ts(a("frm"), a("fri"), 0, OP.is_ge)
-    tt(a("f0", 0, 256), a("x3"), a("frm"), OP.mult)
-    ts(mkA, a("frm"), 2, OP.mult)
-    act(a("f0", 256, 512), a("f0", 0, 256), AF.Identity)
-    own_parts("f0")
+    def next_saved(sv, own, d):
+        n = 32 - d
+        ts(a("s3"), a(sv), 1.0 / 1024, OP.mult, -8192 - 592 - 1.0 / 64, OP.add)
+        tt(a("t4", 0, n), a("s3", 0, n), a("s3", d, 32), OP.mult)
+        ts(a("t5", 0, n), a("t4", 0, n), 5, OP.arith_shift_right, 4095, OP.bitwise_and)
+        tt(a("t6", 0, n), a("t5", 0, n), a("s3", d, 32), OP.add)
+        ts(a("t7", 0, n), a("t6", 0, n), 1024, OP.mult, 1024, OP.add)
+        ts(a("t8", 0, n), a("t7", 0, n), U - 1, OP.bitwise_and)
+        tt(a("mx", d, 32), a("t8", 0, n), own, OP.add)
+        for c in range(0, 32, 2 * d):
+            if "mx" in VS:
+                ts(a("mx", c, c + d), a(sv, c, c + d), -2 * L, OP.add)
+            else:
+                act(a("mx", c, c + d), a(sv, c, c + d), AF.Identity, 1.0, -2.0 * L)
+
+    def sign(o, x, name):
+        if name in VS:
+            ts(o, x, 1, OP.min, -1, OP.max)
+        else:
+            act(o, x, AF.Sign)
+
+    ts(a("wq", 0, 16), a("ini", 0, 16), 1024, OP.mult, 16, OP.add)
+    tt(a("wq", 16, 32), a("wq", 0, 16), a("ini", 16, 32), OP.add)
+    tt(a("lh", 0, 128), ind(a("wq", 16, 32), a("ek")), a("go"), OP.mult)
+    tt(a("lh", 128, 256), ind(a("ini", 32, 48), a("ek")), a("gok"), OP.mult)
+    for ch in H:
+        for x in H:
+            mm(a("pl", 16 * ch + 8 * x, 16 * ch + 8 * x + 8), a("lh", *PH[x]), a("mske", 8 * ch, 8 * ch + 8))
+    tt(a("w"), a("iu"), a("pl", 0, 32), OP.add)
+    ts(a("sv"), a("w"), 2 * L, OP.add)
+    for ch in H:
+        lists(4, ch, H)
+        act(a("fb0", *PH[ch]), ind(a("tabb", 0, 528), a("gl", 256 + 32 * ch, 264 + 32 * ch)), AF.Identity)
+    ts(a("frs"), a("fri"), (1 << 30) - 512, OP.bitwise_and)
+    tt(a("frm"), a("fri"), a("frs"), OP.add)
+    ts(a("f0", *OWN), a("frm"), 16 + O, OP.add, 2 * L, OP.min)
+    act(a("f0", *GH), a("f0", *OWN), AF.Identity)
+    act(a("fu"), a("f0", *OWN), AF.Identity, 1.0, -float(L))
     for j in range(8):
         s = 512 * j
         if j in KS:
-            h = a(("pr", "sr")[j % 2])
+            h = a(("fa", "fb")[j // 2 % 2])
             cp(a("skv", s, s + 512), a("ski", s, s + 512))
             act(a("sks", s, s + 512), a("skv", s, s + 512), AF.Sign, -1.0, 4095.5)
             mm(h, a("idf"), a("skv", s, s + 512), True, False)
             mm(h, a("idk"), a("sks", s, s + 512), False, True)
-            act(a("skt", s, s + 512), h, AF.Identity, 1024.0, float(U))
+            act(a("skt", s + 592, s + 1104), h, AF.Identity, 1024.0, O - 1.5 * U)
             continue
-        h = a(("d0", "d1")[j % 2])
-        ts(h, a("ski", s, s + 512), 4096, OP.is_lt, 16384, OP.mult)
+        h = a(("d0", "d1")[sum(k not in KS for k in range(j)) % 2])
+        ts(h, a("ski", s, s + 512), 4096, OP.is_lt, -20480, OP.mult)
         tt(a("skv", s, s + 512), a("ski", s, s + 512), h, OP.add)
-        act(a("skt", s, s + 512), a("skv", s, s + 512), AF.Identity, 1024.0, -float(U))
-    act(a("b16"), a("j8"), AF.Copy, 16.0)
-    ts(a("k0"), a("pm", 0, 8), 0, OP.is_equal)
-    ts(a("rst"), a("cm"), 0, OP.not_equal)
-    ts(a("thf", 0, 1), a("thi", 0, 1), 16, OP.mult, 16, OP.add)
-    act(a("dg"), a("idf"), AF.Copy, a("thf", 0, 1))
-    mm(a("pr", 0, 128), a("onef"), a("dg"))
+        act(a("skt", s + 592, s + 1104), a("skv", s, s + 512), AF.Identity, 1024.0, float(O + U))
     for ch in H:
-        act(a("thrt", 128 * ch, 128 * ch + 128), a("pr", 0, 128), AF.Copy)
-    ts(a("thj", 0, 1), a("thi", 0, 1), -1, OP.add)
-    ts(a("thj", 1, 2), a("thj", 0, 1), 1, OP.arith_shift_right)
-    ts(a("thf", 1, 2), a("thj", 1, 2), 16, OP.mult, 16, OP.add)
-    act(a("sv"), a("lsb"), AF.Copy)
-    next_saved()
+        clause_part(4, "f0", ch)
+    for j, w in enumerate((16.0, -2.0, -4.0)):
+        act(a("bw", 8 * j, 8 * j + 8), a("j8"), AF.Copy, w)
+    act(a("rstb"), a("rst"), AF.Copy)
+    ts(a("vals", 0, 1), a("pm", 0, 1), -1, OP.mult, 16, OP.add)
+    ts(a("thj", 0, 1), a("thi", 0, 1), 4080, OP.bitwise_and)
+    ts(a("thj", 1, 2), a("thi", 0, 1), 15, OP.bitwise_and)
+    for j, w in ((2, 1), (4, -1)):
+        ts(a("vals", j, j + 1), a("thj", 0, 1), 2, OP.mult)
+        ts(a("vals", j + 1, j + 2), a("thj", 1, 2), 2, OP.mult, w, OP.add)
+    for j in range(3):
+        mm(a("pl", 64 + 128 * j, 192 + 128 * j, 1, 2), a("vals", 2 * j, 2 * j + 2), a("idf"))
+    act(a("crow"), a("pl", 64, 448, 1, 2), AF.Copy)
+    next_saved("sv", a("iu", 8, 32), 8)
 
-    def places(raw, m, p, q, pr, r, u):
-        for w in PH:
-            ts(a(m, *w), a(raw, *w), U - 1, OP.bitwise_and)
-            ts(a(q, *w), a(raw, *w), 1023, OP.bitwise_and)
-            ts(a(p, *w), a(m, *w), 1.0 / 1024, OP.mult, 592 - 1.0 / 64, OP.add)
-            tt(a(pr, *w), a(p, *w), a(q, *w), OP.mult)
-            ts(a(r, *w), a(pr, *w), 4, OP.arith_shift_right, 4095, OP.bitwise_and)
-            cp(a(u, *w), a(r, *w))
+    def places(w, raw, m, p, q, pr, r, u):
+        ts(a(q, *w), a(raw, *w), 1023, OP.bitwise_and)
+        ts(a(p, *w), a(raw, *w), 10, OP.arith_shift_right, 8191, OP.bitwise_and)
+        ts(a(m, *w), a(raw, *w), L - 1, OP.bitwise_and)
+        tt(a(pr, *w), a(p, *w), a(q, *w), OP.mult)
+        ts(a(r, *w), a(pr, *w), 4, OP.arith_shift_right, 4095, OP.bitwise_and)
+        cp(a(u, *w), a(r, *w))
+
+    def outputs(F, ch):
+        (lo, hi), c, d = PH[ch], 16 * ch, 32 * ch
+        w = a("w", c, c + 16)
+        tt(w, a("mx", c, c + 16), a(EX[ch], 0, 256, 16), OP.max)
+        ts(a("fi", c, c + 16), w, L - 1, OP.bitwise_and)
+        ts(a("fq", c, c + 16), w, 1023, OP.bitwise_and)
+        ts(a("w2", c, c + 16), w, 23, OP.arith_shift_right, 1, OP.bitwise_and)
+        ts(a("t4", 8 * ch, 8 * ch + 8), a("w", c + 8, c + 16), 10, OP.arith_shift_right, 8191, OP.bitwise_and)
+        tt(a("fim", d, d + 16), a("fi", c, c + 16), a("fq", c, c + 16), OP.add)
+        ts(a("we", 8 * ch, 8 * ch + 8), a("t4", 8 * ch, 8 * ch + 8), 2, OP.mult, 32 + O - 1184, OP.add)
+        ts(a("sg1", c, c + 16), a("w2", c, c + 16), -1, OP.mult, 1, OP.add)
+        tt(a("sh", c, c + 16), a("sg1", c, c + 16), a("sv", c, c + 16), OP.mult)
+        tt(a("svs", c, c + 8), a("fim", d, d + 8), a("w2", c, c + 8), OP.mult)
+        tt(a("svs", c + 8, c + 16), a("we", 8 * ch, 8 * ch + 8), a("w2", c + 8, c + 16), OP.mult)
+        tt(a("fim", d + 16, d + 32), a("svs", c, c + 16), a("sh", c, c + 16), OP.add)
+        mm(a("pl", lo, hi, 1, 32), a("fim", d, d + 32), a("idf"))
+        ts(a("fot", lo, hi), a("pl", lo, hi, 1, 32), 0.5, OP.mult, -16 - O // 2, OP.add)
+        e = a("fa", 256 + lo, 256 + hi)
+        mm(e, a("five"), a("cu", 0, 128), True, False)
+        mm(e, a("gon"), a("rs", lo, hi), False, False)
+        mm(e, a("idf"), a(F, 528 + lo, 528 + hi), False, True)
+        tt(a("fu", lo, hi), a("fu", lo, hi), e, OP.min)
+        e = a("p3", 256 + lo, 256 + hi)
+        ts(e, a("fu", lo, hi), L, OP.is_ge, -32 - O, OP.add)
+        ts(a("o2", lo, hi), a("oi", lo, hi), 2 * L - 1, OP.bitwise_and)
+        ts(a("oq", lo, hi), a("oi", lo, hi), 1023, OP.bitwise_and)
+        tt(a("o3", lo, hi), a("o2", lo, hi), a("oq", lo, hi), OP.add)
+        tt(a("hb", lo, hi), a("o3", lo, hi), e, OP.add)
+        ts(a("oz", lo, hi), a("hb", lo, hi), -1, OP.max)
+        dma("y", dr(T.yf[:, lo:hi]), a("oz", lo, hi))
 
     for t in range(RO):
         F, last = "f%d" % t, t == RO - 1
-        b = 32 * ((t + 4) % 5)
-        mark[0] = len(prog) - 500 if t else mark[0]
-        if t == 0:
-            clause_side(4)
-        if t == 0:
-            tt(a("tg"), ind(a("skt"), a("sl", b, b + 16)), a("fb"), OP.add)
-            tt(a("rawg"), ind(a(F, 0, 512), a("fl")), a("tg"), OP.max)
-        else:
-            tt(a("tg"), ind(a("skt"), a("sarr", 16 * t, 16 * t + 16)), a("tabb", 256, 512), OP.add)
-            for lo, hi in PH:
-                tt(a("rawg", lo, hi), a(F, 256 + lo, 256 + hi), a("tg", lo, hi), OP.max)
-        boost[0] = UP
-        places("rawg", "ga", "pg", "qg", "prg", "rg", "ug")
-        boost[0] = 0.0
-        for lo, hi in GCH:
+        B = "f%d" % max(t - 1, 0)
+        mark[1] = t
+        for ch, (lo, hi) in enumerate(PH):
+            up("g%d" % ch)
+            if t == 0:
+                tt(a("tg", lo, hi), ind(a("skt"), a("gl", 272 + 32 * ch, 280 + 32 * ch)), a("fb0", lo, hi), OP.add)
+                tt(a("rawg", lo, hi), ind(a(F, 0, 528), a("gl", 256 + 32 * ch, 264 + 32 * ch)), a("tg", lo, hi), OP.min)
+            else:
+                c, C = 48 * (t - 1) + 24 * ch, a("r%d" % (t - 1))
+                tt(a("tg", lo, hi), ind(a("skt"), a("arr", c + 16 - 8 * ch, c + 24 - 8 * ch)), a("tabb", 272 + lo, 272 + hi), OP.add)
+                tt(a("rawg", lo, hi), ind(C, a("arr", c, c + 8)), a("tg", lo, hi), OP.min)
+                up(("col", "col1")[ch])
+                act(a(F, 272 + lo, 272 + hi), ind(C, a("arr", c, c + 8)), AF.Identity)
+            up("g%d" % ch)
+            places((lo, hi), "rawg", "ga", "pg", "qg", "prg", "rg", "ug")
+        to = T.cores[(rank + 1 + t % 3) % N]
+        if not last:
+            send(a("r%d" % t, *GH), a(F, *GH), to, "ag%d" % t)
+        for j, (lo, hi) in enumerate(GCH):
+            up("u%d" % j)
             act(a("ub", lo, hi), ind(a("xr"), a("ug", lo // 16, hi // 16)), AF.Identity)
-        for lo, hi in PH:
-            e = a("b0", lo, hi)
-            tt(e, a("pe", 256 + lo, 256 + hi), a("ga", lo, hi), OP.mult)
-            tt(a(F, 512 + lo, 512 + hi), a("own3", lo, hi), e, OP.add)
-        tt(a("rawc"), ind(a(F), a("hl")), a("tc"), OP.max)
-        places("rawc", "ca", "pc", "qc", "prc", "rc", "uc")
+        for ch, (lo, hi) in enumerate(PH):
+            up(("c0", "x1")[ch])
+            e = XP[ch]
+            tt(e, a("ga", lo, hi), e, OP.add)
+            tt(a(F, 528 + lo, 528 + hi), a(B, 16 + lo, 16 + hi), e, OP.min)
+            up("c%d" % ch)
+            tt(a("rawc", lo, hi), ind(a(F, 0, 528 + hi), hl((t + 4) % 5, ch)), a("tc", lo, hi), OP.min)
+            places((lo, hi), "rawc", "ca", "pc", "qc", "prc", "rc", "uc")
         for lo, hi in VCH:
+            up("w4" if hi == 4096 else "w%d" % (lo // 1024), lo % 1024 / 730)
             tt(a("df", lo, hi), ind(a("xr"), a("uc", lo // 16, hi // 16)), a("ub", lo, hi), OP.subtract)
+        for lo, hi in ACH:
+            up("a4" if hi == 4096 else "a%d" % (lo // 1024), lo % 1024 / 730)
             act(a("ab", lo, hi), a("df", lo, hi), AF.Abs)
         for ch in H:
+            up("d%d" % ch)
             D = ("d0", "d1")[ch]
-            mm(a(D, 0, 128), a("oneb", 0, 128, 1, 1), a("krow", 0, 128, 1, 1), True, False)
-            for k in range(16):
-                mm(a(D, k, 128, 16), a("ab", 2048 * ch + k, 2048 * ch + 2048, 16), a("b16"), False, k == 15)
-        mm(a("pr", 256, 512), a("idf"), a(F, 512, 768))
-        tt(a("fr5"), a("rawc"), a("pr", 256, 512), OP.is_equal)
-        tt(a("mk2"), a("fr5"), mkA, OP.max)
+            mm(fcs[ch], a("idf"), a("fu", *PH[ch]), True, False)
+            for p0, p1 in DCH[ch]:
+                mm(a(D, 0, 384, 1, p1, p0), a("oneb", p0, p1, 1, 2), a("crow"), True, False)
+                for k0 in range(0, 16, 4):
+                    mms([(a(D, k, 384, 16, p1, p0), a("ab", 2048 * ch + 16 * p0 + k, 2048 * ch + 16 * p1, 16), a("bw"), False, k == 15)
+                         for k in range(k0, k0 + 4)])
         for ch in H:
-            D, R = a(("d0", "d1")[ch], 0, 128), a(("sr", "pe")[ch], 0, 128)
+            D = ("d0", "d1")[ch]
+            R = a(D, 384, 512)
             lo, hi, l8 = 128 * ch, 128 * ch + 128, (8 * ch, 8 * ch + 8)
-            tt(a("nov", lo, hi), D, a("thrt", lo, hi), OP.is_le)
-            tt(a("key", lo, hi), a("nov", lo, hi), D, OP.mult)
-            scan(a("cnt", lo, hi), a("rst", lo, hi), a("nov", lo, hi), OP.mult, OP.add)
-            scan(a("sm", lo, hi), a("rst", lo, hi), a("key", lo, hi), OP.mult, OP.max)
-            tt(a("cl", *l8), a("cnt", lo + 15, hi, 16), a("lim", *l8), OP.is_le)
-            tt(a("smx", *l8), a("sm", lo + 15, hi, 16), a("cl", *l8), OP.add)
-            tt(a("sel", lo, hi), ind(a("smx", *l8), a("el", 0, 8)), a("key", lo, hi), OP.is_equal)
+            s1, s2 = a("sg", 2 * lo, 2 * lo + 128), a("sg", 2 * lo + 128, 2 * lo + 256)
+            up("f%d" % ch)
+            both = ("y%d" % ch in VS) == ("z%d" % ch in VS) and not ch
+            sign(a("sg", 2 * lo, 2 * lo + 256) if both else s1, a(D, 128, 384 if both else 256), "y%d" % ch)
+            scan(a("cnt", lo, hi), a("rstb"), s1, OP.mult, OP.add)
+            act(a("clx", lo, hi), ind(a("cnt", lo, hi), a("el", 16, 24)), AF.Sign, -1.0, a("lim", ch, ch + 1), None if last else a("par", ch, ch + 1))
+            mm(fcs[ch], a("clx", lo, hi), a("idu"), False, True)
+            tt(a("oi", lo, hi) if last else a(F, 16 + lo, 16 + hi), a(F, 528 + lo, 528 + hi), fcs[ch], OP.max)
+            if not last:
+                send(a("r%d" % t, 16 + lo, 16 + hi), a(F, 16 + lo, 16 + hi), to, "ao%d" % (2 * t + ch))
+            if ch == 0 and not last:
+                up("fu")
+                mm(fus, a("five"), a("cu"), True, False)
+            up("m%d" % ch)
+            tt(a("key", lo, hi), s1, a(D, 0, 128), OP.mult)
+            if not both:
+                sign(s2, a(D, 256, 384), "z%d" % ch)
+            scan(a("sm", lo, hi), a("rst"), a("key", lo, hi), OP.mult, OP.max)
+            tt(a("sel", lo, hi), ind(a("sm", lo, hi), a("el", 16, 24)), a("key", lo, hi), OP.is_equal)
             mm(R, a("sel", lo, hi), a("idb"))
-            tt(a("pgc", lo, hi), a("ga", lo, hi), R, OP.mult)
-            tt(a("pgc", 256 + lo, 256 + hi), a("ca", lo, hi), R, OP.mult)
-        act(a("lhb", 0, 256), ind(a("cl"), a("el")), AF.Identity)
-        for ch in H:
-            mm(a("pr", 128 * ch, 128 * ch + 128), a("lhb", 128 * ch, 128 * ch + 128), a("idb"))
-        tt(keep, a("mk2"), a("pr", 0, 256), OP.is_gt)
-        tt(a("oi") if last else a(F, 0, 256), a(F, 512, 768), keep, OP.mult)
-        if not last:
-            act(a("rcb"), a("pr", 0, 256), AF.Copy)
-        for ch in H:
-            act(a("thp", 128 * ch, 128 * ch + 128), a(("sr", "pe")[ch], 0, 128), AF.Copy, a("thf", 1, 2))
-        tt(a("clst", 0, 16), a("cl"), a("sv", 0, 16), OP.mult)
-        tt(a("clst", 16, 32), a("cl"), a("st"), OP.mult)
-        for x in H:
-            B, c = (("pl", 0), ("d1", 128))[x]
-            mm(a(B, c, c + 16), a("idb"), a("zero"), True, False)
-            mm(a(B, c, c + 8), a("pgc", 256 * x, 256 * x + 128), a("j8"), False, False)
-            mm(a(B, c, c + 16), a("idf"), a("clst", 16 * x, 16 * x + 16), False, False)
-            mm(a(B, c + 8, c + 16), a("pgc", 256 * x + 128, 256 * x + 256), a("j8"), False, True)
-            cp(a("lsb", 16 * x, 16 * x + 16), a(B, c, c + 16))
-        if not last:
-            to = T.cores[(rank + 1 + t % 3) % N]
-            to_w(0)
-            goal_lists(t)
-            send(a("sarr", 16 * t + 16, 16 * t + 32), a("sl", 32 * t, 32 * t + 16), to, "as%d" % t)
-            act(a("snd%d" % t), ind(a(F, 0, 512), a("fl")), AF.Identity)
-            send(a("f%d" % (t + 1), 256, 512), a("snd%d" % t), to, "ac%d" % t)
-            to_w(1)
-        for ch in H:
-            mm(a("pl", 32 + 8 * ch, 40 + 8 * ch), a("thp", 128 * ch, 128 * ch + 128), a("j8"))
-        if not last:
-            for ch in H:
-                mm(a("pl", 48 + 8 * ch, 56 + 8 * ch), a("rcb", 128 * ch, 128 * ch + 128), a("k0"))
-        tt(a("sc", 0, 16), a("smx"), a("pl", 32, 48), OP.is_le)
-        if not last:
-            clause_lists(t)
-            act(a("par", 0, 16), a("pl", 48, 64), AF.Abs, 1.0, -4.0)
-            act(a("par", 16, 32), a("par", 0, 16), AF.Abs, 1.0, -2.0)
-            act(a("par", 32, 48), a("par", 16, 32), AF.Abs, 1.0, -1.0)
-            act(a("lim"), a("par", 32, 48), AF.Identity, 1.0, 7.0)
-            own_parts(F)
-            act(a("f%d" % (t + 1), 0, 256), a(F, 0, 256), AF.Identity)
-            clause_side(t)
-        boost[0] = UQ
-        act(a("lhb", 256, 512), ind(a("sc", 0, 16), a("el")), AF.Identity, -1.0, 1.0)
-        boost[0] = 0.0
-        tt(a("s1"), a("lsb"), a("sv"), OP.subtract)
-        tt(a("sc", 16, 32), a("sc", 0, 16), a("cl"), OP.add)
-        tt(a("s2"), a("s1"), a("sc"), OP.mult)
-        tt(a("sv"), a("sv"), a("s2"), OP.add)
-        boost[0] = UQ
-        for ch in H:
-            mm(a("pr", 256 + 128 * ch, 384 + 128 * ch), a("lhb", 256 + 128 * ch, 384 + 128 * ch), a("idb"))
-        boost[0] = 0.0
-        if not last:
-            next_saved()
-        boost[0] = UQ
-        tt(a("eqm"), a("mk2"), a("pr", 256, 512), OP.is_gt)
+            mm(a("p3", lo, hi), s2, a("idh"), True, False)
+            mm(a("p3", lo, hi), a("clx", lo, hi), a("idc"), False, False)
+            mm(a("p3", lo, hi), a("sel", lo, hi), a("id4"), False, True)
+            if "r%d" % ch in VS:
+                ts(a("rs", lo, hi), a("p3", lo, hi), -3.5, OP.add, 0, OP.max)
+            else:
+                act(a("rs", lo, hi), a("p3", lo, hi), AF.Relu, 1.0, -3.5)
+            for x in H:
+                c = 256 * x + lo
+                tt(a("pgc", c, c + 128), a(("ga", "ca")[x], lo, hi), R, OP.mult)
+            for x in H:
+                up("lj"[x] + str(ch))
+                c, e = 256 * x + lo, a(EX[ch], *PH[x]) if last else a(EX[x], lo, hi)
+                mm(e, a("mtwo"), a("cu", 0, 128), True, False)
+                mm(e, a("pgc", c, c + 128), a("go"), False, False)
+                mm(e, a("rs", lo, hi), a("gou"), False, True)
+                if last:
+                    continue
+                to_w(x, ch)
+                if ch or x:
+                    c = (16 + 8 * x, 24 + 8 * x) if ch else (0, 16)
+                    tt(a("w", *c), a("mx", *c), a("pl", *c), OP.max)
+                    lists(t, ch, (x,) if ch else H)
+                if ch != x:
+                    c = 64 * t + 32 * ch
+                    send(a("arr", 48 * t + 24 * ch, 48 * t + 24 * ch + 24 - 8 * ch), a("gl", c, c + 24 - 8 * ch), to, "al%d" % (2 * t + ch))
+            if last:
+                up("o%d" % ch)
+                outputs(F, ch)
+                continue
+            up("fu")
+            mm(a("fa", 256 + lo, 256 + hi), a("gon"), a("rs", lo, hi), False, False)
         if last:
             break
-        tt(mkA, keep, a("eqm"), OP.add)
-        boost[0] = 0.0
-
-    boost[0] = 0.0
-    ts(a("op"), a("oi"), 10, OP.arith_shift_right, 4095, OP.bitwise_and)
-    ts(mkA, a("op"), -512, OP.mult, -16 - U, OP.add)
-    tt(a("oy"), a("oi"), mkA, OP.add)
-    tt(a("oy2"), keep, a("eqm"), OP.subtract)
-    ts(mkA, a("oy"), 2, OP.mult, -1, OP.max)
-    tt(a("oz"), a("oy2"), mkA, OP.add)
-    dma("y", dr(T.yf[:]), a("oz"))
-    cp(a("fin", 0, 32), a("lsb"))
-    cp(a("fin", 32, 64), a("sv"))
-    upper(a("fip"), a("fin"))
-    ts(a("fiq", 0, 48), a("fip", 0, 48), -512, OP.mult, -16, OP.add)
-    tt(a("fim", 0, 48), a("fin", 0, 48), a("fiq", 0, 48), OP.add)
-    cp(a("fim", 48, 64), a("fip", 48, 64))
-    tr(a("pl", 0, 128, 1, 64), a("fim"), a("idf"))
-    cp(a("fot"), a("pl", 0, 128, 1, 64))
-    for j, y in enumerate((T.yg, T.yc, T.ysg, T.yk)):
+        for lo, hi in PH:
+            mm(a("fa", 256 + lo, 256 + hi), a("idf"), a(F, 528 + lo, 528 + hi), False, lo > 0)
+        tt(a("fu"), a("fu"), fus, OP.min)
+        dma("y", a("f%d" % (t + 1), *OWN), a(F, *OWN), 2.8)
         for ch in H:
-            r0 = 16 * j + 8 * ch
-            dma("ys"[(2 * j + ch) % 2], dr(y[:, 128 * ch:128 * ch + 128]), a("fot", 0, 128, 1, r0 + 8, r0))
+            up("k%d" % ch)
+            clause_part(t, F, ch)
+        up("sv")
+        if "par" in VS:
+            ts(a("thj", 2, 4), a("par", 0, 2), 1.0 / 32, OP.mult, 4, OP.add)
+            ts(a("thj", 4, 6), a("thj", 2, 4), 1, OP.bitwise_and)
+            ts(a("lim", 0, 2), a("thj", 4, 6), -2, OP.mult, 1, OP.add)
+        else:
+            act(a("par", 2, 4), a("par", 0, 2), AF.Abs, 1.0 / 32)
+            act(a("par", 4, 6), a("par", 2, 4), AF.Abs, 1.0, -2.0)
+            act(a("par", 6, 8), a("par", 4, 6), AF.Abs, 2.0, -2.0)
+            act(a("lim", 0, 2), a("par", 6, 8), AF.Identity, 1.0, -1.0)
+        save(a("sv"), a("sv"))
+        if t < RO - 2:
+            next_saved("sv", a("iu", 8, 32), 8)
+        else:
+            for x in H:
+                tt(a("lh", 256 * x, 256 * x + 256), ind(a("sv", 8 * x, 8 * x + 24), a("el", 0, 16)), a("mske"), OP.mult)
+                for ch in H:
+                    c = 256 * x + 128 * ch
+                    mm(a("pl", 32 + 16 * ch + 8 * x, 40 + 16 * ch + 8 * x), a("lh", c, c + 128), a("j8"))
+            act(a("svs"), a("pl", 32, 64), AF.Copy)
+            next_saved("svs", a("il"), 8)
+            cp(a("w2"), a("svs"))
+            ts(a("fi", 0, 32), a("w2"), L - 1, OP.bitwise_and)
+            ts(a("fq", 0, 32), a("w2"), 1023, OP.bitwise_and)
+            tt(a("sv"), a("fi", 0, 32), a("fq", 0, 32), OP.add)
+            for c in (8, 24):
+                ts(a("sv", c, c + 8), a("s3", c, c + 8), 2, OP.mult, 32 + O, OP.add)
+
+    up("o1")
+    for j, y in enumerate((T.yg, T.yc, T.ysg, T.yk)):
+        dma("sy"[j % 2], dr(y[:]), a("fot", 0, 256, 1, 8 * j + 8, 8 * j))
 
     lg, n = {}, len(prog)
     dep, succ = [[] for _ in range(n)], [[] for _ in range(n)]
     for i, p in enumerate(prog):
         ds, q = {}, p["q"] if p["kind"] == "c" else "#%d" % i
         for e, kind in meets(q, p["acc"], lg):
-            ds[e[3]] = 0.0 if (p["q"] == "t" and prog[e[3]]["q"] == "t") else WAKE
+            inq = e[4] == q and (q == "t" or NOWAR and e[2] == "r")
+            ds[e[3]] = max(ds.get(e[3], 0.0), 0.0 if inq else WAKE.get(prog[e[3]]["q"] + p["q"], WAKE[prog[e[3]]["q"]]))
         if p["kind"] == "n":
             ds[p["extra"][2]] = 0.0
         note(q, p["acc"], lg, i)
         dep[i] = sorted(ds.items())
         for d, w in dep[i]:
             succ[d].append((i, w))
-    rankp, base = [0.0] * n, [0.0] * n
-    for i in range(n - 1, -1, -1):
-        p = prog[i]
-        base[i] = p["dur"] + p["lat"] + max([w + base[j] for j, w in succ[i]] + [0.0])
-        rankp[i] = base[i] + p["up"] + PREF.get(p["id"], 0.0)
-    free = {q: 0.0 for q in list(Q) + ["net"]}
-    left = [len(d) for d in dep]
-    done = [0.0] * n
-    ready = {q: [] for q in free}
-    for i in range(n):
-        if not left[i]:
-            ready[prog[i]["q"]].append((0.0, i))
-    plan = []
-    for _ in range(n):
+    dur, lat = [p["dur"] for p in prog], [p["lat"] for p in prog]
+    before = [[(d, w + lat[d]) for d, w in dep[i]] for i in range(n)]
+    after = [[(j, w + lat[i]) for j, w in succ[i]] for i in range(n)]
+    for i in range(2, len(LD)):
+        before[i].append((i - 2, 0.0))
+        after[i - 2].append((i, 0.0))
+
+    def schedule(pre, post, first, prio):
+        free = {q: 0.0 for q in list(Q) + ["net"]}
+        left, done, order = [len(d) for d in pre], [0.0] * n, []
+        ready = {q: [(first[i], i) for i in range(n) if not left[i] and prog[i]["q"] == q] for q in free}
+        for _ in range(n):
+            best = None
+            for q in free:
+                if not ready[q]:
+                    continue
+                t0 = max(free[q], min(ready[q])[0]) if q != "net" else min(ready[q])[0]
+                c = max((prio[i], -i, e) for e, i in ready[q] if e <= t0 + SLACK)
+                i = -c[1]
+                if c[2] > t0:
+                    short = [(prio[k], -k) for e, k in ready[q] if e <= t0 + 1e-9 and t0 + dur[k] <= c[2] + OVER]
+                    if short:
+                        i = -max(short)[1]
+                    else:
+                        t0 = c[2]
+                if best is None or t0 < best[0]:
+                    best = (t0, i, q)
+            t0, i, q = best
+            ready[q] = [x for x in ready[q] if x[1] != i]
+            done[i] = t0 + dur[i]
+            if q != "net":
+                free[q] = done[i]
+            order.append(i)
+            for j, w in post[i]:
+                left[j] -= 1
+                if not left[j]:
+                    ready[prog[j]["q"]].append((max([done[d] + w2 for d, w2 in pre[j]] + [first[j]]), j))
+        return order, done
+
+    def improve(order, seed):
+        qs = [p["q"] for p in prog]
+        prev, last = [-1] * n, {}
+        for i in order:
+            if qs[i] != "net":
+                prev[i], last[qs[i]] = last.get(qs[i], -1), i
+
+        done, rest, pos = [0.0] * n, [0.0] * n, [0] * n
+        best, arcs, lo, hi = (1e9, order), None, 0, n
+        for step in range(STEPS + 1):
+            if arcs is None:
+                nxt = {prev[i]: i for i in range(n) if prev[i] >= 0}
+                for i in order[lo:]:
+                    t0 = done[prev[i]] if prev[i] >= 0 else 0.0
+                    for d, w in before[i]:
+                        if done[d] + w > t0:
+                            t0 = done[d] + w
+                    done[i] = t0 + dur[i]
+                for k in range(hi - 1, -1, -1):
+                    i = order[k]
+                    t0 = max(lat[i], rest[nxt[i]] if i in nxt else 0.0)
+                    for d, w in after[i]:
+                        if rest[d] + w > t0:
+                            t0 = rest[d] + w
+                    rest[i] = t0 + dur[i]
+                for k in range(lo, hi):
+                    pos[order[k]] = k
+                span = max(rest)
+                arcs = [j for j in order if prev[j] >= 0 and done[prev[j]] + rest[j] > span - 1e-6]
+                if span < best[0]:
+                    best = (span, list(order), list(done))
+            seed = (seed * 1103515245 + 12345) % 2147483648
+            j = arcs[(seed >> 8) % len(arcs)]
+            i, q, far = prev[j], qs[j], (seed >> 20) % (8 if seed >> 28 else FAR)
+            if far % 2:
+                for _ in range(far // 2):
+                    i = prev[i] if prev[i] >= 0 else i
+                seg, move = order[pos[i]:pos[j] + 1], {j}
+                for k in reversed(seg):
+                    if k in move:
+                        move.update(d for d, w in before[k])
+                        if qs[k] != q:
+                            move.add(prev[k])
+                if i in move:
+                    continue
+                seg = [k for k in seg if k in move] + [k for k in seg if k not in move]
+            else:
+                for _ in range(far // 2):
+                    j = nxt.get(j, j)
+                seg, move = order[pos[i]:pos[j] + 1], {i}
+                for k in seg:
+                    if k in move:
+                        move.update(d for d, w in after[k])
+                        if qs[k] != q:
+                            move.add(nxt.get(k, -1))
+                if j in move:
+                    continue
+                seg = [k for k in seg if k not in move] + [k for k in seg if k in move]
+            p2, d2, c, s2, b = {}, {}, prev[i], 0.0, pos[j]
+            for k in seg:
+                if qs[k] == q:
+                    p2[k], c = c, k
+                e = p2.get(k, prev[k])
+                t0 = d2.get(e, done[e]) if e >= 0 else 0.0
+                for d, w in before[k]:
+                    e = d2.get(d, done[d]) + w
+                    if e > t0:
+                        t0 = e
+                t0 = d2[k] = t0 + dur[k]
+                e = t0 + lat[k]
+                for d, w in after[k]:
+                    if pos[d] > b and t0 + w + rest[d] > e:
+                        e = t0 + w + rest[d]
+                if qs[k] != q and k in nxt and pos[nxt[k]] > b and t0 + rest[nxt[k]] > e:
+                    e = t0 + rest[nxt[k]]
+                if e > s2:
+                    s2 = e
+            if j in nxt:
+                p2[nxt[j]] = c
+                s2 = max(s2, d2[c] + rest[nxt[j]])
+            seed = (seed * 1103515245 + 12345) % 2147483648
+            if s2 <= span + HEAT * (1 - step / STEPS) * (seed >> 8 & 1023) ** 2 / 1048576:
+                lo, hi, arcs = pos[i], b + 1, None
+                order[lo:hi] = seg
+                for k in p2:
+                    prev[k] = p2[k]
+        return best
+
+    if not PLAN:
+        prio, zero = [0.0] * n, [0.0] * n
+        for i in range(n - 1, -1, -1):
+            prio[i] = dur[i] + max([w + prio[j] for j, w in after[i]] + [lat[i]])
+        due = schedule(before, after, zero, prio)[1]
+        for i, p in enumerate(prog):
+            if p["up"] is not None:
+                due[i] = max([p["up"]] + [due[d] + w for d, w in before[i]]) + dur[i]
         best = None
-        for q in free:
-            if not ready[q]:
-                continue
-            t0 = max(free[q], min(e for e, i in ready[q])) if q != "net" else min(e for e, i in ready[q])
-            c = max((rankp[i], -i, e) for e, i in ready[q] if e <= t0 + SLACK)
-            i = -c[1]
-            if c[2] > t0:
-                short = [(rankp[k], -k) for e, k in ready[q] if e <= t0 + 1e-9 and t0 + prog[k]["dur"] <= c[2] + OVER]
-                if short:
-                    i = -max(short)[1]
-                else:
-                    t0 = c[2]
-            if best is None or t0 < best[0]:
-                best = (t0, i, q)
-        t0, i, q = best
-        ready[q] = [x for x in ready[q] if x[1] != i]
-        if q != "net":
-            free[q] = t0 + prog[i]["dur"]
-        done[i] = t0 + prog[i]["dur"] + prog[i]["lat"]
-        plan.append(i)
-        for j, w in succ[i]:
-            left[j] -= 1
-            if not left[j]:
-                ready[prog[j]["q"]].append((max(done[d] + w2 for d, w2 in dep[j]), j))
+        for turn in range(TURNS):
+            now = improve(sorted(range(n), key=lambda i: (due[i] - dur[i], i)), turn + 1)
+            best = now if not best or now[0] < best[0] else best
+            end = {p["id"]: now[2][i] for i, p in enumerate(prog) if p["id"]}
+            span, t = min((end[(t, "w4", 0)] - end[(t - 1, "w4", 0)], t) for t in (1, 2, 3))
+            for i, p in enumerate(prog):
+                due[i] = now[2][i]
+                if p["id"]:
+                    r, name, k = p["id"]
+                    s = t if end.get((t, name, k), 1e9) <= end[(t, "w4", 0)] else t - 1
+                    e = end[(s, name, k)] + (r - s) * span + end[(0, "w4", 0)] - end[(t, "w4", 0)] + t * span if (s, name, k) in end else 0.0
+                    due[i] = max([e - dur[i]] + [due[d] + w for d, w in before[i]]) + dur[i]
+        PLAN.extend(best[:2])
+        PLAN.extend((prog, before, dur, lat))
+    plan = PLAN[1]
 
     def wait(q, sem, c):
         if know[q].get(sem, 0) < c:
@@ -490,7 +704,7 @@ def rank_program(g, core, T, topo):
         if p["kind"] != "n":
             want = {}
             for d, w in dep[i]:
-                if q == "t" and prog[d]["q"] == "t":
+                if not w:
                     continue
                 sem, c = ref[d]
                 want[sem] = max(want.get(sem, 0), c)

@@ -1,3 +1,4 @@
+import math
 from concourse.mybir import AluOpType, ActivationFunctionType
 
 OP = AluOpType
@@ -16,14 +17,14 @@ def _bufs(where, dtype, text):
         SCRATCH[n] = (where, [int(r), int(c)], dtype)
 
 
-_bufs("sbuf", F32, "skv:4096 skt:4688 tabb:784 j8:8 mske:256 rst:128 idf:128 go:128 gok:128 onef:128 e8:8x128 m16:16x128 vals:8 "
+_bufs("sbuf", F32, "skv:4096 skt:4688 tabb:784 j8:8 mske:256 rst:128 rsb:128 idf:128 go:128 gok:128 onef:128 e8:8x128 m16:16x128 vals:8 gaf:512 sum:512 "
       "iw:32 iu:32 il:24 lim:8 hb:256 tg:256 tc:256 fu:256 key:256 sm:256 pgc:512 lh:512 we:16 wf:16 sv:32 svs:32 sg1:32 sh:32 mx:32 par:8 "
       "fim:64 fot:32x256 oz:256 f0:784 f1:784 f2:784 f3:784 f4:784 r0:528 r1:528 r2:528 r3:528")
-_bufs("sbuf", BF, "idk:128 xr:4096 ub:4096 df:4096 ab:4096 bw:24 idb:128 id4:128 idh:128 gou:128 gon:128 oneb:128 crow:2x384 cu:1x256 five:1x128 mtwo:1x128 idu:128 idn:128 idc:128 "
-      "rstb:128 sg:512 cnt:256 sel:256 rs:256 clx:256 sa:256 sb:256")
+_bufs("sbuf", BF, "idk:128 xr:4096 ub:4096 df:4096 ab:4096 bw:24 idb:128 id4:128 idh:128 gou:128 gon:128 oneb:128 crow:2x384 cu:1x256 cn:1x128 idl:128 id2:128 tr:1x512 row:1x384 "
+      "idu:128 idc:128 ids:128 idx:128 rstb:128 sg:512 cnt:256 sel:256 rs:256 clx:256 sa:256 sb:256 sc:256")
 _bufs("sbuf", I32, "ski:4096 ini:48 fri:256 thi:8 thj:8 pi:8 ci:40 pm:8 rawg:256 rawc:256 ga:256 ca:256 "
-      "pg:256 qg:256 prg:256 rg:256 pc:256 qc:256 prc:256 rc:256 w:32 w2:32 wq:64 s3:32 t4:24 t5:24 t6:24 t7:24 t8:24 fi:64 fq:64 oi:256")
-_bufs("sbuf", U16, "ug:256 uc:256 el:24 ek:8 gl:320 arr:192")
+      "pg:256 qg:256 prg:256 rg:256 pc:256 qc:256 prc:256 rc:256 w:32 w2:32 wq:80 s3:32 t4:24 t5:24 t6:24 t7:24 t8:24 fi:32 fq:32 oi:256")
+_bufs("sbuf", U16, "ug:256 uc:256 el:24 ek:8 gl:400 arr:192")
 _bufs("psum", F32, "d0:512 d1:512 p3:512 ea:512 eb:512 pl:512 fa:512 fb:512")
 SEMAPHORES = ["sv", "ss", "st", "sg", "rl"] + [n + str(t) for n in ("al", "ao", "ag") for t in range(8)] + ["d%d" % t for t in range(32)]
 VIEW = {"sks": ("df", 0, 4096), "frs": ("oi", 0, 256), "frm": ("oz", 0, 256), "o2": ("pg", 0, 256), "oq": ("qg", 0, 256), "o3": ("tg", 0, 256), "fb0": ("key", 0, 256)}
@@ -31,23 +32,23 @@ PSUM = [n for n in SCRATCH if SCRATCH[n][0] == "psum"]
 OWN, GH, F3 = (16, 272), (272, 528), (528, 784)
 GCH = [(0, 1024), (1024, 2048), (2048, 3072), (3072, 4096)]
 VCH = [(0, 1024), (1024, 2048), (2048, 3072), (3072, 3584), (3584, 4096)]
-DCH = [[(0, 128)], [(0, 128)]]
-PH = [(0, 128), (128, 256)]
 ACH = [(0, 1024), (1024, 2048), (2048, 3072), (3072, 3584), (3584, 4096)]
-SKW = 512
-KS = (1, 3, 5)
-CYC, CG, FIX, GFIX, SFIX, PEC, PFIX = 0.00085, 1.2, 0.005, 0.05, 0.05, 0.0005, 0.015
+SW = None
+PH = [(0, 128), (128, 256)]
+KS = (0, 2, 4)
+INI, FRI = 0, 0
+FAST, TG, SPLIT, SHORT, QUICK, TC, CP = (1, 1, 0), (), (0, 1), (), (), (), (0, 1)
+CYC, CG, FIX, GFIX, SFIX, PEC, PFIX = 0.0009, 1.28, 0.005, 0.05, 0.05, 0.00053, 0.015
 WAKE = {"v": 0.16, "vv": 0.22, "s": 0.24, "t": 0.3, "tt": 0.0, "g": 0.1, "y": 0.2, "net": 0.2, "vg": 0.3}
 RI, RL, RB = 0.25, 1.3, 0.4
-NOWAR = False
-VS = {"y1", "r1"}
-SLACK, OVER, PASSES = 0.1, 0.05, 2
-T0, PERIOD = 8.0, 17.6
-UPS = {"g0": 5.0, "col": 5.0, "u0": 7.3, "u1": 8.7, "c0": 6.0, "g1": 7.0, "w0": 9.9, "w1": 11.3, "c1": 12.7, "u2": 10.2, "a0": 11.6, "w2": 14.0, "a1": 12.8, "u3": 13.7,
-       "d0": 10, "w3": 15.9, "a2": 15.5, "f0": 15, "m0": 15, "w4": 16.8, "a3": 16.8, "a4": 17.6, "d1": 10, "f1": 18, "m1": 18, "l0": 15, "l1": 18, "k0": 20.5, "k1": 21,
-       "fu": 22, "sv": 22, "o0": 17, "o1": 18, "x1": 8.5, "j0": 15, "j1": 21, "col1": 5}
+VS = set()
+T0, PERIOD, SLACK = 8.0, 17.6, 0.1
+DUE = {"g0": 5.0, "col0": 5.0, "col1": 5, "u0": 7.3, "u1": 8.7, "c0": 6.0, "g1": 7.0, "x0": 6.0, "x1": 8.5, "w0": 9.9, "w1": 11.3, "c1": 12.7, "u2": 10.2, "a0": 11.6,
+       "w2": 14.0, "a1": 12.8, "u3": 13.7, "d0": 10, "w3": 15, "a2": 15.5, "f0": 16, "m0": 16, "w4": 15.7, "a3": 16, "a4": 16.7, "d1": 10, "f1": 18, "m1": 18,
+       "l0": 17, "l1": 18, "j0": 18, "j1": 21, "k0": 20.5, "k1": 21, "fu": 22, "sv": 22, "o0": 17, "o1": 18}
 PLAN = []
-TURNS, STEPS, HEAT, FAR = 12, 40000, 0.2, 40
+TURNS, STEPS, HEAT, FAR, ALL, SPANS = 2, 150000, 0.5, 40, 1, []
+SOFT, WARM, NEAR, SEED = 0.3, 6.0, 0.05, 1
 
 
 def rank_program(g, core, T, topo):
@@ -58,7 +59,7 @@ def rank_program(g, core, T, topo):
     SEM = {"v": "sv", "s": "ss", "t": "st", "g": "sg"}
     know = {q: {} for q in Q}
     cnt, snap, nd = {}, {}, [0]
-    prog, boost, mark, seen = [], [0.0], [0, 0], {}
+    prog, step, seen = [], [None, None], {}
 
     def a(n, lo=0, hi=None, st=1, r=None, r0=0):
         if n in VIEW:
@@ -92,25 +93,26 @@ def rank_program(g, core, T, topo):
         for kind, (n, lo, hi, st, r0, r1) in acc:
             for e in lg.get(n, []):
                 if n in PSUM and e[4] != q:
-                    yield e, kind
+                    yield e
                 elif lo < e[1] and e[0] < hi and "w" in (kind, e[2]):
-                    yield e, kind
+                    yield e
                 elif n in PSUM and q == "t" and kind == "w" and e[2] == "w":
-                    yield e, kind
+                    yield e
 
     def note(q, acc, lg, ref):
         for kind, (n, lo, hi, st, r0, r1) in acc:
             old = lg.get(n, [])
-            if kind == "w" and st == 1 and n not in PSUM:
-                old = [e for e in old if not (lo <= e[0] and e[1] <= hi)]
-            if n in PSUM and kind == "w":
-                old = [e for e in old if (q != "t" if e[4] != q else not (st == 1 and lo <= e[0] and e[1] <= hi))]
+            if kind == "w":
+                old = [e for e in old if (q != "t" if n in PSUM and e[4] != q else not (st == 1 and lo <= e[0] and e[1] <= hi))]
             lg[n] = old + [(lo, hi, kind, ref, q)]
 
     def add(q, call, reads, writes, dur, lat=0.0, kind="c", extra=None):
-        key = None if boost[0] is None else (mark[1], mark[0])
-        seen[key] = seen.get(key, -1) + 1
-        prog.append({"up": boost[0], "id": key and key + (seen[key],), "q": q, "call": call, "acc": flat(reads, writes), "dur": dur, "lat": lat, "kind": kind, "extra": extra})
+        seen[step[1]] = seen.get(step[1], -1) + 1
+        prog.append({"due": step[0], "id": step[1] and step[1] + (seen[step[1]],), "q": q, "call": call, "acc": flat(reads, writes), "dur": dur, "lat": lat,
+                     "kind": kind, "extra": extra})
+
+    def up(t, name, more=0.0):
+        step[0], step[1] = T0 + PERIOD * t + DUE[name] + more, (t, name)
 
     def vcost(o, ins, two=False):
         n = max(size(x) for x in ins)
@@ -128,8 +130,8 @@ def rank_program(g, core, T, topo):
         def call():
             if op1 is None:
                 return g.vector.tensor_scalar(ap(o), ap(x), s1, None, op0)
-            return g.vector.tensor_scalar(ap(o), ap(x), s1, ap(s2), op0, op1)
-        add("v", call, [x, s2], [o], vcost(o, [x]))
+            return g.vector.tensor_scalar(ap(o), ap(x), s1, s2, op0, op1)
+        add("v", call, [x], [o], vcost(o, [x]))
 
     def cp(o, x):
         add("v", lambda: g.vector.tensor_copy(ap(o), ap(x)), [x], [o], vcost(o, [x]))
@@ -151,9 +153,6 @@ def rank_program(g, core, T, topo):
     def mm(o, l, r, start=True, stop=True):
         mms([(o, l, r, start, stop)])
 
-    def tr(o, x, i):
-        add("t", lambda: g.tensor.transpose(ap(o), ap(x), ap(i)), [x, i], [o], 0.35)
-
     def iota(o, pat, base, cmul):
         def call():
             if SCRATCH[o[0]][2] == I32:
@@ -167,9 +166,6 @@ def rank_program(g, core, T, topo):
     def dma(q, out, in_, lat=2.0):
         add(q, lambda: Q[q].dma_start(ap(out), ap(in_)), [in_], [out], 0.1, lat, "d")
 
-    def dr(x):
-        return ("!", x)
-
     def send(dst, src, to, rsem):
         def call():
             rid, pid, _ = topo.addr(to)
@@ -177,15 +173,14 @@ def rank_program(g, core, T, topo):
         add("g", call, [src], [], RI + (2.0 if rsem == "ag0" else 0.0), 0.0, "r", (rsem, len(topo.engines(core, to))))
         add("net", None, [], [dst], 0.0, RL + RB * size(dst) / 256, "n", (rsem, len(topo.engines(core, to)), len(prog) - 1))
 
-    boost[0] = None
-    LD = [("ini", 0, 16, T.gs[:], 0.35), ("ini", 16, 32, T.gf[:], 0.35), ("ini", 32, 48, T.gcl[:], 0.35), ("fri", 0, 256, T.fr[:], 0.5)]
-    LD += [("ski", w, w + SKW, T.sk[:, w:w + SKW], 0.7 * SKW / 512) for w in range(0, 4096, SKW)]
+    LD = [("ski", w, w + 512, T.sk[:, w:w + 512], 0.7) for w in range(0, 4096, 512)]
+    LD[FRI:FRI] = [("fri", 0, 256, T.fr[:], 0.5)]
+    LD[INI:INI] = [("ini", 0, 16, T.gs[:], 0.35), ("ini", 16, 32, T.gf[:], 0.35), ("ini", 32, 48, T.gcl[:], 0.35)]
     LD += [("thi", 0, 1, T.th[:], 0.35), ("xr", 592, 4096, T.x[:, 0:3504], 1.6), ("xr", 0, 592, T.x[:, 3504:4096], 0.55)]
     came = 0.0
     for j, (n, lo, hi, src, us) in enumerate(LD):
         came += us
-        dma("ys"[j % 2], a(n, lo, hi), dr(src), 2.2 + came - 0.05 * j)
-    boost[0] = None
+        dma("ys"[j % 2], a(n, lo, hi), ("!", src), 2.2 + came - 0.05 * j)
     iota(a("onef"), [[0, 128]], 1, 0)
     pick(a("idf"), a("onef"), [[-1, 128]], OP.is_equal, 0, 1)
     pick(a("m16"), a("onef", 0, 128, 1, 16), [[0, 8], [1, 16]], OP.is_equal, 0, -1)
@@ -200,9 +195,12 @@ def rank_program(g, core, T, topo):
     iota(a("tabb", *F3), [[1, 256]], L + 16, 0)
     iota(a("skt", 0, 592), [[0, 592]], 0, 0)
     iota(a("lim"), [[0, 8]], 1, 0)
-    iota(a("five"), [[0, 128]], 5, 0)
-    iota(a("mtwo"), [[0, 128]], -2, 0)
+    iota(a("row", 0, 256), [[1, 2], [0, 128]], -2, 0)
+    iota(a("row", 256, 384), [[0, 128]], 5, 0)
     iota(a("cu"), [[0, 256]], L, 0)
+    iota(a("cn"), [[0, 128]], -L, 0)
+    iota(a("tr", 0, 256), [[16, 16], [0, 16]], 256, 0)
+    iota(a("tr", 256, 512), [[0, 16], [1, 16]], 16, 0)
     iota(a("vals"), [[0, 8]], 0, 0)
     iota(a("il"), [[64, 3], [0, 8]], O - L + 16, 1)
     for t in range(RO):
@@ -217,24 +215,25 @@ def rank_program(g, core, T, topo):
     act(a("j8"), a("ea", 128, 136), AF.Copy)
     for ch in H:
         act(a("mske", *PH[ch]), a("eb", 0, 128), AF.Copy)
-    for n, w in (("idb", 1.0), ("idk", -10240.0), ("id4", 4.0), ("idh", 0.5), ("idc", -2.0), ("idn", -1.0), ("idu", float(L))):
+    for n, w in (("idb", 1.0), ("idk", -10240.0), ("id4", 4.0), ("idh", 0.5), ("idc", -2.0), ("id2", 2.0), ("idu", float(L)), ("ids", 0.5 * L), ("idl", -float(L)), ("idx", -1.5 * L)):
         act(a(n), a("idf"), AF.Copy, w)
     act(a("oneb"), a("onef"), AF.Copy)
+    act(a("rstb"), a("rst"), AF.Copy)
+    act(a("rsb"), a("rst"), AF.Identity, float(U), -float(U))
+    for j, w in enumerate((16.0, -2.0, -4.0)):
+        act(a("bw", 8 * j, 8 * j + 8), a("j8"), AF.Copy, w)
     ts(a("pm"), a("pi"), 15, OP.bitwise_and)
     cp(a("el"), a("ci", 0, 24))
     cp(a("ek"), a("pm"))
     for ch in H:
         tt(a("iu", 16 * ch + 8, 16 * ch + 16), a("ci", 24 + 8 * ch, 32 + 8 * ch), a("pm"), OP.add)
     act(a("iw"), a("iu"), AF.Identity, 1.0, float(L - O))
-    EX = ("ea", "eb")
-    fcs, xp, fus = (a("fa", 0, 128), a("fb", 256, 384)), a("fb", 0, 256), a("fa", 256, 512)
+    EX, e15 = ("ea", "eb"), a("el", 16, 24)
+    fcs, fus, XP = (a("fa", 0, 128), a("fb", 256, 384)), a("fa", 256, 512), (a("fb", 0, 128), a("eb", 256, 384))
+    mtwo, mone, five = a("row", 0, 128), a("row", 128, 256), a("row", 256, 384)
 
-    XP = (a("fb", 0, 128), a("eb", 256, 384))
-
-    def to_w(x, ch):
-        c = 256 * x + 128 * ch
-        tt(a("lh", c, c + 128), a("mske", 0, 128), a(EX[x], 128 * ch, 128 * ch + 128), OP.mult)
-        mm(a("pl", 16 * ch + 8 * x, 16 * ch + 8 * x + 8), a("lh", c, c + 128), a("j8"))
+    def GF(last, ch):
+        return (256 * ch, 256 * ch + 128) if last else PH[ch]
 
     def lists(t, ch, xs):
         n, l8 = 8 * len(xs), (8 * ch, 8 * ch + 8)
@@ -245,50 +244,55 @@ def rank_program(g, core, T, topo):
             h = a("wq", c + n - 8, c + n)
             tt(a("we", *l8), h, a("iw", 16 * ch + 8, 16 * ch + 16), OP.is_equal)
             ts(a("wf", *l8), a("we", *l8), 512, OP.mult)
+            if ch in SHORT and t < 4:
+                cp(a("gl", 80 * t + c, 80 * t + c + 16), a("wq", c, c + 16))
+                tt(a("wq", 64 + 8 * ch, 72 + 8 * ch), a("wf", *l8), h, OP.add)
+                cp(hl(t, ch), a("wq", 64 + 8 * ch, 72 + 8 * ch))
+                return
             tt(h, a("wf", *l8), h, OP.add)
-        cp(a("gl", 64 * t + c, 64 * t + c + 2 * n), a("wq", c, c + 2 * n))
+        cp(a("gl", 80 * t + c, 80 * t + c + 2 * n), a("wq", c, c + 2 * n))
 
     def hl(t, ch):
-        c = 64 * t + 32 * ch + (16 if ch and t < 4 else 8)
+        c = 80 * t + (32 * ch + 8 if t == 4 or ch not in SPLIT else 64 + 8 * ch if ch in SHORT else 32 * ch + 16)
         return a("gl", c, c + 8)
 
     def clause_part(t, F, ch):
-        (lo, hi), c = PH[ch], 64 * t + 32 * ch
-        y = a("p3", 256 + lo, 256 + hi)
-        act(a("hb", lo, hi), ind(a("tabb"), hl(t, ch)), AF.Identity)
-        tt(a("tc", lo, hi), ind(a("skt"), a("gl", c + 24, c + 32)), a("hb", lo, hi), OP.add)
-        if "x" in VS:
-            tt(a("hb", lo, hi), a(F, 16 + lo, 16 + hi), a("tc", lo, hi), OP.min)
-            ts(XP[ch], a("hb", lo, hi), 2 * L, OP.is_lt, 2 * L, OP.mult)
-            return
+        (lo, hi), c = PH[ch], 80 * t + 32 * ch
+        y, cl = a("p3", 256 + lo, 256 + hi), a("gl", c + 24, c + 32)
         act(a("sb", lo, hi), a(F, 16 + lo, 16 + hi), AF.Sign, 1.0, -1.5 * L)
+        if ch in SHORT and t < 4 or (t // 4, ch) in QUICK:
+            act(a("sa", lo, hi), ind(a("skt"), cl), AF.Sign)
+            act(a("sc", lo, hi), ind(a("tabb"), hl(t, ch)), AF.Sign, 1.0, -float(L))
+            mms([(y, a("idb"), a("sb", lo, hi), True, False), (y, a("idb"), a("sa", lo, hi), False, False)])
+            mm(y, a("idb"), a("sc", lo, hi), False, True)
+            act(XP[ch], y, AF.Relu, -float(L), 3.0 * L)
+            act(a("hb", lo, hi), ind(a("tabb"), a("gl", c + 16, c + 24) if ch in SHORT and t < 4 else hl(t, ch)), AF.Identity)
+            tt(a("tc", lo, hi), ind(a("skt"), cl), a("hb", lo, hi), OP.add)
+            return
+        act(a("hb", lo, hi), ind(a("tabb"), hl(t, ch)), AF.Identity)
+        if ch in TC and t < 4:
+            act(a("key", lo, hi), ind(a("skt"), cl), AF.Identity)
+            mms([(y, a("idf"), a("hb", lo, hi), True, False), (y, a("idf"), a("key", lo, hi), False, True)])
+            act(a("tc", lo, hi), y, AF.Identity)
+        else:
+            tt(a("tc", lo, hi), ind(a("skt"), cl), a("hb", lo, hi), OP.add)
         act(a("sa", lo, hi), a("tc", lo, hi), AF.Sign, 1.0, -2.0 * L)
+        if ch in CP:
+            mms([(XP[ch], mtwo, a("cn"), True, False), (XP[ch], a("idl"), a("sb", lo, hi), False, False), (XP[ch], a("idl"), a("sa", lo, hi), False, False)])
+            return
         mms([(y, a("idb"), a("sb", lo, hi), True, False), (y, a("idb"), a("sa", lo, hi), False, True)])
         act(XP[ch], y, AF.Relu, -float(L), 2.0 * L)
 
-    def up(name, more=0.0):
-        boost[0], mark[0] = T0 + PERIOD * mark[1] + UPS[name] + more, name
-
-    def save(sv, out):
-        ts(a("w2"), a("w"), 2 * L - 1, OP.bitwise_and)
-        ts(a("sg1"), a("w2"), L, OP.is_ge, -2 * L, OP.mult)
-        tt(a("sh"), sv, a("sg1"), OP.add)
-        tt(out, a("w2"), a("sh"), OP.max)
-
-    def next_saved(sv, own, d):
-        n = 32 - d
+    def next_saved(sv, own):
         ts(a("s3"), a(sv), 1.0 / 1024, OP.mult, -8192 - 592 - 1.0 / 64, OP.add)
-        tt(a("t4", 0, n), a("s3", 0, n), a("s3", d, 32), OP.mult)
-        ts(a("t5", 0, n), a("t4", 0, n), 5, OP.arith_shift_right, 4095, OP.bitwise_and)
-        tt(a("t6", 0, n), a("t5", 0, n), a("s3", d, 32), OP.add)
-        ts(a("t7", 0, n), a("t6", 0, n), 1024, OP.mult, 1024, OP.add)
-        ts(a("t8", 0, n), a("t7", 0, n), U - 1, OP.bitwise_and)
-        tt(a("mx", d, 32), a("t8", 0, n), own, OP.add)
-        for c in range(0, 32, 2 * d):
-            if "mx" in VS:
-                ts(a("mx", c, c + d), a(sv, c, c + d), -2 * L, OP.add)
-            else:
-                act(a("mx", c, c + d), a(sv, c, c + d), AF.Identity, 1.0, -2.0 * L)
+        tt(a("t4"), a("s3", 0, 24), a("s3", 8, 32), OP.mult)
+        ts(a("t5"), a("t4"), 5, OP.arith_shift_right, 4095, OP.bitwise_and)
+        tt(a("t6"), a("t5"), a("s3", 8, 32), OP.add)
+        ts(a("t7"), a("t6"), 1024, OP.mult, 1024, OP.add)
+        ts(a("t8"), a("t7"), U - 1, OP.bitwise_and)
+        tt(a("mx", 8, 32), a("t8"), own, OP.add)
+        for c in (0, 16):
+            act(a("mx", c, c + 8), a(sv, c, c + 8), AF.Identity, 1.0, -2.0 * L)
 
     def sign(o, x, name):
         if name in VS:
@@ -307,7 +311,7 @@ def rank_program(g, core, T, topo):
     ts(a("sv"), a("w"), 2 * L, OP.add)
     for ch in H:
         lists(4, ch, H)
-        act(a("fb0", *PH[ch]), ind(a("tabb", 0, 528), a("gl", 256 + 32 * ch, 264 + 32 * ch)), AF.Identity)
+        act(a("fb0", *PH[ch]), ind(a("tabb", 0, 528), a("gl", 320 + 32 * ch, 328 + 32 * ch)), AF.Identity)
     ts(a("frs"), a("fri"), (1 << 30) - 512, OP.bitwise_and)
     tt(a("frm"), a("fri"), a("frs"), OP.add)
     ts(a("f0", *OWN), a("frm"), 16 + O, OP.add, 2 * L, OP.min)
@@ -316,7 +320,7 @@ def rank_program(g, core, T, topo):
     for j in range(8):
         s = 512 * j
         if j in KS:
-            h = a(("fa", "fb")[j // 2 % 2])
+            h = a(("fa", "fb")[KS.index(j) % 2])
             cp(a("skv", s, s + 512), a("ski", s, s + 512))
             act(a("sks", s, s + 512), a("skv", s, s + 512), AF.Sign, -1.0, 4095.5)
             mm(h, a("idf"), a("skv", s, s + 512), True, False)
@@ -329,9 +333,6 @@ def rank_program(g, core, T, topo):
         act(a("skt", s + 592, s + 1104), a("skv", s, s + 512), AF.Identity, 1024.0, float(O + U))
     for ch in H:
         clause_part(4, "f0", ch)
-    for j, w in enumerate((16.0, -2.0, -4.0)):
-        act(a("bw", 8 * j, 8 * j + 8), a("j8"), AF.Copy, w)
-    act(a("rstb"), a("rst"), AF.Copy)
     ts(a("vals", 0, 1), a("pm", 0, 1), -1, OP.mult, 16, OP.add)
     ts(a("thj", 0, 1), a("thi", 0, 1), 4080, OP.bitwise_and)
     ts(a("thj", 1, 2), a("thi", 0, 1), 15, OP.bitwise_and)
@@ -341,7 +342,7 @@ def rank_program(g, core, T, topo):
     for j in range(3):
         mm(a("pl", 64 + 128 * j, 192 + 128 * j, 1, 2), a("vals", 2 * j, 2 * j + 2), a("idf"))
     act(a("crow"), a("pl", 64, 448, 1, 2), AF.Copy)
-    next_saved("sv", a("iu", 8, 32), 8)
+    next_saved("sv", a("iu", 8, 32))
 
     def places(w, raw, m, p, q, pr, r, u):
         ts(a(q, *w), a(raw, *w), 1023, OP.bitwise_and)
@@ -354,7 +355,7 @@ def rank_program(g, core, T, topo):
     def outputs(F, ch):
         (lo, hi), c, d = PH[ch], 16 * ch, 32 * ch
         w = a("w", c, c + 16)
-        tt(w, a("mx", c, c + 16), a(EX[ch], 0, 256, 16), OP.max)
+        tt(w, a("mx", c, c + 16), a("sum", 256 * ch + 15, 256 * ch + 256, 16) if FAST[2] else a(EX[ch], 0, 256, 16), OP.max)
         ts(a("fi", c, c + 16), w, L - 1, OP.bitwise_and)
         ts(a("fq", c, c + 16), w, 1023, OP.bitwise_and)
         ts(a("w2", c, c + 16), w, 23, OP.arith_shift_right, 1, OP.bitwise_and)
@@ -369,7 +370,7 @@ def rank_program(g, core, T, topo):
         mm(a("pl", lo, hi, 1, 32), a("fim", d, d + 32), a("idf"))
         ts(a("fot", lo, hi), a("pl", lo, hi, 1, 32), 0.5, OP.mult, -16 - O // 2, OP.add)
         e = a("fa", 256 + lo, 256 + hi)
-        mm(e, a("five"), a("cu", 0, 128), True, False)
+        mm(e, five, a("cu", 0, 128), True, False)
         mm(e, a("gon"), a("rs", lo, hi), False, False)
         mm(e, a("idf"), a(F, 528 + lo, 528 + hi), False, True)
         tt(a("fu", lo, hi), a("fu", lo, hi), e, OP.min)
@@ -380,78 +381,110 @@ def rank_program(g, core, T, topo):
         tt(a("o3", lo, hi), a("o2", lo, hi), a("oq", lo, hi), OP.add)
         tt(a("hb", lo, hi), a("o3", lo, hi), e, OP.add)
         ts(a("oz", lo, hi), a("hb", lo, hi), -1, OP.max)
-        dma("y", dr(T.yf[:, lo:hi]), a("oz", lo, hi))
+        dma("y", ("!", T.yf[:, lo:hi]), a("oz", lo, hi))
 
     for t in range(RO):
-        F, last = "f%d" % t, t == RO - 1
+        F, last, to = "f%d" % t, t == RO - 1, T.cores[(rank + 1 + t % 3) % N]
         B = "f%d" % max(t - 1, 0)
-        mark[1] = t
         for ch, (lo, hi) in enumerate(PH):
-            up("g%d" % ch)
+            up(t, "g%d" % ch)
             if t == 0:
-                tt(a("tg", lo, hi), ind(a("skt"), a("gl", 272 + 32 * ch, 280 + 32 * ch)), a("fb0", lo, hi), OP.add)
-                tt(a("rawg", lo, hi), ind(a(F, 0, 528), a("gl", 256 + 32 * ch, 264 + 32 * ch)), a("tg", lo, hi), OP.min)
+                tt(a("tg", lo, hi), ind(a("skt"), a("gl", 336 + 32 * ch, 344 + 32 * ch)), a("fb0", lo, hi), OP.add)
+                tt(a("rawg", lo, hi), ind(a(F, 0, 528), a("gl", 320 + 32 * ch, 328 + 32 * ch)), a("tg", lo, hi), OP.min)
             else:
                 c, C = 48 * (t - 1) + 24 * ch, a("r%d" % (t - 1))
-                tt(a("tg", lo, hi), ind(a("skt"), a("arr", c + 16 - 8 * ch, c + 24 - 8 * ch)), a("tabb", 272 + lo, 272 + hi), OP.add)
-                tt(a("rawg", lo, hi), ind(C, a("arr", c, c + 8)), a("tg", lo, hi), OP.min)
-                up(("col", "col1")[ch])
+                sl, e = a("arr", c + 16 - 8 * (ch in SPLIT), c + 24 - 8 * (ch in SPLIT)), a("d%d" % ch, 0, 128)
+                if ch in TG:
+                    act(a("tg", lo, hi), ind(a("skt"), sl), AF.Identity)
+                    mms([(e, a("oneb", 0, 128, 1, 1), a("tr", c2 + lo, c2 + hi), not c2, False) for c2 in (0, 256)])
+                    mm(e, a("idf"), a("tg", lo, hi), False, True)
+                else:
+                    tt(a("tg", lo, hi), ind(a("skt"), sl), a("tabb", 272 + lo, 272 + hi), OP.add)
+                    tt(a("rawg", lo, hi), ind(C, a("arr", c, c + 8)), a("tg", lo, hi), OP.min)
+                up(t, "col%d" % ch)
                 act(a(F, 272 + lo, 272 + hi), ind(C, a("arr", c, c + 8)), AF.Identity)
-            up("g%d" % ch)
+                if ch in TG:
+                    tt(a("rawg", lo, hi), a(F, 272 + lo, 272 + hi), e, OP.min)
+            up(t, "g%d" % ch)
             places((lo, hi), "rawg", "ga", "pg", "qg", "prg", "rg", "ug")
-        to = T.cores[(rank + 1 + t % 3) % N]
         if not last:
             send(a("r%d" % t, *GH), a(F, *GH), to, "ag%d" % t)
         for j, (lo, hi) in enumerate(GCH):
-            up("u%d" % j)
+            up(t, "u%d" % (lo // 1024), lo % 1024 / 730)
             act(a("ub", lo, hi), ind(a("xr"), a("ug", lo // 16, hi // 16)), AF.Identity)
         for ch, (lo, hi) in enumerate(PH):
-            up(("c0", "x1")[ch])
-            e = XP[ch]
-            tt(e, a("ga", lo, hi), e, OP.add)
-            tt(a(F, 528 + lo, 528 + hi), a(B, 16 + lo, 16 + hi), e, OP.min)
-            up("c%d" % ch)
-            tt(a("rawc", lo, hi), ind(a(F, 0, 528 + hi), hl((t + 4) % 5, ch)), a("tc", lo, hi), OP.min)
+            up(t, "x%d" % ch)
+            if ch in CP:
+                cp(a("gaf", *GF(last, ch)), a("ga", lo, hi))
+                mm(XP[ch], a("idf"), a("gaf", *GF(last, ch)), False, True)
+            else:
+                tt(XP[ch], a("ga", lo, hi), XP[ch], OP.add)
+            if ch in SHORT and t:
+                tt(a("hb", lo, hi), ind(a(F, 0, 528), a("gl", 80 * t - 64 + 32 * ch, 80 * t - 56 + 32 * ch)), a("tc", lo, hi), OP.min)
+                tt(a("rawc", lo, hi), a("hb", lo, hi), XP[ch], OP.min)
+            tt(a(F, 528 + lo, 528 + hi), a(B, 16 + lo, 16 + hi), XP[ch], OP.min)
+            up(t, "c%d" % ch)
+            if not (ch in SHORT and t):
+                tt(a("rawc", lo, hi), ind(a(F, 0, 528 + hi), hl((t + 4) % 5, ch)), a("tc", lo, hi), OP.min)
             places((lo, hi), "rawc", "ca", "pc", "qc", "prc", "rc", "uc")
         for lo, hi in VCH:
-            up("w4" if hi == 4096 else "w%d" % (lo // 1024), lo % 1024 / 730)
+            up(t, "w4" if hi == 4096 else "w%d" % (lo // 1024), lo % 1024 / 730)
+            if (lo, hi) == SW:
+                act(a("df", lo, hi), ind(a("xr"), a("uc", lo // 16, hi // 16)), AF.Identity)
+                mms([(a("pl", 0, hi - lo), a("idc"), a("ub", lo, hi), True, False), (a("pl", 0, hi - lo), a("id2"), a("df", lo, hi), False, True)])
+                continue
             tt(a("df", lo, hi), ind(a("xr"), a("uc", lo // 16, hi // 16)), a("ub", lo, hi), OP.subtract)
         for lo, hi in ACH:
-            up("a4" if hi == 4096 else "a%d" % (lo // 1024), lo % 1024 / 730)
-            act(a("ab", lo, hi), a("df", lo, hi), AF.Abs)
+            up(t, "a4" if hi == 4096 else "a%d" % (lo // 1024), lo % 1024 / 730)
+            if (lo, hi) == SW:
+                act(a("ab", lo, hi), a("pl", 0, hi - lo), AF.Abs, 0.5)
+            else:
+                act(a("ab", lo, hi), a("df", lo, hi), AF.Abs)
         for ch in H:
-            up("d%d" % ch)
+            up(t, "d%d" % ch)
             D = ("d0", "d1")[ch]
             mm(fcs[ch], a("idf"), a("fu", *PH[ch]), True, False)
-            for p0, p1 in DCH[ch]:
-                mm(a(D, 0, 384, 1, p1, p0), a("oneb", p0, p1, 1, 2), a("crow"), True, False)
-                for k0 in range(0, 16, 4):
-                    mms([(a(D, k, 384, 16, p1, p0), a("ab", 2048 * ch + 16 * p0 + k, 2048 * ch + 16 * p1, 16), a("bw"), False, k == 15)
-                         for k in range(k0, k0 + 4)])
-        for ch in H:
+            mm(a(D, 0, 384), a("oneb", 0, 128, 1, 2), a("crow"), True, False)
+            for k0 in range(0, 16, 4):
+                mms([(a(D, k, 384, 16), a("ab", 2048 * ch + k, 2048 * ch + 2048, 16), a("bw"), False, k == 15) for k in range(k0, k0 + 4)])
+        for ch, (lo, hi) in enumerate(PH):
             D = ("d0", "d1")[ch]
             R = a(D, 384, 512)
-            lo, hi, l8 = 128 * ch, 128 * ch + 128, (8 * ch, 8 * ch + 8)
             s1, s2 = a("sg", 2 * lo, 2 * lo + 128), a("sg", 2 * lo + 128, 2 * lo + 256)
-            up("f%d" % ch)
-            both = ("y%d" % ch in VS) == ("z%d" % ch in VS) and not ch
-            sign(a("sg", 2 * lo, 2 * lo + 256) if both else s1, a(D, 128, 384 if both else 256), "y%d" % ch)
+            fast = FAST[2] if last else FAST[ch]
+            up(t, "f%d" % ch)
+            sign(s1 if ch else a("sg", 0, 256), a(D, 128, 256 if ch else 384), "y%d" % ch)
             scan(a("cnt", lo, hi), a("rstb"), s1, OP.mult, OP.add)
-            act(a("clx", lo, hi), ind(a("cnt", lo, hi), a("el", 16, 24)), AF.Sign, -1.0, a("lim", ch, ch + 1), None if last else a("par", ch, ch + 1))
+            act(a("clx", lo, hi), ind(a("cnt", lo, hi), e15), AF.Sign, -1.0, a("lim", ch, ch + 1), None if last else a("par", ch, ch + 1))
             mm(fcs[ch], a("clx", lo, hi), a("idu"), False, True)
             tt(a("oi", lo, hi) if last else a(F, 16 + lo, 16 + hi), a(F, 528 + lo, 528 + hi), fcs[ch], OP.max)
             if not last:
                 send(a("r%d" % t, 16 + lo, 16 + hi), a(F, 16 + lo, 16 + hi), to, "ao%d" % (2 * t + ch))
             if ch == 0 and not last:
-                up("fu")
-                mm(fus, a("five"), a("cu"), True, False)
-            up("m%d" % ch)
+                up(t, "fu")
+                mm(fus, five, a("cu"), True, False)
+            up(t, "m%d" % ch)
             tt(a("key", lo, hi), s1, a(D, 0, 128), OP.mult)
-            if not both:
-                sign(s2, a(D, 256, 384), "z%d" % ch)
-            scan(a("sm", lo, hi), a("rst"), a("key", lo, hi), OP.mult, OP.max)
-            tt(a("sel", lo, hi), ind(a("sm", lo, hi), a("el", 16, 24)), a("key", lo, hi), OP.is_equal)
-            mm(R, a("sel", lo, hi), a("idb"))
+            if ch:
+                sign(s2, a(D, 256, 384), "z1")
+            scan(a("sm", lo, hi), a("rsb"), a("key", lo, hi), OP.add, OP.max)
+            tt(a("sel", lo, hi), ind(a("sm", lo, hi), e15), a("key", lo, hi), OP.is_equal)
+            for x in range(fast):
+                up(t, "lj"[x] + str(ch))
+                e, c = a(EX[x], lo, hi), ((256 * ch + 128 * x, 256 * ch + 128 * x + 128) if last else (256 * x + lo, 256 * x + hi))
+                if x or ch not in CP:
+                    cp(a("gaf", *c), a(("ga", "ca")[x], lo, hi))
+                mm(e, mone, a("cu", 0, 128), True, False)
+                mm(e, a("gaf", *c), a("idf"), False, False)
+                mm(e, a("idx"), a("clx", lo, hi), False, False)
+                mm(e, a("ids"), s2, False, True)
+                tt(a("pgc", *c), a("sel", lo, hi), e, OP.mult)
+                scan(a("sum", *c), a("rst"), a("pgc", *c), OP.mult, OP.add)
+                if not last:
+                    tt(a("lh", *c), ind(a("sum", *c), e15), a("mske", 0, 128), OP.mult)
+            up(t, "m%d" % ch)
+            if fast < 2:
+                mm(R, a("sel", lo, hi), a("idb"))
             mm(a("p3", lo, hi), s2, a("idh"), True, False)
             mm(a("p3", lo, hi), a("clx", lo, hi), a("idc"), False, False)
             mm(a("p3", lo, hi), a("sel", lo, hi), a("id4"), False, True)
@@ -459,30 +492,33 @@ def rank_program(g, core, T, topo):
                 ts(a("rs", lo, hi), a("p3", lo, hi), -3.5, OP.add, 0, OP.max)
             else:
                 act(a("rs", lo, hi), a("p3", lo, hi), AF.Relu, 1.0, -3.5)
+            for x in H[fast:]:
+                tt(a("pgc", 256 * x + lo, 256 * x + hi), a(("ga", "ca")[x], lo, hi), R, OP.mult)
             for x in H:
-                c = 256 * x + lo
-                tt(a("pgc", c, c + 128), a(("ga", "ca")[x], lo, hi), R, OP.mult)
-            for x in H:
-                up("lj"[x] + str(ch))
+                up(t, "lj"[x] + str(ch))
                 c, e = 256 * x + lo, a(EX[ch], *PH[x]) if last else a(EX[x], lo, hi)
-                mm(e, a("mtwo"), a("cu", 0, 128), True, False)
-                mm(e, a("pgc", c, c + 128), a("go"), False, False)
-                mm(e, a("rs", lo, hi), a("gou"), False, True)
+                if x >= fast:
+                    mm(e, mtwo, a("cu", 0, 128), True, False)
+                    mm(e, a("pgc", c, c + 128), a("go"), False, False)
+                    mm(e, a("rs", lo, hi), a("gou"), False, True)
                 if last:
                     continue
-                to_w(x, ch)
-                if ch or x:
-                    c = (16 + 8 * x, 24 + 8 * x) if ch else (0, 16)
+                if x >= fast:
+                    tt(a("lh", c, c + 128), a("mske", 0, 128), e, OP.mult)
+                mm(a("pl", 16 * ch + 8 * x, 16 * ch + 8 * x + 8), a("lh", c, c + 128), a("j8"))
+                sp = ch in SPLIT
+                if sp or x:
+                    c = (16 * ch + 8 * x, 16 * ch + 8 * x + 8) if sp else (0, 16)
                     tt(a("w", *c), a("mx", *c), a("pl", *c), OP.max)
-                    lists(t, ch, (x,) if ch else H)
-                if ch != x:
-                    c = 64 * t + 32 * ch
-                    send(a("arr", 48 * t + 24 * ch, 48 * t + 24 * ch + 24 - 8 * ch), a("gl", c, c + 24 - 8 * ch), to, "al%d" % (2 * t + ch))
+                    lists(t, ch, (x,) if sp else H)
+                if sp != x:
+                    c = 80 * t + 32 * ch
+                    send(a("arr", 48 * t + 24 * ch, 48 * t + 24 * ch + 24 - 8 * sp), a("gl", c, c + 24 - 8 * sp), to, "al%d" % (2 * t + ch))
             if last:
-                up("o%d" % ch)
+                up(t, "o%d" % ch)
                 outputs(F, ch)
                 continue
-            up("fu")
+            up(t, "fu")
             mm(a("fa", 256 + lo, 256 + hi), a("gon"), a("rs", lo, hi), False, False)
         if last:
             break
@@ -491,102 +527,83 @@ def rank_program(g, core, T, topo):
         tt(a("fu"), a("fu"), fus, OP.min)
         dma("y", a("f%d" % (t + 1), *OWN), a(F, *OWN), 2.8)
         for ch in H:
-            up("k%d" % ch)
+            up(t, "k%d" % ch)
             clause_part(t, F, ch)
-        up("sv")
-        if "par" in VS:
-            ts(a("thj", 2, 4), a("par", 0, 2), 1.0 / 32, OP.mult, 4, OP.add)
-            ts(a("thj", 4, 6), a("thj", 2, 4), 1, OP.bitwise_and)
-            ts(a("lim", 0, 2), a("thj", 4, 6), -2, OP.mult, 1, OP.add)
-        else:
-            act(a("par", 2, 4), a("par", 0, 2), AF.Abs, 1.0 / 32)
-            act(a("par", 4, 6), a("par", 2, 4), AF.Abs, 1.0, -2.0)
-            act(a("par", 6, 8), a("par", 4, 6), AF.Abs, 2.0, -2.0)
-            act(a("lim", 0, 2), a("par", 6, 8), AF.Identity, 1.0, -1.0)
-        save(a("sv"), a("sv"))
+        up(t, "sv")
+        act(a("par", 2, 4), a("par", 0, 2), AF.Abs, 1.0 / 32)
+        act(a("par", 4, 6), a("par", 2, 4), AF.Abs, 1.0, -2.0)
+        act(a("par", 6, 8), a("par", 4, 6), AF.Abs, 2.0, -2.0)
+        act(a("lim", 0, 2), a("par", 6, 8), AF.Identity, 1.0, -1.0)
+        ts(a("w2"), a("w"), 2 * L - 1, OP.bitwise_and)
+        ts(a("sg1"), a("w2"), L, OP.is_ge, -2 * L, OP.mult)
+        tt(a("sh"), a("sv"), a("sg1"), OP.add)
+        tt(a("sv"), a("w2"), a("sh"), OP.max)
         if t < RO - 2:
-            next_saved("sv", a("iu", 8, 32), 8)
-        else:
-            for x in H:
-                tt(a("lh", 256 * x, 256 * x + 256), ind(a("sv", 8 * x, 8 * x + 24), a("el", 0, 16)), a("mske"), OP.mult)
-                for ch in H:
-                    c = 256 * x + 128 * ch
-                    mm(a("pl", 32 + 16 * ch + 8 * x, 40 + 16 * ch + 8 * x), a("lh", c, c + 128), a("j8"))
-            act(a("svs"), a("pl", 32, 64), AF.Copy)
-            next_saved("svs", a("il"), 8)
-            cp(a("w2"), a("svs"))
-            ts(a("fi", 0, 32), a("w2"), L - 1, OP.bitwise_and)
-            ts(a("fq", 0, 32), a("w2"), 1023, OP.bitwise_and)
-            tt(a("sv"), a("fi", 0, 32), a("fq", 0, 32), OP.add)
-            for c in (8, 24):
-                ts(a("sv", c, c + 8), a("s3", c, c + 8), 2, OP.mult, 32 + O, OP.add)
-
-    up("o1")
+            next_saved("sv", a("iu", 8, 32))
+            continue
+        for x in H:
+            tt(a("lh", 256 * x, 256 * x + 256), ind(a("sv", 8 * x, 8 * x + 24), a("el", 0, 16)), a("mske"), OP.mult)
+            for ch in H:
+                c = 256 * x + 128 * ch
+                mm(a("pl", 32 + 16 * ch + 8 * x, 40 + 16 * ch + 8 * x), a("lh", c, c + 128), a("j8"))
+        act(a("svs"), a("pl", 32, 64), AF.Copy)
+        next_saved("svs", a("il"))
+        cp(a("w2"), a("svs"))
+        ts(a("fi"), a("w2"), L - 1, OP.bitwise_and)
+        ts(a("fq"), a("w2"), 1023, OP.bitwise_and)
+        tt(a("sv"), a("fi"), a("fq"), OP.add)
+        for c in (8, 24):
+            ts(a("sv", c, c + 8), a("s3", c, c + 8), 2, OP.mult, 32 + O, OP.add)
     for j, y in enumerate((T.yg, T.yc, T.ysg, T.yk)):
-        dma("sy"[j % 2], dr(y[:]), a("fot", 0, 256, 1, 8 * j + 8, 8 * j))
+        dma("sy"[j % 2], ("!", y[:]), a("fot", 0, 256, 1, 8 * j + 8, 8 * j))
 
     lg, n = {}, len(prog)
-    dep, succ = [[] for _ in range(n)], [[] for _ in range(n)]
+    dep = [[] for _ in range(n)]
     for i, p in enumerate(prog):
         ds, q = {}, p["q"] if p["kind"] == "c" else "#%d" % i
-        for e, kind in meets(q, p["acc"], lg):
-            inq = e[4] == q and (q == "t" or NOWAR and e[2] == "r")
-            ds[e[3]] = max(ds.get(e[3], 0.0), 0.0 if inq else WAKE.get(prog[e[3]]["q"] + p["q"], WAKE[prog[e[3]]["q"]]))
+        for e in meets(q, p["acc"], lg):
+            ds[e[3]] = WAKE.get(prog[e[3]]["q"] + p["q"], WAKE[prog[e[3]]["q"]])
         if p["kind"] == "n":
             ds[p["extra"][2]] = 0.0
         note(q, p["acc"], lg, i)
         dep[i] = sorted(ds.items())
-        for d, w in dep[i]:
-            succ[d].append((i, w))
-    dur, lat = [p["dur"] for p in prog], [p["lat"] for p in prog]
-    before = [[(d, w + lat[d]) for d, w in dep[i]] for i in range(n)]
-    after = [[(j, w + lat[i]) for j, w in succ[i]] for i in range(n)]
+    dur, lat, qs = [p["dur"] for p in prog], [p["lat"] for p in prog], [p["q"] for p in prog]
+    before, after = [[(d, w + lat[d]) for d, w in dep[i]] for i in range(n)], [[] for _ in range(n)]
     for i in range(2, len(LD)):
         before[i].append((i - 2, 0.0))
-        after[i - 2].append((i, 0.0))
+    for i in range(n):
+        for d, w in before[i]:
+            after[d].append((i, w))
 
-    def schedule(pre, post, first, prio):
+    def schedule(prio):
         free = {q: 0.0 for q in list(Q) + ["net"]}
-        left, done, order = [len(d) for d in pre], [0.0] * n, []
-        ready = {q: [(first[i], i) for i in range(n) if not left[i] and prog[i]["q"] == q] for q in free}
+        left, done = [len(d) for d in before], [0.0] * n
+        ready = {q: [(0.0, i) for i in range(n) if not left[i] and qs[i] == q] for q in free}
         for _ in range(n):
             best = None
             for q in free:
-                if not ready[q]:
-                    continue
-                t0 = max(free[q], min(ready[q])[0]) if q != "net" else min(ready[q])[0]
-                c = max((prio[i], -i, e) for e, i in ready[q] if e <= t0 + SLACK)
-                i = -c[1]
-                if c[2] > t0:
-                    short = [(prio[k], -k) for e, k in ready[q] if e <= t0 + 1e-9 and t0 + dur[k] <= c[2] + OVER]
-                    if short:
-                        i = -max(short)[1]
-                    else:
-                        t0 = c[2]
-                if best is None or t0 < best[0]:
-                    best = (t0, i, q)
+                if ready[q]:
+                    t0 = max(free[q], min(ready[q])[0]) if q != "net" else min(ready[q])[0]
+                    c = max((prio[i], -i, e) for e, i in ready[q] if e <= t0 + SLACK)
+                    if best is None or max(t0, c[2]) < best[0]:
+                        best = (max(t0, c[2]), -c[1], q)
             t0, i, q = best
             ready[q] = [x for x in ready[q] if x[1] != i]
-            done[i] = t0 + dur[i]
-            if q != "net":
-                free[q] = done[i]
-            order.append(i)
-            for j, w in post[i]:
+            done[i] = free[q] = t0 + dur[i]
+            for j, w in after[i]:
                 left[j] -= 1
                 if not left[j]:
-                    ready[prog[j]["q"]].append((max([done[d] + w2 for d, w2 in pre[j]] + [first[j]]), j))
-        return order, done
+                    ready[qs[j]].append((max(done[d] + w2 for d, w2 in before[j]), j))
+        return done
 
-    def improve(order, seed):
-        qs = [p["q"] for p in prog]
+    def improve(order, seed, part):
         prev, last = [-1] * n, {}
         for i in order:
             if qs[i] != "net":
                 prev[i], last[qs[i]] = last.get(qs[i], -1), i
-
         done, rest, pos = [0.0] * n, [0.0] * n, [0] * n
         best, arcs, lo, hi = (1e9, order), None, 0, n
-        for step in range(STEPS + 1):
+        for turn in range(STEPS + 1):
             if arcs is None:
                 nxt = {prev[i]: i for i in range(n) if prev[i] >= 0}
                 for i in order[lo:]:
@@ -605,7 +622,7 @@ def rank_program(g, core, T, topo):
                 for k in range(lo, hi):
                     pos[order[k]] = k
                 span = max(rest)
-                arcs = [j for j in order if prev[j] >= 0 and done[prev[j]] + rest[j] > span - 1e-6]
+                arcs = [j for j in order[pos[part[0]]:pos[part[1]]] if prev[j] >= 0 and done[prev[j]] + rest[j] > span - NEAR]
                 if span < best[0]:
                     best = (span, list(order), list(done))
             seed = (seed * 1103515245 + 12345) % 2147483648
@@ -635,7 +652,7 @@ def rank_program(g, core, T, topo):
                 if j in move:
                     continue
                 seg = [k for k in seg if k not in move] + [k for k in seg if k in move]
-            p2, d2, c, s2, b = {}, {}, prev[i], 0.0, pos[j]
+            p2, d2, r2, c, b = {}, {}, {}, prev[i], pos[j]
             for k in seg:
                 if qs[k] == q:
                     p2[k], c = c, k
@@ -645,20 +662,28 @@ def rank_program(g, core, T, topo):
                     e = d2.get(d, done[d]) + w
                     if e > t0:
                         t0 = e
-                t0 = d2[k] = t0 + dur[k]
-                e = t0 + lat[k]
-                for d, w in after[k]:
-                    if pos[d] > b and t0 + w + rest[d] > e:
-                        e = t0 + w + rest[d]
-                if qs[k] != q and k in nxt and pos[nxt[k]] > b and t0 + rest[nxt[k]] > e:
-                    e = t0 + rest[nxt[k]]
-                if e > s2:
-                    s2 = e
+                d2[k] = t0 + dur[k]
             if j in nxt:
                 p2[nxt[j]] = c
-                s2 = max(s2, d2[c] + rest[nxt[j]])
+            c, s2, more = nxt.get(j, -1), 0.0, 0.0
+            for k in reversed(seg):
+                if qs[k] == q:
+                    e, c = c, k
+                else:
+                    e = nxt.get(k, -1)
+                t0 = max(lat[k], r2.get(e, rest[e]) if e >= 0 else 0.0)
+                for d, w in after[k]:
+                    e = r2.get(d, rest[d]) + w
+                    if e > t0:
+                        t0 = e
+                r2[k] = t0 + dur[k]
+                e = d2[k] + t0 - span
+                if e > s2:
+                    s2 = e
+                more += math.exp(min(e, 5.0) / SOFT) - math.exp((done[k] - dur[k] + rest[k] - span) / SOFT)
             seed = (seed * 1103515245 + 12345) % 2147483648
-            if s2 <= span + HEAT * (1 - step / STEPS) * (seed >> 8 & 1023) ** 2 / 1048576:
+            e = (1 - turn / STEPS) * (seed >> 8 & 1023) ** 2 / 1048576
+            if s2 <= HEAT * e + 1e-9 and more <= WARM * e:
                 lo, hi, arcs = pos[i], b + 1, None
                 order[lo:hi] = seg
                 for k in p2:
@@ -666,29 +691,30 @@ def rank_program(g, core, T, topo):
         return best
 
     if not PLAN:
-        prio, zero = [0.0] * n, [0.0] * n
+        prio = [0.0] * n
         for i in range(n - 1, -1, -1):
             prio[i] = dur[i] + max([w + prio[j] for j, w in after[i]] + [lat[i]])
-        due = schedule(before, after, zero, prio)[1]
+        due = schedule(prio)
         for i, p in enumerate(prog):
-            if p["up"] is not None:
-                due[i] = max([p["up"]] + [due[d] + w for d, w in before[i]]) + dur[i]
-        best = None
+            if p["id"]:
+                due[i] = max([p["due"]] + [due[d] + w for d, w in before[i]]) + dur[i]
+        best, mark = None, [i for i, p in enumerate(prog) if p["id"] and p["id"][1:] == ("w4", 0)]
         for turn in range(TURNS):
-            now = improve(sorted(range(n), key=lambda i: (due[i] - dur[i], i)), turn + 1)
+            now = improve(sorted(range(n), key=lambda i: (due[i] - dur[i], i)), turn + SEED, (mark[1], mark[2]) if turn % ALL else (0, n - 1))
             best = now if not best or now[0] < best[0] else best
             end = {p["id"]: now[2][i] for i, p in enumerate(prog) if p["id"]}
             span, t = min((end[(t, "w4", 0)] - end[(t - 1, "w4", 0)], t) for t in (1, 2, 3))
+            if turn % ALL == ALL - 1 or ALL == 1:
+                SPANS.append(round(span, 1))
             for i, p in enumerate(prog):
                 due[i] = now[2][i]
                 if p["id"]:
                     r, name, k = p["id"]
                     s = t if end.get((t, name, k), 1e9) <= end[(t, "w4", 0)] else t - 1
-                    e = end[(s, name, k)] + (r - s) * span + end[(0, "w4", 0)] - end[(t, "w4", 0)] + t * span if (s, name, k) in end else 0.0
+                    e = end[(s, name, k)] + (r - s + t) * span + end[(0, "w4", 0)] - end[(t, "w4", 0)] if (s, name, k) in end else 0.0
                     due[i] = max([e - dur[i]] + [due[d] + w for d, w in before[i]]) + dur[i]
         PLAN.extend(best[:2])
         PLAN.extend((prog, before, dur, lat))
-    plan = PLAN[1]
 
     def wait(q, sem, c):
         if know[q].get(sem, 0) < c:
@@ -698,16 +724,15 @@ def rank_program(g, core, T, topo):
             know[q][sem] = c
 
     ref = {}
-    for i in plan:
+    for i in PLAN[1]:
         p = prog[i]
         q = p["q"]
         if p["kind"] != "n":
             want = {}
             for d, w in dep[i]:
-                if not w:
-                    continue
-                sem, c = ref[d]
-                want[sem] = max(want.get(sem, 0), c)
+                if w:
+                    sem, c = ref[d]
+                    want[sem] = max(want.get(sem, 0), c)
             for sem in sorted(want, key=lambda s: (s == SEM.get(q), s)):
                 wait(q, sem, want[sem])
             inst = p["call"]()

@@ -3,7 +3,8 @@ from concourse.mybir import AluOpType, ActivationFunctionType
 
 OP = AluOpType
 AF = ActivationFunctionType
-U, L, O = 1 << 22, 1 << 23, 592 * 1024
+U, L, O = 1 << 22, 1 << 23, 16 * 8192 + 592
+C0 = 592 - 2048 - L // 2
 NF, RO, N = 256, 5, 4
 H = (0, 1)
 F32, BF, I32, U16 = "float32", "bfloat16", "int32", "uint16"
@@ -17,38 +18,42 @@ def _bufs(where, dtype, text):
         SCRATCH[n] = (where, [int(r), int(c)], dtype)
 
 
-_bufs("sbuf", F32, "skv:4096 skt:4688 tabb:784 j8:8 mske:256 rst:128 rsb:128 idf:128 go:128 gok:128 onef:128 e8:8x128 m16:16x128 vals:8 gaf:512 sum:512 "
-      "iw:32 iu:32 il:24 lim:8 hb:256 tg:256 tc:256 fu:256 key:256 sm:256 pgc:512 lh:512 we:16 wf:16 sv:32 svs:32 sg1:32 sh:32 mx:32 par:8 "
-      "fim:64 fot:32x256 oz:256 f0:784 f1:784 f2:784 f3:784 f4:784 r0:528 r1:528 r2:528 r3:528")
-_bufs("sbuf", BF, "idk:128 xr:4096 ub:4096 df:4096 ab:4096 bw:24 idb:128 id4:128 idh:128 gou:128 gon:128 oneb:128 crow:2x384 cu:1x256 cn:1x128 idl:128 id2:128 tr:1x512 row:1x384 "
-      "idu:128 idc:128 ids:128 idx:128 rstb:128 sg:512 cnt:256 sel:256 rs:256 clx:256 sa:256 sb:256 sc:256")
-_bufs("sbuf", I32, "ski:4096 ini:48 fri:256 thi:8 thj:8 pi:8 ci:40 pm:8 rawg:256 rawc:256 ga:256 ca:256 "
-      "pg:256 qg:256 prg:256 rg:256 pc:256 qc:256 prc:256 rc:256 w:32 w2:32 wq:80 s3:32 t4:24 t5:24 t6:24 t7:24 t8:24 fi:32 fq:32 oi:256")
-_bufs("sbuf", U16, "ug:256 uc:256 el:24 ek:8 gl:400 arr:192")
+_bufs("sbuf", F32, "skt:4688 tabb:784 bg:256 j8:8 mske:256 rst:128 rsb:128 idf:128 go:128 onef:128 e8:8x128 m16:16x128 inf:16x384 id8:16x16 gaf:512 sum:512 "
+      "iw:16 iu:32 il:16 lim:8 hb:256 tg:256 tc:256 fu:256 key:256 sm:256 pgc:512 lh:512 we:16 wf:16 svy:64 sg1:32 sh:32 mx:32 par:8 "
+      "fim:64 fot:64x128 oz:256 f0:784 f1:784 f2:784 f3:784 f4:784 r0:528 r1:528 r2:528 r3:528")
+_bufs("sbuf", BF, "idk:128 idm:128 idn:128 xr:4096 ub:4096 df:4096 ab:4096 bw:48 idb:128 id4:128 idh:128 gou:128 gon:128 oneb:128 crow:33x384 cu:1x256 cn:1x128 idl:128 row:1x384 "
+      "idu:128 idc:128 ids:128 idx:128 rstb:128 sg:512 cnt:256 sel:256 rs:256 clx:256 sa:256 sb:256")
+_bufs("sbuf", I32, "ski:4096 ini:16x384 fri:256 thi:33x128 thj:33x128 pi:16 ci:72 pm:16 rawg:256 rawc:256 ga:256 ca:256 sv:32 svs:32 "
+      "pg:256 qg:256 prg:256 rg:256 pc:256 qc:256 prc:256 rc:256 w:32 w2:32 wq:64 s2:32 s3:32 t4:16 t5:16 t6:16 t7:16 t8:16 fi:32 fq:32 oi:256")
+_bufs("sbuf", U16, "ug:256 uc:256 el:24 ek:32 gl:320 arr:128")
 _bufs("psum", F32, "d0:512 d1:512 p3:512 ea:512 eb:512 pl:512 fa:512 fb:512")
-SEMAPHORES = ["sv", "ss", "st", "sg", "rl"] + [n + str(t) for n in ("al", "ao", "ag") for t in range(8)] + ["d%d" % t for t in range(32)]
+SEMAPHORES = ["sv", "ss", "st", "sg", "rl"] + [n + str(t) for n in ("al", "ao", "ag") for t in range(8)] + ["d%d" % t for t in range(40)]
 VIEW = {"sks": ("df", 0, 4096), "frs": ("oi", 0, 256), "frm": ("oz", 0, 256), "o2": ("pg", 0, 256), "oq": ("qg", 0, 256), "o3": ("tg", 0, 256), "fb0": ("key", 0, 256)}
 PSUM = [n for n in SCRATCH if SCRATCH[n][0] == "psum"]
 OWN, GH, F3 = (16, 272), (272, 528), (528, 784)
-GCH = [(0, 1024), (1024, 2048), (2048, 3072), (3072, 4096)]
-VCH = [(0, 1024), (1024, 2048), (2048, 3072), (3072, 3584), (3584, 4096)]
-ACH = [(0, 1024), (1024, 2048), (2048, 3072), (3072, 3584), (3584, 4096)]
-SW = None
+GCH = [(c, c + 512) for c in range(0, 4096, 512)]
+VCH = [(c, c + 512) for c in range(0, 4096, 512)]
+ACH = [(c, c + 512) for c in range(0, 4096, 512)]
+RELU = (1,)
 PH = [(0, 128), (128, 256)]
-KS = (0, 2, 4)
-INI, FRI = 0, 0
-FAST, TG, SPLIT, SHORT, QUICK, TC, CP = (1, 1, 0), (), (0, 1), (), (), (), (0, 1)
-CYC, CG, FIX, GFIX, SFIX, PEC, PFIX = 0.0009, 1.28, 0.005, 0.05, 0.05, 0.00053, 0.015
+SKP = [(c, c + 512) for c in range(0, 3584, 512)] + [(3584, 3904), (3904, 4096)]
+SKL = [(0, 1024), (1024, 2048), (2048, 3072), (3072, 3584), (3584, 3904), (3904, 4096)]
+INI, FRI = 0, 3
+FAST, JOIN, LATE = (1, 1, 2), 0, (((0, 128),), ((0, 128),))
+SW = {}
+ONS = ("gaf0", "ug0", "s3", "t7", "gaf1", "ug1", "mx", "caf1", "caf0", "uc0", "uc1", "inf", "sh", "crow", "idu", "ids", "idx", "idl", "id4", "t4", "sg1")
+CYC, CG, FIX, GFIX, SFIX, PEC, PFIX = 0.00095, 1.42, 0.005, 0.05, 0.05, 0.00056, 0.015
 WAKE = {"v": 0.16, "vv": 0.22, "s": 0.24, "t": 0.3, "tt": 0.0, "g": 0.1, "y": 0.2, "net": 0.2, "vg": 0.3}
 RI, RL, RB = 0.25, 1.3, 0.4
-VS = set()
 T0, PERIOD, SLACK = 8.0, 17.6, 0.1
 DUE = {"g0": 5.0, "col0": 5.0, "col1": 5, "u0": 7.3, "u1": 8.7, "c0": 6.0, "g1": 7.0, "x0": 6.0, "x1": 8.5, "w0": 9.9, "w1": 11.3, "c1": 12.7, "u2": 10.2, "a0": 11.6,
        "w2": 14.0, "a1": 12.8, "u3": 13.7, "d0": 10, "w3": 15, "a2": 15.5, "f0": 16, "m0": 16, "w4": 15.7, "a3": 16, "a4": 16.7, "d1": 10, "f1": 18, "m1": 18,
        "l0": 17, "l1": 18, "j0": 18, "j1": 21, "k0": 20.5, "k1": 21, "fu": 22, "sv": 22, "o0": 17, "o1": 18}
 PLAN = []
-TURNS, STEPS, HEAT, FAR, ALL, SPANS = 2, 150000, 0.5, 40, 1, []
-SOFT, WARM, NEAR, SEED = 0.3, 6.0, 0.05, 1
+STEPS, HEAT, FAR, SPANS = (100000, 300000), (0.5, 0.12), 40, []
+SOFT, WARM, NEAR, SEEDS = 0.3, 0.25, 0.05, (2,)
+WIDE, STAY = 260, 1000
+ROUND, CUTS, COOL, LEAVE = 5000, 8, 0.3, 0
 
 
 def rank_program(g, core, T, topo):
@@ -94,7 +99,7 @@ def rank_program(g, core, T, topo):
             for e in lg.get(n, []):
                 if n in PSUM and e[4] != q:
                     yield e
-                elif lo < e[1] and e[0] < hi and "w" in (kind, e[2]):
+                elif lo < e[1] and e[0] < hi and r0 < e[6] and e[5] < r1 and "w" in (kind, e[2]):
                     yield e
                 elif n in PSUM and q == "t" and kind == "w" and e[2] == "w":
                     yield e
@@ -103,8 +108,8 @@ def rank_program(g, core, T, topo):
         for kind, (n, lo, hi, st, r0, r1) in acc:
             old = lg.get(n, [])
             if kind == "w":
-                old = [e for e in old if (q != "t" if n in PSUM and e[4] != q else not (st == 1 and lo <= e[0] and e[1] <= hi))]
-            lg[n] = old + [(lo, hi, kind, ref, q)]
+                old = [e for e in old if (q != "t" if n in PSUM and e[4] != q else not (st == 1 and lo <= e[0] and e[1] <= hi and r0 <= e[5] and e[6] <= r1))]
+            lg[n] = old + [(lo, hi, kind, ref, q, r0, r1)]
 
     def add(q, call, reads, writes, dur, lat=0.0, kind="c", extra=None):
         seen[step[1]] = seen.get(step[1], -1) + 1
@@ -136,6 +141,9 @@ def rank_program(g, core, T, topo):
     def cp(o, x):
         add("v", lambda: g.vector.tensor_copy(ap(o), ap(x)), [x], [o], vcost(o, [x]))
 
+    def fill(o, c):
+        add("v", lambda: g.vector.memset(ap(o), c), [], [o], vcost(o, [o]))
+
     def scan(o, d0, d1, op0, op1):
         add("v", lambda: g.vector.tensor_tensor_scan(ap(o), ap(d0), ap(d1), 0.0, op0, op1), [d0, d1], [o], vcost(o, [d0, d1]))
 
@@ -145,6 +153,16 @@ def rank_program(g, core, T, topo):
                 return g.scalar.activation(ap(o), ap(x), func, ap(bias), scale, accum_out=ap(acc))
             return g.scalar.activation(ap(o), ap(x), func, ap(bias), scale)
         add("s", call, [x, bias], [o, acc], 0.065 + CYC * CG * size(x) if x[0] == "@" else SFIX + CYC * max(64, size(x)))
+
+    def lin(name, o, x, scale=1.0, bias=0.0):
+        if name in ONS:
+            act(o, x, AF.Identity, float(scale), float(bias))
+        elif bias:
+            ts(o, x, scale, OP.mult, bias, OP.add)
+        elif scale != 1:
+            ts(o, x, scale, OP.mult)
+        else:
+            cp(o, x)
 
     def mms(ms):
         add("t", lambda: [g.tensor.matmul(ap(o), ap(l), ap(r), s0, s1) for o, l, r, s0, s1 in ms][-1], [x for m in ms for x in m[1:3]], [m[0] for m in ms],
@@ -173,61 +191,54 @@ def rank_program(g, core, T, topo):
         add("g", call, [src], [], RI + (2.0 if rsem == "ag0" else 0.0), 0.0, "r", (rsem, len(topo.engines(core, to))))
         add("net", None, [], [dst], 0.0, RL + RB * size(dst) / 256, "n", (rsem, len(topo.engines(core, to)), len(prog) - 1))
 
-    LD = [("ski", w, w + 512, T.sk[:, w:w + 512], 0.7) for w in range(0, 4096, 512)]
-    LD[FRI:FRI] = [("fri", 0, 256, T.fr[:], 0.5)]
-    LD[INI:INI] = [("ini", 0, 16, T.gs[:], 0.35), ("ini", 16, 32, T.gf[:], 0.35), ("ini", 32, 48, T.gcl[:], 0.35)]
-    LD += [("thi", 0, 1, T.th[:], 0.35), ("xr", 592, 4096, T.x[:, 0:3504], 1.6), ("xr", 0, 592, T.x[:, 3504:4096], 0.55)]
+    LD = [(a("ski", lo, hi), T.sk[:, lo:hi], 0.2 + 0.5 * (hi - lo) / 512) for lo, hi in SKL]
+    LD[FRI:FRI] = [(a("fri"), T.fr[:], 0.45)]
+    LD[INI:INI] = [(a("ini", 128 * j, 128 * j + 128), y[:], 0.06) for j, y in enumerate((T.gs, T.gf, T.gcl))]
+    LD += [(a("xr", 592, 4096), T.x[:, 0:3504], 1.9), (a("xr", 0, 592), T.x[:, 3504:4096], 0.5)]
+    LD += [(a("thi", 0, 128, 1, r + 1, r), T.th[:], 0.06) for r in (0, 32)]
     came = 0.0
-    for j, (n, lo, hi, src, us) in enumerate(LD):
+    for j, (o, src, us) in enumerate(LD):
         came += us
-        dma("ys"[j % 2], a(n, lo, hi), ("!", src), 2.2 + came - 0.05 * j)
-    iota(a("onef"), [[0, 128]], 1, 0)
+        dma("ys"[j % 2], o, ("!", src), 2.2 + came - 0.05 * j)
+    fill(a("onef"), 1.0)
     pick(a("idf"), a("onef"), [[-1, 128]], OP.is_equal, 0, 1)
     pick(a("m16"), a("onef", 0, 128, 1, 16), [[0, 8], [1, 16]], OP.is_equal, 0, -1)
     pick(a("e8"), a("onef", 0, 128, 1, 8), [[1, 8], [0, 16]], OP.is_equal, 0, -1)
-    pick(a("rst"), a("onef"), [[0, 8], [1, 16]], OP.not_equal, 0, 0)
-    iota(a("pi"), [[0, 8]], 0, 1)
-    iota(a("iu"), [[0, 32]], O - L, 0)
-    iota(a("ci", 0, 16), [[16, 2], [1, 8]], 0, 0)
+    iota(a("pi"), [[0, 16]], 0, 1)
+    iota(a("ci", 0, 16), [[1, 16]], 0, 0)
     iota(a("ci", 16, 24), [[16, 8]], 15, 0)
-    iota(a("ci", 24, 40), [[16, 16]], O - L + 16, 0)
+    iota(a("ci", 24, 40), [[16, 16]], 16, 0)
+    iota(a("ci", 40, 72), [[1, 2], [2, 16]], 0, 0)
     iota(a("tabb", 0, 528), [[1, 528]], 0, 0)
-    iota(a("tabb", *F3), [[1, 256]], L + 16, 0)
-    iota(a("skt", 0, 592), [[0, 592]], 0, 0)
-    iota(a("lim"), [[0, 8]], 1, 0)
-    iota(a("row", 0, 256), [[1, 2], [0, 128]], -2, 0)
-    iota(a("row", 256, 384), [[0, 128]], 5, 0)
-    iota(a("cu"), [[0, 256]], L, 0)
-    iota(a("cn"), [[0, 128]], -L, 0)
-    iota(a("tr", 0, 256), [[16, 16], [0, 16]], 256, 0)
-    iota(a("tr", 256, 512), [[0, 16], [1, 16]], 16, 0)
-    iota(a("vals"), [[0, 8]], 0, 0)
-    iota(a("il"), [[64, 3], [0, 8]], O - L + 16, 1)
+    iota(a("tabb", *F3), [[1, 256]], 1024 + 16, 0)
+    iota(a("t8"), [[0, 8], [128, 2]], 16, 1)
+    for n, lo, hi, st, c in (("skt", 0, 592, 1, 0), ("lim", 0, 8, 1, 1), ("row", 0, 128, 1, -2), ("row", 128, 256, 1, -1), ("row", 256, 384, 1, 5), ("cu", 0, 256, 1, L),
+                             ("cn", 0, 128, 1, -L), ("oneb", 0, 128, 1, 1), ("rst", 0, 128, 1, 1), ("rst", 0, 128, 16, 0), ("rstb", 0, 128, 1, 1),
+                             ("rstb", 0, 128, 16, 0), ("rsb", 0, 128, 1, 0), ("rsb", 0, 128, 16, -U), ("iu", 0, 16, 1, O - L), ("svy", 0, 32, 1, 0)):
+        fill(a(n, lo, hi, st), float(c))
     for t in range(RO):
-        iota(a("f%d" % t, 0, 16), [[0, 16]], 0, 0)
+        fill(a("f%d" % t, 0, 16), 0.0)
         if t < RO - 1:
-            iota(a("r%d" % t, 0, 16), [[0, 16]], 0, 0)
+            fill(a("r%d" % t, 0, 16), 0.0)
     mm(a("ea", 0, 128), a("e8"), a("e8"))
     mm(a("ea", 128, 136), a("e8"), a("idf", 0, 8, 1, 8))
     mm(a("eb", 0, 128), a("m16"), a("m16"))
-    for n, w in (("go", 1.0), ("gok", 1024.0), ("gou", float(L)), ("gon", -2.0 * L)):
+    for n, w in (("go", 1.0), ("gou", float(L)), ("gon", -2.0 * L)):
         act(a(n), a("ea", 0, 128), AF.Copy, w)
     act(a("j8"), a("ea", 128, 136), AF.Copy)
     for ch in H:
         act(a("mske", *PH[ch]), a("eb", 0, 128), AF.Copy)
-    for n, w in (("idb", 1.0), ("idk", -10240.0), ("id4", 4.0), ("idh", 0.5), ("idc", -2.0), ("id2", 2.0), ("idu", float(L)), ("ids", 0.5 * L), ("idl", -float(L)), ("idx", -1.5 * L)):
-        act(a(n), a("idf"), AF.Copy, w)
-    act(a("oneb"), a("onef"), AF.Copy)
-    act(a("rstb"), a("rst"), AF.Copy)
-    act(a("rsb"), a("rst"), AF.Identity, float(U), -float(U))
-    for j, w in enumerate((16.0, -2.0, -4.0)):
-        act(a("bw", 8 * j, 8 * j + 8), a("j8"), AF.Copy, w)
+    for n, w in (("idb", 1.0), ("idn", -1.0), ("idk", 1.5 * L), ("idm", -2048.0), ("id4", 4.0), ("idh", 0.5), ("idc", -2.0), ("idu", float(L)), ("ids", 0.5 * L), ("idl", -float(L)), ("idx", -1.5 * L)):
+        lin(n, a(n), a("idf"), w)
+    for j, w in enumerate((16.0, -2.0, -4.0) + ((-16.0, 2.0, 4.0) if RELU else ())):
+        lin("bw", a("bw", 8 * j, 8 * j + 8), a("j8"), w)
     ts(a("pm"), a("pi"), 15, OP.bitwise_and)
     cp(a("el"), a("ci", 0, 24))
-    cp(a("ek"), a("pm"))
-    for ch in H:
-        tt(a("iu", 16 * ch + 8, 16 * ch + 16), a("ci", 24 + 8 * ch, 32 + 8 * ch), a("pm"), OP.add)
-    act(a("iw"), a("iu"), AF.Identity, 1.0, float(L - O))
+    cp(a("ek"), a("ci", 40, 72))
+    tt(a("iw"), a("ci", 24, 40), a("pm"), OP.add)
+    lin("iu", a("iu", 16, 32), a("iw"), 8192, 592 - L)
+    lin("il", a("il"), a("t8"), 8192, 592 - L)
+    act(a("bg"), a("tabb", *GH), AF.Identity, 8192.0, float(C0))
     EX, e15 = ("ea", "eb"), a("el", 16, 24)
     fcs, fus, XP = (a("fa", 0, 128), a("fb", 256, 384)), a("fa", 256, 512), (a("fb", 0, 128), a("eb", 256, 384))
     mtwo, mone, five = a("row", 0, 128), a("row", 128, 256), a("row", 256, 384)
@@ -235,150 +246,127 @@ def rank_program(g, core, T, topo):
     def GF(last, ch):
         return (256 * ch, 256 * ch + 128) if last else PH[ch]
 
-    def lists(t, ch, xs):
-        n, l8 = 8 * len(xs), (8 * ch, 8 * ch + 8)
-        c, w = 32 * ch + 16 * xs[0], a("w", 16 * ch + 8 * xs[0], 16 * ch + 8 * xs[0] + n)
-        ts(a("wq", c, c + n), w, 1023, OP.bitwise_and)
-        ts(a("wq", c + n, c + 2 * n), w, 10, OP.arith_shift_right, 8191, OP.bitwise_and)
-        if 1 in xs:
-            h = a("wq", c + n - 8, c + n)
-            tt(a("we", *l8), h, a("iw", 16 * ch + 8, 16 * ch + 16), OP.is_equal)
-            ts(a("wf", *l8), a("we", *l8), 512, OP.mult)
-            if ch in SHORT and t < 4:
-                cp(a("gl", 80 * t + c, 80 * t + c + 16), a("wq", c, c + 16))
-                tt(a("wq", 64 + 8 * ch, 72 + 8 * ch), a("wf", *l8), h, OP.add)
-                cp(hl(t, ch), a("wq", 64 + 8 * ch, 72 + 8 * ch))
-                return
+    def lists(t, lo, hi):
+        n, c, w, l8 = hi - lo, 2 * lo, a("w", lo, hi), (max(lo - 16, 0), hi - 16)
+        ts(a("wq", c, c + n), w, 13, OP.arith_shift_right, 1023, OP.bitwise_and)
+        ts(a("wq", c + n, c + 2 * n), w, 8191, OP.bitwise_and)
+        if hi > 16:
+            h = a("wq", c + n - l8[1] + l8[0], c + n)
+            tt(a("we", *l8), h, a("iw", *l8), OP.is_equal)
+            lin("wf%d" % (lo // 8 % 2), a("wf", *l8), a("we", *l8), 512)
             tt(h, a("wf", *l8), h, OP.add)
-        cp(a("gl", 80 * t + c, 80 * t + c + 2 * n), a("wq", c, c + 2 * n))
+        lin("gl%d%d" % (lo // 16, lo // 8 % 2), a("gl", 64 * t + c, 64 * t + c + 2 * n), a("wq", c, c + 2 * n))
 
-    def hl(t, ch):
-        c = 80 * t + (32 * ch + 8 if t == 4 or ch not in SPLIT else 64 + 8 * ch if ch in SHORT else 32 * ch + 16)
+    def gl(t, x, k, ch):
+        c = 64 * t + (32 * k + 16 * x + 8 * ch if t == 4 else 32 + 16 * k + 8 * ch if x and JOIN else 32 * x + 16 * ch + 8 * k)
         return a("gl", c, c + 8)
 
+    def hl(t, ch):
+        return gl(t, 1, 0, ch)
+
     def clause_part(t, F, ch):
-        (lo, hi), c = PH[ch], 80 * t + 32 * ch
-        y, cl = a("p3", 256 + lo, 256 + hi), a("gl", c + 24, c + 32)
+        lo, hi = PH[ch]
+        y, cl = a("p3", 256 + lo, 256 + hi), gl(t, 1, 1, ch)
         act(a("sb", lo, hi), a(F, 16 + lo, 16 + hi), AF.Sign, 1.0, -1.5 * L)
-        if ch in SHORT and t < 4 or (t // 4, ch) in QUICK:
-            act(a("sa", lo, hi), ind(a("skt"), cl), AF.Sign)
-            act(a("sc", lo, hi), ind(a("tabb"), hl(t, ch)), AF.Sign, 1.0, -float(L))
-            mms([(y, a("idb"), a("sb", lo, hi), True, False), (y, a("idb"), a("sa", lo, hi), False, False)])
-            mm(y, a("idb"), a("sc", lo, hi), False, True)
-            act(XP[ch], y, AF.Relu, -float(L), 3.0 * L)
-            act(a("hb", lo, hi), ind(a("tabb"), a("gl", c + 16, c + 24) if ch in SHORT and t < 4 else hl(t, ch)), AF.Identity)
-            tt(a("tc", lo, hi), ind(a("skt"), cl), a("hb", lo, hi), OP.add)
-            return
-        act(a("hb", lo, hi), ind(a("tabb"), hl(t, ch)), AF.Identity)
-        if ch in TC and t < 4:
+        act(a("hb", lo, hi), ind(a("tabb"), hl(t, ch)), AF.Identity, 8192.0, float(C0))
+        if "tc%d" % ch in ONS and t < 4:
             act(a("key", lo, hi), ind(a("skt"), cl), AF.Identity)
             mms([(y, a("idf"), a("hb", lo, hi), True, False), (y, a("idf"), a("key", lo, hi), False, True)])
             act(a("tc", lo, hi), y, AF.Identity)
         else:
             tt(a("tc", lo, hi), ind(a("skt"), cl), a("hb", lo, hi), OP.add)
         act(a("sa", lo, hi), a("tc", lo, hi), AF.Sign, 1.0, -2.0 * L)
-        if ch in CP:
-            mms([(XP[ch], mtwo, a("cn"), True, False), (XP[ch], a("idl"), a("sb", lo, hi), False, False), (XP[ch], a("idl"), a("sa", lo, hi), False, False)])
-            return
-        mms([(y, a("idb"), a("sb", lo, hi), True, False), (y, a("idb"), a("sa", lo, hi), False, True)])
-        act(XP[ch], y, AF.Relu, -float(L), 2.0 * L)
+        mms([(XP[ch], mtwo, a("cn"), True, False), (XP[ch], a("idl"), a("sb", lo, hi), False, False), (XP[ch], a("idl"), a("sa", lo, hi), False, False)])
 
     def next_saved(sv, own):
-        ts(a("s3"), a(sv), 1.0 / 1024, OP.mult, -8192 - 592 - 1.0 / 64, OP.add)
-        tt(a("t4"), a("s3", 0, 24), a("s3", 8, 32), OP.mult)
+        ts(a("s2"), a(sv), 8191, OP.bitwise_and)
+        lin("s3", a("s3"), a("s2"), 1, -592)
+        lin("t7", a("t7"), a("s2", 16, 32), 1, -591)
+        tt(a("t4"), a("s3", 0, 16), a("s3", 16, 32), OP.mult)
         ts(a("t5"), a("t4"), 5, OP.arith_shift_right, 4095, OP.bitwise_and)
-        tt(a("t6"), a("t5"), a("s3", 8, 32), OP.add)
-        ts(a("t7"), a("t6"), 1024, OP.mult, 1024, OP.add)
-        ts(a("t8"), a("t7"), U - 1, OP.bitwise_and)
-        tt(a("mx", 8, 32), a("t8"), own, OP.add)
-        for c in (0, 16):
-            act(a("mx", c, c + 8), a(sv, c, c + 8), AF.Identity, 1.0, -2.0 * L)
+        tt(a("t6"), a("t5"), a("t7"), OP.add)
+        ts(a("t8"), a("t6"), 4095, OP.bitwise_and)
+        tt(a("mx", 16, 32), a("t8"), own, OP.add)
+        lin("mx", a("mx", 0, 16), a(sv, 0, 16), 1.0, -2.0 * L)
 
-    def sign(o, x, name):
-        if name in VS:
-            ts(o, x, 1, OP.min, -1, OP.max)
-        else:
-            act(o, x, AF.Sign)
-
-    ts(a("wq", 0, 16), a("ini", 0, 16), 1024, OP.mult, 16, OP.add)
-    tt(a("wq", 16, 32), a("wq", 0, 16), a("ini", 16, 32), OP.add)
-    tt(a("lh", 0, 128), ind(a("wq", 16, 32), a("ek")), a("go"), OP.mult)
-    tt(a("lh", 128, 256), ind(a("ini", 32, 48), a("ek")), a("gok"), OP.mult)
+    lin("inf", a("inf"), a("ini"))
+    lin("id8", a("id8"), a("idf", 0, 16, 1, 16), 8192)
+    mms([(a("pl", 64 + 16 * (j // 2), 80 + 16 * (j // 2)), a("inf", 128 * j, 128 * j + 128), a("id8" if j == 1 else "idf", 0, 16, 1, 16), j != 1, j != 0) for j in range(3)])
+    lin("sh", a("sh"), a("pl", 64, 96))
     for ch in H:
-        for x in H:
-            mm(a("pl", 16 * ch + 8 * x, 16 * ch + 8 * x + 8), a("lh", *PH[x]), a("mske", 8 * ch, 8 * ch + 8))
+        tt(a("lh", 256 * ch, 256 * ch + 256), ind(a("sh"), a("ek", 16 * ch, 16 * ch + 16)), a("mske"), OP.mult)
+        mms([(a("pl", 16 * x + 8 * ch, 16 * x + 8 * ch + 8), a("lh", 256 * ch + 128 * x, 256 * ch + 128 * x + 128), a("j8"), True, True) for x in H])
     tt(a("w"), a("iu"), a("pl", 0, 32), OP.add)
-    ts(a("sv"), a("w"), 2 * L, OP.add)
-    for ch in H:
-        lists(4, ch, H)
-        act(a("fb0", *PH[ch]), ind(a("tabb", 0, 528), a("gl", 320 + 32 * ch, 328 + 32 * ch)), AF.Identity)
-    ts(a("frs"), a("fri"), (1 << 30) - 512, OP.bitwise_and)
-    tt(a("frm"), a("fri"), a("frs"), OP.add)
-    ts(a("f0", *OWN), a("frm"), 16 + O, OP.add, 2 * L, OP.min)
+    lin("sv", a("sv"), a("w"), 1, 2 * L)
+    lists(4, 0, 32)
+    act(a("fb0"), ind(a("tabb", 0, 528), a("gl", 256, 272)), AF.Identity, 8192.0, float(C0))
+    ts(a("frs"), a("fri"), 511 + (1 << 21), OP.bitwise_and)
+    ts(a("pc"), a("fri"), 9, OP.arith_shift_right)
+    act(a("p3", 0, 256), a("frs"), AF.Identity, 8192.0, float(O))
+    tt(a("frm"), a("pc"), a("p3", 0, 256), OP.add)
+    ts(a("f0", *OWN), a("frm"), 2 * L, OP.min)
     act(a("f0", *GH), a("f0", *OWN), AF.Identity)
     act(a("fu"), a("f0", *OWN), AF.Identity, 1.0, -float(L))
-    for j in range(8):
-        s = 512 * j
-        if j in KS:
-            h = a(("fa", "fb")[KS.index(j) % 2])
-            cp(a("skv", s, s + 512), a("ski", s, s + 512))
-            act(a("sks", s, s + 512), a("skv", s, s + 512), AF.Sign, -1.0, 4095.5)
-            mm(h, a("idf"), a("skv", s, s + 512), True, False)
-            mm(h, a("idk"), a("sks", s, s + 512), False, True)
-            act(a("skt", s + 592, s + 1104), h, AF.Identity, 1024.0, O - 1.5 * U)
-            continue
-        h = a(("d0", "d1")[sum(k not in KS for k in range(j)) % 2])
-        ts(h, a("ski", s, s + 512), 4096, OP.is_lt, -20480, OP.mult)
-        tt(a("skv", s, s + 512), a("ski", s, s + 512), h, OP.add)
-        act(a("skt", s + 592, s + 1104), a("skv", s, s + 512), AF.Identity, 1024.0, float(O + U))
+    for j, (lo, hi) in enumerate(SKP):
+        h = a(("d0", "d1", "fa", "fb")[j % 4], 0, hi - lo)
+        act(a("sks", lo, hi), a("ski", lo, hi), AF.Sign, 1.0, -4095.5)
+        mms([(h, a("idk"), a("sks", lo, hi), True, False), (h, a("idm"), a("sks", lo, hi), False, True)])
+        tt(a("skt", lo + 592, hi + 592), a("ski", lo, hi), h, OP.add)
     for ch in H:
         clause_part(4, "f0", ch)
-    ts(a("vals", 0, 1), a("pm", 0, 1), -1, OP.mult, 16, OP.add)
-    ts(a("thj", 0, 1), a("thi", 0, 1), 4080, OP.bitwise_and)
-    ts(a("thj", 1, 2), a("thi", 0, 1), 15, OP.bitwise_and)
-    for j, w in ((2, 1), (4, -1)):
-        ts(a("vals", j, j + 1), a("thj", 0, 1), 2, OP.mult)
-        ts(a("vals", j + 1, j + 2), a("thj", 1, 2), 2, OP.mult, w, OP.add)
-    for j in range(3):
-        mm(a("pl", 64 + 128 * j, 192 + 128 * j, 1, 2), a("vals", 2 * j, 2 * j + 2), a("idf"))
-    act(a("crow"), a("pl", 64, 448, 1, 2), AF.Copy)
-    next_saved("sv", a("iu", 8, 32))
+    fill(a("crow"), 0.0)
+    iota(a("crow", 0, 128, 1, 1), [[0, 8], [-1, 16]], 16, 0)
+    for r, m in ((0, 4080), (32, 15)):
+        ts(a("thj", 0, 128, 1, r + 1, r), a("thi", 0, 128, 1, r + 1, r), m, OP.bitwise_and)
+        for j, w in ((1, 1), (2, -1)):
+            lin("crow", a("crow", 128 * j, 128 * j + 128, 1, r + 1, r), a("thj", 0, 128, 1, r + 1, r), 2, w * (r > 0))
+    next_saved("sv", a("iu", 16, 32))
 
-    def places(w, raw, m, p, q, pr, r, u):
-        ts(a(q, *w), a(raw, *w), 1023, OP.bitwise_and)
-        ts(a(p, *w), a(raw, *w), 10, OP.arith_shift_right, 8191, OP.bitwise_and)
+    def places(ch, raw, m, p, q, pr, r, u):
+        w = PH[ch]
+        ts(a(q, *w), a(raw, *w), 13, OP.arith_shift_right, 1023, OP.bitwise_and)
+        ts(a(p, *w), a(raw, *w), 8191, OP.bitwise_and)
         ts(a(m, *w), a(raw, *w), L - 1, OP.bitwise_and)
-        tt(a(pr, *w), a(p, *w), a(q, *w), OP.mult)
+        if q + str(ch) in ONS:
+            e = a("pl", 256 + w[0], 256 + w[1]) if q == "qg" else a("p3", 256 + w[0], 256 + w[1])
+            act(e, a(q, *w), AF.Identity)
+            tt(a(pr, *w), a(p, *w), e, OP.mult)
+        else:
+            tt(a(pr, *w), a(p, *w), a(q, *w), OP.mult)
         ts(a(r, *w), a(pr, *w), 4, OP.arith_shift_right, 4095, OP.bitwise_and)
-        cp(a(u, *w), a(r, *w))
+        lin(u + str(ch), a(u, *w), a(r, *w))
 
     def outputs(F, ch):
-        (lo, hi), c, d = PH[ch], 16 * ch, 32 * ch
-        w = a("w", c, c + 16)
-        tt(w, a("mx", c, c + 16), a("sum", 256 * ch + 15, 256 * ch + 256, 16) if FAST[2] else a(EX[ch], 0, 256, 16), OP.max)
-        ts(a("fi", c, c + 16), w, L - 1, OP.bitwise_and)
-        ts(a("fq", c, c + 16), w, 1023, OP.bitwise_and)
-        ts(a("w2", c, c + 16), w, 23, OP.arith_shift_right, 1, OP.bitwise_and)
-        ts(a("t4", 8 * ch, 8 * ch + 8), a("w", c + 8, c + 16), 10, OP.arith_shift_right, 8191, OP.bitwise_and)
-        tt(a("fim", d, d + 16), a("fi", c, c + 16), a("fq", c, c + 16), OP.add)
-        ts(a("we", 8 * ch, 8 * ch + 8), a("t4", 8 * ch, 8 * ch + 8), 2, OP.mult, 32 + O - 1184, OP.add)
-        ts(a("sg1", c, c + 16), a("w2", c, c + 16), -1, OP.mult, 1, OP.add)
-        tt(a("sh", c, c + 16), a("sg1", c, c + 16), a("sv", c, c + 16), OP.mult)
-        tt(a("svs", c, c + 8), a("fim", d, d + 8), a("w2", c, c + 8), OP.mult)
-        tt(a("svs", c + 8, c + 16), a("we", 8 * ch, 8 * ch + 8), a("w2", c + 8, c + 16), OP.mult)
-        tt(a("fim", d + 16, d + 32), a("svs", c, c + 16), a("sh", c, c + 16), OP.add)
-        mm(a("pl", lo, hi, 1, 32), a("fim", d, d + 32), a("idf"))
-        ts(a("fot", lo, hi), a("pl", lo, hi, 1, 32), 0.5, OP.mult, -16 - O // 2, OP.add)
+        lo, hi = PH[ch]
+        for x in H:
+            c, d = (16 * x + ch, 16 * x + 16, 2), 256 * ch + 128 * x
+            tt(a("w", *c), a("mx", *c), a("sum", d + 15, d + 128, 16) if FAST[2] else a(EX[ch], 8 * x, 8 * x + 8), OP.max)
+        if ch:
+            mm(a("pl", 0, 128, 1, 64), a("svy"), a("idf"), True, False)
+            ts(a("fi"), a("w"), 8191, OP.bitwise_and)
+            ts(a("fq"), a("w"), 13, OP.arith_shift_right, 1023, OP.bitwise_and)
+            ts(a("w2"), a("w"), 23, OP.arith_shift_right, 1, OP.bitwise_and)
+            ts(a("s2"), a("fi"), 512, OP.mult, -512 * 592 - 16, OP.add)
+            tt(a("sh", 0, 16), a("fq", 0, 16), a("svy", 32, 48), OP.subtract)
+            tt(a("svs", 16, 32), a("fi", 16, 32), a("sg1", 16, 32), OP.subtract)
+            tt(a("svs", 0, 16), a("s2", 0, 16), a("sh", 0, 16), OP.add)
+            tt(a("fim", 0, 32), a("s2"), a("fq"), OP.add)
+            tt(a("fim", 32, 64), a("svs"), a("w2"), OP.mult)
+            mm(a("pl", 0, 128, 1, 64), a("fim"), a("idf"), False, True)
+            cp(a("fot"), a("pl", 0, 128, 1, 64))
+            for j, y in enumerate((T.yg, T.yc, T.ysg, T.yk)):
+                dma("sy"[j % 2], ("!", y[:]), a("fot", 0, 128, 1, 16 * j + 16, 16 * j))
         e = a("fa", 256 + lo, 256 + hi)
         mm(e, five, a("cu", 0, 128), True, False)
         mm(e, a("gon"), a("rs", lo, hi), False, False)
         mm(e, a("idf"), a(F, 528 + lo, 528 + hi), False, True)
         tt(a("fu", lo, hi), a("fu", lo, hi), e, OP.min)
         e = a("p3", 256 + lo, 256 + hi)
-        ts(e, a("fu", lo, hi), L, OP.is_ge, -32 - O, OP.add)
-        ts(a("o2", lo, hi), a("oi", lo, hi), 2 * L - 1, OP.bitwise_and)
-        ts(a("oq", lo, hi), a("oi", lo, hi), 1023, OP.bitwise_and)
-        tt(a("o3", lo, hi), a("o2", lo, hi), a("oq", lo, hi), OP.add)
+        ts(e, a("fu", lo, hi), L, OP.is_ge, -32 - 1024 * 592, OP.add)
+        ts(a("o2", lo, hi), a("oi", lo, hi), 8191, OP.bitwise_and)
+        ts(a("oq", lo, hi), a("oi", lo, hi), 12, OP.arith_shift_right, 2046, OP.bitwise_and)
+        act(a("fb", lo, hi), a("o2", lo, hi), AF.Identity, 1024.0)
+        tt(a("o3", lo, hi), a("oq", lo, hi), a("fb", lo, hi), OP.add)
         tt(a("hb", lo, hi), a("o3", lo, hi), e, OP.add)
         ts(a("oz", lo, hi), a("hb", lo, hi), -1, OP.max)
         dma("y", ("!", T.yf[:, lo:hi]), a("oz", lo, hi))
@@ -389,24 +377,16 @@ def rank_program(g, core, T, topo):
         for ch, (lo, hi) in enumerate(PH):
             up(t, "g%d" % ch)
             if t == 0:
-                tt(a("tg", lo, hi), ind(a("skt"), a("gl", 336 + 32 * ch, 344 + 32 * ch)), a("fb0", lo, hi), OP.add)
-                tt(a("rawg", lo, hi), ind(a(F, 0, 528), a("gl", 320 + 32 * ch, 328 + 32 * ch)), a("tg", lo, hi), OP.min)
+                tt(a("tg", lo, hi), ind(a("skt"), gl(4, 0, 1, ch)), a("fb0", lo, hi), OP.add)
+                tt(a("rawg", lo, hi), ind(a(F, 0, 528), gl(4, 0, 0, ch)), a("tg", lo, hi), OP.min)
             else:
-                c, C = 48 * (t - 1) + 24 * ch, a("r%d" % (t - 1))
-                sl, e = a("arr", c + 16 - 8 * (ch in SPLIT), c + 24 - 8 * (ch in SPLIT)), a("d%d" % ch, 0, 128)
-                if ch in TG:
-                    act(a("tg", lo, hi), ind(a("skt"), sl), AF.Identity)
-                    mms([(e, a("oneb", 0, 128, 1, 1), a("tr", c2 + lo, c2 + hi), not c2, False) for c2 in (0, 256)])
-                    mm(e, a("idf"), a("tg", lo, hi), False, True)
-                else:
-                    tt(a("tg", lo, hi), ind(a("skt"), sl), a("tabb", 272 + lo, 272 + hi), OP.add)
-                    tt(a("rawg", lo, hi), ind(C, a("arr", c, c + 8)), a("tg", lo, hi), OP.min)
+                c, C = 32 * (t - 1) + 16 * ch, a("r%d" % (t - 1))
+                tt(a("tg", lo, hi), ind(a("skt"), a("arr", c + 8, c + 16)), a("bg", lo, hi), OP.add)
+                tt(a("rawg", lo, hi), ind(C, a("arr", c, c + 8)), a("tg", lo, hi), OP.min)
                 up(t, "col%d" % ch)
                 act(a(F, 272 + lo, 272 + hi), ind(C, a("arr", c, c + 8)), AF.Identity)
-                if ch in TG:
-                    tt(a("rawg", lo, hi), a(F, 272 + lo, 272 + hi), e, OP.min)
             up(t, "g%d" % ch)
-            places((lo, hi), "rawg", "ga", "pg", "qg", "prg", "rg", "ug")
+            places(ch, "rawg", "ga", "pg", "qg", "prg", "rg", "ug")
         if not last:
             send(a("r%d" % t, *GH), a(F, *GH), to, "ag%d" % t)
         for j, (lo, hi) in enumerate(GCH):
@@ -414,46 +394,49 @@ def rank_program(g, core, T, topo):
             act(a("ub", lo, hi), ind(a("xr"), a("ug", lo // 16, hi // 16)), AF.Identity)
         for ch, (lo, hi) in enumerate(PH):
             up(t, "x%d" % ch)
-            if ch in CP:
-                cp(a("gaf", *GF(last, ch)), a("ga", lo, hi))
-                mm(XP[ch], a("idf"), a("gaf", *GF(last, ch)), False, True)
-            else:
-                tt(XP[ch], a("ga", lo, hi), XP[ch], OP.add)
-            if ch in SHORT and t:
-                tt(a("hb", lo, hi), ind(a(F, 0, 528), a("gl", 80 * t - 64 + 32 * ch, 80 * t - 56 + 32 * ch)), a("tc", lo, hi), OP.min)
-                tt(a("rawc", lo, hi), a("hb", lo, hi), XP[ch], OP.min)
+            lin("gaf%d" % ch, a("gaf", *GF(last, ch)), a("ga", lo, hi))
+            mm(XP[ch], a("idf"), a("gaf", *GF(last, ch)), False, True)
             tt(a(F, 528 + lo, 528 + hi), a(B, 16 + lo, 16 + hi), XP[ch], OP.min)
             up(t, "c%d" % ch)
-            if not (ch in SHORT and t):
-                tt(a("rawc", lo, hi), ind(a(F, 0, 528 + hi), hl((t + 4) % 5, ch)), a("tc", lo, hi), OP.min)
-            places((lo, hi), "rawc", "ca", "pc", "qc", "prc", "rc", "uc")
+            tt(a("rawc", lo, hi), ind(a(F, 0, 528 + hi), hl((t + 4) % 5, ch)), a("tc", lo, hi), OP.min)
+            places(ch, "rawc", "ca", "pc", "qc", "prc", "rc", "uc")
         for lo, hi in VCH:
             up(t, "w4" if hi == 4096 else "w%d" % (lo // 1024), lo % 1024 / 730)
-            if (lo, hi) == SW:
+            if lo in SW:
+                e = a(SW[lo], 0, hi - lo)
                 act(a("df", lo, hi), ind(a("xr"), a("uc", lo // 16, hi // 16)), AF.Identity)
-                mms([(a("pl", 0, hi - lo), a("idc"), a("ub", lo, hi), True, False), (a("pl", 0, hi - lo), a("id2"), a("df", lo, hi), False, True)])
+                mms([(e, a("idn"), a("ub", lo, hi), True, False), (e, a("idb"), a("df", lo, hi), False, True)])
+                act(a("ab", lo, hi), e, AF.Abs)
                 continue
             tt(a("df", lo, hi), ind(a("xr"), a("uc", lo // 16, hi // 16)), a("ub", lo, hi), OP.subtract)
         for lo, hi in ACH:
             up(t, "a4" if hi == 4096 else "a%d" % (lo // 1024), lo % 1024 / 730)
-            if (lo, hi) == SW:
-                act(a("ab", lo, hi), a("pl", 0, hi - lo), AF.Abs, 0.5)
+            if lo in SW:
+                continue
+            if lo // 1024 in RELU:
+                ts(a("ab", lo, hi), a("df", lo, hi), 0, OP.max, 2, OP.mult)
             else:
                 act(a("ab", lo, hi), a("df", lo, hi), AF.Abs)
         for ch in H:
             up(t, "d%d" % ch)
             D = ("d0", "d1")[ch]
             mm(fcs[ch], a("idf"), a("fu", *PH[ch]), True, False)
-            mm(a(D, 0, 384), a("oneb", 0, 128, 1, 2), a("crow"), True, False)
-            for k0 in range(0, 16, 4):
-                mms([(a(D, k, 384, 16), a("ab", 2048 * ch + k, 2048 * ch + 2048, 16), a("bw"), False, k == 15) for k in range(k0, k0 + 4)])
+            mm(a(D, 0, 384), a("oneb", 0, 128, 1, 33), a("crow"), True, False)
+            rl = [j % 2 for j in RELU if j // 2 == ch]
+            if rl:
+                lo, hi = 64 * min(rl), 64 * max(rl) + 64
+                for k0 in range(0, 16, 4):
+                    mms([(a(D, k, 384, 16, hi, lo), a("df", 2048 * ch + 16 * lo + k, 2048 * ch + 16 * hi, 16), a("bw", 24, 48), False, False) for k in range(k0, k0 + 4)])
+            for lo, hi in LATE[ch]:
+                for k0 in range(0, 16, 4):
+                    mms([(a(D, k, 384, 16, hi, lo), a("ab", 2048 * ch + 16 * lo + k, 2048 * ch + 16 * hi, 16), a("bw", 0, 24), False, k == 15 and hi == 128) for k in range(k0, k0 + 4)])
         for ch, (lo, hi) in enumerate(PH):
             D = ("d0", "d1")[ch]
             R = a(D, 384, 512)
             s1, s2 = a("sg", 2 * lo, 2 * lo + 128), a("sg", 2 * lo + 128, 2 * lo + 256)
             fast = FAST[2] if last else FAST[ch]
             up(t, "f%d" % ch)
-            sign(s1 if ch else a("sg", 0, 256), a(D, 128, 256 if ch else 384), "y%d" % ch)
+            act(s1 if ch else a("sg", 0, 256), a(D, 128, 256 if ch else 384), AF.Sign)
             scan(a("cnt", lo, hi), a("rstb"), s1, OP.mult, OP.add)
             act(a("clx", lo, hi), ind(a("cnt", lo, hi), e15), AF.Sign, -1.0, a("lim", ch, ch + 1), None if last else a("par", ch, ch + 1))
             mm(fcs[ch], a("clx", lo, hi), a("idu"), False, True)
@@ -466,14 +449,14 @@ def rank_program(g, core, T, topo):
             up(t, "m%d" % ch)
             tt(a("key", lo, hi), s1, a(D, 0, 128), OP.mult)
             if ch:
-                sign(s2, a(D, 256, 384), "z1")
+                act(s2, a(D, 256, 384), AF.Sign)
             scan(a("sm", lo, hi), a("rsb"), a("key", lo, hi), OP.add, OP.max)
             tt(a("sel", lo, hi), ind(a("sm", lo, hi), e15), a("key", lo, hi), OP.is_equal)
             for x in range(fast):
                 up(t, "lj"[x] + str(ch))
                 e, c = a(EX[x], lo, hi), ((256 * ch + 128 * x, 256 * ch + 128 * x + 128) if last else (256 * x + lo, 256 * x + hi))
-                if x or ch not in CP:
-                    cp(a("gaf", *c), a(("ga", "ca")[x], lo, hi))
+                if x:
+                    lin("caf%d" % ch, a("gaf", *c), a("ca", lo, hi))
                 mm(e, mone, a("cu", 0, 128), True, False)
                 mm(e, a("gaf", *c), a("idf"), False, False)
                 mm(e, a("idx"), a("clx", lo, hi), False, False)
@@ -488,32 +471,30 @@ def rank_program(g, core, T, topo):
             mm(a("p3", lo, hi), s2, a("idh"), True, False)
             mm(a("p3", lo, hi), a("clx", lo, hi), a("idc"), False, False)
             mm(a("p3", lo, hi), a("sel", lo, hi), a("id4"), False, True)
-            if "r%d" % ch in VS:
-                ts(a("rs", lo, hi), a("p3", lo, hi), -3.5, OP.add, 0, OP.max)
-            else:
-                act(a("rs", lo, hi), a("p3", lo, hi), AF.Relu, 1.0, -3.5)
+            act(a("rs", lo, hi), a("p3", lo, hi), AF.Relu, 1.0, -3.5)
             for x in H[fast:]:
                 tt(a("pgc", 256 * x + lo, 256 * x + hi), a(("ga", "ca")[x], lo, hi), R, OP.mult)
             for x in H:
                 up(t, "lj"[x] + str(ch))
-                c, e = 256 * x + lo, a(EX[ch], *PH[x]) if last else a(EX[x], lo, hi)
+                c, e, st = 256 * x + lo, a(EX[ch], 8 * x, 8 * x + 8) if last else a(EX[x], lo, hi), 16 if last else 1
                 if x >= fast:
-                    mm(e, mtwo, a("cu", 0, 128), True, False)
-                    mm(e, a("pgc", c, c + 128), a("go"), False, False)
-                    mm(e, a("rs", lo, hi), a("gou"), False, True)
+                    mm(e, mtwo, a("cu", 0, 128, st), True, False)
+                    mm(e, a("pgc", c, c + 128), a("go", 0, 128, st), False, False)
+                    mm(e, a("rs", lo, hi), a("gou", 0, 128, st), False, True)
                 if last:
                     continue
                 if x >= fast:
                     tt(a("lh", c, c + 128), a("mske", 0, 128), e, OP.mult)
-                mm(a("pl", 16 * ch + 8 * x, 16 * ch + 8 * x + 8), a("lh", c, c + 128), a("j8"))
-                sp = ch in SPLIT
-                if sp or x:
-                    c = (16 * ch + 8 * x, 16 * ch + 8 * x + 8) if sp else (0, 16)
-                    tt(a("w", *c), a("mx", *c), a("pl", *c), OP.max)
-                    lists(t, ch, (x,) if sp else H)
-                if sp != x:
-                    c = 80 * t + 32 * ch
-                    send(a("arr", 48 * t + 24 * ch, 48 * t + 24 * ch + 24 - 8 * sp), a("gl", c, c + 24 - 8 * sp), to, "al%d" % (2 * t + ch))
+                mm(a("pl", 16 * x + 8 * ch, 16 * x + 8 * ch + 8), a("lh", c, c + 128), a("j8"))
+                if x and JOIN and not ch:
+                    continue
+                chs = H if x and JOIN else (ch,)
+                c = (16 * x + 8 * chs[0], 16 * x + 8 * ch + 8)
+                tt(a("w", *c), a("mx", *c), a("pl", *c), OP.max)
+                lists(t, *c)
+                if not x:
+                    c = 64 * t + 16 * ch
+                    send(a("arr", 32 * t + 16 * ch, 32 * t + 16 * ch + 16), a("gl", c, c + 16), to, "al%d" % (2 * t + ch))
             if last:
                 up(t, "o%d" % ch)
                 outputs(F, ch)
@@ -539,23 +520,20 @@ def rank_program(g, core, T, topo):
         tt(a("sh"), a("sv"), a("sg1"), OP.add)
         tt(a("sv"), a("w2"), a("sh"), OP.max)
         if t < RO - 2:
-            next_saved("sv", a("iu", 8, 32))
+            next_saved("sv", a("iu", 16, 32))
             continue
         for x in H:
-            tt(a("lh", 256 * x, 256 * x + 256), ind(a("sv", 8 * x, 8 * x + 24), a("el", 0, 16)), a("mske"), OP.mult)
+            tt(a("lh", 256 * x, 256 * x + 256), ind(a("sv", 16 * x, 16 * x + 16), a("el", 0, 16)), a("mske"), OP.mult)
             for ch in H:
                 c = 256 * x + 128 * ch
-                mm(a("pl", 32 + 16 * ch + 8 * x, 40 + 16 * ch + 8 * x), a("lh", c, c + 128), a("j8"))
-        act(a("svs"), a("pl", 32, 64), AF.Copy)
+                mm(a("pl", 32 + 16 * x + ch, 48 + 16 * x, 2), a("lh", c, c + 128), a("j8"))
+        lin("svs", a("svs"), a("pl", 32, 64))
         next_saved("svs", a("il"))
-        cp(a("w2"), a("svs"))
-        ts(a("fi"), a("w2"), L - 1, OP.bitwise_and)
-        ts(a("fq"), a("w2"), 1023, OP.bitwise_and)
-        tt(a("sv"), a("fi"), a("fq"), OP.add)
-        for c in (8, 24):
-            ts(a("sv", c, c + 8), a("s3", c, c + 8), 2, OP.mult, 32 + O, OP.add)
-    for j, y in enumerate((T.yg, T.yc, T.ysg, T.yk)):
-        dma("sy"[j % 2], ("!", y[:]), a("fot", 0, 256, 1, 8 * j + 8, 8 * j))
+        ts(a("fq"), a("svs"), 13, OP.arith_shift_right, 1023, OP.bitwise_and)
+        lin("fi", a("fi", 0, 16), a("s3", 0, 16), 512, -16)
+        tt(a("svy", 32, 48), a("fi", 0, 16), a("fq", 0, 16), OP.add)
+        lin("svy", a("svy", 48, 64), a("s3", 16, 32))
+        lin("svy", a("sg1", 16, 32), a("s2", 16, 32))
 
     lg, n = {}, len(prog)
     dep = [[] for _ in range(n)]
@@ -575,44 +553,44 @@ def rank_program(g, core, T, topo):
         for d, w in before[i]:
             after[d].append((i, w))
 
-    def schedule(prio):
-        free = {q: 0.0 for q in list(Q) + ["net"]}
-        left, done = [len(d) for d in before], [0.0] * n
-        ready = {q: [(0.0, i) for i in range(n) if not left[i] and qs[i] == q] for q in free}
-        for _ in range(n):
-            best = None
-            for q in free:
-                if ready[q]:
-                    t0 = max(free[q], min(ready[q])[0]) if q != "net" else min(ready[q])[0]
-                    c = max((prio[i], -i, e) for e, i in ready[q] if e <= t0 + SLACK)
-                    if best is None or max(t0, c[2]) < best[0]:
-                        best = (max(t0, c[2]), -c[1], q)
-            t0, i, q = best
-            ready[q] = [x for x in ready[q] if x[1] != i]
-            done[i] = free[q] = t0 + dur[i]
-            for j, w in after[i]:
-                left[j] -= 1
-                if not left[j]:
-                    ready[qs[j]].append((max(done[d] + w2 for d, w2 in before[j]), j))
+    def pack(order, needs, head):
+        done, busy = [0.0] * n, {q: [] for q in Q}
+        for i in order:
+            t0 = max([head[i]] + [done[d] + w for d, w in needs[i]])
+            if qs[i] != "net":
+                b = busy[qs[i]]
+                lo, hi = 0, len(b)
+                while lo < hi:
+                    m = (lo + hi) // 2
+                    lo, hi = (m + 1, hi) if b[m][1] <= t0 else (lo, m)
+                while lo < len(b) and b[lo][0] < t0 + dur[i] - 1e-9:
+                    t0 = max(t0, b[lo][1])
+                    lo += 1
+                b.insert(lo, (t0, t0 + dur[i]))
+            done[i] = t0 + dur[i]
         return done
 
-    def improve(order, seed, part):
+    def improve(order, seed, heat, steps):
         prev, last = [-1] * n, {}
         for i in order:
             if qs[i] != "net":
                 prev[i], last[qs[i]] = last.get(qs[i], -1), i
         done, rest, pos = [0.0] * n, [0.0] * n, [0] * n
-        best, arcs, lo, hi = (1e9, order), None, 0, n
-        for turn in range(STEPS + 1):
+        best, arcs, nxt = (1e9, order), None, {prev[i]: i for i in range(n) if prev[i] >= 0}
+        for turn in range(steps + 1):
+            whole = turn % STAY == 0 or turn == steps
+            if whole:
+                seed = (seed * 1103515245 + 12345) % 2147483648
+                first = min(max((seed >> 8) % (n + WIDE // 2) - WIDE * 3 // 4, 0), n - WIDE)
+                arcs, lo, hi = None, 0, n
             if arcs is None:
-                nxt = {prev[i]: i for i in range(n) if prev[i] >= 0}
-                for i in order[lo:]:
+                for i in order[lo:n if whole else first + WIDE]:
                     t0 = done[prev[i]] if prev[i] >= 0 else 0.0
                     for d, w in before[i]:
                         if done[d] + w > t0:
                             t0 = done[d] + w
                     done[i] = t0 + dur[i]
-                for k in range(hi - 1, -1, -1):
+                for k in range(hi - 1, -1 if whole else first - 1, -1):
                     i = order[k]
                     t0 = max(lat[i], rest[nxt[i]] if i in nxt else 0.0)
                     for d, w in after[i]:
@@ -621,16 +599,19 @@ def rank_program(g, core, T, topo):
                     rest[i] = t0 + dur[i]
                 for k in range(lo, hi):
                     pos[order[k]] = k
-                span = max(rest)
-                arcs = [j for j in order[pos[part[0]]:pos[part[1]]] if prev[j] >= 0 and done[prev[j]] + rest[j] > span - NEAR]
-                if span < best[0]:
-                    best = (span, list(order), list(done))
+                part = order[first:first + WIDE]
+                span = max(done[i] - dur[i] + rest[i] for i in part)
+                arcs = [j for j in part if prev[j] >= 0 and pos[prev[j]] >= first and done[prev[j]] + rest[j] > span - NEAR]
+                if whole and max(rest) < best[0]:
+                    best = (max(rest), list(order), list(done))
+            if not arcs:
+                continue
             seed = (seed * 1103515245 + 12345) % 2147483648
             j = arcs[(seed >> 8) % len(arcs)]
             i, q, far = prev[j], qs[j], (seed >> 20) % (8 if seed >> 28 else FAR)
             if far % 2:
                 for _ in range(far // 2):
-                    i = prev[i] if prev[i] >= 0 else i
+                    i = prev[i] if prev[i] >= 0 and pos[prev[i]] >= first else i
                 seg, move = order[pos[i]:pos[j] + 1], {j}
                 for k in reversed(seg):
                     if k in move:
@@ -642,7 +623,7 @@ def rank_program(g, core, T, topo):
                 seg = [k for k in seg if k in move] + [k for k in seg if k not in move]
             else:
                 for _ in range(far // 2):
-                    j = nxt.get(j, j)
+                    j = nxt[j] if j in nxt and pos[nxt[j]] < first + WIDE else j
                 seg, move = order[pos[i]:pos[j] + 1], {i}
                 for k in seg:
                     if k in move:
@@ -682,37 +663,180 @@ def rank_program(g, core, T, topo):
                     s2 = e
                 more += math.exp(min(e, 5.0) / SOFT) - math.exp((done[k] - dur[k] + rest[k] - span) / SOFT)
             seed = (seed * 1103515245 + 12345) % 2147483648
-            e = (1 - turn / STEPS) * (seed >> 8 & 1023) ** 2 / 1048576
-            if s2 <= HEAT * e + 1e-9 and more <= WARM * e:
+            e = (1 - turn / steps) * (seed >> 8 & 1023) ** 2 / 1048576
+            if s2 <= heat * e + 1e-9 and more <= 12 * heat * e:
                 lo, hi, arcs = pos[i], b + 1, None
                 order[lo:hi] = seg
                 for k in p2:
+                    nxt.pop(k, 0) if k in d2 else 0
+                for k in p2:
                     prev[k] = p2[k]
+                    nxt[p2[k]] = k
+                nxt.pop(-1, 0)
         return best
+
+    def circle(end, cut, seed, heat):
+        ids = {prog[i]["id"]: i for i in range(n) if prog[i]["id"]}
+        names = [k[1:] for k in ids if k[0] == 2]
+        m, num = len(names), {k: j for j, k in enumerate(names)}
+        span = end[(2,) + names[0]] - end[(1,) + names[0]]
+        back = [math.ceil((end[(2,) + k] - cut) / span - 1e-9) for k in names]
+        needs = [(num[prog[d]["id"][1:]], j, 2 - prog[d]["id"][0], w) for j, k in enumerate(names) for d, w in before[ids[(2,) + k]] if prog[d]["id"] and prog[d]["id"][1:] in num]
+        for _ in range(3):
+            for i, j, s, w in needs:
+                back[j] = max(back[j], back[i] - s)
+        now, old = [[] for _ in names], [[] for _ in names]
+        for i, j, s, w in needs:
+            if s + back[j] - back[i] < 2:
+                (old if s + back[j] - back[i] else now)[j].append((i, w))
+        later = [[] for _ in names]
+        for j in range(m):
+            for i, w in now[j]:
+                later[i].append((j, w))
+        du, qu = [dur[ids[(2,) + k]] for k in names], [qs[ids[(2,) + k]] for k in names]
+        done = [end[(2,) + names[j]] - back[j] * span for j in range(m)]
+        for _ in range(m):
+            for j in range(m):
+                done[j] = max([done[j]] + [done[i] + du[j] + 1e-6 for i, w in now[j]])
+        order = sorted(range(m), key=lambda j: (done[j] - du[j], j))
+
+        newer = [[] for _ in names]
+        for j in range(m):
+            for i, w in old[j]:
+                newer[i].append((j, w))
+        rest, pos, prev, nxt = [0.0] * m, [0] * m, [-1] * m, [-1] * m
+        best, arcs = (1e9, order, done), None
+        for turn in range(ROUND + 1):
+            if arcs is None:
+                last = {}
+                for k, j in enumerate(order + order):
+                    if qu[j] not in ("net", "y"):
+                        prev[j], last[qu[j]] = last.get(qu[j], -1), j
+                        nxt[prev[j]] = j
+                    pos[j] = k - m
+                for _ in range(2 if turn else 8):
+                    was = sum(done)
+                    for j in order:
+                        e = prev[j]
+                        t0 = -1e9 if e < 0 else done[e] if pos[e] < pos[j] else done[e] - span
+                        for d, w in now[j]:
+                            if done[d] + w > t0:
+                                t0 = done[d] + w
+                        for d, w in old[j]:
+                            if done[d] + w - span > t0:
+                                t0 = done[d] + w - span
+                        done[j] = t0 + du[j]
+                    span += (sum(done) - was) / m
+                    for j in reversed(order):
+                        e = nxt[j] if prev[j] >= 0 else -1
+                        t0 = -99.0 if e < 0 else rest[e] if pos[e] > pos[j] else rest[e] - span
+                        for d, w in later[j]:
+                            if rest[d] + w > t0:
+                                t0 = rest[d] + w
+                        for d, w in newer[j]:
+                            if rest[d] + w - span > t0:
+                                t0 = rest[d] + w - span
+                        rest[j] = t0 + du[j]
+                top = max(done[j] - du[j] + rest[j] for j in range(m))
+                arcs = [j for j in order if prev[j] >= 0 and pos[prev[j]] < pos[j] and done[prev[j]] + rest[j] > top - NEAR]
+                if span < best[0] and abs(sum(done) - was) < 0.005 * m and turn >= ROUND * LEAVE:
+                    best = (span, list(order), list(done))
+            seed = (seed * 1103515245 + 12345) % 2147483648
+            j = arcs[(seed >> 8) % len(arcs)]
+            i, q, far = prev[j], qu[j], (seed >> 20) % (8 if seed >> 28 else FAR)
+            if far % 2:
+                for _ in range(far // 2):
+                    i = prev[i] if pos[prev[i]] < pos[i] else i
+                seg, move = order[pos[i]:pos[j] + 1], {j}
+                for k in reversed(seg):
+                    if k in move:
+                        move.update(d for d, w in now[k])
+                        if qu[k] != q:
+                            move.add(prev[k])
+                if i in move:
+                    continue
+                seg = [k for k in seg if k in move] + [k for k in seg if k not in move]
+            else:
+                for _ in range(far // 2):
+                    j = nxt[j] if pos[nxt[j]] > pos[j] else j
+                seg, move = order[pos[i]:pos[j] + 1], {i}
+                for k in seg:
+                    if k in move:
+                        move.update(d for d, w in later[k])
+                        if qu[k] != q and prev[k] >= 0:
+                            move.add(nxt[k])
+                if j in move:
+                    continue
+                seg = [k for k in seg if k not in move] + [k for k in seg if k in move]
+            d2, r2 = {}, {}
+            c = done[prev[i]] - span * (pos[prev[i]] > pos[i])
+            for k in seg:
+                e = prev[k]
+                t0 = c if qu[k] == q else -1e9 if e < 0 else d2.get(e, done[e]) if pos[e] < pos[k] else done[e] - span
+                for d, w in now[k]:
+                    e = d2.get(d, done[d]) + w
+                    if e > t0:
+                        t0 = e
+                for d, w in old[k]:
+                    if done[d] + w - span > t0:
+                        t0 = done[d] + w - span
+                d2[k] = t0 + du[k]
+                if qu[k] == q:
+                    c = d2[k]
+            c, s2, more = rest[nxt[j]] - span * (pos[nxt[j]] < pos[j]), 0.0, 0.0
+            for k in reversed(seg):
+                e = nxt[k] if prev[k] >= 0 else -1
+                t0 = c if qu[k] == q else -99.0 if e < 0 else r2.get(e, rest[e]) if pos[e] > pos[k] else rest[e] - span
+                for d, w in later[k]:
+                    e = r2.get(d, rest[d]) + w
+                    if e > t0:
+                        t0 = e
+                for d, w in newer[k]:
+                    if rest[d] + w - span > t0:
+                        t0 = rest[d] + w - span
+                r2[k] = t0 + du[k]
+                if qu[k] == q:
+                    c = r2[k]
+                e = d2[k] + t0 - top
+                if e > s2:
+                    s2 = e
+                more += math.exp(min(e, 5.0) / SOFT) - math.exp((done[k] - du[k] + rest[k] - top) / SOFT)
+            seed = (seed * 1103515245 + 12345) % 2147483648
+            e = (seed >> 8 & 1023) ** 2 / 1048576
+            if s2 <= heat * e + 1e-9 and more <= 12 * heat * e:
+                order[pos[i]:pos[j] + 1] = seg
+                arcs = None
+        span, order, was = best if best[0] < 1e9 else (span, order, done)
+        top = max(was)
+        return span, {(2,) + names[j]: was[j] - top + cut + back[j] * span for j in range(m)}
 
     if not PLAN:
         prio = [0.0] * n
         for i in range(n - 1, -1, -1):
             prio[i] = dur[i] + max([w + prio[j] for j, w in after[i]] + [lat[i]])
-        due = schedule(prio)
+        due = pack(sorted(range(n), key=lambda i: (-prio[i], i)), before, [0.0] * n)
         for i, p in enumerate(prog):
             if p["id"]:
                 due[i] = max([p["due"]] + [due[d] + w for d, w in before[i]]) + dur[i]
-        best, mark = None, [i for i, p in enumerate(prog) if p["id"] and p["id"][1:] == ("w4", 0)]
-        for turn in range(TURNS):
-            now = improve(sorted(range(n), key=lambda i: (due[i] - dur[i], i)), turn + SEED, (mark[1], mark[2]) if turn % ALL else (0, n - 1))
+        best = kept = None
+        for seed in SEEDS:
+            now = improve(sorted(range(n), key=lambda i: (due[i] - dur[i], i)), seed, HEAT[0], STEPS[0])
             best = now if not best or now[0] < best[0] else best
             end = {p["id"]: now[2][i] for i, p in enumerate(prog) if p["id"]}
-            span, t = min((end[(t, "w4", 0)] - end[(t - 1, "w4", 0)], t) for t in (1, 2, 3))
-            if turn % ALL == ALL - 1 or ALL == 1:
-                SPANS.append(round(span, 1))
-            for i, p in enumerate(prog):
-                due[i] = now[2][i]
-                if p["id"]:
-                    r, name, k = p["id"]
-                    s = t if end.get((t, name, k), 1e9) <= end[(t, "w4", 0)] else t - 1
-                    e = end[(s, name, k)] + (r - s + t) * span + end[(0, "w4", 0)] - end[(t, "w4", 0)] if (s, name, k) in end else 0.0
-                    due[i] = max([e - dur[i]] + [due[d] + w for d, w in before[i]]) + dur[i]
+            for k in range(CUTS):
+                span, mid = circle(end, end[(2, "w4", 0)] - k * 11 % 18, seed + k, WARM * COOL ** (k / CUTS))
+                end = {(r,) + k[1:]: mid[k] + (r - 2) * span for k in mid for r in range(RO)}
+                kept = (span, end, now[2]) if not kept or span < kept[0] else kept
+            SPANS.append((seed, round(now[0], 1), round(span, 2)))
+        span, end, due = kept
+        start = max(due[i] for i, p in enumerate(prog) if p["id"] == (0, "w4", 0))
+        for i, p in enumerate(prog):
+            if p["id"]:
+                e = end[p["id"]] + start - end[(0, "w4", 0)] if p["id"] in end else 0.0
+                due[i] = max([e - dur[i]] + [due[d] + w for d, w in before[i]]) + dur[i]
+        now = improve(sorted(range(n), key=lambda i: (due[i] - dur[i], i)), SEEDS[0], HEAT[1], STEPS[1])
+        best = now if now[0] < best[0] else best
+        SPANS.append(round(now[0], 1))
         PLAN.extend(best[:2])
         PLAN.extend((prog, before, dur, lat))
 

@@ -1,5 +1,5 @@
 import math
-from concourse.mybir import AluOpType, ActivationFunctionType
+from concourse.mybir import AluOpType, ActivationFunctionType, AxisListType
 
 OP = AluOpType
 AF = ActivationFunctionType
@@ -18,42 +18,53 @@ def _bufs(where, dtype, text):
         SCRATCH[n] = (where, [int(r), int(c)], dtype)
 
 
-_bufs("sbuf", F32, "skt:4688 tabb:784 bg:256 j8:8 mske:256 rst:128 rsb:128 idf:128 go:128 onef:128 e8:8x128 m16:16x128 inf:16x384 id8:16x16 gaf:512 sum:512 "
-      "iw:16 iu:32 il:16 lim:8 hb:256 tg:256 tc:256 fu:256 key:256 sm:256 pgc:512 lh:512 we:16 wf:16 svy:64 sg1:32 sh:32 mx:32 par:8 "
-      "fim:64 fot:64x128 oz:256 f0:784 f1:784 f2:784 f3:784 f4:784 r0:528 r1:528 r2:528 r3:528")
-_bufs("sbuf", BF, "idk:128 idm:128 idn:128 xr:4096 ub:4096 df:4096 ab:4096 bw:48 idb:128 id4:128 idh:128 gou:128 gon:128 oneb:128 crow:33x384 cu:1x256 cn:1x128 idl:128 row:1x384 "
-      "idu:128 idc:128 ids:128 idx:128 rstb:128 sg:512 cnt:256 sel:256 rs:256 clx:256 sa:256 sb:256")
+_bufs("sbuf", F32, "skt:4688 tabb:784 bg:256 j8:8 rst:256 rsb:128 onef:128 e8:8x128 m16:16x128 inf:16x384 id8:16x16 k8:16x128 e16:16x256 gaf:512 sum:512 "
+      "iw:16 iu:32 il:16 lim:24 hb:256 tg:256 tc:256 fu:256 key:256 sm:256 pgc:512 lh:512 we:16 wf:16 svy:64 sg1:32 sh:32 mx:32 id2:128 "
+      "fim:64 fot:64x128 oz:256 ft:5968")
+_bufs("sbuf", BF, "idk:128 idm:128 idn:128 xr:4096 ub:4096 df:4096 ab:4096 bw:48 idb:128 id4:128 idh:128 gou:128 gon:128 oneb:128 crow:33x384 cu:1x256 idw:128 idl:128 row:1x512 "
+      "idu:128 idc:128 ids:128 idx:128 rstb:128 sg:512 cnt:256 sel:256 rs:256 clx:256 sa:512 mko:128")
 _bufs("sbuf", I32, "ski:4096 ini:16x384 fri:256 thi:33x128 thj:33x128 pi:16 ci:72 pm:16 rawg:256 rawc:256 ga:256 ca:256 sv:32 svs:32 "
       "pg:256 qg:256 prg:256 rg:256 pc:256 qc:256 prc:256 rc:256 w:32 w2:32 wq:64 s2:32 s3:32 t4:16 t5:16 t6:16 t7:16 t8:16 fi:32 fq:32 oi:256")
 _bufs("sbuf", U16, "ug:256 uc:256 el:24 ek:32 gl:320 arr:128")
 _bufs("psum", F32, "d0:512 d1:512 p3:512 ea:512 eb:512 pl:512 fa:512 fb:512")
-SEMAPHORES = ["sv", "ss", "st", "sg", "rl"] + [n + str(t) for n in ("al", "ao", "ag") for t in range(8)] + ["d%d" % t for t in range(40)]
-VIEW = {"sks": ("df", 0, 4096), "frs": ("oi", 0, 256), "frm": ("oz", 0, 256), "o2": ("pg", 0, 256), "oq": ("qg", 0, 256), "o3": ("tg", 0, 256), "fb0": ("key", 0, 256)}
+SEMAPHORES = ["sv", "ss", "st", "sg", "rl"] + [n + str(t) for n in ("al", "ao", "ag", "ap") for t in range(8)] + ["d%d" % t for t in range(40)]
+VIEW = {"sks": ("df", 0, 4096), "frs": ("oi", 0, 256), "frm": ("oz", 0, 256), "o2": ("pg", 0, 256), "oq": ("qg", 0, 256), "o3": ("tg", 0, 256), "fb0": ("key", 0, 256),
+        "svx": ("pgc", 0, 128), "svz": ("pgc", 128, 128), "idf": ("skt", 0, 128), "go": ("skt", 128, 128), "mske": ("skt", 256, 256), "wl": ("lim", 8, 8), "par": ("lim", 16, 8), "sb": ("sa", 256, 256)}
+for _t in range(RO):
+    VIEW["f%d" % _t], VIEW["r%d" % _t] = ("ft", 1280 * _t, 784), ("ft", 1280 * _t + 768, 528)
 PSUM = [n for n in SCRATCH if SCRATCH[n][0] == "psum"]
 OWN, GH, F3 = (16, 272), (272, 528), (528, 784)
 GCH = [(c, c + 512) for c in range(0, 4096, 512)]
-VCH = [(c, c + 512) for c in range(0, 4096, 512)]
-ACH = [(c, c + 512) for c in range(0, 4096, 512)]
-RELU = (1,)
+WAY = "aarraaaA"
+SPLIT, MK, BARE, SB, TC0, TG0 = (), 4, (0, 0), 1, (2, 2), (2, 2)
+DEF, BANKS, GB0 = 3, ("d0", "d1", "fa"), ("ea", "ea")
+WAYS, PAR, S2, ONE, FU2 = {0: "rrraaaaA"}, 1, 1, 0, 1
+GE, LB = ("ea", "pl"), ("ea", "ea", "ea", "ea")
+SWB = ("pl", "p3")
+TG = (0, 0)
 PH = [(0, 128), (128, 256)]
-SKP = [(c, c + 512) for c in range(0, 3584, 512)] + [(3584, 3904), (3904, 4096)]
-SKL = [(0, 1024), (1024, 2048), (2048, 3072), (3072, 3584), (3584, 3904), (3904, 4096)]
-INI, FRI = 0, 3
-FAST, JOIN, LATE = (1, 1, 2), 0, (((0, 128),), ((0, 128),))
-SW = {}
-ONS = ("gaf0", "ug0", "s3", "t7", "gaf1", "ug1", "mx", "caf1", "caf0", "uc0", "uc1", "inf", "sh", "crow", "idu", "ids", "idx", "idl", "id4", "t4", "sg1")
+SKP = [(c, c + 512) for c in range(0, 4096, 512)]
+SKL = [(0, 512), (512, 1536), (1536, 2560), (2560, 3584), (3584, 4096)]
+THI = 3
+INI, FRI = 0, 0
+FAST, JOIN, LATE = (1, 1, 2), 0, (((0, 128),), ((0, 64), (64, 96), (96, 128)))
+ONS = ("gaf0", "s3", "t7", "gaf1", "ug1", "mx", "caf1", "caf0", "uc0", "uc1", "inf", "idu", "ids", "idx", "idl", "id4", "sg2", "wf0", "wf1", "gl10", "gl11",
+       "go", "mske", "fu", "idw", "idh", "idc", "sb0", "bg", "bw")
 CYC, CG, FIX, GFIX, SFIX, PEC, PFIX = 0.00095, 1.42, 0.005, 0.05, 0.05, 0.00056, 0.015
 WAKE = {"v": 0.16, "vv": 0.22, "s": 0.24, "t": 0.3, "tt": 0.0, "g": 0.1, "y": 0.2, "net": 0.2, "vg": 0.3}
-RI, RL, RB = 0.25, 1.3, 0.4
-T0, PERIOD, SLACK = 8.0, 17.6, 0.1
+RI, RL, RB = 0.45, 1.1, 0.4
+T0, PERIOD, START, FILL = 8.0, 17.6, 11.5, -2.0
+EARLY, GAP = 5, 12.0
 DUE = {"g0": 5.0, "col0": 5.0, "col1": 5, "u0": 7.3, "u1": 8.7, "c0": 6.0, "g1": 7.0, "x0": 6.0, "x1": 8.5, "w0": 9.9, "w1": 11.3, "c1": 12.7, "u2": 10.2, "a0": 11.6,
        "w2": 14.0, "a1": 12.8, "u3": 13.7, "d0": 10, "w3": 15, "a2": 15.5, "f0": 16, "m0": 16, "w4": 15.7, "a3": 16, "a4": 16.7, "d1": 10, "f1": 18, "m1": 18,
-       "l0": 17, "l1": 18, "j0": 18, "j1": 21, "k0": 20.5, "k1": 21, "fu": 22, "sv": 22, "o0": 17, "o1": 18}
+       "l0": 17, "l1": 18, "j0": 18, "j1": 21, "k0": 20.5, "k1": 21, "fu": 22, "sv": 22, "o0": 17, "o1": 18, "z1": 16, "p1": 18, "sk": 18}
 PLAN = []
-STEPS, HEAT, FAR, SPANS = (100000, 300000), (0.5, 0.12), 40, []
-SOFT, WARM, NEAR, SEEDS = 0.3, 0.25, 0.05, (2,)
-WIDE, STAY = 260, 1000
-ROUND, CUTS, COOL, LEAVE = 5000, 8, 0.3, 0
+SPANS, SEED, REST = [], 4, 10
+KICK, LOOSE, SHAKE, STRETCH, CALM = 10, 0.08, 1.2, 6.0, 10
+SOFT, WEIGH, NEAR, FAR, SOME, STRAY = 0.4, 0.025, 0.03, 20, 4, 0.35
+ROUND, CUTS, STAY, STEPS, PART = 300, 90, 1500, 72, 24
+TURNS = ((6, (0, 0, 170), (0.08, 0.16, 180), (0.03, 0.1, 180), (0.15, 0.25, 180)), (1, (1, 1, 130), (0.86, 0.95, 150), (1, 1, 100), (0.75, 0.85, 180), (0.9, 1, 120)),
+         (1, (0.2, 0.8, 200), (0, 0.2, 200), (0.8, 1, 150)))
 
 
 def rank_program(g, core, T, topo):
@@ -147,12 +158,12 @@ def rank_program(g, core, T, topo):
     def scan(o, d0, d1, op0, op1):
         add("v", lambda: g.vector.tensor_tensor_scan(ap(o), ap(d0), ap(d1), 0.0, op0, op1), [d0, d1], [o], vcost(o, [d0, d1]))
 
+    def prod(o, x):
+        add("v", lambda: g.vector.tensor_reduce(ap(o), ap(x), AxisListType.X, OP.mult), [x], [o], FIX + CYC * 64)
+
     def act(o, x, func, scale=1.0, bias=0.0, acc=None):
-        def call():
-            if acc:
-                return g.scalar.activation(ap(o), ap(x), func, ap(bias), scale, accum_out=ap(acc))
-            return g.scalar.activation(ap(o), ap(x), func, ap(bias), scale)
-        add("s", call, [x, bias], [o, acc], 0.065 + CYC * CG * size(x) if x[0] == "@" else SFIX + CYC * max(64, size(x)))
+        add("s", lambda: g.scalar.activation(ap(o), ap(x), func, ap(bias), scale, accum_out=ap(acc)), [x, bias], [o, acc],
+            0.065 + CYC * CG * size(x) if x[0] == "@" else SFIX + CYC * max(64, size(x)))
 
     def lin(name, o, x, scale=1.0, bias=0.0):
         if name in ONS:
@@ -188,14 +199,14 @@ def rank_program(g, core, T, topo):
         def call():
             rid, pid, _ = topo.addr(to)
             g.remote_dma(ap(dst), ap(src), T.sem[rsem], T.sem["rl"], pid, rid, topo.mask(core, to))
-        add("g", call, [src], [], RI + (2.0 if rsem == "ag0" else 0.0), 0.0, "r", (rsem, len(topo.engines(core, to))))
-        add("net", None, [], [dst], 0.0, RL + RB * size(dst) / 256, "n", (rsem, len(topo.engines(core, to)), len(prog) - 1))
+        add("g", call, [src], [], RI + RB * size(dst) / 256 + (2.0 if rsem == "ag0" else 0.0), 0.0, "r", (rsem, len(topo.engines(core, to))))
+        add("net", None, [], [dst], 0.0, RL, "n", (rsem, len(topo.engines(core, to)), len(prog) - 1))
 
     LD = [(a("ski", lo, hi), T.sk[:, lo:hi], 0.2 + 0.5 * (hi - lo) / 512) for lo, hi in SKL]
     LD[FRI:FRI] = [(a("fri"), T.fr[:], 0.45)]
     LD[INI:INI] = [(a("ini", 128 * j, 128 * j + 128), y[:], 0.06) for j, y in enumerate((T.gs, T.gf, T.gcl))]
     LD += [(a("xr", 592, 4096), T.x[:, 0:3504], 1.9), (a("xr", 0, 592), T.x[:, 3504:4096], 0.5)]
-    LD += [(a("thi", 0, 128, 1, r + 1, r), T.th[:], 0.06) for r in (0, 32)]
+    LD[THI:THI] = [(a("thi", 0, 128, 1, r + 1, r), T.th[:], 0.06) for r in (0, 32)]
     came = 0.0
     for j, (o, src, us) in enumerate(LD):
         came += us
@@ -204,6 +215,9 @@ def rank_program(g, core, T, topo):
     pick(a("idf"), a("onef"), [[-1, 128]], OP.is_equal, 0, 1)
     pick(a("m16"), a("onef", 0, 128, 1, 16), [[0, 8], [1, 16]], OP.is_equal, 0, -1)
     pick(a("e8"), a("onef", 0, 128, 1, 8), [[1, 8], [0, 16]], OP.is_equal, 0, -1)
+    iota(a("k8"), [[0, 128]], 8192, 0)
+    for ch in H:
+        pick(a("e16", *PH[ch]), a("k8"), [[2, 8], [0, 16]], OP.is_equal, ch, -1)
     iota(a("pi"), [[0, 16]], 0, 1)
     iota(a("ci", 0, 16), [[1, 16]], 0, 0)
     iota(a("ci", 16, 24), [[16, 8]], 15, 0)
@@ -212,36 +226,36 @@ def rank_program(g, core, T, topo):
     iota(a("tabb", 0, 528), [[1, 528]], 0, 0)
     iota(a("tabb", *F3), [[1, 256]], 1024 + 16, 0)
     iota(a("t8"), [[0, 8], [128, 2]], 16, 1)
-    for n, lo, hi, st, c in (("skt", 0, 592, 1, 0), ("lim", 0, 8, 1, 1), ("row", 0, 128, 1, -2), ("row", 128, 256, 1, -1), ("row", 256, 384, 1, 5), ("cu", 0, 256, 1, L),
-                             ("cn", 0, 128, 1, -L), ("oneb", 0, 128, 1, 1), ("rst", 0, 128, 1, 1), ("rst", 0, 128, 16, 0), ("rstb", 0, 128, 1, 1),
+    for n, lo, hi, st, c in (("skt", 512, 592, 1, 0), ("lim", 0, 8, 1, 1), ("row", 0, 128, 1, -2), ("row", 128, 256, 1, -1), ("row", 256, 384, 1, 5), ("cu", 0, 256, 1, L),
+                             ("oneb", 0, 128, 1, 1), ("rst", 0, 256, 1, 0), ("rst", 0, 256, 16, -8 * L), ("rstb", 0, 128, 1, 1),
                              ("rstb", 0, 128, 16, 0), ("rsb", 0, 128, 1, 0), ("rsb", 0, 128, 16, -U), ("iu", 0, 16, 1, O - L), ("svy", 0, 32, 1, 0)):
         fill(a(n, lo, hi, st), float(c))
-    for t in range(RO):
-        fill(a("f%d" % t, 0, 16), 0.0)
-        if t < RO - 1:
-            fill(a("r%d" % t, 0, 16), 0.0)
+    fill(a("f0", 0, 16), 0.0)
     mm(a("ea", 0, 128), a("e8"), a("e8"))
     mm(a("ea", 128, 136), a("e8"), a("idf", 0, 8, 1, 8))
     mm(a("eb", 0, 128), a("m16"), a("m16"))
     for n, w in (("go", 1.0), ("gou", float(L)), ("gon", -2.0 * L)):
-        act(a(n), a("ea", 0, 128), AF.Copy, w)
-    act(a("j8"), a("ea", 128, 136), AF.Copy)
+        lin(n, a(n), a("ea", 0, 128), w)
+    lin("j8", a("j8"), a("ea", 128, 136))
     for ch in H:
-        act(a("mske", *PH[ch]), a("eb", 0, 128), AF.Copy)
-    for n, w in (("idb", 1.0), ("idn", -1.0), ("idk", 1.5 * L), ("idm", -2048.0), ("id4", 4.0), ("idh", 0.5), ("idc", -2.0), ("idu", float(L)), ("ids", 0.5 * L), ("idl", -float(L)), ("idx", -1.5 * L)):
+        lin("mske", a("mske", *PH[ch]), a("eb", 0, 128))
+    for n, w in (("idb", 1.0), ("idn", -1.0), ("idk", 1.5 * L), ("idm", -2048.0), ("id4", -4.0), ("idw", -2.0 * L), ("idh", 0.5), ("idc", -2.0), ("idu", float(L)), ("ids", 0.5 * L), ("idx", -1.5 * L)) + ((("idl", -float(L)),) if BARE[1] else ()) + (() if SB else (("id2", -2.0),)):
         lin(n, a(n), a("idf"), w)
-    for j, w in enumerate((16.0, -2.0, -4.0) + ((-16.0, 2.0, 4.0) if RELU else ())):
+    for j, w in enumerate((16.0, -2.0, -4.0) + ((-16.0, 2.0, 4.0) if "r" in WAY.lower() else ())):
         lin("bw", a("bw", 8 * j, 8 * j + 8), a("j8"), w)
+    if BARE[1]:
+        lin("mko", a("mko"), a("mske", 0, 128), 2.0 * L, -3.0 * L)
     ts(a("pm"), a("pi"), 15, OP.bitwise_and)
     cp(a("el"), a("ci", 0, 24))
     cp(a("ek"), a("ci", 40, 72))
     tt(a("iw"), a("ci", 24, 40), a("pm"), OP.add)
     lin("iu", a("iu", 16, 32), a("iw"), 8192, 592 - L)
     lin("il", a("il"), a("t8"), 8192, 592 - L)
-    act(a("bg"), a("tabb", *GH), AF.Identity, 8192.0, float(C0))
+    iota(a("bg"), [[8192, 256]], 8192 * GH[0] + C0, 0)
     EX, e15 = ("ea", "eb"), a("el", 16, 24)
     fcs, fus, XP = (a("fa", 0, 128), a("fb", 256, 384)), a("fa", 256, 512), (a("fb", 0, 128), a("eb", 256, 384))
-    mtwo, mone, five = a("row", 0, 128), a("row", 128, 256), a("row", 256, 384)
+    mtwo, mone, five, four = a("row", 0, 128), a("row", 128, 256), a("row", 256, 384), a("row", 384, 512)
+    Y0 = (a("p3", 256, 384), a("pl", 256, 384))
 
     def GF(last, ch):
         return (256 * ch, 256 * ch + 128) if last else PH[ch]
@@ -250,11 +264,18 @@ def rank_program(g, core, T, topo):
         n, c, w, l8 = hi - lo, 2 * lo, a("w", lo, hi), (max(lo - 16, 0), hi - 16)
         ts(a("wq", c, c + n), w, 13, OP.arith_shift_right, 1023, OP.bitwise_and)
         ts(a("wq", c + n, c + 2 * n), w, 8191, OP.bitwise_and)
-        if hi > 16:
+        if hi > 16 and t < 4:
             h = a("wq", c + n - l8[1] + l8[0], c + n)
             tt(a("we", *l8), h, a("iw", *l8), OP.is_equal)
             lin("wf%d" % (lo // 8 % 2), a("wf", *l8), a("we", *l8), 512)
             tt(h, a("wf", *l8), h, OP.add)
+        if t == 4:
+            cp(a("gl", 256, 272), a("wq", 0, 16))
+            ts(a("gl", 288, 320), a("wq", 32, 64), -592, OP.add)
+            return
+        if ONE and not lo:
+            lin("gl00", a("f%d" % t, 0, 16), a("wq", 0, 16))
+            return
         lin("gl%d%d" % (lo // 16, lo // 8 % 2), a("gl", 64 * t + c, 64 * t + c + 2 * n), a("wq", c, c + 2 * n))
 
     def gl(t, x, k, ch):
@@ -264,19 +285,36 @@ def rank_program(g, core, T, topo):
     def hl(t, ch):
         return gl(t, 1, 0, ch)
 
+    def rows(e, v, s, offs, way, more=0):
+        act(v, ind(a("skt" if way == 1 else "ski"), offs), AF.Identity, 1.0, float(more))
+        mm(e, a("idf"), v, False, way == 1)
+        if way > 1:
+            act(s, v, AF.Sign, 1.0, -4095.5 - more)
+            mms([(e, a("idk"), s, False, False), (e, a("idm"), s, False, True)])
+
     def clause_part(t, F, ch):
         lo, hi = PH[ch]
         y, cl = a("p3", 256 + lo, 256 + hi), gl(t, 1, 1, ch)
-        act(a("sb", lo, hi), a(F, 16 + lo, 16 + hi), AF.Sign, 1.0, -1.5 * L)
-        act(a("hb", lo, hi), ind(a("tabb"), hl(t, ch)), AF.Identity, 8192.0, float(C0))
-        if "tc%d" % ch in ONS and t < 4:
+        if t == 4:
+            iota(a("hb", lo, hi), [[8192, 128]], 8192 * (1040 + lo) + C0, 0)
+        else:
+            act(a("hb", lo, hi), ind(a("tabb"), hl(t, ch)), AF.Identity, 8192.0, float(C0))
+        if t == 4 and TC0[ch]:
+            mm(Y0[ch], a("idf"), a("hb", lo, hi), True, False)
+            rows(Y0[ch], a("tc", lo, hi), a("sel", lo, hi), cl, TC0[ch])
+        elif "tc%d" % ch in ONS and t < 4:
             act(a("key", lo, hi), ind(a("skt"), cl), AF.Identity)
             mms([(y, a("idf"), a("hb", lo, hi), True, False), (y, a("idf"), a("key", lo, hi), False, True)])
             act(a("tc", lo, hi), y, AF.Identity)
         else:
             tt(a("tc", lo, hi), ind(a("skt"), cl), a("hb", lo, hi), OP.add)
-        act(a("sa", lo, hi), a("tc", lo, hi), AF.Sign, 1.0, -2.0 * L)
-        mms([(XP[ch], mtwo, a("cn"), True, False), (XP[ch], a("idl"), a("sb", lo, hi), False, False), (XP[ch], a("idl"), a("sa", lo, hi), False, False)])
+        act(a("sa", lo, hi), Y0[ch] if t == 4 and TC0[ch] else a("tc", lo, hi), AF.Relu, -8.0, 16.0 * L)
+        if SB:
+            lin("sb%d" % (t == 4), a("sb", lo, hi), a(F, 16 + lo, 16 + hi), -1.0, 2.0 * L)
+            mm(XP[ch], a("idb"), a("sb", lo, hi), True, False)
+        else:
+            mms([(XP[ch], four, a("cu", 0, 128), True, False), (XP[ch], a("id2"), a(F, 16 + lo, 16 + hi), False, False)])
+        mm(XP[ch], a("idb"), a("sa", lo, hi), False, False)
 
     def next_saved(sv, own):
         ts(a("s2"), a(sv), 8191, OP.bitwise_and)
@@ -299,19 +337,22 @@ def rank_program(g, core, T, topo):
     tt(a("w"), a("iu"), a("pl", 0, 32), OP.add)
     lin("sv", a("sv"), a("w"), 1, 2 * L)
     lists(4, 0, 32)
-    act(a("fb0"), ind(a("tabb", 0, 528), a("gl", 256, 272)), AF.Identity, 8192.0, float(C0))
     ts(a("frs"), a("fri"), 511 + (1 << 21), OP.bitwise_and)
     ts(a("pc"), a("fri"), 9, OP.arith_shift_right)
-    act(a("p3", 0, 256), a("frs"), AF.Identity, 8192.0, float(O))
+    lin("frs", a("p3", 0, 256), a("frs"), 8192.0, float(O))
     tt(a("frm"), a("pc"), a("p3", 0, 256), OP.add)
     ts(a("f0", *OWN), a("frm"), 2 * L, OP.min)
-    act(a("f0", *GH), a("f0", *OWN), AF.Identity)
-    act(a("fu"), a("f0", *OWN), AF.Identity, 1.0, -float(L))
-    for j, (lo, hi) in enumerate(SKP):
-        h = a(("d0", "d1", "fa", "fb")[j % 4], 0, hi - lo)
+    lin("fu", a("fu"), a("f0", *OWN), 1.0, -float(L))
+    def table(lo, hi, bank):
+        h = a(bank, 0, hi - lo)
         act(a("sks", lo, hi), a("ski", lo, hi), AF.Sign, 1.0, -4095.5)
         mms([(h, a("idk"), a("sks", lo, hi), True, False), (h, a("idm"), a("sks", lo, hi), False, True)])
         tt(a("skt", lo + 592, hi + 592), a("ski", lo, hi), h, OP.add)
+
+    for j, (lo, hi) in enumerate(SKP[:len(SKP) - DEF]):
+        table(lo, hi, BANKS[j % len(BANKS)])
+        for p in prog[-3:]:
+            p["extra"] = 0.1 + 0.01 * j if j < EARLY else START + FILL
     for ch in H:
         clause_part(4, "f0", ch)
     fill(a("crow"), 0.0)
@@ -322,8 +363,14 @@ def rank_program(g, core, T, topo):
             lin("crow", a("crow", 128 * j, 128 * j + 128, 1, r + 1, r), a("thj", 0, 128, 1, r + 1, r), 2, w * (r > 0))
     next_saved("sv", a("iu", 16, 32))
 
-    def places(ch, raw, m, p, q, pr, r, u):
-        w = PH[ch]
+    def cut(name, ch):
+        lo, hi = PH[ch]
+        return [(lo, lo + 64), (lo + 64, hi)] if name + str(ch) in SPLIT else [(lo, hi)]
+
+    def part(o, lo, hi):
+        return a(o[0], o[1] + lo % 128 // 16, o[1] + lo % 128 // 16 + (hi - lo) // 16)
+
+    def places(ch, w, raw, m, p, q, pr, r, u):
         ts(a(q, *w), a(raw, *w), 13, OP.arith_shift_right, 1023, OP.bitwise_and)
         ts(a(p, *w), a(raw, *w), 8191, OP.bitwise_and)
         ts(a(m, *w), a(raw, *w), L - 1, OP.bitwise_and)
@@ -338,9 +385,7 @@ def rank_program(g, core, T, topo):
 
     def outputs(F, ch):
         lo, hi = PH[ch]
-        for x in H:
-            c, d = (16 * x + ch, 16 * x + 16, 2), 256 * ch + 128 * x
-            tt(a("w", *c), a("mx", *c), a("sum", d + 15, d + 128, 16) if FAST[2] else a(EX[ch], 8 * x, 8 * x + 8), OP.max)
+        tt(a("w", ch, 32, 2), a("mx", ch, 32, 2), a("sum", 256 * ch + 15, 256 * ch + 256, 16), OP.max)
         if ch:
             mm(a("pl", 0, 128, 1, 64), a("svy"), a("idf"), True, False)
             ts(a("fi"), a("w"), 8191, OP.bitwise_and)
@@ -357,38 +402,62 @@ def rank_program(g, core, T, topo):
             for j, y in enumerate((T.yg, T.yc, T.ysg, T.yk)):
                 dma("sy"[j % 2], ("!", y[:]), a("fot", 0, 128, 1, 16 * j + 16, 16 * j))
         e = a("fa", 256 + lo, 256 + hi)
-        mm(e, five, a("cu", 0, 128), True, False)
-        mm(e, a("gon"), a("rs", lo, hi), False, False)
-        mm(e, a("idf"), a(F, 528 + lo, 528 + hi), False, True)
-        tt(a("fu", lo, hi), a("fu", lo, hi), e, OP.min)
-        e = a("p3", 256 + lo, 256 + hi)
-        ts(e, a("fu", lo, hi), L, OP.is_ge, -32 - 1024 * 592, OP.add)
+        act(a("rs", lo, hi), ind(a("sum", 256 * ch, 256 * ch + 128), e15), AF.Relu, 128.0, -128.0 * L)
+        mm(e, a("rs", lo, hi), a("idb"))
+        tt(a("sa", lo, hi), a("fu", lo, hi), e, OP.is_gt)
         ts(a("o2", lo, hi), a("oi", lo, hi), 8191, OP.bitwise_and)
         ts(a("oq", lo, hi), a("oi", lo, hi), 12, OP.arith_shift_right, 2046, OP.bitwise_and)
-        act(a("fb", lo, hi), a("o2", lo, hi), AF.Identity, 1024.0)
-        tt(a("o3", lo, hi), a("oq", lo, hi), a("fb", lo, hi), OP.add)
-        tt(a("hb", lo, hi), a("o3", lo, hi), e, OP.add)
-        ts(a("oz", lo, hi), a("hb", lo, hi), -1, OP.max)
+        act(a("o3", lo, hi), a("o2", lo, hi), AF.Identity, 1024.0, -1024.0 * 592)
+        act(a("hb", lo, hi), a("oq", lo, hi), AF.Identity, 1.0, -32.0)
+        e = a(("eb", "d1")[ch], 0, 128)
+        mm(e, a("idf"), a("o3", lo, hi), True, False)
+        mm(e, a("idf"), a("hb", lo, hi), False, False)
+        mm(e, a("idb"), a("sa", lo, hi), False, True)
+        ts(a("oz", lo, hi), e, -1, OP.max)
         dma("y", ("!", T.yf[:, lo:hi]), a("oz", lo, hi))
+
+    def runs(js):
+        out = []
+        for j in js:
+            if out and out[-1][1] == 32 * j and (out[-1][0] == 0 or (out[-1][0], j) == (64, 3)):
+                out[-1] = (out[-1][0], 32 * j + 32)
+            else:
+                out.append((32 * j, 32 * j + 32))
+        return out
 
     for t in range(RO):
         F, last, to = "f%d" % t, t == RO - 1, T.cores[(rank + 1 + t % 3) % N]
         B = "f%d" % max(t - 1, 0)
         for ch, (lo, hi) in enumerate(PH):
             up(t, "g%d" % ch)
-            if t == 0:
+            if t == 0 and TG0[ch]:
+                e = a(GB0[ch], 256, 384)
+                lin("fc%d" % ch, a("sm", lo, hi), ind(a(F, 0, 272), gl(4, 0, 0, ch)))
+                mm(e, a("e16", lo, hi), a("inf", 128, 256), True, False)
+                rows(e, a("tg", lo, hi), a("clx", lo, hi), gl(4, 0, 1, ch), TG0[ch], 16 * 8192 + C0)
+                tt(a("rawg", lo, hi), a("sm", lo, hi), e, OP.min)
+            elif t == 0:
                 tt(a("tg", lo, hi), ind(a("skt"), gl(4, 0, 1, ch)), a("fb0", lo, hi), OP.add)
                 tt(a("rawg", lo, hi), ind(a(F, 0, 528), gl(4, 0, 0, ch)), a("tg", lo, hi), OP.min)
             else:
                 c, C = 32 * (t - 1) + 16 * ch, a("r%d" % (t - 1))
-                tt(a("tg", lo, hi), ind(a("skt"), a("arr", c + 8, c + 16)), a("bg", lo, hi), OP.add)
-                tt(a("rawg", lo, hi), ind(C, a("arr", c, c + 8)), a("tg", lo, hi), OP.min)
                 up(t, "col%d" % ch)
                 act(a(F, 272 + lo, 272 + hi), ind(C, a("arr", c, c + 8)), AF.Identity)
+                up(t, "g%d" % ch)
+                if TG[ch]:
+                    e = a(("d0", "d1")[ch], 384, 512)
+                    act(a("tg", lo, hi), ind(a("skt"), a("arr", c + 8, c + 16)), AF.Identity)
+                    mms([(e, a("idf"), a("bg", lo, hi), True, False), (e, a("idf"), a("tg", lo, hi), False, True)])
+                    tt(a("rawg", lo, hi), a(F, 272 + lo, 272 + hi), e, OP.min)
+                else:
+                    tt(a("tg", lo, hi), ind(a("skt"), a("arr", c + 8, c + 16)), a("bg", lo, hi), OP.add)
             up(t, "g%d" % ch)
-            places(ch, "rawg", "ga", "pg", "qg", "prg", "rg", "ug")
+            for w in cut("g", ch):
+                if t and not TG[ch]:
+                    tt(a("rawg", *w), ind(C, part(a("arr", c, c + 8), *w)), a("tg", *w), OP.min)
+                places(ch, w, "rawg", "ga", "pg", "qg", "prg", "rg", "ug")
         if not last:
-            send(a("r%d" % t, *GH), a(F, *GH), to, "ag%d" % t)
+            send(a("r%d" % t, *GH), a(F, *(GH if t else OWN)), to, "ag%d" % t)
         for j, (lo, hi) in enumerate(GCH):
             up(t, "u%d" % (lo // 1024), lo % 1024 / 730)
             act(a("ub", lo, hi), ind(a("xr"), a("ug", lo // 16, hi // 16)), AF.Identity)
@@ -398,80 +467,106 @@ def rank_program(g, core, T, topo):
             mm(XP[ch], a("idf"), a("gaf", *GF(last, ch)), False, True)
             tt(a(F, 528 + lo, 528 + hi), a(B, 16 + lo, 16 + hi), XP[ch], OP.min)
             up(t, "c%d" % ch)
-            tt(a("rawc", lo, hi), ind(a(F, 0, 528 + hi), hl((t + 4) % 5, ch)), a("tc", lo, hi), OP.min)
-            places(ch, "rawc", "ca", "pc", "qc", "prc", "rc", "uc")
-        for lo, hi in VCH:
+            for w in cut("c", ch):
+                if t:
+                    tt(a("rawc", *w), ind(a(F, 0, 528 + hi), part(hl(t - 1, ch), *w)), a("tc", *w), OP.min)
+                else:
+                    y = Y0[ch]
+                    tt(a("rawc", *w), a(F, 528 + w[0], 528 + w[1]), a(y[0], y[1] + w[0] - lo, y[1] + w[1] - lo) if TC0[ch] else a("tc", *w), OP.min)
+                places(ch, w, "rawc", "ca", "pc", "qc", "prc", "rc", "uc")
+        if t == 0:
+            step[1] = None
+            for c, bank in zip(SKP[len(SKP) - DEF:], ("pl", "eb", "p3")):
+                table(c[0], c[1], bank)
+                prog[-3]["extra"], prog[-2]["extra"], prog[-1]["extra"] = START + FILL, START + FILL, START + 10.5
+        way = WAYS.get(t, WAY)
+        pieces = [(w.lower(), 512 * j + c, 512 * j + c + (512 if w.islower() else 256)) for j, w in enumerate(way) for c in ((0,) if w.islower() else (0, 256))]
+        for w, lo, hi in pieces:
             up(t, "w4" if hi == 4096 else "w%d" % (lo // 1024), lo % 1024 / 730)
-            if lo in SW:
-                e = a(SW[lo], 0, hi - lo)
+            if w == "s":
+                e = a(SWB[way.lower()[:lo // 512].count("s") % 2], lo % 512, lo % 512 + hi - lo)
                 act(a("df", lo, hi), ind(a("xr"), a("uc", lo // 16, hi // 16)), AF.Identity)
                 mms([(e, a("idn"), a("ub", lo, hi), True, False), (e, a("idb"), a("df", lo, hi), False, True)])
                 act(a("ab", lo, hi), e, AF.Abs)
                 continue
             tt(a("df", lo, hi), ind(a("xr"), a("uc", lo // 16, hi // 16)), a("ub", lo, hi), OP.subtract)
-        for lo, hi in ACH:
+        for w, lo, hi in pieces:
             up(t, "a4" if hi == 4096 else "a%d" % (lo // 1024), lo % 1024 / 730)
-            if lo in SW:
-                continue
-            if lo // 1024 in RELU:
+            if w == "r":
                 ts(a("ab", lo, hi), a("df", lo, hi), 0, OP.max, 2, OP.mult)
-            else:
+            elif w == "b":
+                act(a("ab", lo - 512, hi), a("df", lo - 512, hi), AF.Abs)
+            elif w == "a" and way[hi // 512:hi // 512 + 1] != "b":
                 act(a("ab", lo, hi), a("df", lo, hi), AF.Abs)
         for ch in H:
             up(t, "d%d" % ch)
             D = ("d0", "d1")[ch]
             mm(fcs[ch], a("idf"), a("fu", *PH[ch]), True, False)
             mm(a(D, 0, 384), a("oneb", 0, 128, 1, 33), a("crow"), True, False)
-            rl = [j % 2 for j in RELU if j // 2 == ch]
-            if rl:
-                lo, hi = 64 * min(rl), 64 * max(rl) + 64
-                for k0 in range(0, 16, 4):
-                    mms([(a(D, k, 384, 16, hi, lo), a("df", 2048 * ch + 16 * lo + k, 2048 * ch + 16 * hi, 16), a("bw", 24, 48), False, False) for k in range(k0, k0 + 4)])
-            for lo, hi in LATE[ch]:
-                for k0 in range(0, 16, 4):
-                    mms([(a(D, k, 384, 16, hi, lo), a("ab", 2048 * ch + 16 * lo + k, 2048 * ch + 16 * hi, 16), a("bw", 0, 24), False, k == 15 and hi == 128) for k in range(k0, k0 + 4)])
+            for l0, h0 in LATE[ch]:
+                for x, lo, hi in [("df",) + r for r in runs([j for j in range(l0 // 32, h0 // 32) if way[4 * ch + j] in "rR"])] + [("ab", l0, h0)]:
+                    for k0 in range(0, 16, MK):
+                        mms([(a(D, k, 384, 16, hi, lo), a(x, 2048 * ch + 16 * lo + k, 2048 * ch + 16 * hi, 16), a("bw", 24 * (x == "df"), 24 + 24 * (x == "df")), False,
+                              k == 15 and x == "ab") for k in range(k0, k0 + MK)])
         for ch, (lo, hi) in enumerate(PH):
             D = ("d0", "d1")[ch]
             R = a(D, 384, 512)
             s1, s2 = a("sg", 2 * lo, 2 * lo + 128), a("sg", 2 * lo + 128, 2 * lo + 256)
-            fast = FAST[2] if last else FAST[ch]
+            fast, bare = FAST[2] if last else FAST[ch], BARE[ch] and not last
             up(t, "f%d" % ch)
-            act(s1 if ch else a("sg", 0, 256), a(D, 128, 256 if ch else 384), AF.Sign)
+            act(s1 if ch or S2 else a("sg", 0, 256), a(D, 128, 256 if ch or S2 else 384), AF.Sign)
             scan(a("cnt", lo, hi), a("rstb"), s1, OP.mult, OP.add)
-            act(a("clx", lo, hi), ind(a("cnt", lo, hi), e15), AF.Sign, -1.0, a("lim", ch, ch + 1), None if last else a("par", ch, ch + 1))
+            act(a("clx", lo, hi), ind(a("cnt", lo, hi), e15), AF.Sign, -1.0, a("lim", ch, ch + 1), a("par", ch, ch + 1) if PAR and not last else None)
             mm(fcs[ch], a("clx", lo, hi), a("idu"), False, True)
             tt(a("oi", lo, hi) if last else a(F, 16 + lo, 16 + hi), a(F, 528 + lo, 528 + hi), fcs[ch], OP.max)
-            if not last:
+            if not last and (ch or not ONE):
                 send(a("r%d" % t, 16 + lo, 16 + hi), a(F, 16 + lo, 16 + hi), to, "ao%d" % (2 * t + ch))
             if ch == 0 and not last:
                 up(t, "fu")
                 mm(fus, five, a("cu"), True, False)
             up(t, "m%d" % ch)
             tt(a("key", lo, hi), s1, a(D, 0, 128), OP.mult)
-            if ch:
+            if ch or S2:
                 act(s2, a(D, 256, 384), AF.Sign)
             scan(a("sm", lo, hi), a("rsb"), a("key", lo, hi), OP.add, OP.max)
-            tt(a("sel", lo, hi), ind(a("sm", lo, hi), e15), a("key", lo, hi), OP.is_equal)
-            for x in range(fast):
+            tt(a("sel", lo, hi), ind(a("sm", lo, hi), e15), a("key", lo, hi), OP.not_equal)
+            if last:
+                up(t, "l%d" % ch)
+                c, b = 256 * ch, ("ea", "d0")[ch]
+                lin("caf%d" % ch, a("gaf", c + 128, c + 256), a("ca", lo, hi))
+                mm(a(b, 0, 256), mone, a("cu"), True, False)
+                for x in H:
+                    mm(a(b, 128 * x, 128 * x + 128), a("gaf", c + 128 * x, c + 128 * x + 128), a("idf"), False, False)
+                for w, y in ((a("idx"), a("clx", lo, hi)), (a("ids"), s2), (a("idw"), a("sel", lo, hi))):
+                    mms([(a(b, 128 * x, 128 * x + 128), w, y, False, w[0] == "idw" and x == 1) for x in H])
+                scan(a("sum", c, c + 256), a("rst"), a(b, 0, 256), OP.add, OP.max)
+            for x in range(0 if last else fast):
                 up(t, "lj"[x] + str(ch))
-                e, c = a(EX[x], lo, hi), ((256 * ch + 128 * x, 256 * ch + 128 * x + 128) if last else (256 * x + lo, 256 * x + hi))
+                e, c = a(GE[ch] if not x else EX[x], lo, hi), ((256 * ch + 128 * x, 256 * ch + 128 * x + 128) if last else (256 * x + lo, 256 * x + hi))
                 if x:
                     lin("caf%d" % ch, a("gaf", *c), a("ca", lo, hi))
                 mm(e, mone, a("cu", 0, 128), True, False)
                 mm(e, a("gaf", *c), a("idf"), False, False)
-                mm(e, a("idx"), a("clx", lo, hi), False, False)
-                mm(e, a("ids"), s2, False, True)
-                tt(a("pgc", *c), a("sel", lo, hi), e, OP.mult)
-                scan(a("sum", *c), a("rst"), a("pgc", *c), OP.mult, OP.add)
+                if bare and not x:
+                    mm(e, a("idl"), a("clx", lo, hi), False, False)
+                    mm(e, a("idw"), a("sel", lo, hi), False, True)
+                    scan(a("sum", *c), a("rstb"), e, OP.mult, OP.max)
+                else:
+                    mm(e, a("idx"), a("clx", lo, hi), False, False)
+                    mm(e, a("ids"), s2, False, False)
+                    mm(e, a("idw"), a("sel", lo, hi), False, True)
+                    scan(a("sum", *c), a("rst", 0, 128), e, OP.add, OP.max)
                 if not last:
                     tt(a("lh", *c), ind(a("sum", *c), e15), a("mske", 0, 128), OP.mult)
             up(t, "m%d" % ch)
             if fast < 2:
-                mm(R, a("sel", lo, hi), a("idb"))
-            mm(a("p3", lo, hi), s2, a("idh"), True, False)
-            mm(a("p3", lo, hi), a("clx", lo, hi), a("idc"), False, False)
-            mm(a("p3", lo, hi), a("sel", lo, hi), a("id4"), False, True)
-            act(a("rs", lo, hi), a("p3", lo, hi), AF.Relu, 1.0, -3.5)
+                mms([(R, a("oneb", 0, 128, 1, 1), a("oneb", 0, 128, 1, 1), True, False), (R, a("sel", lo, hi), a("idn"), False, True)])
+            if not last:
+                e = a("p3", lo, hi)
+                mm(e, s2, a("idh"), True, False)
+                mm(e, a("clx", lo, hi), a("idc"), False, False)
+                mm(e, a("sel", lo, hi), a("id4"), False, True)
+                act(a("rs", lo, hi), e, AF.Relu, 1.0, 0.5)
             for x in H[fast:]:
                 tt(a("pgc", 256 * x + lo, 256 * x + hi), a(("ga", "ca")[x], lo, hi), R, OP.mult)
             for x in H:
@@ -485,14 +580,35 @@ def rank_program(g, core, T, topo):
                     continue
                 if x >= fast:
                     tt(a("lh", c, c + 128), a("mske", 0, 128), e, OP.mult)
-                mm(a("pl", 16 * x + 8 * ch, 16 * x + 8 * ch + 8), a("lh", c, c + 128), a("j8"))
+                if bare and not x:
+                    e, y, c, d = a("d0", 128, 256), a("pl", 8 * ch, 8 * ch + 8), 64 * t + 16 * ch, 32 * t + 16 * ch
+                    up(t, "z%d" % ch)
+                    act(a("svx"), ind(a("sv", 8 * ch, 8 * ch + 8), a("el", 0, 8)), AF.Identity, 1.0, -float(L))
+                    mms([(e, a("svx"), a("idf"), True, False), (e, a("idb"), a("mko"), False, False)])
+                    up(t, "l%d" % ch)
+                    mm(e, a("idu"), a("clx", lo, hi), False, True)
+                    act(a("svz"), e, AF.Relu)
+                    mm(y, a("svz"), a("j8"), True, False)
+                    mm(y, a("lh", lo, hi), a("j8"), False, True)
+                    lin("gq", a("gl", c, c + 8), y, 1 / 8192, -591.5 / 8192)
+                    send(a("arr", d, d + 8), a("gl", c, c + 8), to, "al%d" % (2 * t + ch))
+                    up(t, "p%d" % ch)
+                    lin("gw", a("w", 8 * ch, 8 * ch + 8), y)
+                    ts(a("wq", 8, 16), a("w", 8 * ch, 8 * ch + 8), 8191, OP.bitwise_and)
+                    lin("gp", a("gl", c + 8, c + 16), a("wq", 8, 16))
+                    send(a("arr", d + 8, d + 16), a("gl", c + 8, c + 16), to, "ap%d" % (2 * t + ch))
+                    continue
+                mm(a(LB[2 * ch + x], 16 * x + 8 * ch, 16 * x + 8 * ch + 8), a("lh", c, c + 128), a("j8"))
                 if x and JOIN and not ch:
                     continue
                 chs = H if x and JOIN else (ch,)
                 c = (16 * x + 8 * chs[0], 16 * x + 8 * ch + 8)
-                tt(a("w", *c), a("mx", *c), a("pl", *c), OP.max)
+                tt(a("w", *c), a("mx", *c), a(LB[2 * ch + x], *c), OP.max)
                 lists(t, *c)
-                if not x:
+                if ONE and not x and not ch:
+                    send(a("r%d" % t, 0, 144), a(F, 0, 144), to, "ao%d" % (2 * t))
+                    lin("arr", a("arr", 32 * t, 32 * t + 16), a("r%d" % t, 0, 16))
+                elif not x:
                     c = 64 * t + 16 * ch
                     send(a("arr", 32 * t + 16 * ch, 32 * t + 16 * ch + 16), a("gl", c, c + 16), to, "al%d" % (2 * t + ch))
             if last:
@@ -501,23 +617,32 @@ def rank_program(g, core, T, topo):
                 continue
             up(t, "fu")
             mm(a("fa", 256 + lo, 256 + hi), a("gon"), a("rs", lo, hi), False, False)
+
         if last:
             break
         for lo, hi in PH:
             mm(a("fa", 256 + lo, 256 + hi), a("idf"), a(F, 528 + lo, 528 + hi), False, lo > 0)
-        tt(a("fu"), a("fu"), fus, OP.min)
+        for lo, hi in PH if FU2 else ((0, 256),):
+            tt(a("fu", lo, hi), a("fu", lo, hi), a("fa", 256 + lo, 256 + hi), OP.min)
         dma("y", a("f%d" % (t + 1), *OWN), a(F, *OWN), 2.8)
         for ch in H:
             up(t, "k%d" % ch)
             clause_part(t, F, ch)
         up(t, "sv")
-        act(a("par", 2, 4), a("par", 0, 2), AF.Abs, 1.0 / 32)
-        act(a("par", 4, 6), a("par", 2, 4), AF.Abs, 1.0, -2.0)
-        act(a("par", 6, 8), a("par", 4, 6), AF.Abs, 2.0, -2.0)
-        act(a("lim", 0, 2), a("par", 6, 8), AF.Identity, 1.0, -1.0)
+        if PAR:
+            act(a("par", 2, 4), a("par", 0, 2), AF.Abs, 1.0 / 32)
+            act(a("par", 4, 6), a("par", 2, 4), AF.Abs, 1.0, -2.0)
+            act(a("par", 6, 8), a("par", 4, 6), AF.Abs, 2.0, -2.0)
+            act(a("lim", 0, 2), a("par", 6, 8), AF.Identity, 1.0, -1.0)
+        for ch, (lo, hi) in enumerate(() if PAR else PH):
+            prod(a("lim", ch, ch + 1), a("clx", lo, hi, 16))
+        for ch in H:
+            if BARE[ch]:
+                ts(a("wl"), a("w", 16 + 8 * ch, 24 + 8 * ch), L, OP.is_ge, L, OP.mult)
+                tt(a("w", 8 * ch, 8 * ch + 8), a("w", 8 * ch, 8 * ch + 8), a("wl"), OP.add)
         ts(a("w2"), a("w"), 2 * L - 1, OP.bitwise_and)
-        ts(a("sg1"), a("w2"), L, OP.is_ge, -2 * L, OP.mult)
-        tt(a("sh"), a("sv"), a("sg1"), OP.add)
+        lin("sg2", a("sg1"), a("w2"), -16, 16 * L)
+        tt(a("sh"), a("sv"), a("sg1"), OP.min)
         tt(a("sv"), a("w2"), a("sh"), OP.max)
         if t < RO - 2:
             next_saved("sv", a("iu", 16, 32))
@@ -810,6 +935,143 @@ def rank_program(g, core, T, topo):
         top = max(was)
         return span, {(2,) + names[j]: was[j] - top + cut + back[j] * span for j in range(m)}
 
+    seed, tops = [SEED], []
+
+    def rnd():
+        seed[0] = (seed[0] * 1103515245 + 12345) % 2147483648
+        return (seed[0] >> 8) / 8388608
+
+    def search(du, qu, arcs, st, span, edge, turns):
+        m = len(du)
+        now, old, later, newer = ([[] for _ in range(m)] for _ in range(4))
+        for i, j, w, s in arcs:
+            if s < 2:
+                (old if s else now)[j].append((i, w))
+                (newer if s else later)[i].append((j, w))
+        head, tail, ends = edge or ([-1e9] * m, [-99.0] * m, None)
+        for _ in range(6):
+            for j in range(m):
+                st[j] = max([st[j]] + [st[i] + 1e-6 for i, w in now[j]])
+        order, seq = sorted(range(m), key=lambda j: st[j]), {}
+        for j in order:
+            if qu[j] != "net" and (ends or qu[j] != "y"):
+                seq.setdefault(qu[j], []).append(j)
+        rest, hh, tl, prev, nxt, rests = [0.0] * m, [0.0] * m, [0.0] * m, [-1] * m, [-1] * (m + 1), [0] * m
+        best, undo = (1e9, list(st), order), None
+        for turn in range(turns):
+            for q in seq.values():
+                e = m
+                for j in q:
+                    prev[j], nxt[e], e = e, j, j
+                prev[q[0]] = nxt[e] = -1
+            if turn:
+                deg = [len(now[j]) + (prev[j] >= 0) for j in range(m)]
+                order = [j for j in range(m) if not deg[j]]
+                for j in order:
+                    for d, w in later[j]:
+                        deg[d] -= 1
+                        if not deg[d]:
+                            order.append(d)
+                    d = nxt[j]
+                    if d >= 0:
+                        deg[d] -= 1
+                        if not deg[d]:
+                            order.append(d)
+                if len(order) < m:
+                    seq[qu[undo[0]]] = undo[1]
+                    continue
+            for _ in range(1 if ends else 3 if turn else 8):
+                was = sum(st)
+                for j in order:
+                    t0 = head[j]
+                    for d, w in now[j]:
+                        if st[d] + w > t0:
+                            t0 = st[d] + w
+                    for d, w in old[j]:
+                        if st[d] + w - span > t0:
+                            t0 = st[d] + w - span
+                    hh[j] = t0
+                    e = prev[j]
+                    if e >= 0:
+                        e = st[e] + du[e]
+                    elif qu[j] in seq:
+                        e = seq[qu[j]][-1]
+                        e = ends[qu[j]][0] if ends else st[e] + du[e] - span
+                    else:
+                        e = t0
+                    st[j] = t0 if t0 > e else e
+                more = 0.0 if ends else (sum(st) - was) / m
+                span += more
+                if -1e-4 < more < 1e-4:
+                    break
+            for _ in range(1 if ends else 2 if turn else 8):
+                for j in reversed(order):
+                    t0 = tail[j]
+                    for d, w in later[j]:
+                        if rest[d] + w > t0:
+                            t0 = rest[d] + w
+                    for d, w in newer[j]:
+                        if rest[d] + w - span > t0:
+                            t0 = rest[d] + w - span
+                    tl[j] = t0
+                    e = nxt[j]
+                    if e >= 0:
+                        e = rest[e] + du[j]
+                    elif qu[j] in seq:
+                        e = du[j] + (ends[qu[j]][1] if ends else rest[seq[qu[j]][0]] - span)
+                    else:
+                        e = t0
+                    rest[j] = t0 if t0 > e else e
+            way = [st[j] + rest[j] for j in range(m)]
+            top = max(way)
+            if (top if ends else span) < best[0] - 1e-4 and abs(more) < 0.003:
+                best = (top if ends else span, list(st), order)
+            e = top - NEAR
+            hot = [j for j in range(m) if way[j] > e and qu[j] in seq and rests[j] <= turn and
+                   ((prev[j] >= 0 and st[prev[j]] + du[prev[j]] > st[j] - NEAR and way[prev[j]] > e) or (nxt[j] >= 0 and rest[nxt[j]] + du[j] > rest[j] - NEAR and way[nxt[j]] > e))]
+            move = None
+            for _ in range(min(SOME, len(hot))):
+                j = hot.pop(int(rnd() * len(hot)))
+                q = seq[qu[j]]
+                p, k = q.index(j), len(q)
+                for sign in (-1, 1):
+                    for x in range(p + sign, min(max(p + sign * FAR, -1), k), sign):
+                        if sign < 0:
+                            if st[q[x]] + du[q[x]] <= hh[j]:
+                                break
+                            seg, lo, hi = [j] + q[x:p], x - 1, p + 1
+                        else:
+                            if rest[q[x]] <= tl[j]:
+                                break
+                            seg, lo, hi = q[p + 1:x + 1] + [j], p - 1, x + 1
+                        t0 = st[q[lo]] + du[q[lo]] if lo >= 0 else ends[qu[j]][0] if ends else st[q[-1]] + du[q[-1]] - span
+                        hs = []
+                        for y in seg:
+                            if hh[y] > t0:
+                                t0 = hh[y]
+                            hs.append(t0)
+                            t0 += du[y]
+                        t0 = rest[q[hi]] if hi < k else ends[qu[j]][1] if ends else rest[q[0]] - span
+                        e = soft = 0.0
+                        for y in reversed(seg):
+                            t0 += du[y]
+                            if tl[y] > t0:
+                                t0 = tl[y]
+                            f = hs.pop() + t0 - top
+                            if f > e:
+                                e = f
+                            soft += math.exp(f / SOFT) - math.exp((way[y] - top) / SOFT)
+                        e += WEIGH * soft + 0.01 * rnd()
+                        if not move or e < move[0]:
+                            move = (e, j, x)
+            if move:
+                e, j, x = move
+                undo, q = (j, list(seq[qu[j]])), seq[qu[j]]
+                q.remove(j)
+                q.insert(x, j)
+                rests[j] = turn + REST + int(2 * REST * rnd())
+        return best, (span, st)
+
     if not PLAN:
         prio = [0.0] * n
         for i in range(n - 1, -1, -1):
@@ -818,27 +1080,78 @@ def rank_program(g, core, T, topo):
         for i, p in enumerate(prog):
             if p["id"]:
                 due[i] = max([p["due"]] + [due[d] + w for d, w in before[i]]) + dur[i]
-        best = kept = None
-        for seed in SEEDS:
-            now = improve(sorted(range(n), key=lambda i: (due[i] - dur[i], i)), seed, HEAT[0], STEPS[0])
-            best = now if not best or now[0] < best[0] else best
-            end = {p["id"]: now[2][i] for i, p in enumerate(prog) if p["id"]}
-            for k in range(CUTS):
-                span, mid = circle(end, end[(2, "w4", 0)] - k * 11 % 18, seed + k, WARM * COOL ** (k / CUTS))
-                end = {(r,) + k[1:]: mid[k] + (r - 2) * span for k in mid for r in range(RO)}
-                kept = (span, end, now[2]) if not kept or span < kept[0] else kept
-            SPANS.append((seed, round(now[0], 1), round(span, 2)))
-        span, end, due = kept
-        start = max(due[i] for i, p in enumerate(prog) if p["id"] == (0, "w4", 0))
+        ids = {prog[i]["id"]: i for i in range(n) if prog[i]["id"]}
+        names = [k[1:] for k in ids if k[0] == 2]
+        m, num, own = len(names), {k: j for j, k in enumerate(names)}, [ids[(2,) + k] for k in names]
+        needs = [(num[prog[d]["id"][1:]], j, 2 - prog[d]["id"][0], w + dur[d]) for j in range(m) for d, w in before[own[j]] if prog[d]["id"] and prog[d]["id"][1:] in num]
+        at, span, best, kept = [due[i] - dur[i] for i in own], PERIOD, (1e9,), (1e9,)
+        for turn in range(CUTS):
+            if turn % KICK == KICK - 1:
+                kept = best if best[0] < kept[0] + LOOSE * rnd() else kept
+                (span, at), best, c = kept, (1e9,), rnd() * kept[0]
+                at = [x + SHAKE * rnd() * ((x - c) % span < STRETCH) for x in at]
+                tops.append(kept)
+            cut = min(at) + span * (1 + rnd())
+            back = [math.ceil((x - cut) / span) for x in at]
+            for _ in range(4):
+                for i, j, s, w in needs:
+                    back[j] = max(back[j], back[i] - s)
+            arcs = [(i, j, w, s + back[j] - back[i]) for i, j, s, w in needs]
+            good, now = search([dur[i] for i in own], [qs[i] for i in own], arcs, [x - b * span for x, b in zip(at, back)], span, None, ROUND)
+            if good[0] < best[0]:
+                best = (good[0], [x + b * good[0] for x, b in zip(good[1], back)])
+            span, at = best if now[0] > best[0] + STRAY else (now[0], [x + b * now[0] for x, b in zip(now[1], back)])
+        span, at = min(tops + [best])
+        SPANS.append([round(x[0], 2) for x in tops])
+        SPANS.append(round(span, 2))
         for i, p in enumerate(prog):
-            if p["id"]:
-                e = end[p["id"]] + start - end[(0, "w4", 0)] if p["id"] in end else 0.0
-                due[i] = max([e - dur[i]] + [due[d] + w for d, w in before[i]]) + dur[i]
-        now = improve(sorted(range(n), key=lambda i: (due[i] - dur[i], i)), SEEDS[0], HEAT[1], STEPS[1])
-        best = now if now[0] < best[0] else best
-        SPANS.append(round(now[0], 1))
-        PLAN.extend(best[:2])
-        PLAN.extend((prog, before, dur, lat))
+            if not p["id"]:
+                due[i] = max([min(due[i], START)] + [due[d] + 1e-6 + dur[i] - dur[d] for d, w in before[i]])
+            else:
+                e = at[num[p["id"][1:]]] - at[num["u0", 0]] + p["id"][0] * span + START if p["id"][1:] in num else 0.0
+                due[i] = max([e] + [due[d] + w if e < START + GAP else due[d] - dur[d] + 1e-6 for d, w in before[i]]) + dur[i]
+        order = sorted(range(n), key=lambda i: (due[i] - dur[i], i))
+        if FILL:
+            key = [due[i] - dur[i] for i in range(n)]
+            for i, p in enumerate(prog):
+                key[i] = max([p["extra"] if p["kind"] == "c" and p["extra"] else key[i]] + [key[d] + 1e-6 for d, w in before[i]])
+            cut = sorted(range(n), key=lambda i: key[i])
+            some = [i for i in cut if key[i] < START + GAP]
+            due = pack(some, before, [0.0] * n)
+            order = sorted(some, key=lambda i: (due[i] - dur[i], key[i])) + cut[len(some):]
+        for turn in range(STEPS + 1):
+            st, rest, prev, nxt, last = [0.0] * n, [0.0] * n, [-1] * n, [-1] * n, {}
+            for i in order:
+                if qs[i] != "net" and qs[i] in last:
+                    prev[i], nxt[last[qs[i]]] = last[qs[i]], i
+                last[qs[i]] = i
+                st[i] = max([st[d] + dur[d] + w for d, w in before[i]] + [st[prev[i]] + dur[prev[i]] if prev[i] >= 0 else 0.0])
+            for i in reversed(order):
+                rest[i] = dur[i] + max([lat[i], rest[nxt[i]] if nxt[i] >= 0 else 0.0] + [rest[d] + w for d, w in after[i]])
+            order.sort(key=lambda i: st[i])
+            if turn % 10 == 0:
+                SPANS.append(round(max(rest), 1))
+            if turn == STEPS:
+                break
+            part = TURNS[turn // PART]
+            if turn % PART == 0:
+                seed[0] = part[0]
+            lo, hi, wide = part[1 + turn % (len(part) - 1)]
+            first = int((n - wide) * (lo + (hi - lo) * rnd()))
+            some = order[first:first + wide]
+            loc = {i: j for j, i in enumerate(some)}
+            arcs = [(loc[d], loc[i], w + dur[d], 0) for i in some for d, w in before[i] if d in loc]
+            head = [max([0.0] + [st[d] + dur[d] + w for d, w in before[i] if d not in loc]) for i in some]
+            tail = [dur[i] + max([lat[i]] + [rest[d] + w for d, w in after[i] if d not in loc]) for i in some]
+            ends = {}
+            for i in some:
+                ends[qs[i]] = (ends[qs[i]][0] if qs[i] in ends else st[prev[i]] + dur[prev[i]] if prev[i] >= 0 else 0.0, rest[nxt[i]] if nxt[i] >= 0 else 0.0)
+            c, e = st[some[int(rnd() * wide)]], SHAKE * rnd() * (turn % PART >= CALM)
+            at = [st[i] + e * rnd() * (c - 2 < st[i] < c + 2) for i in some]
+            good, now = search([dur[i] for i in some], [qs[i] for i in some], arcs, at, 0.0, (head, tail, ends), STAY)
+            if good[0] < max(rest) + 1e-6:
+                order[first:first + wide] = [some[j] for j in good[2]]
+        PLAN.extend((max(rest), order, prog, before, dur, lat))
 
     def wait(q, sem, c):
         if know[q].get(sem, 0) < c:

@@ -1,11 +1,13 @@
 import math
+from concourse.bass import DstId, RemoteDMATransfer
 from concourse.mybir import AluOpType, ActivationFunctionType, AxisListType
 
 OP = AluOpType
 AF = ActivationFunctionType
-U, L, O = 1 << 22, 1 << 23, 16 * 8192 + 592
+U, L, O, K = 1 << 22, 1 << 23, 16 * 8192 + 592, float(1 << 24)
+Z = float(1 << 42)
 C0 = 592 - 2048 - L // 2
-NF, RO, N = 256, 5, 4
+RO, N = 5, 4
 H = (0, 1)
 F32, BF, I32, U16 = "float32", "bfloat16", "int32", "uint16"
 SCRATCH = {}
@@ -18,58 +20,82 @@ def _bufs(where, dtype, text):
         SCRATCH[n] = (where, [int(r), int(c)], dtype)
 
 
-_bufs("sbuf", F32, "skt:4688 tabb:784 bg:256 j8:8 rst:256 rsb:128 onef:128 e8:8x128 m16:16x128 inf:16x384 id8:16x16 k8:16x128 e16:16x256 gaf:512 sum:512 "
-      "iw:16 iu:32 il:16 lim:24 hb:256 tg:256 tc:256 fu:256 key:256 sm:256 pgc:512 lh:512 we:16 wf:16 svy:64 sg1:32 sh:32 mx:32 id2:128 "
-      "fim:64 fot:64x128 oz:256 ft:5968")
-_bufs("sbuf", BF, "idk:128 idm:128 idn:128 xr:4096 ub:4096 df:4096 ab:4096 bw:48 idb:128 id4:128 idh:128 gou:128 gon:128 oneb:128 crow:33x384 cu:1x256 idw:128 idl:128 row:1x512 "
-      "idu:128 idc:128 ids:128 idx:128 rstb:128 sg:512 cnt:256 sel:256 rs:256 clx:256 sa:512 mko:128")
+_bufs("sbuf", F32, "skt:4688 tabb:768 bg:256 j8:8 rsb:128 onef:128 e8:8x128 m16:16x128 inf:16x384 id8:16x16 gaf:512 sum:512 "
+      "iw:16 iu:32 il:16 lim:8 par:8 hb:256 tg:256 tc:256 key:256 sm:256 lh:512 we:16 wf:16 svy:64 sg1:32 sh:32 mx:32 "
+      "fim:64 fot:64x128 oz:256 ft:5888 fia:64 fib:64 old:48 flag:48")
+_bufs("sbuf", BF, "idk:128 idm:128 idn:128 xr:4096 ub:4096 df:4096 ab:4096 um:1536 bw:72 idb:128 idh:128 big:33x128 k33:33x128 hz:33x256 e16:16x256 inb:16x128 cv:1x256 oneb:1x128 cw:1x128 mko:128 crow:33x384 idw:128 "
+      "idu:128 idz:128 ids:128 idx:128 rstb:128 sg:512 cnt:256 dd:256 rs:256 clx:256 sa:512 zz:256")
 _bufs("sbuf", I32, "ski:4096 ini:16x384 fri:256 thi:33x128 thj:33x128 pi:16 ci:72 pm:16 rawg:256 rawc:256 ga:256 ca:256 sv:32 svs:32 "
-      "pg:256 qg:256 prg:256 rg:256 pc:256 qc:256 prc:256 rc:256 w:32 w2:32 wq:64 s2:32 s3:32 t4:16 t5:16 t6:16 t7:16 t8:16 fi:32 fq:32 oi:256")
-_bufs("sbuf", U16, "ug:256 uc:256 el:24 ek:32 gl:320 arr:128")
-_bufs("psum", F32, "d0:512 d1:512 p3:512 ea:512 eb:512 pl:512 fa:512 fb:512")
-SEMAPHORES = ["sv", "ss", "st", "sg", "rl"] + [n + str(t) for n in ("al", "ao", "ag", "ap") for t in range(8)] + ["d%d" % t for t in range(40)]
-VIEW = {"sks": ("df", 0, 4096), "frs": ("oi", 0, 256), "frm": ("oz", 0, 256), "o2": ("pg", 0, 256), "oq": ("qg", 0, 256), "o3": ("tg", 0, 256), "fb0": ("key", 0, 256),
-        "svx": ("pgc", 0, 128), "svz": ("pgc", 128, 128), "idf": ("skt", 0, 128), "go": ("skt", 128, 128), "mske": ("skt", 256, 256), "wl": ("lim", 8, 8), "par": ("lim", 16, 8), "sb": ("sa", 256, 256)}
+      "pg:256 qg:256 prg:256 rg:256 pc:256 qc:256 prc:256 rc:256 w:32 w2:32 wq:64 s2:32 s3:32 t4:32 t5:32 t6:32 t7:32 t8:32 fi:32 fq:32 oi:256 wl:8")
+_bufs("sbuf", U16, "ug:256 uc:256 el:32 ek:32 gl:320 g0:64 arr:256")
+_bufs("psum", F32, "d0:512 d1:512 fa0:512 fa1:512 ea0:512 ea1:512 xa0:512 xa1:512")
+SEMAPHORES = ["sv", "ss", "st", "sg", "rl", "rf"] + [n + str(t) for n in ("al", "ao", "ag", "ap", "h") for t in range(8)] + ["d%d" % t for t in range(40)]
+VIEW = {"sks": ("df", 0, 4096), "frs": ("oi", 0, 256), "frm": ("oz", 0, 256), "o2": ("pg", 0, 256), "oq": ("qg", 0, 256), "o3": ("tg", 0, 256),
+        "idf": ("skt", 0, 128), "id2": ("skt", 128, 128), "mske": ("skt", 256, 256)}
 for _t in range(RO):
-    VIEW["f%d" % _t], VIEW["r%d" % _t] = ("ft", 1280 * _t, 784), ("ft", 1280 * _t + 768, 528)
+    VIEW["f%d" % _t], VIEW["r%d" % _t] = ("ft", 1280 * _t, 768), ("ft", 1280 * _t + 768, 512)
 PSUM = [n for n in SCRATCH if SCRATCH[n][0] == "psum"]
-OWN, GH, F3 = (16, 272), (272, 528), (528, 784)
-GCH = [(c, c + 512) for c in range(0, 4096, 512)]
-WAY = "aarraaaA"
-SPLIT, MK, BARE, SB, TC0, TG0 = (), 4, (0, 0), 1, (2, 2), (2, 2)
-DEF, BANKS, GB0 = 3, ("d0", "d1", "fa"), ("ea", "ea")
-WAYS, PAR, S2, ONE, FU2 = {0: "rrraaaaA"}, 1, 1, 0, 1
-GE, LB = ("ea", "pl"), ("ea", "ea", "ea", "ea")
-SWB = ("pl", "p3")
-TG = (0, 0)
+OWN, GH, F3 = (0, 256), (256, 512), (512, 768)
 PH = [(0, 128), (128, 256)]
+GCH = [(c, c + 512) for c in range(0, 4096, 512)]
+WAY, WAYS, ONCE = "mrrraaaA", {}, 1
+MK, S2, TG, JOIN, OUT, PAR, KB = 4, (0, 1), (0, 0), (0, 0), 0, 1, ("xa1", "d0")
+DEF, BANKS, PARK = 3, ("d0", "d1", "fa0"), ("fa0", "fa1", "ea1")
 SKP = [(c, c + 512) for c in range(0, 4096, 512)]
 SKL = [(0, 512), (512, 1536), (1536, 2560), (2560, 3584), (3584, 4096)]
-THI = 3
-INI, FRI = 0, 0
-FAST, JOIN, LATE = (1, 1, 2), 0, (((0, 128),), ((0, 64), (64, 96), (96, 128)))
-ONS = ("gaf0", "s3", "t7", "gaf1", "ug1", "mx", "caf1", "caf0", "uc0", "uc1", "inf", "idu", "ids", "idx", "idl", "id4", "sg2", "wf0", "wf1", "gl10", "gl11",
-       "go", "mske", "fu", "idw", "idh", "idc", "sb0", "bg", "bw")
-CYC, CG, FIX, GFIX, SFIX, PEC, PFIX = 0.00095, 1.42, 0.005, 0.05, 0.05, 0.00056, 0.015
+SPLIT, PS, WIDE, BARE, CQ = {}, (0, 0), (), (0, 0), (0, 0)
+THI = 9
+LATE = (((0, 128),), ((0, 64), (64, 96), (96, 128)))
+ONS = ("gaf", "ug0", "glg0", "inb", "svs", "svy", "fi", "s3", "t7", "ug1", "mx", "caf", "uc1", "inf", "idu", "ids", "idx", "idz", "sg2", "wf", "glc", "mske", "idw", "idh", "sb", "bw", "t5")
+CYC, CG, FIX, GFIX, SFIX, PEC, PFIX = 0.0009, 1.45, 0.02, 0.06, 0.05, 0.00056, 0.015
 WAKE = {"v": 0.16, "vv": 0.22, "s": 0.24, "t": 0.3, "tt": 0.0, "g": 0.1, "y": 0.2, "net": 0.2, "vg": 0.3}
-RI, RL, RB = 0.45, 1.1, 0.4
+RI, RL, RB, RF, R1 = 0.45, 1.1, 0.4, 2.3, 1.5
 T0, PERIOD, START, FILL = 8.0, 17.6, 11.5, -2.0
-EARLY, GAP = 5, 12.0
+EARLY, TAIL, MAP, GAP = 5, 0.0, 1, 12.0
 DUE = {"g0": 5.0, "col0": 5.0, "col1": 5, "u0": 7.3, "u1": 8.7, "c0": 6.0, "g1": 7.0, "x0": 6.0, "x1": 8.5, "w0": 9.9, "w1": 11.3, "c1": 12.7, "u2": 10.2, "a0": 11.6,
        "w2": 14.0, "a1": 12.8, "u3": 13.7, "d0": 10, "w3": 15, "a2": 15.5, "f0": 16, "m0": 16, "w4": 15.7, "a3": 16, "a4": 16.7, "d1": 10, "f1": 18, "m1": 18,
-       "l0": 17, "l1": 18, "j0": 18, "j1": 21, "k0": 20.5, "k1": 21, "fu": 22, "sv": 22, "o0": 17, "o1": 18, "z1": 16, "p1": 18, "sk": 18}
+       "l0": 17, "l1": 18, "j0": 18, "j1": 21, "k0": 20.5, "k1": 21, "z0": 22, "z1": 22, "sv": 22, "o0": 17, "o1": 18, "b1": 17, "p1": 18, "sl": 22}
 PLAN = []
 SPANS, SEED, REST = [], 4, 10
 KICK, LOOSE, SHAKE, STRETCH, CALM = 10, 0.08, 1.2, 6.0, 10
 SOFT, WEIGH, NEAR, FAR, SOME, STRAY = 0.4, 0.025, 0.03, 20, 4, 0.35
-ROUND, CUTS, STAY, STEPS, PART = 300, 90, 1500, 72, 24
+ROUND, CUTS, STAY, STEPS, PART = 300, 220, 1200, 135, 45
 TURNS = ((6, (0, 0, 170), (0.08, 0.16, 180), (0.03, 0.1, 180), (0.15, 0.25, 180)), (1, (1, 1, 130), (0.86, 0.95, 150), (1, 1, 100), (0.75, 0.85, 180), (0.9, 1, 120)),
          (1, (0.2, 0.8, 200), (0, 0.2, 200), (0.8, 1, 150)))
 
 
+def folds(t):
+    out = []
+    for j, w in enumerate(WAYS.get(t, WAY)):
+        if w in "fm":
+            out.append((j, 512 * j, 512 * j + 512))
+        elif w == "g":
+            out[-1] = (out[-1][0], out[-1][1], 512 * j + 512)
+    return out
+
+
+def hand_back(g, core, to, T, topo):
+    rid, pid, _ = topo.addr(to)
+    n, m, got, sent = len(topo.engines(to, core)), len(topo.engines(core, to)), {}, 0
+    for t in range(RO):
+        for j, lo, hi in folds(t):
+            got[j] = got.get(j, 0) + n
+            g.wait_ge(T.sem["h%d" % j], got[j])
+            g.remote_dma(T["ab"][:, lo:hi], T["ab"][:, lo:hi], T.sem["h%d" % j], T.sem["rl"], pid, rid, topo.mask(core, to))
+            sent += m
+    if sent:
+        g.wait_ge(T.sem["rl"], sent)
+
+
 def rank_program(g, core, T, topo):
     rank = T.rank_of(core)
+    near = {}
+    for c in T.cores:
+        near[c] = [h for h in topo.cores_of(c) if T.rank_of(h) is None and topo.die(h) == topo.die(c) and h not in near.values()][0]
     if rank is None:
+        for c in T.cores:
+            if near[c] == core:
+                hand_back(g, core, c, T, topo)
         return
     Q = {"v": g.vector, "s": g.scalar, "t": g.tensor, "g": g, "y": g.sync}
     SEM = {"v": "sv", "s": "ss", "t": "st", "g": "sg"}
@@ -123,8 +149,9 @@ def rank_program(g, core, T, topo):
             lg[n] = old + [(lo, hi, kind, ref, q, r0, r1)]
 
     def add(q, call, reads, writes, dur, lat=0.0, kind="c", extra=None):
-        seen[step[1]] = seen.get(step[1], -1) + 1
-        prog.append({"due": step[0], "id": step[1] and step[1] + (seen[step[1]],), "q": q, "call": call, "acc": flat(reads, writes), "dur": dur, "lat": lat,
+        k = step[1] and step[1] + (q + "".join(p[0] for c, p in flat([], writes)[:1]),)
+        seen[k] = seen.get(k, -1) + 1
+        prog.append({"due": step[0], "id": k and k[:2] + (k[2] + str(seen[k]),), "q": q, "call": call, "acc": flat(reads, writes), "dur": dur, "lat": lat,
                      "kind": kind, "extra": extra})
 
     def up(t, name, more=0.0):
@@ -166,7 +193,7 @@ def rank_program(g, core, T, topo):
             0.065 + CYC * CG * size(x) if x[0] == "@" else SFIX + CYC * max(64, size(x)))
 
     def lin(name, o, x, scale=1.0, bias=0.0):
-        if name in ONS:
+        if name in ONS or name.rstrip("01") in ONS:
             act(o, x, AF.Identity, float(scale), float(bias))
         elif bias:
             ts(o, x, scale, OP.mult, bias, OP.add)
@@ -202,9 +229,18 @@ def rank_program(g, core, T, topo):
         add("g", call, [src], [], RI + RB * size(dst) / 256 + (2.0 if rsem == "ag0" else 0.0), 0.0, "r", (rsem, len(topo.engines(core, to))))
         add("net", None, [], [dst], 0.0, RL, "n", (rsem, len(topo.engines(core, to)), len(prog) - 1))
 
-    LD = [(a("ski", lo, hi), T.sk[:, lo:hi], 0.2 + 0.5 * (hi - lo) / 512) for lo, hi in SKL]
-    LD[FRI:FRI] = [(a("fri"), T.fr[:], 0.45)]
-    LD[INI:INI] = [(a("ini", 128 * j, 128 * j + 128), y[:], 0.06) for j, y in enumerate((T.gs, T.gf, T.gcl))]
+    def fold(dst, srcs, rsem):
+        to = near[core]
+
+        def call():
+            rid, pid, _ = topo.addr(to)
+            g.remote_dma_fused([RemoteDMATransfer(dst_ids=[DstId(rid=rid, pnc=pid)], dma_engine_mask=topo.mask(core, to), remote_sem=T.sem[rsem],
+                                                  srcs=[ap(x) for x in srcs], dsts=[ap(dst)], alu_op=2)], local_sem=T.sem["rf"])
+        add("g", call, srcs, [dst], RI + RB * size(dst) / 512, 0.0, "f", (rsem, len(topo.engines(core, to))))
+        add("net", None, srcs, [dst], 0.0, RF + RB * size(dst) / 512 + (0.0 if any(p["kind"] == "f" for p in prog[:-1]) else R1), "n", (rsem, len(topo.engines(to, core)), len(prog) - 1))
+
+    LD = [(a("ini", 128 * j, 128 * j + 128), y[:], 0.06) for j, y in enumerate((T.gs, T.gf, T.gcl))] + [(a("fri"), T.fr[:], 0.45)]
+    LD += [(a("ski", lo, hi), T.sk[:, lo:hi], 0.2 + 0.5 * (hi - lo) / 512) for lo, hi in SKL]
     LD += [(a("xr", 592, 4096), T.x[:, 0:3504], 1.9), (a("xr", 0, 592), T.x[:, 3504:4096], 0.5)]
     LD[THI:THI] = [(a("thi", 0, 128, 1, r + 1, r), T.th[:], 0.06) for r in (0, 32)]
     came = 0.0
@@ -215,134 +251,131 @@ def rank_program(g, core, T, topo):
     pick(a("idf"), a("onef"), [[-1, 128]], OP.is_equal, 0, 1)
     pick(a("m16"), a("onef", 0, 128, 1, 16), [[0, 8], [1, 16]], OP.is_equal, 0, -1)
     pick(a("e8"), a("onef", 0, 128, 1, 8), [[1, 8], [0, 16]], OP.is_equal, 0, -1)
-    iota(a("k8"), [[0, 128]], 8192, 0)
+    fill(a("k33"), 8192.0)
     for ch in H:
-        pick(a("e16", *PH[ch]), a("k8"), [[2, 8], [0, 16]], OP.is_equal, ch, -1)
+        pick(a("e16", *PH[ch]), a("k33", 0, 128, 1, 16), [[2, 8], [0, 16]], OP.is_equal, ch, -1)
     iota(a("pi"), [[0, 16]], 0, 1)
     iota(a("ci", 0, 16), [[1, 16]], 0, 0)
-    iota(a("ci", 16, 24), [[16, 8]], 15, 0)
-    iota(a("ci", 24, 40), [[16, 16]], 16, 0)
+    iota(a("ci", 16, 32), [[16, 16]], 15, 0)
     iota(a("ci", 40, 72), [[1, 2], [2, 16]], 0, 0)
-    iota(a("tabb", 0, 528), [[1, 528]], 0, 0)
+    iota(a("tabb", 0, 512), [[1, 512]], 16, 0)
     iota(a("tabb", *F3), [[1, 256]], 1024 + 16, 0)
-    iota(a("t8"), [[0, 8], [128, 2]], 16, 1)
-    for n, lo, hi, st, c in (("skt", 512, 592, 1, 0), ("lim", 0, 8, 1, 1), ("row", 0, 128, 1, -2), ("row", 128, 256, 1, -1), ("row", 256, 384, 1, 5), ("cu", 0, 256, 1, L),
-                             ("oneb", 0, 128, 1, 1), ("rst", 0, 256, 1, 0), ("rst", 0, 256, 16, -8 * L), ("rstb", 0, 128, 1, 1),
-                             ("rstb", 0, 128, 16, 0), ("rsb", 0, 128, 1, 0), ("rsb", 0, 128, 16, -U), ("iu", 0, 16, 1, O - L), ("svy", 0, 32, 1, 0)):
+    iota(a("t8", 0, 16), [[0, 8], [128, 2]], 0, 1)
+    for n, lo, hi, st, c in (("skt", 512, 592, 1, 0), ("lim", 0, 8, 1, 1), ("big", 0, 128, 1, K), ("rstb", 0, 128, 1, 1), ("rstb", 0, 128, 16, 0),
+                             ("rsb", 0, 128, 1, 0), ("rsb", 0, 128, 16, -K * (1 << 20)), ("iu", 0, 32, 1, 592), ("svy", 0, 32, 1, 0)):
         fill(a(n, lo, hi, st), float(c))
-    fill(a("f0", 0, 16), 0.0)
-    mm(a("ea", 0, 128), a("e8"), a("e8"))
-    mm(a("ea", 128, 136), a("e8"), a("idf", 0, 8, 1, 8))
-    mm(a("eb", 0, 128), a("m16"), a("m16"))
-    for n, w in (("go", 1.0), ("gou", float(L)), ("gon", -2.0 * L)):
-        lin(n, a(n), a("ea", 0, 128), w)
-    lin("j8", a("j8"), a("ea", 128, 136))
+    if any(w in WAYS.get(t, WAY) for t in range(RO) for w in "fg"):
+        fill(a("um", 512, 1024 + 512 * any("fg" in WAYS.get(t, WAY) for t in range(RO))), 0.0)
+    mm(a("ea0", 128, 136), a("e8"), a("idf", 0, 8, 1, 8))
+    mm(a("ea1", 0, 128), a("m16"), a("m16"))
+    lin("j8", a("j8"), a("ea0", 128, 136))
     for ch in H:
-        lin("mske", a("mske", *PH[ch]), a("eb", 0, 128))
-    for n, w in (("idb", 1.0), ("idn", -1.0), ("idk", 1.5 * L), ("idm", -2048.0), ("id4", -4.0), ("idw", -2.0 * L), ("idh", 0.5), ("idc", -2.0), ("idu", float(L)), ("ids", 0.5 * L), ("idx", -1.5 * L)) + ((("idl", -float(L)),) if BARE[1] else ()) + (() if SB else (("id2", -2.0),)):
+        lin("mske", a("mske", *PH[ch]), a("ea1", 0, 128))
+    for n, w in (("idb", 1.0), ("idn", -1.0), ("idk", 1.5 * L), ("idm", -2048.0), ("idu", float(L)), ("ids", -0.5 * U), ("idx", -1.5 * U), ("id2", -1.0)):
         lin(n, a(n), a("idf"), w)
-    for j, w in enumerate((16.0, -2.0, -4.0) + ((-16.0, 2.0, 4.0) if "r" in WAY.lower() else ())):
-        lin("bw", a("bw", 8 * j, 8 * j + 8), a("j8"), w)
-    if BARE[1]:
+    fill(a("cv", 0, 128), 1.0 + 1 / 128)
+    fill(a("cv", 128, 256), 0.375 + 1 / 128)
+    fill(a("hz"), 0.0)
+    iota(a("hz", 0, 256, 1, 1), [[0, 2], [1, 128]], 0, 0)
+    for lo, hi in PH:
+        fill(a("hz", lo, hi, 1, 33, 32), 1040.0 + lo)
+    if max(BARE):
+        fill(a("oneb"), 1.0)
+        fill(a("cw"), -1.5 * U)
         lin("mko", a("mko"), a("mske", 0, 128), 2.0 * L, -3.0 * L)
+    for j, w in enumerate((16.0, -2.0, -4.0)):
+        lin("bw", a("bw", 8 * j, 8 * j + 8), a("j8"), w * K)
+    for j, w in ((1, -1.0), (2, 2.0)):
+        lin("bw2", a("bw", 24 * j, 24 * j + 24), a("bw", 0, 24), w)
     ts(a("pm"), a("pi"), 15, OP.bitwise_and)
-    cp(a("el"), a("ci", 0, 24))
+    cp(a("el"), a("ci", 0, 32))
     cp(a("ek"), a("ci", 40, 72))
-    tt(a("iw"), a("ci", 24, 40), a("pm"), OP.add)
-    lin("iu", a("iu", 16, 32), a("iw"), 8192, 592 - L)
-    lin("il", a("il"), a("t8"), 8192, 592 - L)
-    iota(a("bg"), [[8192, 256]], 8192 * GH[0] + C0, 0)
-    EX, e15 = ("ea", "eb"), a("el", 16, 24)
-    fcs, fus, XP = (a("fa", 0, 128), a("fb", 256, 384)), a("fa", 256, 512), (a("fb", 0, 128), a("eb", 256, 384))
-    mtwo, mone, five, four = a("row", 0, 128), a("row", 128, 256), a("row", 256, 384), a("row", 384, 512)
-    Y0 = (a("p3", 256, 384), a("pl", 256, 384))
-
-    def GF(last, ch):
-        return (256 * ch, 256 * ch + 128) if last else PH[ch]
-
-    def lists(t, lo, hi):
-        n, c, w, l8 = hi - lo, 2 * lo, a("w", lo, hi), (max(lo - 16, 0), hi - 16)
-        ts(a("wq", c, c + n), w, 13, OP.arith_shift_right, 1023, OP.bitwise_and)
-        ts(a("wq", c + n, c + 2 * n), w, 8191, OP.bitwise_and)
-        if hi > 16 and t < 4:
-            h = a("wq", c + n - l8[1] + l8[0], c + n)
-            tt(a("we", *l8), h, a("iw", *l8), OP.is_equal)
-            lin("wf%d" % (lo // 8 % 2), a("wf", *l8), a("we", *l8), 512)
-            tt(h, a("wf", *l8), h, OP.add)
-        if t == 4:
-            cp(a("gl", 256, 272), a("wq", 0, 16))
-            ts(a("gl", 288, 320), a("wq", 32, 64), -592, OP.add)
-            return
-        if ONE and not lo:
-            lin("gl00", a("f%d" % t, 0, 16), a("wq", 0, 16))
-            return
-        lin("gl%d%d" % (lo // 16, lo // 8 % 2), a("gl", 64 * t + c, 64 * t + c + 2 * n), a("wq", c, c + 2 * n))
+    tt(a("fq", 0, 16), a("ci", 16, 32), a("pm"), OP.add)
+    lin("iw", a("iw"), a("fq", 0, 16), 1, -15)
+    for ch in H:
+        lin("iu", a("iu", 16 * ch + 8, 16 * ch + 16), a("iw", 8 * ch, 8 * ch + 8), 8192, 592)
+    lin("il", a("il"), a("t8", 0, 16), 8192, 592)
+    iota(a("bg"), [[8192, 256]], 8192 * (GH[0] + 16) + C0, 0)
+    e15 = a("el", 16, 24)
+    E0, Y0, XP = ([a(b % ch, c, c + 128) for ch in H] for b, c in (("ea%d", 256), ("xa%d", 256), ("xa%d", 0)))
 
     def gl(t, x, k, ch):
-        c = 64 * t + (32 * k + 16 * x + 8 * ch if t == 4 else 32 + 16 * k + 8 * ch if x and JOIN else 32 * x + 16 * ch + 8 * k)
+        if t == 4:
+            c = 16 * ch + 8 * x + 32 * (1 - k)
+            return a("g0", c, c + 8)
+        c = 40 * (2 * t + ch) + ((0, 16, 32, 24) if JOIN[ch] else (0, 8, 16, 24))[2 * x + k]
         return a("gl", c, c + 8)
 
-    def hl(t, ch):
-        return gl(t, 1, 0, ch)
+    def lists(t, ch, xs):
+        n, c, b = 8 * len(xs), 32 * ch + 16 * xs[0], 40 * (2 * t + ch) + 16 * xs[0]
+        w = a("w", 16 * ch + 8 * xs[0], 16 * ch + 8 * xs[0] + n)
+        ts(a("wq", c, c + n), w, 13, OP.arith_shift_right, 511, OP.bitwise_and)
+        ts(a("wq", c + n, c + 2 * n), w, 8191, OP.bitwise_and)
+        if 0 in xs:
+            lin("glg%d" % ch, a("gl", b, b + 2 * n), a("wq", c, c + 2 * n))
+        if 1 in xs:
+            h, l8 = a("wq", c + n - 8, c + n), (8 * ch, 8 * ch + 8)
+            tt(a("we", *l8), h, a("iw", *l8), OP.is_equal)
+            lin("wf%d" % ch, a("wf", *l8), a("we", *l8), 512)
+            tt(h, a("wf", *l8), h, OP.add)
+            lin("glc%d" % ch, gl(t, 1, 0, ch) if 0 in xs else a("gl", b, b + 16), h if 0 in xs else a("wq", c, c + 16))
 
-    def rows(e, v, s, offs, way, more=0):
-        act(v, ind(a("skt" if way == 1 else "ski"), offs), AF.Identity, 1.0, float(more))
-        mm(e, a("idf"), v, False, way == 1)
-        if way > 1:
-            act(s, v, AF.Sign, 1.0, -4095.5 - more)
-            mms([(e, a("idk"), s, False, False), (e, a("idm"), s, False, True)])
+    def rows(e, v, s, offs, more=0):
+        act(v, ind(a("ski"), offs), AF.Identity, 1.0, float(more))
+        mm(e, a("idf"), v, False, False)
+        act(s, v, AF.Sign, 1.0, -4095.5 - more)
+        mms([(e, a("idk"), s, False, False), (e, a("idm"), s, False, True)])
 
     def clause_part(t, F, ch):
         lo, hi = PH[ch]
-        y, cl = a("p3", 256 + lo, 256 + hi), gl(t, 1, 1, ch)
+        y, cl = Y0[ch], gl(t, 1, 1, ch)
         if t == 4:
-            iota(a("hb", lo, hi), [[8192, 128]], 8192 * (1040 + lo) + C0, 0)
+            mm(y, a("k33"), a("hz", lo, hi), True, False)
+            rows(y, a("tc", lo, hi), a("dd", lo, hi), cl, C0)
         else:
-            act(a("hb", lo, hi), ind(a("tabb"), hl(t, ch)), AF.Identity, 8192.0, float(C0))
-        if t == 4 and TC0[ch]:
-            mm(Y0[ch], a("idf"), a("hb", lo, hi), True, False)
-            rows(Y0[ch], a("tc", lo, hi), a("sel", lo, hi), cl, TC0[ch])
-        elif "tc%d" % ch in ONS and t < 4:
-            act(a("key", lo, hi), ind(a("skt"), cl), AF.Identity)
-            mms([(y, a("idf"), a("hb", lo, hi), True, False), (y, a("idf"), a("key", lo, hi), False, True)])
-            act(a("tc", lo, hi), y, AF.Identity)
-        else:
-            tt(a("tc", lo, hi), ind(a("skt"), cl), a("hb", lo, hi), OP.add)
-        act(a("sa", lo, hi), Y0[ch] if t == 4 and TC0[ch] else a("tc", lo, hi), AF.Relu, -8.0, 16.0 * L)
-        if SB:
-            lin("sb%d" % (t == 4), a("sb", lo, hi), a(F, 16 + lo, 16 + hi), -1.0, 2.0 * L)
-            mm(XP[ch], a("idb"), a("sb", lo, hi), True, False)
-        else:
-            mms([(XP[ch], four, a("cu", 0, 128), True, False), (XP[ch], a("id2"), a(F, 16 + lo, 16 + hi), False, False)])
+            act(a("hb", lo, hi), ind(a("tabb"), gl(t, 1, 0, ch)), AF.Identity, 8192.0, float(C0))
+            if "tc%d" % ch in ONS:
+                act(a("key", lo, hi), ind(a("skt"), cl), AF.Identity)
+                mms([(y, a("idf"), a("hb", lo, hi), True, False), (y, a("idf"), a("key", lo, hi), False, True)])
+                act(a("tc", lo, hi), y, AF.Identity)
+            else:
+                tt(a("tc", lo, hi), ind(a("skt"), cl), a("hb", lo, hi), OP.add)
+                y = a("tc", lo, hi)
+        act(a("sa", lo, hi), y, AF.Relu, -8.0, 16.0 * L)
+        mms([(XP[ch], a("big", 0, 128, 1, 1), a("cv", 128 * (t == 4), 128 + 128 * (t == 4)), True, False),
+             (XP[ch], a("idx"), a("zz", lo, hi), False, False) if t == 4 else (XP[ch], a("id2"), a(F, lo, hi), False, False)])
         mm(XP[ch], a("idb"), a("sa", lo, hi), False, False)
 
-    def next_saved(sv, own):
+    def next_saved(sv, own, gs, cs):
         ts(a("s2"), a(sv), 8191, OP.bitwise_and)
         lin("s3", a("s3"), a("s2"), 1, -592)
-        lin("t7", a("t7"), a("s2", 16, 32), 1, -591)
-        tt(a("t4"), a("s3", 0, 16), a("s3", 16, 32), OP.mult)
-        ts(a("t5"), a("t4"), 5, OP.arith_shift_right, 4095, OP.bitwise_and)
-        tt(a("t6"), a("t5"), a("t7"), OP.add)
-        ts(a("t8"), a("t6"), 4095, OP.bitwise_and)
-        tt(a("mx", 16, 32), a("t8"), own, OP.add)
-        lin("mx", a("mx", 0, 16), a(sv, 0, 16), 1.0, -2.0 * L)
+        lin("t7", a("t7", *gs), a("s2", *cs), 1, -591)
+        tt(a("t4", *gs), a("s3", *gs), a("s3", *cs), OP.mult)
+        ts(a("t5", *gs), a("t4", *gs), 5, OP.arith_shift_right)
+        tt(a("t6", *gs), a("t5", *gs), a("t7", *gs), OP.add)
+        ts(a("t8", *gs), a("t6", *gs), 4095, OP.bitwise_and)
+        tt(a("mx", *cs), a("t8", *gs), own, OP.add)
 
     lin("inf", a("inf"), a("ini"))
+    lin("inb", a("inb"), a("ini", 128, 256))
     lin("id8", a("id8"), a("idf", 0, 16, 1, 16), 8192)
-    mms([(a("pl", 64 + 16 * (j // 2), 80 + 16 * (j // 2)), a("inf", 128 * j, 128 * j + 128), a("id8" if j == 1 else "idf", 0, 16, 1, 16), j != 1, j != 0) for j in range(3)])
-    lin("sh", a("sh"), a("pl", 64, 96))
+    mms([(a("xa1", 64 + 16 * (j // 2), 80 + 16 * (j // 2)), a("inf", 128 * j, 128 * j + 128), a("id8" if j == 1 else "idf", 0, 16, 1, 16), j != 1, j != 0) for j in range(3)])
+    lin("sh", a("sh"), a("xa1", 64, 96))
     for ch in H:
         tt(a("lh", 256 * ch, 256 * ch + 256), ind(a("sh"), a("ek", 16 * ch, 16 * ch + 16)), a("mske"), OP.mult)
-        mms([(a("pl", 16 * x + 8 * ch, 16 * x + 8 * ch + 8), a("lh", 256 * ch + 128 * x, 256 * ch + 128 * x + 128), a("j8"), True, True) for x in H])
-    tt(a("w"), a("iu"), a("pl", 0, 32), OP.add)
-    lin("sv", a("sv"), a("w"), 1, 2 * L)
-    lists(4, 0, 32)
+        mms([(a("xa1", 16 * ch + 8 * x, 16 * ch + 8 * x + 8), a("lh", 256 * ch + 128 * x, 256 * ch + 128 * x + 128), a("j8"), True, True) for x in H])
+    cp(a("fi"), a("xa1", 0, 32))
+    ts(a("wq", 0, 32), a("fi"), 8191, OP.bitwise_and)
+    ts(a("wq", 32, 64), a("fi"), 13, OP.arith_shift_right)
+    lin("g0", a("g0"), a("wq"))
+    tt(a("sv"), a("iu"), a("xa1", 0, 32), OP.add)
     ts(a("frs"), a("fri"), 511 + (1 << 21), OP.bitwise_and)
     ts(a("pc"), a("fri"), 9, OP.arith_shift_right)
-    lin("frs", a("p3", 0, 256), a("frs"), 8192.0, float(O))
-    tt(a("frm"), a("pc"), a("p3", 0, 256), OP.add)
+    lin("frs", a("xa0", 0, 256), a("frs"), 8192.0, float(O))
+    tt(a("frm"), a("pc"), a("xa0", 0, 256), OP.add)
     ts(a("f0", *OWN), a("frm"), 2 * L, OP.min)
-    lin("fu", a("fu"), a("f0", *OWN), 1.0, -float(L))
+    act(a("zz"), a("frm"), AF.Sign, 1.0, -1.5 * L)
+
     def table(lo, hi, bank):
         h = a(bank, 0, hi - lo)
         act(a("sks", lo, hi), a("ski", lo, hi), AF.Sign, 1.0, -4095.5)
@@ -361,55 +394,72 @@ def rank_program(g, core, T, topo):
         ts(a("thj", 0, 128, 1, r + 1, r), a("thi", 0, 128, 1, r + 1, r), m, OP.bitwise_and)
         for j, w in ((1, 1), (2, -1)):
             lin("crow", a("crow", 128 * j, 128 * j + 128, 1, r + 1, r), a("thj", 0, 128, 1, r + 1, r), 2, w * (r > 0))
-    next_saved("sv", a("iu", 16, 32))
+    next_saved("sv", a("iu", 8, 32), (0, 24), (8, 32))
+    for ch in H:
+        if JOIN[ch]:
+            lin("mx", a("mx", 16 * ch, 16 * ch + 8), a("sv", 16 * ch, 16 * ch + 8))
 
-    def cut(name, ch):
+    def places(ch, raw, m, p, q, pr, r, u):
         lo, hi = PH[ch]
-        return [(lo, lo + 64), (lo + 64, hi)] if name + str(ch) in SPLIT else [(lo, hi)]
+        if m == "ga" or not CQ[ch]:
+            ts(a(m, lo, hi), a(raw, lo, hi), L - 1, OP.bitwise_and)
+        c, d = (lo + x for x in SPLIT.get(u + str(ch), (128, 128)))
+        for w in ((lo, c), (c, hi))[:1 + (c < hi)]:
+            ts(a(q, *w), a(raw, *w), 13, OP.arith_shift_right, 1023, OP.bitwise_and)
+            ts(a(p, *w), a(raw, *w), 8191, OP.bitwise_and)
+        for w in ((lo, d), (d, hi))[:1 + (d < hi)]:
+            if q + str(ch) in ONS:
+                e = a("fa%d" % ch, 256 + 128 * (q == "qc") + w[0] - lo, 256 + 128 * (q == "qc") + w[1] - lo)
+                act(e, a(q, *w), AF.Identity)
+                tt(a(pr, *w), a(p, *w), e, OP.mult)
+            else:
+                tt(a(pr, *w), a(p, *w), a(q, *w), OP.mult)
+            ts(a(r, *w), a(pr, *w), 4, OP.arith_shift_right, 4095, OP.bitwise_and)
+            lin(u + str(ch), a(u, *w), a(r, *w))
 
-    def part(o, lo, hi):
-        return a(o[0], o[1] + lo % 128 // 16, o[1] + lo % 128 // 16 + (hi - lo) // 16)
-
-    def places(ch, w, raw, m, p, q, pr, r, u):
-        ts(a(q, *w), a(raw, *w), 13, OP.arith_shift_right, 1023, OP.bitwise_and)
-        ts(a(p, *w), a(raw, *w), 8191, OP.bitwise_and)
-        ts(a(m, *w), a(raw, *w), L - 1, OP.bitwise_and)
-        if q + str(ch) in ONS:
-            e = a("pl", 256 + w[0], 256 + w[1]) if q == "qg" else a("p3", 256 + w[0], 256 + w[1])
-            act(e, a(q, *w), AF.Identity)
-            tt(a(pr, *w), a(p, *w), e, OP.mult)
-        else:
-            tt(a(pr, *w), a(p, *w), a(q, *w), OP.mult)
-        ts(a(r, *w), a(pr, *w), 4, OP.arith_shift_right, 4095, OP.bitwise_and)
-        lin(u + str(ch), a(u, *w), a(r, *w))
-
-    def outputs(F, ch):
+    def outputs(ch):
         lo, hi = PH[ch]
         tt(a("w", ch, 32, 2), a("mx", ch, 32, 2), a("sum", 256 * ch + 15, 256 * ch + 256, 16), OP.max)
         if ch:
-            mm(a("pl", 0, 128, 1, 64), a("svy"), a("idf"), True, False)
-            ts(a("fi"), a("w"), 8191, OP.bitwise_and)
-            ts(a("fq"), a("w"), 13, OP.arith_shift_right, 1023, OP.bitwise_and)
-            ts(a("w2"), a("w"), 23, OP.arith_shift_right, 1, OP.bitwise_and)
-            ts(a("s2"), a("fi"), 512, OP.mult, -512 * 592 - 16, OP.add)
-            tt(a("sh", 0, 16), a("fq", 0, 16), a("svy", 32, 48), OP.subtract)
-            tt(a("svs", 16, 32), a("fi", 16, 32), a("sg1", 16, 32), OP.subtract)
-            tt(a("svs", 0, 16), a("s2", 0, 16), a("sh", 0, 16), OP.add)
-            tt(a("fim", 0, 32), a("s2"), a("fq"), OP.add)
-            tt(a("fim", 32, 64), a("svs"), a("w2"), OP.mult)
-            mm(a("pl", 0, 128, 1, 64), a("fim"), a("idf"), False, True)
-            cp(a("fot"), a("pl", 0, 128, 1, 64))
+            mm(a("d0", 0, 128, 1, 64), a("svy"), a("idf"), True, False)
+            if OUT:
+                ts(a("fi"), a("w"), 8191, OP.bitwise_and)
+                ts(a("flag", 16, 48), a("w"), 2 * U, OP.is_lt)
+                ts(a("wq", 0, 32), a("w"), 13, OP.arith_shift_right, 511, OP.bitwise_and)
+                lin("oa", a("flag", 0, 16), a("flag", 16, 32), 512)
+                lin("ob", a("fia", 0, 32), a("fi"), 512, -512 * 592)
+                tt(a("fim", 32, 64), a("old", 0, 32), a("flag", 16, 48), OP.mult)
+                mm(a("d0", 0, 128, 1, 64), a("fim"), a("idf"), False, False)
+                lin("oc", a("fib", 0, 32), a("wq", 0, 32))
+                tt(a("fib", 32, 48), a("wq", 0, 16), a("flag", 16, 32), OP.mult)
+                mm(a("d0", 0, 128, 1, 48), a("fib", 0, 48), a("idf"), False, False)
+                tt(a("fia", 48, 64), a("fi", 16, 32), a("flag", 32, 48), OP.mult)
+                tt(a("fia", 32, 48), a("fi", 0, 16), a("flag", 0, 16), OP.mult)
+                mm(a("d0", 0, 128, 1, 64), a("fia"), a("idf"), False, True)
+            else:
+                ts(a("fi"), a("w"), 8191, OP.bitwise_and)
+                ts(a("fq"), a("w"), 13, OP.arith_shift_right, 511, OP.bitwise_and)
+                ts(a("w2"), a("w"), 2 * U, OP.is_lt)
+                ts(a("s2"), a("fi"), 512, OP.mult, -512 * 592, OP.add)
+                tt(a("sh", 0, 16), a("fq", 0, 16), a("svy", 32, 48), OP.subtract)
+                tt(a("svs", 16, 32), a("fi", 16, 32), a("sg1", 16, 32), OP.subtract)
+                tt(a("svs", 0, 16), a("s2", 0, 16), a("sh", 0, 16), OP.add)
+                tt(a("fim", 0, 32), a("s2"), a("fq"), OP.add)
+                tt(a("fim", 32, 64), a("svs"), a("w2"), OP.mult)
+                mm(a("d0", 0, 128, 1, 64), a("fim"), a("idf"), False, True)
+            cp(a("fot"), a("d0", 0, 128, 1, 64))
             for j, y in enumerate((T.yg, T.yc, T.ysg, T.yk)):
                 dma("sy"[j % 2], ("!", y[:]), a("fot", 0, 128, 1, 16 * j + 16, 16 * j))
-        e = a("fa", 256 + lo, 256 + hi)
-        act(a("rs", lo, hi), ind(a("sum", 256 * ch, 256 * ch + 128), e15), AF.Relu, 128.0, -128.0 * L)
-        mm(e, a("rs", lo, hi), a("idb"))
-        tt(a("sa", lo, hi), a("fu", lo, hi), e, OP.is_gt)
+        e = a("fa%d" % ch, 128, 256)
+        mm(e, a("idb"), a("zz", lo, hi), True, False)
+        act(a("rs", lo, hi), ind(a("sum", 256 * ch, 256 * ch + 128), e15), AF.Sign, -1.0, 2.0 * U - 0.5)
+        mm(e, a("rs", lo, hi), a("idn"), False, True)
+        act(a("sa", lo, hi), e, AF.Relu, 0.5)
         ts(a("o2", lo, hi), a("oi", lo, hi), 8191, OP.bitwise_and)
         ts(a("oq", lo, hi), a("oi", lo, hi), 12, OP.arith_shift_right, 2046, OP.bitwise_and)
         act(a("o3", lo, hi), a("o2", lo, hi), AF.Identity, 1024.0, -1024.0 * 592)
         act(a("hb", lo, hi), a("oq", lo, hi), AF.Identity, 1.0, -32.0)
-        e = a(("eb", "d1")[ch], 0, 128)
+        e = XP[ch]
         mm(e, a("idf"), a("o3", lo, hi), True, False)
         mm(e, a("idf"), a("hb", lo, hi), False, False)
         mm(e, a("idb"), a("sa", lo, hi), False, True)
@@ -430,53 +480,49 @@ def rank_program(g, core, T, topo):
         B = "f%d" % max(t - 1, 0)
         for ch, (lo, hi) in enumerate(PH):
             up(t, "g%d" % ch)
-            if t == 0 and TG0[ch]:
-                e = a(GB0[ch], 256, 384)
-                lin("fc%d" % ch, a("sm", lo, hi), ind(a(F, 0, 272), gl(4, 0, 0, ch)))
-                mm(e, a("e16", lo, hi), a("inf", 128, 256), True, False)
-                rows(e, a("tg", lo, hi), a("clx", lo, hi), gl(4, 0, 1, ch), TG0[ch], 16 * 8192 + C0)
+            e = E0[ch]
+            if t == 0:
+                lin("fc%d" % ch, a("sm", lo, hi), ind(a(F, *OWN), gl(4, 0, 0, ch)))
+                mm(e, a("e16", lo, hi), a("inb"), True, False)
+                rows(e, a("tg", lo, hi), a("clx", lo, hi), gl(4, 0, 1, ch), 16 * 8192 + C0)
                 tt(a("rawg", lo, hi), a("sm", lo, hi), e, OP.min)
-            elif t == 0:
-                tt(a("tg", lo, hi), ind(a("skt"), gl(4, 0, 1, ch)), a("fb0", lo, hi), OP.add)
-                tt(a("rawg", lo, hi), ind(a(F, 0, 528), gl(4, 0, 0, ch)), a("tg", lo, hi), OP.min)
             else:
-                c, C = 32 * (t - 1) + 16 * ch, a("r%d" % (t - 1))
+                c, C = 32 * (2 * t - 2 + ch), a("r%d" % (t - 1))
+                fr, sk = a("arr", c, c + 8), a("arr", c + 8 + 8 * JOIN[ch], c + 16 + 8 * JOIN[ch])
                 up(t, "col%d" % ch)
-                act(a(F, 272 + lo, 272 + hi), ind(C, a("arr", c, c + 8)), AF.Identity)
+                act(a(F, 256 + lo, 256 + hi), ind(C, fr), AF.Identity)
                 up(t, "g%d" % ch)
                 if TG[ch]:
-                    e = a(("d0", "d1")[ch], 384, 512)
-                    act(a("tg", lo, hi), ind(a("skt"), a("arr", c + 8, c + 16)), AF.Identity)
+                    act(a("tg", lo, hi), ind(a("skt"), sk), AF.Identity)
                     mms([(e, a("idf"), a("bg", lo, hi), True, False), (e, a("idf"), a("tg", lo, hi), False, True)])
-                    tt(a("rawg", lo, hi), a(F, 272 + lo, 272 + hi), e, OP.min)
+                    if TG[ch] == 1:
+                        tt(a("rawg", lo, hi), a(F, 256 + lo, 256 + hi), e, OP.min)
+                    else:
+                        act(a("sm", lo, hi), e, AF.Identity)
+                        tt(a("rawg", lo, hi), ind(C, fr), a("sm", lo, hi), OP.min)
                 else:
-                    tt(a("tg", lo, hi), ind(a("skt"), a("arr", c + 8, c + 16)), a("bg", lo, hi), OP.add)
-            up(t, "g%d" % ch)
-            for w in cut("g", ch):
-                if t and not TG[ch]:
-                    tt(a("rawg", *w), ind(C, part(a("arr", c, c + 8), *w)), a("tg", *w), OP.min)
-                places(ch, w, "rawg", "ga", "pg", "qg", "prg", "rg", "ug")
+                    tt(a("tg", lo, hi), ind(a("skt"), sk), a("bg", lo, hi), OP.add)
+                    tt(a("rawg", lo, hi), ind(C, fr), a("tg", lo, hi), OP.min)
+            places(ch, "rawg", "ga", "pg", "qg", "prg", "rg", "ug")
         if not last:
             send(a("r%d" % t, *GH), a(F, *(GH if t else OWN)), to, "ag%d" % t)
         for j, (lo, hi) in enumerate(GCH):
             up(t, "u%d" % (lo // 1024), lo % 1024 / 730)
-            act(a("ub", lo, hi), ind(a("xr"), a("ug", lo // 16, hi // 16)), AF.Identity)
+            act(a("ub" if lo or WAYS.get(t, WAY)[0] != "m" else "um", lo, hi), ind(a("xr"), a("ug", lo // 16, hi // 16)), AF.Identity)
         for ch, (lo, hi) in enumerate(PH):
             up(t, "x%d" % ch)
-            lin("gaf%d" % ch, a("gaf", *GF(last, ch)), a("ga", lo, hi))
-            mm(XP[ch], a("idf"), a("gaf", *GF(last, ch)), False, True)
-            tt(a(F, 528 + lo, 528 + hi), a(B, 16 + lo, 16 + hi), XP[ch], OP.min)
+            lin("gaf%d" % ch, a("gaf", 2 * lo, 2 * lo + 128), a("ga", lo, hi), 1, -16 * 8192)
+            mm(XP[ch], a("idf"), a("gaf", 2 * lo, 2 * lo + 128), False, True)
+            tt(a(F, 512 + lo, 512 + hi), a(B, lo, hi), XP[ch], OP.min)
             up(t, "c%d" % ch)
-            for w in cut("c", ch):
-                if t:
-                    tt(a("rawc", *w), ind(a(F, 0, 528 + hi), part(hl(t - 1, ch), *w)), a("tc", *w), OP.min)
-                else:
-                    y = Y0[ch]
-                    tt(a("rawc", *w), a(F, 528 + w[0], 528 + w[1]), a(y[0], y[1] + w[0] - lo, y[1] + w[1] - lo) if TC0[ch] else a("tc", *w), OP.min)
-                places(ch, w, "rawc", "ca", "pc", "qc", "prc", "rc", "uc")
+            if t:
+                tt(a("rawc", lo, hi), ind(a(F, 0, 512 + hi), gl(t - 1, 1, 0, ch)), a("tc", lo, hi), OP.min)
+            else:
+                tt(a("rawc", lo, hi), a(F, 512 + lo, 512 + hi), Y0[ch], OP.min)
+            places(ch, "rawc", "ca", "pc", "qc", "prc", "rc", "uc")
         if t == 0:
             step[1] = None
-            for c, bank in zip(SKP[len(SKP) - DEF:], ("pl", "eb", "p3")):
+            for c, bank in zip(SKP[len(SKP) - DEF:], PARK):
                 table(c[0], c[1], bank)
                 prog[-3]["extra"], prog[-2]["extra"], prog[-1]["extra"] = START + FILL, START + FILL, START + 10.5
         way = WAYS.get(t, WAY)
@@ -484,146 +530,127 @@ def rank_program(g, core, T, topo):
         for w, lo, hi in pieces:
             up(t, "w4" if hi == 4096 else "w%d" % (lo // 1024), lo % 1024 / 730)
             if w == "s":
-                e = a(SWB[way.lower()[:lo // 512].count("s") % 2], lo % 512, lo % 512 + hi - lo)
+                e = a("ea%d" % (lo // 2048), lo % 512, lo % 512 + hi - lo)
                 act(a("df", lo, hi), ind(a("xr"), a("uc", lo // 16, hi // 16)), AF.Identity)
                 mms([(e, a("idn"), a("ub", lo, hi), True, False), (e, a("idb"), a("df", lo, hi), False, True)])
                 act(a("ab", lo, hi), e, AF.Abs)
-                continue
-            tt(a("df", lo, hi), ind(a("xr"), a("uc", lo // 16, hi // 16)), a("ub", lo, hi), OP.subtract)
+            elif w == "m":
+                act(a("df", lo, hi), ind(a("xr"), a("uc", lo // 16, hi // 16)), AF.Identity)
+            elif lo // 512 not in WIDE:
+                lo -= 512 * (lo // 512 - 1 in WIDE)
+                tt(a("df", lo, hi), ind(a("xr"), a("uc", lo // 16, hi // 16)), a("ub", lo, hi), OP.subtract)
         for w, lo, hi in pieces:
             up(t, "a4" if hi == 4096 else "a%d" % (lo // 1024), lo % 1024 / 730)
             if w == "r":
-                ts(a("ab", lo, hi), a("df", lo, hi), 0, OP.max, 2, OP.mult)
+                ts(a("ab", lo, hi), a("df", lo, hi), 0, OP.max)
             elif w == "b":
                 act(a("ab", lo - 512, hi), a("df", lo - 512, hi), AF.Abs)
             elif w == "a" and way[hi // 512:hi // 512 + 1] != "b":
                 act(a("ab", lo, hi), a("df", lo, hi), AF.Abs)
+        for j, lo, hi in folds(t):
+            up(t, "a%d" % ((hi - 1) // 1024), (hi - 1) % 1024 / 730)
+            fold(a("ab", lo, hi), [a("df", lo, hi), a("um", 0, hi - lo) if way[j] == "m" and j == 0 else a("ub", lo, hi) if way[j] == "m" else a("um", 512, 512 + hi - lo)], "h%d" % j)
         for ch in H:
             up(t, "d%d" % ch)
-            D = ("d0", "d1")[ch]
-            mm(fcs[ch], a("idf"), a("fu", *PH[ch]), True, False)
-            mm(a(D, 0, 384), a("oneb", 0, 128, 1, 33), a("crow"), True, False)
+            D = "d%d" % ch
+            mm(a("fa%d" % ch, 0, 128), a("idu"), a("zz", *PH[ch]), True, False)
+            mm(a(D, 0, 384), a("big"), a("crow"), True, False)
             for l0, h0 in LATE[ch]:
-                for x, lo, hi in [("df",) + r for r in runs([j for j in range(l0 // 32, h0 // 32) if way[4 * ch + j] in "rR"])] + [("ab", l0, h0)]:
+                todo = [(x, c) + r for x, c, ws in (("ub", 24, "m"), ("df", 24, "rRfgm"), ("ab", 48, "rR"[2 * ONCE:]), ("ab", 0, "aAbs"), ("ab", 48, "fgm" + "rR" * ONCE))
+                        for r in runs([j for j in range(l0 // 32, h0 // 32) if way[4 * ch + j] in ws])]
+                for x, c, lo, hi in todo:
+                    x = "um" if (x, ch, lo) == ("ub", 0, 0) else x
                     for k0 in range(0, 16, MK):
-                        mms([(a(D, k, 384, 16, hi, lo), a(x, 2048 * ch + 16 * lo + k, 2048 * ch + 16 * hi, 16), a("bw", 24 * (x == "df"), 24 + 24 * (x == "df")), False,
+                        mms([(a(D, k, 384, 16, hi, lo), a(x, 2048 * ch + 16 * lo + k, 2048 * ch + 16 * hi, 16), a("bw", c, c + 24), False,
                               k == 15 and x == "ab") for k in range(k0, k0 + MK)])
         for ch, (lo, hi) in enumerate(PH):
-            D = ("d0", "d1")[ch]
-            R = a(D, 384, 512)
+            D, FA, EA = "d%d" % ch, "fa%d" % ch, "ea%d" % ch
             s1, s2 = a("sg", 2 * lo, 2 * lo + 128), a("sg", 2 * lo + 128, 2 * lo + 256)
-            fast, bare = FAST[2] if last else FAST[ch], BARE[ch] and not last
+            gc = [(2 * lo + 128 * x, 2 * lo + 128 * x + 128) for x in H]
+            EX = (a(EA, 0, 128), a("xa%d" % ch, 384, 512))
             up(t, "f%d" % ch)
-            act(s1 if ch or S2 else a("sg", 0, 256), a(D, 128, 256 if ch or S2 else 384), AF.Sign)
+            act(s1 if S2[ch] else a("sg", 2 * lo, 2 * lo + 256), a(D, 128, 256 if S2[ch] else 384), AF.Sign)
             scan(a("cnt", lo, hi), a("rstb"), s1, OP.mult, OP.add)
             act(a("clx", lo, hi), ind(a("cnt", lo, hi), e15), AF.Sign, -1.0, a("lim", ch, ch + 1), a("par", ch, ch + 1) if PAR and not last else None)
-            mm(fcs[ch], a("clx", lo, hi), a("idu"), False, True)
-            tt(a("oi", lo, hi) if last else a(F, 16 + lo, 16 + hi), a(F, 528 + lo, 528 + hi), fcs[ch], OP.max)
-            if not last and (ch or not ONE):
-                send(a("r%d" % t, 16 + lo, 16 + hi), a(F, 16 + lo, 16 + hi), to, "ao%d" % (2 * t + ch))
-            if ch == 0 and not last:
-                up(t, "fu")
-                mm(fus, five, a("cu"), True, False)
-            up(t, "m%d" % ch)
-            tt(a("key", lo, hi), s1, a(D, 0, 128), OP.mult)
-            if ch or S2:
-                act(s2, a(D, 256, 384), AF.Sign)
-            scan(a("sm", lo, hi), a("rsb"), a("key", lo, hi), OP.add, OP.max)
-            tt(a("sel", lo, hi), ind(a("sm", lo, hi), e15), a("key", lo, hi), OP.not_equal)
-            if last:
-                up(t, "l%d" % ch)
-                c, b = 256 * ch, ("ea", "d0")[ch]
-                lin("caf%d" % ch, a("gaf", c + 128, c + 256), a("ca", lo, hi))
-                mm(a(b, 0, 256), mone, a("cu"), True, False)
-                for x in H:
-                    mm(a(b, 128 * x, 128 * x + 128), a("gaf", c + 128 * x, c + 128 * x + 128), a("idf"), False, False)
-                for w, y in ((a("idx"), a("clx", lo, hi)), (a("ids"), s2), (a("idw"), a("sel", lo, hi))):
-                    mms([(a(b, 128 * x, 128 * x + 128), w, y, False, w[0] == "idw" and x == 1) for x in H])
-                scan(a("sum", c, c + 256), a("rst"), a(b, 0, 256), OP.add, OP.max)
-            for x in range(0 if last else fast):
-                up(t, "lj"[x] + str(ch))
-                e, c = a(GE[ch] if not x else EX[x], lo, hi), ((256 * ch + 128 * x, 256 * ch + 128 * x + 128) if last else (256 * x + lo, 256 * x + hi))
-                if x:
-                    lin("caf%d" % ch, a("gaf", *c), a("ca", lo, hi))
-                mm(e, mone, a("cu", 0, 128), True, False)
-                mm(e, a("gaf", *c), a("idf"), False, False)
-                if bare and not x:
-                    mm(e, a("idl"), a("clx", lo, hi), False, False)
-                    mm(e, a("idw"), a("sel", lo, hi), False, True)
-                    scan(a("sum", *c), a("rstb"), e, OP.mult, OP.max)
-                else:
-                    mm(e, a("idx"), a("clx", lo, hi), False, False)
-                    mm(e, a("ids"), s2, False, False)
-                    mm(e, a("idw"), a("sel", lo, hi), False, True)
-                    scan(a("sum", *c), a("rst", 0, 128), e, OP.add, OP.max)
-                if not last:
-                    tt(a("lh", *c), ind(a("sum", *c), e15), a("mske", 0, 128), OP.mult)
-            up(t, "m%d" % ch)
-            if fast < 2:
-                mms([(R, a("oneb", 0, 128, 1, 1), a("oneb", 0, 128, 1, 1), True, False), (R, a("sel", lo, hi), a("idn"), False, True)])
+            mm(a(FA, 0, 128), a("clx", lo, hi), a("idu"), False, True)
+            tt(a("oi", lo, hi) if last else a(F, lo, hi), a(F, 512 + lo, 512 + hi), a(FA, 0, 128), OP.max)
             if not last:
-                e = a("p3", lo, hi)
-                mm(e, s2, a("idh"), True, False)
-                mm(e, a("clx", lo, hi), a("idc"), False, False)
-                mm(e, a("sel", lo, hi), a("id4"), False, True)
-                act(a("rs", lo, hi), e, AF.Relu, 1.0, 0.5)
-            for x in H[fast:]:
-                tt(a("pgc", 256 * x + lo, 256 * x + hi), a(("ga", "ca")[x], lo, hi), R, OP.mult)
+                send(a("r%d" % t, lo, hi), a(F, lo, hi), to, "ao%d" % (2 * t + ch))
+            up(t, "m%d" % ch)
+            key = a(KB[ch], 128, 256) if S2[ch] else a(D, 384, 512)
+            cuts = ((0, 64), (64, 128)) if PS[ch] else ((0, 128),)
+
+            def sub(o, c):
+                return a(o[0], o[1] + c[0], o[1] + c[1])
+            for c in cuts:
+                tt(sub(key, c), sub(s1, c), a(D, *c), OP.mult)
+            if S2[ch]:
+                act(s2, a(D, 256, 384), AF.Sign)
+            for c in cuts:
+                scan(a("sm", lo + c[0], lo + c[1]), a("rsb", *c), sub(key, c), OP.add, OP.max)
+            for c in cuts:
+                tt(a("dd", lo + c[0], lo + c[1]), a("sm", lo + c[0], lo + c[1]), sub(key, c), OP.subtract)
             for x in H:
                 up(t, "lj"[x] + str(ch))
-                c, e, st = 256 * x + lo, a(EX[ch], 8 * x, 8 * x + 8) if last else a(EX[x], lo, hi), 16 if last else 1
-                if x >= fast:
-                    mm(e, mtwo, a("cu", 0, 128, st), True, False)
-                    mm(e, a("pgc", c, c + 128), a("go", 0, 128, st), False, False)
-                    mm(e, a("rs", lo, hi), a("gou", 0, 128, st), False, True)
-                if last:
+                if x and CQ[ch]:
+                    act(a("gaf", *gc[x]), a("qc", lo, hi), AF.Identity, 8192.0, -16.0 * 8192)
+                    act(a("key", lo, hi), a("pc", lo, hi), AF.Identity)
+                elif x:
+                    lin("caf%d" % ch, a("gaf", *gc[x]), a("ca", lo, hi), 1, -16 * 8192)
+                mm(EX[x], a("gaf", *gc[x]), a("idf"), True, False)
+                if x and CQ[ch]:
+                    mm(EX[x], a("key", lo, hi), a("idf"), False, False)
+                mm(EX[x], a("idx"), a("clx", lo, hi), False, False)
+                bare = BARE[ch] and not last and not x
+                mm(EX[x], *((a("oneb"), a("cw")) if bare else (a("ids"), s2)), False, False)
+                mm(EX[x], a("idn"), a("dd", lo, hi), False, True)
+                scan(a("sum", *gc[x]), a("dd", lo, hi), EX[x], OP.min, OP.max)
+                if last or (JOIN[ch] and not x):
                     continue
-                if x >= fast:
-                    tt(a("lh", c, c + 128), a("mske", 0, 128), e, OP.mult)
-                if bare and not x:
-                    e, y, c, d = a("d0", 128, 256), a("pl", 8 * ch, 8 * ch + 8), 64 * t + 16 * ch, 32 * t + 16 * ch
-                    up(t, "z%d" % ch)
-                    act(a("svx"), ind(a("sv", 8 * ch, 8 * ch + 8), a("el", 0, 8)), AF.Identity, 1.0, -float(L))
-                    mms([(e, a("svx"), a("idf"), True, False), (e, a("idb"), a("mko"), False, False)])
-                    up(t, "l%d" % ch)
+                if bare:
+                    e, y, c, d = a("d0", 0, 128), a(EA, 384, 392), 40 * (2 * t + ch), 32 * (2 * t + ch)
+                    up(t, "b%d" % ch)
+                    act(a("key", 0, 128), ind(a("sv", 16 * ch, 16 * ch + 8), a("el", 0, 8)), AF.Identity)
+                    mms([(e, a("key", 0, 128), a("idf"), True, False), (e, a("idb"), a("mko"), False, False)])
                     mm(e, a("idu"), a("clx", lo, hi), False, True)
-                    act(a("svz"), e, AF.Relu)
-                    mm(y, a("svz"), a("j8"), True, False)
-                    mm(y, a("lh", lo, hi), a("j8"), False, True)
+                    act(a("key", 128, 256), e, AF.Relu)
+                    mm(y, a("key", 128, 256), a("j8"), True, False)
+                    up(t, "l%d" % ch)
+                    tt(a("lh", *gc[0]), ind(a("sum", *gc[0]), e15), a("mske", 0, 128), OP.mult)
+                    mm(y, a("lh", *gc[0]), a("j8"), False, True)
                     lin("gq", a("gl", c, c + 8), y, 1 / 8192, -591.5 / 8192)
                     send(a("arr", d, d + 8), a("gl", c, c + 8), to, "al%d" % (2 * t + ch))
                     up(t, "p%d" % ch)
-                    lin("gw", a("w", 8 * ch, 8 * ch + 8), y)
-                    ts(a("wq", 8, 16), a("w", 8 * ch, 8 * ch + 8), 8191, OP.bitwise_and)
-                    lin("gp", a("gl", c + 8, c + 16), a("wq", 8, 16))
+                    lin("gw", a("w", 16 * ch, 16 * ch + 8), y)
+                    ts(a("wq", 32 * ch + 8, 32 * ch + 16), a("w", 16 * ch, 16 * ch + 8), 8191, OP.bitwise_and)
+                    lin("gp", a("gl", c + 8, c + 16), a("wq", 32 * ch + 8, 32 * ch + 16))
                     send(a("arr", d + 8, d + 16), a("gl", c + 8, c + 16), to, "ap%d" % (2 * t + ch))
                     continue
-                mm(a(LB[2 * ch + x], 16 * x + 8 * ch, 16 * x + 8 * ch + 8), a("lh", c, c + 128), a("j8"))
-                if x and JOIN and not ch:
-                    continue
-                chs = H if x and JOIN else (ch,)
-                c = (16 * x + 8 * chs[0], 16 * x + 8 * ch + 8)
-                tt(a("w", *c), a("mx", *c), a(LB[2 * ch + x], *c), OP.max)
-                lists(t, *c)
-                if ONE and not x and not ch:
-                    send(a("r%d" % t, 0, 144), a(F, 0, 144), to, "ao%d" % (2 * t))
-                    lin("arr", a("arr", 32 * t, 32 * t + 16), a("r%d" % t, 0, 16))
-                elif not x:
-                    c = 64 * t + 16 * ch
-                    send(a("arr", 32 * t + 16 * ch, 32 * t + 16 * ch + 16), a("gl", c, c + 16), to, "al%d" % (2 * t + ch))
+                xs = H if JOIN[ch] else (x,)
+                c, n = gc[xs[0]][0], len(xs)
+                tt(a("lh", c, c + 128 * n), ind(a("sum", c, c + 128 * n), a("el", 16, 16 + 8 * n)), a("mske", 0, 128 * n), OP.mult)
+                mms([(a(EA, 384 + 8 * y, 392 + 8 * y), a("lh", *gc[y]), a("j8"), True, True) for y in xs])
+                c = (16 * ch + 8 * xs[0], 16 * ch + 8 * x + 8)
+                tt(a("w", *c), a("mx" if x else "sv", *c), a(EA, 384 + 8 * xs[0], 392 + 8 * x), OP.max)
+                lists(t, ch, xs)
+                if not xs[0]:
+                    c, d = 40 * (2 * t + ch), 32 * (2 * t + ch)
+                    send(a("arr", d, d + 8 + 8 * n), a("gl", c, c + 8 + 8 * n), to, "al%d" % (2 * t + ch))
             if last:
                 up(t, "o%d" % ch)
-                outputs(F, ch)
+                outputs(ch)
                 continue
-            up(t, "fu")
-            mm(a("fa", 256 + lo, 256 + hi), a("gon"), a("rs", lo, hi), False, False)
+            up(t, "z%d" % ch)
+            e = a(FA, 128, 256)
+            act(a("rs", lo, hi), ind(a("sum", *gc[BARE[ch]]), e15), AF.Sign, -1.0, 2.0 * U - 0.5)
+            mm(e, a("idu"), a("zz", lo, hi), True, False)
+            mm(e, a("idf"), a(F, lo, hi), False, False)
+            mm(e, a("rs", lo, hi), a("idx"), False, True)
+            act(a("zz", lo, hi), e, AF.Sign, 1.0, -1.25 * L)
 
         if last:
             break
-        for lo, hi in PH:
-            mm(a("fa", 256 + lo, 256 + hi), a("idf"), a(F, 528 + lo, 528 + hi), False, lo > 0)
-        for lo, hi in PH if FU2 else ((0, 256),):
-            tt(a("fu", lo, hi), a("fu", lo, hi), a("fa", 256 + lo, 256 + hi), OP.min)
+        up(t, "z1")
         dma("y", a("f%d" % (t + 1), *OWN), a(F, *OWN), 2.8)
         for ch in H:
             up(t, "k%d" % ch)
@@ -638,27 +665,37 @@ def rank_program(g, core, T, topo):
             prod(a("lim", ch, ch + 1), a("clx", lo, hi, 16))
         for ch in H:
             if BARE[ch]:
-                ts(a("wl"), a("w", 16 + 8 * ch, 24 + 8 * ch), L, OP.is_ge, L, OP.mult)
-                tt(a("w", 8 * ch, 8 * ch + 8), a("w", 8 * ch, 8 * ch + 8), a("wl"), OP.add)
-        ts(a("w2"), a("w"), 2 * L - 1, OP.bitwise_and)
-        lin("sg2", a("sg1"), a("w2"), -16, 16 * L)
-        tt(a("sh"), a("sv"), a("sg1"), OP.min)
-        tt(a("sv"), a("w2"), a("sh"), OP.max)
+                ts(a("wl"), a("w", 16 * ch + 8, 16 * ch + 16), 2 * U, OP.bitwise_and)
+                tt(a("w", 16 * ch, 16 * ch + 8), a("w", 16 * ch, 16 * ch + 8), a("wl"), OP.add)
+        ts(a("w2"), a("w"), 3 * U - 1, OP.bitwise_and)
+        lin("sg2", a("sg1"), a("w"), -2048, 4096 * U)
+        tt(a("sh"), a("sv"), a("sg1"), OP.max)
+        tt(a("sv"), a("w2"), a("sh"), OP.min)
         if t < RO - 2:
-            next_saved("sv", a("iu", 16, 32))
-            continue
-        for x in H:
-            tt(a("lh", 256 * x, 256 * x + 256), ind(a("sv", 16 * x, 16 * x + 16), a("el", 0, 16)), a("mske"), OP.mult)
+            next_saved("sv", a("iu", 8, 32), (0, 24), (8, 32))
             for ch in H:
-                c = 256 * x + 128 * ch
-                mm(a("pl", 32 + 16 * x + ch, 48 + 16 * x, 2), a("lh", c, c + 128), a("j8"))
-        lin("svs", a("svs"), a("pl", 32, 64))
-        next_saved("svs", a("il"))
-        ts(a("fq"), a("svs"), 13, OP.arith_shift_right, 1023, OP.bitwise_and)
-        lin("fi", a("fi", 0, 16), a("s3", 0, 16), 512, -16)
+                if JOIN[ch]:
+                    lin("mx", a("mx", 16 * ch, 16 * ch + 8), a("sv", 16 * ch, 16 * ch + 8))
+            continue
+        up(t, "sl")
+        for ch in H:
+            tt(a("lh", 256 * ch, 256 * ch + 256), ind(a("sv", 16 * ch, 16 * ch + 16), a("el", 0, 16)), a("mske"), OP.mult)
+            for x in H:
+                c = 256 * ch + 128 * x
+                mm(a("fa1", 256 + 16 * x + ch, 272 + 16 * x, 2), a("lh", c, c + 128), a("j8"))
+        lin("svs", a("svs"), a("fa1", 256, 288))
+        next_saved("svs", a("il"), (0, 16), (16, 32))
+        lin("mx", a("mx", 0, 16), a("svs", 0, 16))
+        ts(a("fq"), a("svs"), 13, OP.arith_shift_right, 511, OP.bitwise_and)
+        lin("fi", a("fi", 0, 16), a("s3", 0, 16), 512)
         tt(a("svy", 32, 48), a("fi", 0, 16), a("fq", 0, 16), OP.add)
         lin("svy", a("svy", 48, 64), a("s3", 16, 32))
-        lin("svy", a("sg1", 16, 32), a("s2", 16, 32))
+        if OUT:
+            lin("old", a("old", 0, 16), a("svy", 32, 48), -1, -512 * 592)
+            lin("old", a("old", 16, 32), a("s2", 16, 32), -1)
+            fill(a("fim", 0, 32), 0.0)
+        else:
+            lin("svy", a("sg1", 16, 32), a("s2", 16, 32))
 
     lg, n = {}, len(prog)
     dep = [[] for _ in range(n)]
@@ -668,15 +705,19 @@ def rank_program(g, core, T, topo):
             ds[e[3]] = WAKE.get(prog[e[3]]["q"] + p["q"], WAKE[prog[e[3]]["q"]])
         if p["kind"] == "n":
             ds[p["extra"][2]] = 0.0
-        note(q, p["acc"], lg, i)
+        if p["kind"] != "f":
+            note(q, p["acc"], lg, i)
         dep[i] = sorted(ds.items())
     dur, lat, qs = [p["dur"] for p in prog], [p["lat"] for p in prog], [p["q"] for p in prog]
     before, after = [[(d, w + lat[d]) for d, w in dep[i]] for i in range(n)], [[] for _ in range(n)]
     for i in range(2, len(LD)):
         before[i].append((i - 2, 0.0))
+    above = [0] * n
     for i in range(n):
+        before[i] = [(d, w) for d, w in before[i] if not any(above[e] >> d & 1 and w <= dur[e] + x for e, x in before[i])]
         for d, w in before[i]:
             after[d].append((i, w))
+            above[i] |= above[d] | 1 << d
 
     def pack(order, needs, head):
         done, busy = [0.0] * n, {q: [] for q in Q}
@@ -694,246 +735,6 @@ def rank_program(g, core, T, topo):
                 b.insert(lo, (t0, t0 + dur[i]))
             done[i] = t0 + dur[i]
         return done
-
-    def improve(order, seed, heat, steps):
-        prev, last = [-1] * n, {}
-        for i in order:
-            if qs[i] != "net":
-                prev[i], last[qs[i]] = last.get(qs[i], -1), i
-        done, rest, pos = [0.0] * n, [0.0] * n, [0] * n
-        best, arcs, nxt = (1e9, order), None, {prev[i]: i for i in range(n) if prev[i] >= 0}
-        for turn in range(steps + 1):
-            whole = turn % STAY == 0 or turn == steps
-            if whole:
-                seed = (seed * 1103515245 + 12345) % 2147483648
-                first = min(max((seed >> 8) % (n + WIDE // 2) - WIDE * 3 // 4, 0), n - WIDE)
-                arcs, lo, hi = None, 0, n
-            if arcs is None:
-                for i in order[lo:n if whole else first + WIDE]:
-                    t0 = done[prev[i]] if prev[i] >= 0 else 0.0
-                    for d, w in before[i]:
-                        if done[d] + w > t0:
-                            t0 = done[d] + w
-                    done[i] = t0 + dur[i]
-                for k in range(hi - 1, -1 if whole else first - 1, -1):
-                    i = order[k]
-                    t0 = max(lat[i], rest[nxt[i]] if i in nxt else 0.0)
-                    for d, w in after[i]:
-                        if rest[d] + w > t0:
-                            t0 = rest[d] + w
-                    rest[i] = t0 + dur[i]
-                for k in range(lo, hi):
-                    pos[order[k]] = k
-                part = order[first:first + WIDE]
-                span = max(done[i] - dur[i] + rest[i] for i in part)
-                arcs = [j for j in part if prev[j] >= 0 and pos[prev[j]] >= first and done[prev[j]] + rest[j] > span - NEAR]
-                if whole and max(rest) < best[0]:
-                    best = (max(rest), list(order), list(done))
-            if not arcs:
-                continue
-            seed = (seed * 1103515245 + 12345) % 2147483648
-            j = arcs[(seed >> 8) % len(arcs)]
-            i, q, far = prev[j], qs[j], (seed >> 20) % (8 if seed >> 28 else FAR)
-            if far % 2:
-                for _ in range(far // 2):
-                    i = prev[i] if prev[i] >= 0 and pos[prev[i]] >= first else i
-                seg, move = order[pos[i]:pos[j] + 1], {j}
-                for k in reversed(seg):
-                    if k in move:
-                        move.update(d for d, w in before[k])
-                        if qs[k] != q:
-                            move.add(prev[k])
-                if i in move:
-                    continue
-                seg = [k for k in seg if k in move] + [k for k in seg if k not in move]
-            else:
-                for _ in range(far // 2):
-                    j = nxt[j] if j in nxt and pos[nxt[j]] < first + WIDE else j
-                seg, move = order[pos[i]:pos[j] + 1], {i}
-                for k in seg:
-                    if k in move:
-                        move.update(d for d, w in after[k])
-                        if qs[k] != q:
-                            move.add(nxt.get(k, -1))
-                if j in move:
-                    continue
-                seg = [k for k in seg if k not in move] + [k for k in seg if k in move]
-            p2, d2, r2, c, b = {}, {}, {}, prev[i], pos[j]
-            for k in seg:
-                if qs[k] == q:
-                    p2[k], c = c, k
-                e = p2.get(k, prev[k])
-                t0 = d2.get(e, done[e]) if e >= 0 else 0.0
-                for d, w in before[k]:
-                    e = d2.get(d, done[d]) + w
-                    if e > t0:
-                        t0 = e
-                d2[k] = t0 + dur[k]
-            if j in nxt:
-                p2[nxt[j]] = c
-            c, s2, more = nxt.get(j, -1), 0.0, 0.0
-            for k in reversed(seg):
-                if qs[k] == q:
-                    e, c = c, k
-                else:
-                    e = nxt.get(k, -1)
-                t0 = max(lat[k], r2.get(e, rest[e]) if e >= 0 else 0.0)
-                for d, w in after[k]:
-                    e = r2.get(d, rest[d]) + w
-                    if e > t0:
-                        t0 = e
-                r2[k] = t0 + dur[k]
-                e = d2[k] + t0 - span
-                if e > s2:
-                    s2 = e
-                more += math.exp(min(e, 5.0) / SOFT) - math.exp((done[k] - dur[k] + rest[k] - span) / SOFT)
-            seed = (seed * 1103515245 + 12345) % 2147483648
-            e = (1 - turn / steps) * (seed >> 8 & 1023) ** 2 / 1048576
-            if s2 <= heat * e + 1e-9 and more <= 12 * heat * e:
-                lo, hi, arcs = pos[i], b + 1, None
-                order[lo:hi] = seg
-                for k in p2:
-                    nxt.pop(k, 0) if k in d2 else 0
-                for k in p2:
-                    prev[k] = p2[k]
-                    nxt[p2[k]] = k
-                nxt.pop(-1, 0)
-        return best
-
-    def circle(end, cut, seed, heat):
-        ids = {prog[i]["id"]: i for i in range(n) if prog[i]["id"]}
-        names = [k[1:] for k in ids if k[0] == 2]
-        m, num = len(names), {k: j for j, k in enumerate(names)}
-        span = end[(2,) + names[0]] - end[(1,) + names[0]]
-        back = [math.ceil((end[(2,) + k] - cut) / span - 1e-9) for k in names]
-        needs = [(num[prog[d]["id"][1:]], j, 2 - prog[d]["id"][0], w) for j, k in enumerate(names) for d, w in before[ids[(2,) + k]] if prog[d]["id"] and prog[d]["id"][1:] in num]
-        for _ in range(3):
-            for i, j, s, w in needs:
-                back[j] = max(back[j], back[i] - s)
-        now, old = [[] for _ in names], [[] for _ in names]
-        for i, j, s, w in needs:
-            if s + back[j] - back[i] < 2:
-                (old if s + back[j] - back[i] else now)[j].append((i, w))
-        later = [[] for _ in names]
-        for j in range(m):
-            for i, w in now[j]:
-                later[i].append((j, w))
-        du, qu = [dur[ids[(2,) + k]] for k in names], [qs[ids[(2,) + k]] for k in names]
-        done = [end[(2,) + names[j]] - back[j] * span for j in range(m)]
-        for _ in range(m):
-            for j in range(m):
-                done[j] = max([done[j]] + [done[i] + du[j] + 1e-6 for i, w in now[j]])
-        order = sorted(range(m), key=lambda j: (done[j] - du[j], j))
-
-        newer = [[] for _ in names]
-        for j in range(m):
-            for i, w in old[j]:
-                newer[i].append((j, w))
-        rest, pos, prev, nxt = [0.0] * m, [0] * m, [-1] * m, [-1] * m
-        best, arcs = (1e9, order, done), None
-        for turn in range(ROUND + 1):
-            if arcs is None:
-                last = {}
-                for k, j in enumerate(order + order):
-                    if qu[j] not in ("net", "y"):
-                        prev[j], last[qu[j]] = last.get(qu[j], -1), j
-                        nxt[prev[j]] = j
-                    pos[j] = k - m
-                for _ in range(2 if turn else 8):
-                    was = sum(done)
-                    for j in order:
-                        e = prev[j]
-                        t0 = -1e9 if e < 0 else done[e] if pos[e] < pos[j] else done[e] - span
-                        for d, w in now[j]:
-                            if done[d] + w > t0:
-                                t0 = done[d] + w
-                        for d, w in old[j]:
-                            if done[d] + w - span > t0:
-                                t0 = done[d] + w - span
-                        done[j] = t0 + du[j]
-                    span += (sum(done) - was) / m
-                    for j in reversed(order):
-                        e = nxt[j] if prev[j] >= 0 else -1
-                        t0 = -99.0 if e < 0 else rest[e] if pos[e] > pos[j] else rest[e] - span
-                        for d, w in later[j]:
-                            if rest[d] + w > t0:
-                                t0 = rest[d] + w
-                        for d, w in newer[j]:
-                            if rest[d] + w - span > t0:
-                                t0 = rest[d] + w - span
-                        rest[j] = t0 + du[j]
-                top = max(done[j] - du[j] + rest[j] for j in range(m))
-                arcs = [j for j in order if prev[j] >= 0 and pos[prev[j]] < pos[j] and done[prev[j]] + rest[j] > top - NEAR]
-                if span < best[0] and abs(sum(done) - was) < 0.005 * m and turn >= ROUND * LEAVE:
-                    best = (span, list(order), list(done))
-            seed = (seed * 1103515245 + 12345) % 2147483648
-            j = arcs[(seed >> 8) % len(arcs)]
-            i, q, far = prev[j], qu[j], (seed >> 20) % (8 if seed >> 28 else FAR)
-            if far % 2:
-                for _ in range(far // 2):
-                    i = prev[i] if pos[prev[i]] < pos[i] else i
-                seg, move = order[pos[i]:pos[j] + 1], {j}
-                for k in reversed(seg):
-                    if k in move:
-                        move.update(d for d, w in now[k])
-                        if qu[k] != q:
-                            move.add(prev[k])
-                if i in move:
-                    continue
-                seg = [k for k in seg if k in move] + [k for k in seg if k not in move]
-            else:
-                for _ in range(far // 2):
-                    j = nxt[j] if pos[nxt[j]] > pos[j] else j
-                seg, move = order[pos[i]:pos[j] + 1], {i}
-                for k in seg:
-                    if k in move:
-                        move.update(d for d, w in later[k])
-                        if qu[k] != q and prev[k] >= 0:
-                            move.add(nxt[k])
-                if j in move:
-                    continue
-                seg = [k for k in seg if k not in move] + [k for k in seg if k in move]
-            d2, r2 = {}, {}
-            c = done[prev[i]] - span * (pos[prev[i]] > pos[i])
-            for k in seg:
-                e = prev[k]
-                t0 = c if qu[k] == q else -1e9 if e < 0 else d2.get(e, done[e]) if pos[e] < pos[k] else done[e] - span
-                for d, w in now[k]:
-                    e = d2.get(d, done[d]) + w
-                    if e > t0:
-                        t0 = e
-                for d, w in old[k]:
-                    if done[d] + w - span > t0:
-                        t0 = done[d] + w - span
-                d2[k] = t0 + du[k]
-                if qu[k] == q:
-                    c = d2[k]
-            c, s2, more = rest[nxt[j]] - span * (pos[nxt[j]] < pos[j]), 0.0, 0.0
-            for k in reversed(seg):
-                e = nxt[k] if prev[k] >= 0 else -1
-                t0 = c if qu[k] == q else -99.0 if e < 0 else r2.get(e, rest[e]) if pos[e] > pos[k] else rest[e] - span
-                for d, w in later[k]:
-                    e = r2.get(d, rest[d]) + w
-                    if e > t0:
-                        t0 = e
-                for d, w in newer[k]:
-                    if rest[d] + w - span > t0:
-                        t0 = rest[d] + w - span
-                r2[k] = t0 + du[k]
-                if qu[k] == q:
-                    c = r2[k]
-                e = d2[k] + t0 - top
-                if e > s2:
-                    s2 = e
-                more += math.exp(min(e, 5.0) / SOFT) - math.exp((done[k] - du[k] + rest[k] - top) / SOFT)
-            seed = (seed * 1103515245 + 12345) % 2147483648
-            e = (seed >> 8 & 1023) ** 2 / 1048576
-            if s2 <= heat * e + 1e-9 and more <= 12 * heat * e:
-                order[pos[i]:pos[j] + 1] = seg
-                arcs = None
-        span, order, was = best if best[0] < 1e9 else (span, order, done)
-        top = max(was)
-        return span, {(2,) + names[j]: was[j] - top + cut + back[j] * span for j in range(m)}
 
     seed, tops = [SEED], []
 
@@ -1104,14 +905,26 @@ def rank_program(g, core, T, topo):
         span, at = min(tops + [best])
         SPANS.append([round(x[0], 2) for x in tops])
         SPANS.append(round(span, 2))
-        for i, p in enumerate(prog):
-            if not p["id"]:
-                due[i] = max([min(due[i], START)] + [due[d] + 1e-6 + dur[i] - dur[d] for d, w in before[i]])
-            else:
-                e = at[num[p["id"][1:]]] - at[num["u0", 0]] + p["id"][0] * span + START if p["id"][1:] in num else 0.0
-                due[i] = max([e] + [due[d] + w if e < START + GAP else due[d] - dur[d] + 1e-6 for d, w in before[i]]) + dur[i]
-        order = sorted(range(n), key=lambda i: (due[i] - dur[i], i))
-        if FILL:
+        key, end = [0.0] * n, START + RO * span + TAIL
+        for i in range(n - 1, -1, -1):
+            k = prog[i]["id"]
+            mine = at[num[k[1:]]] - at[num["u1", "sub0"]] + 1.5 + k[0] * span + START if k and k[1:] in num else prog[i]["extra"] if prog[i]["kind"] == "c" else None
+            key[i] = min([key[j] - w - dur[i] for j, w in after[i]] + [mine or end - prio[i]])
+        order, tries = sorted(range(n), key=lambda i: (key[i], i)), []
+        for _ in range(3):
+            due = pack(order, before, [0.0] * n)
+            tries.append((max(due), sorted(range(n), key=lambda i: (due[i] - dur[i], i))))
+            back = pack(sorted(range(n), key=lambda i: (-due[i], -i)), after, lat)
+            order = sorted(range(n), key=lambda i: (-back[i], i))
+        order = min(tries)[1]
+        if MAP:
+            due = pack(sorted(range(n), key=lambda i: (-prio[i], i)), before, [0.0] * n)
+            for i, p in enumerate(prog):
+                if not p["id"]:
+                    due[i] = max([min(due[i], START)] + [due[d] + 1e-6 + dur[i] - dur[d] for d, w in before[i]])
+                else:
+                    e = at[num[p["id"][1:]]] - at[num["u1", "sub0"]] + 1.5 + p["id"][0] * span + START if p["id"][1:] in num else 0.0
+                    due[i] = max([e] + [due[d] + w if e < START + GAP else due[d] - dur[d] + 1e-6 for d, w in before[i]]) + dur[i]
             key = [due[i] - dur[i] for i in range(n)]
             for i, p in enumerate(prog):
                 key[i] = max([p["extra"] if p["kind"] == "c" and p["extra"] else key[i]] + [key[d] + 1e-6 for d, w in before[i]])
@@ -1182,12 +995,12 @@ def rank_program(g, core, T, topo):
             nd[0] += 1
             inst.then_inc(T.sem[sem], 16)
             cnt[sem] = 16
-        elif p["kind"] == "r":
-            sem = "rl"
+        elif p["kind"] in "rf":
+            sem = "rl" if p["kind"] == "r" else "rf"
             cnt[sem] = cnt.get(sem, 0) + p["extra"][1]
         else:
             sem = p["extra"][0]
-            cnt[sem] = p["extra"][1]
+            cnt[sem] = cnt.get(sem, 0) + p["extra"][1]
         ref[i] = (sem, cnt[sem])
         if p["kind"] != "n":
             snap[ref[i]] = dict(know[q])

import math
from concourse.bass import DstId, RemoteDMATransfer
from concourse.mybir import AluOpType, ActivationFunctionType, AxisListType

OP = AluOpType
AF = ActivationFunctionType
U, L, O, K = 1 << 22, 1 << 23, 16 * 8192 + 592, float(1 << 24)
Z = float(1 << 42)
C0 = 592 - 2048 - L // 2
RO, N = 5, 4
H = (0, 1)
F32, BF, I32, U16 = "float32", "bfloat16", "int32", "uint16"
SCRATCH = {}


def _bufs(where, dtype, text):
    for w in text.split():
        n, c = w.split(":")
        r, c = (c.split("x") if "x" in c else (128, c))
        SCRATCH[n] = (where, [int(r), int(c)], dtype)


_bufs("sbuf", F32, "skt:4688 tabb:768 bg:256 j8:8 rsb:128 onef:128 e8:8x128 m16:16x128 inf:16x384 id8:16x16 gaf:512 sum:512 "
      "iw:16 iu:32 il:16 lim:8 par:8 hb:256 tg:256 tc:256 key:256 sm:256 lh:512 we:16 wf:16 svy:64 sg1:32 sh:32 mx:32 "
      "fim:64 fot:64x128 oz:256 ft:5888 fia:64 fib:64 old:48 flag:48")
_bufs("sbuf", BF, "idk:128 idm:128 idn:128 xr:4096 ub:4096 df:4096 ab:4096 um:1536 bw:72 idb:128 idh:128 big:33x128 k33:33x128 hz:33x256 e16:16x256 inb:16x128 cv:1x256 oneb:1x128 cw:1x128 mko:128 crow:33x384 idw:128 "
      "idu:128 idz:128 ids:128 idx:128 rstb:128 sg:512 cnt:256 dd:256 rs:256 clx:256 sa:512 zz:256")
_bufs("sbuf", I32, "ski:4096 ini:16x384 fri:256 thi:33x128 thj:33x128 pi:16 ci:72 pm:16 rawg:256 rawc:256 ga:256 ca:256 sv:32 svs:32 "
      "pg:256 qg:256 prg:256 rg:256 pc:256 qc:256 prc:256 rc:256 w:32 w2:32 wq:64 s2:32 s3:32 t4:32 t5:32 t6:32 t7:32 t8:32 fi:32 fq:32 oi:256 wl:8")
_bufs("sbuf", U16, "ug:256 uc:256 el:32 ek:32 gl:320 g0:64 arr:256")
_bufs("psum", F32, "d0:512 d1:512 fa0:512 fa1:512 ea0:512 ea1:512 xa0:512 xa1:512")
SEMAPHORES = ["sv", "ss", "st", "sg", "rl", "rf"] + [n + str(t) for n in ("al", "ao", "ag", "ap", "h") for t in range(8)] + ["d%d" % t for t in range(40)]
VIEW = {"sks": ("df", 0, 4096), "frs": ("oi", 0, 256), "frm": ("oz", 0, 256), "o2": ("pg", 0, 256), "oq": ("qg", 0, 256), "o3": ("tg", 0, 256),
        "idf": ("skt", 0, 128), "id2": ("skt", 128, 128), "mske": ("skt", 256, 256)}
for _t in range(RO):
    VIEW["f%d" % _t], VIEW["r%d" % _t] = ("ft", 1280 * _t, 768), ("ft", 1280 * _t + 768, 512)
PSUM = [n for n in SCRATCH if SCRATCH[n][0] == "psum"]
OWN, GH, F3 = (0, 256), (256, 512), (512, 768)
PH = [(0, 128), (128, 256)]
GCH = [(c, c + 512) for c in range(0, 4096, 512)]
WAY, WAYS, ONCE = "mrrraaaA", {}, 1
MK, S2, TG, JOIN, OUT, PAR, KB = 4, (0, 1), (0, 0), (0, 0), 0, 1, ("xa1", "d0")
DEF, BANKS, PARK = 3, ("d0", "d1", "fa0"), ("fa0", "fa1", "ea1")
SKP = [(c, c + 512) for c in range(0, 4096, 512)]
SKL = [(0, 512), (512, 1536), (1536, 2560), (2560, 3584), (3584, 4096)]
SPLIT, PS, WIDE, BARE, CQ = {}, (0, 0), (), (0, 0), (0, 0)
THI = 9
LATE = (((0, 128),), ((0, 64), (64, 96), (96, 128)))
ONS = ("gaf", "ug0", "glg0", "inb", "svs", "svy", "fi", "s3", "t7", "ug1", "mx", "caf", "uc1", "inf", "idu", "ids", "idx", "idz", "sg2", "wf", "glc", "mske", "idw", "idh", "sb", "bw", "t5")
CYC, CG, FIX, GFIX, SFIX, PEC, PFIX = 0.0009, 1.45, 0.02, 0.06, 0.05, 0.00056, 0.015
WAKE = {"v": 0.16, "vv": 0.22, "s": 0.24, "t": 0.3, "tt": 0.0, "g": 0.1, "y": 0.2, "net": 0.2, "vg": 0.3}
RI, RL, RB, RF, R1 = 0.45, 1.1, 0.4, 2.3, 1.5
T0, PERIOD, START, FILL = 8.0, 17.6, 11.5, -2.0
EARLY, TAIL, MAP, GAP = 5, 0.0, 1, 12.0
DUE = {"g0": 5.0, "col0": 5.0, "col1": 5, "u0": 7.3, "u1": 8.7, "c0": 6.0, "g1": 7.0, "x0": 6.0, "x1": 8.5, "w0": 9.9, "w1": 11.3, "c1": 12.7, "u2": 10.2, "a0": 11.6,
       "w2": 14.0, "a1": 12.8, "u3": 13.7, "d0": 10, "w3": 15, "a2": 15.5, "f0": 16, "m0": 16, "w4": 15.7, "a3": 16, "a4": 16.7, "d1": 10, "f1": 18, "m1": 18,
       "l0": 17, "l1": 18, "j0": 18, "j1": 21, "k0": 20.5, "k1": 21, "z0": 22, "z1": 22, "sv": 22, "o0": 17, "o1": 18, "b1": 17, "p1": 18, "sl": 22}
PLAN = []
SPANS, SEED, REST = [], 4, 10
KICK, LOOSE, SHAKE, STRETCH, CALM = 10, 0.08, 1.2, 6.0, 10
SOFT, WEIGH, NEAR, FAR, SOME, STRAY = 0.4, 0.025, 0.03, 20, 4, 0.35
ROUND, CUTS, STAY, STEPS, PART = 300, 220, 1200, 135, 45
TURNS = ((6, (0, 0, 170), (0.08, 0.16, 180), (0.03, 0.1, 180), (0.15, 0.25, 180)), (1, (1, 1, 130), (0.86, 0.95, 150), (1, 1, 100), (0.75, 0.85, 180), (0.9, 1, 120)),
         (1, (0.2, 0.8, 200), (0, 0.2, 200), (0.8, 1, 150)))


def folds(t):
    out = []
    for j, w in enumerate(WAYS.get(t, WAY)):
        if w in "fm":
            out.append((j, 512 * j, 512 * j + 512))
        elif w == "g":
            out[-1] = (out[-1][0], out[-1][1], 512 * j + 512)
    return out


def hand_back(g, core, to, T, topo):
    rid, pid, _ = topo.addr(to)
    n, m, got, sent = len(topo.engines(to, core)), len(topo.engines(core, to)), {}, 0
    for t in range(RO):
        for j, lo, hi in folds(t):
            got[j] = got.get(j, 0) + n
            g.wait_ge(T.sem["h%d" % j], got[j])
            g.remote_dma(T["ab"][:, lo:hi], T["ab"][:, lo:hi], T.sem["h%d" % j], T.sem["rl"], pid, rid, topo.mask(core, to))
            sent += m
    if sent:
        g.wait_ge(T.sem["rl"], sent)


def rank_program(g, core, T, topo):
    rank = T.rank_of(core)
    near = {}
    for c in T.cores:
        near[c] = [h for h in topo.cores_of(c) if T.rank_of(h) is None and topo.die(h) == topo.die(c) and h not in near.values()][0]
    if rank is None:
        for c in T.cores:
            if near[c] == core:
                hand_back(g, core, c, T, topo)
        return
    Q = {"v": g.vector, "s": g.scalar, "t": g.tensor, "g": g, "y": g.sync}
    SEM = {"v": "sv", "s": "ss", "t": "st", "g": "sg"}
    know = {q: {} for q in Q}
    cnt, snap, nd = {}, {}, [0]
    prog, step, seen = [], [None, None], {}

    def a(n, lo=0, hi=None, st=1, r=None, r0=0):
        if n in VIEW:
            b, c, w = VIEW[n]
            return a(b, c + lo, c + (w if hi is None else hi), st, r, r0)
        return (n, lo, SCRATCH[n][1][1] if hi is None else hi, st, r0, SCRATCH[n][1][0] if r is None else r)

    def ind(w, o):
        return ("@", w, o)

    def ap(o):
        if not isinstance(o, tuple):
            return o
        if o[0] == "@":
            return ap(o[1]).indirect(ap(o[2]))
        if o[0] == "!":
            return o[1]
        b = T[o[0]]
        return b[o[4]:o[5], o[1]:o[2]] if o[3] == 1 else b[o[4]:o[5], o[1]:o[2]:o[3]]

    def parts(o):
        return [o[1], o[2]] if o[0] == "@" else [] if o[0] == "!" else [o]

    def flat(reads, writes):
        return [(k, p) for k, ops in (("r", reads), ("w", writes)) for o in ops if isinstance(o, tuple) for p in parts(o)]

    def size(o):
        return (o[2][2] - o[2][1]) * 16 if o[0] == "@" else (o[2] - o[1] + o[3] - 1) // o[3]

    def meets(q, acc, lg):
        for kind, (n, lo, hi, st, r0, r1) in acc:
            for e in lg.get(n, []):
                if n in PSUM and e[4] != q:
                    yield e
                elif lo < e[1] and e[0] < hi and r0 < e[6] and e[5] < r1 and "w" in (kind, e[2]):
                    yield e
                elif n in PSUM and q == "t" and kind == "w" and e[2] == "w":
                    yield e

    def note(q, acc, lg, ref):
        for kind, (n, lo, hi, st, r0, r1) in acc:
            old = lg.get(n, [])
            if kind == "w":
                old = [e for e in old if (q != "t" if n in PSUM and e[4] != q else not (st == 1 and lo <= e[0] and e[1] <= hi and r0 <= e[5] and e[6] <= r1))]
            lg[n] = old + [(lo, hi, kind, ref, q, r0, r1)]

    def add(q, call, reads, writes, dur, lat=0.0, kind="c", extra=None):
        k = step[1] and step[1] + (q + "".join(p[0] for c, p in flat([], writes)[:1]),)
        seen[k] = seen.get(k, -1) + 1
        prog.append({"due": step[0], "id": k and k[:2] + (k[2] + str(seen[k]),), "q": q, "call": call, "acc": flat(reads, writes), "dur": dur, "lat": lat,
                     "kind": kind, "extra": extra})

    def up(t, name, more=0.0):
        step[0], step[1] = T0 + PERIOD * t + DUE[name] + more, (t, name)

    def vcost(o, ins, two=False):
        n = max(size(x) for x in ins)
        if any(x[0] == "@" for x in ins):
            return GFIX + CYC * CG * n
        f = 2.0 if two and not any(x[0] in PSUM for x in ins) else 1.0
        if not two and all(SCRATCH[x[0]][2] in (BF, U16) for x in ins + [o]):
            f = 0.5
        return FIX + CYC * max(64, n * f)

    def tt(o, x, y, op):
        add("v", lambda: g.vector.tensor_tensor(ap(o), ap(x), ap(y), op), [x, y], [o], vcost(o, [x, y], True))

    def ts(o, x, s1, op0, s2=None, op1=None):
        def call():
            if op1 is None:
                return g.vector.tensor_scalar(ap(o), ap(x), s1, None, op0)
            return g.vector.tensor_scalar(ap(o), ap(x), s1, s2, op0, op1)
        add("v", call, [x], [o], vcost(o, [x]))

    def cp(o, x):
        add("v", lambda: g.vector.tensor_copy(ap(o), ap(x)), [x], [o], vcost(o, [x]))

    def fill(o, c):
        add("v", lambda: g.vector.memset(ap(o), c), [], [o], vcost(o, [o]))

    def scan(o, d0, d1, op0, op1):
        add("v", lambda: g.vector.tensor_tensor_scan(ap(o), ap(d0), ap(d1), 0.0, op0, op1), [d0, d1], [o], vcost(o, [d0, d1]))

    def prod(o, x):
        add("v", lambda: g.vector.tensor_reduce(ap(o), ap(x), AxisListType.X, OP.mult), [x], [o], FIX + CYC * 64)

    def act(o, x, func, scale=1.0, bias=0.0, acc=None):
        add("s", lambda: g.scalar.activation(ap(o), ap(x), func, ap(bias), scale, accum_out=ap(acc)), [x, bias], [o, acc],
            0.065 + CYC * CG * size(x) if x[0] == "@" else SFIX + CYC * max(64, size(x)))

    def lin(name, o, x, scale=1.0, bias=0.0):
        if name in ONS or name.rstrip("01") in ONS:
            act(o, x, AF.Identity, float(scale), float(bias))
        elif bias:
            ts(o, x, scale, OP.mult, bias, OP.add)
        elif scale != 1:
            ts(o, x, scale, OP.mult)
        else:
            cp(o, x)

    def mms(ms):
        add("t", lambda: [g.tensor.matmul(ap(o), ap(l), ap(r), s0, s1) for o, l, r, s0, s1 in ms][-1], [x for m in ms for x in m[1:3]], [m[0] for m in ms],
            sum(PFIX + PEC * (4 if SCRATCH[l[0]][2] == F32 else 1) * max(min(64, size(l)), size(r)) for o, l, r, s0, s1 in ms))

    def mm(o, l, r, start=True, stop=True):
        mms([(o, l, r, start, stop)])

    def iota(o, pat, base, cmul):
        def call():
            if SCRATCH[o[0]][2] == I32:
                return g.iota(ap(o), pat, base, cmul)
            return g.iota(ap(o), pat, base, cmul, allow_small_or_imprecise_dtypes=True)
        add("g", call, [], [o], 0.14 + 2 * CYC * size(o))

    def pick(o, x, pat, op, base, cmul):
        add("g", lambda: g.affine_select(ap(o), ap(x), pat, op, 0.0, base, cmul), [x], [o], 0.18 + 2 * CYC * size(o))

    def dma(q, out, in_, lat=2.0):
        add(q, lambda: Q[q].dma_start(ap(out), ap(in_)), [in_], [out], 0.1, lat, "d")

    def send(dst, src, to, rsem):
        def call():
            rid, pid, _ = topo.addr(to)
            g.remote_dma(ap(dst), ap(src), T.sem[rsem], T.sem["rl"], pid, rid, topo.mask(core, to))
        add("g", call, [src], [], RI + RB * size(dst) / 256 + (2.0 if rsem == "ag0" else 0.0), 0.0, "r", (rsem, len(topo.engines(core, to))))
        add("net", None, [], [dst], 0.0, RL, "n", (rsem, len(topo.engines(core, to)), len(prog) - 1))

    def fold(dst, srcs, rsem):
        to = near[core]

        def call():
            rid, pid, _ = topo.addr(to)
            g.remote_dma_fused([RemoteDMATransfer(dst_ids=[DstId(rid=rid, pnc=pid)], dma_engine_mask=topo.mask(core, to), remote_sem=T.sem[rsem],
                                                  srcs=[ap(x) for x in srcs], dsts=[ap(dst)], alu_op=2)], local_sem=T.sem["rf"])
        add("g", call, srcs, [dst], RI + RB * size(dst) / 512, 0.0, "f", (rsem, len(topo.engines(core, to))))
        add("net", None, srcs, [dst], 0.0, RF + RB * size(dst) / 512 + (0.0 if any(p["kind"] == "f" for p in prog[:-1]) else R1), "n", (rsem, len(topo.engines(to, core)), len(prog) - 1))

    LD = [(a("ini", 128 * j, 128 * j + 128), y[:], 0.06) for j, y in enumerate((T.gs, T.gf, T.gcl))] + [(a("fri"), T.fr[:], 0.45)]
    LD += [(a("ski", lo, hi), T.sk[:, lo:hi], 0.2 + 0.5 * (hi - lo) / 512) for lo, hi in SKL]
    LD += [(a("xr", 592, 4096), T.x[:, 0:3504], 1.9), (a("xr", 0, 592), T.x[:, 3504:4096], 0.5)]
    LD[THI:THI] = [(a("thi", 0, 128, 1, r + 1, r), T.th[:], 0.06) for r in (0, 32)]
    came = 0.0
    for j, (o, src, us) in enumerate(LD):
        came += us
        dma("ys"[j % 2], o, ("!", src), 2.2 + came - 0.05 * j)
    fill(a("onef"), 1.0)
    pick(a("idf"), a("onef"), [[-1, 128]], OP.is_equal, 0, 1)
    pick(a("m16"), a("onef", 0, 128, 1, 16), [[0, 8], [1, 16]], OP.is_equal, 0, -1)
    pick(a("e8"), a("onef", 0, 128, 1, 8), [[1, 8], [0, 16]], OP.is_equal, 0, -1)
    fill(a("k33"), 8192.0)
    for ch in H:
        pick(a("e16", *PH[ch]), a("k33", 0, 128, 1, 16), [[2, 8], [0, 16]], OP.is_equal, ch, -1)
    iota(a("pi"), [[0, 16]], 0, 1)
    iota(a("ci", 0, 16), [[1, 16]], 0, 0)
    iota(a("ci", 16, 32), [[16, 16]], 15, 0)
    iota(a("ci", 40, 72), [[1, 2], [2, 16]], 0, 0)
    iota(a("tabb", 0, 512), [[1, 512]], 16, 0)
    iota(a("tabb", *F3), [[1, 256]], 1024 + 16, 0)
    iota(a("t8", 0, 16), [[0, 8], [128, 2]], 0, 1)
    for n, lo, hi, st, c in (("skt", 512, 592, 1, 0), ("lim", 0, 8, 1, 1), ("big", 0, 128, 1, K), ("rstb", 0, 128, 1, 1), ("rstb", 0, 128, 16, 0),
                             ("rsb", 0, 128, 1, 0), ("rsb", 0, 128, 16, -K * (1 << 20)), ("iu", 0, 32, 1, 592), ("svy", 0, 32, 1, 0)):
        fill(a(n, lo, hi, st), float(c))
    if any(w in WAYS.get(t, WAY) for t in range(RO) for w in "fg"):
        fill(a("um", 512, 1024 + 512 * any("fg" in WAYS.get(t, WAY) for t in range(RO))), 0.0)
    mm(a("ea0", 128, 136), a("e8"), a("idf", 0, 8, 1, 8))
    mm(a("ea1", 0, 128), a("m16"), a("m16"))
    lin("j8", a("j8"), a("ea0", 128, 136))
    for ch in H:
        lin("mske", a("mske", *PH[ch]), a("ea1", 0, 128))
    for n, w in (("idb", 1.0), ("idn", -1.0), ("idk", 1.5 * L), ("idm", -2048.0), ("idu", float(L)), ("ids", -0.5 * U), ("idx", -1.5 * U), ("id2", -1.0)):
        lin(n, a(n), a("idf"), w)
    fill(a("cv", 0, 128), 1.0 + 1 / 128)
    fill(a("cv", 128, 256), 0.375 + 1 / 128)
    fill(a("hz"), 0.0)
    iota(a("hz", 0, 256, 1, 1), [[0, 2], [1, 128]], 0, 0)
    for lo, hi in PH:
        fill(a("hz", lo, hi, 1, 33, 32), 1040.0 + lo)
    if max(BARE):
        fill(a("oneb"), 1.0)
        fill(a("cw"), -1.5 * U)
        lin("mko", a("mko"), a("mske", 0, 128), 2.0 * L, -3.0 * L)
    for j, w in enumerate((16.0, -2.0, -4.0)):
        lin("bw", a("bw", 8 * j, 8 * j + 8), a("j8"), w * K)
    for j, w in ((1, -1.0), (2, 2.0)):
        lin("bw2", a("bw", 24 * j, 24 * j + 24), a("bw", 0, 24), w)
    ts(a("pm"), a("pi"), 15, OP.bitwise_and)
    cp(a("el"), a("ci", 0, 32))
    cp(a("ek"), a("ci", 40, 72))
    tt(a("fq", 0, 16), a("ci", 16, 32), a("pm"), OP.add)
    lin("iw", a("iw"), a("fq", 0, 16), 1, -15)
    for ch in H:
        lin("iu", a("iu", 16 * ch + 8, 16 * ch + 16), a("iw", 8 * ch, 8 * ch + 8), 8192, 592)
    lin("il", a("il"), a("t8", 0, 16), 8192, 592)
    iota(a("bg"), [[8192, 256]], 8192 * (GH[0] + 16) + C0, 0)
    e15 = a("el", 16, 24)
    E0, Y0, XP = ([a(b % ch, c, c + 128) for ch in H] for b, c in (("ea%d", 256), ("xa%d", 256), ("xa%d", 0)))

    def gl(t, x, k, ch):
        if t == 4:
            c = 16 * ch + 8 * x + 32 * (1 - k)
            return a("g0", c, c + 8)
        c = 40 * (2 * t + ch) + ((0, 16, 32, 24) if JOIN[ch] else (0, 8, 16, 24))[2 * x + k]
        return a("gl", c, c + 8)

    def lists(t, ch, xs):
        n, c, b = 8 * len(xs), 32 * ch + 16 * xs[0], 40 * (2 * t + ch) + 16 * xs[0]
        w = a("w", 16 * ch + 8 * xs[0], 16 * ch + 8 * xs[0] + n)
        ts(a("wq", c, c + n), w, 13, OP.arith_shift_right, 511, OP.bitwise_and)
        ts(a("wq", c + n, c + 2 * n), w, 8191, OP.bitwise_and)
        if 0 in xs:
            lin("glg%d" % ch, a("gl", b, b + 2 * n), a("wq", c, c + 2 * n))
        if 1 in xs:
            h, l8 = a("wq", c + n - 8, c + n), (8 * ch, 8 * ch + 8)
            tt(a("we", *l8), h, a("iw", *l8), OP.is_equal)
            lin("wf%d" % ch, a("wf", *l8), a("we", *l8), 512)
            tt(h, a("wf", *l8), h, OP.add)
            lin("glc%d" % ch, gl(t, 1, 0, ch) if 0 in xs else a("gl", b, b + 16), h if 0 in xs else a("wq", c, c + 16))

    def rows(e, v, s, offs, more=0):
        act(v, ind(a("ski"), offs), AF.Identity, 1.0, float(more))
        mm(e, a("idf"), v, False, False)
        act(s, v, AF.Sign, 1.0, -4095.5 - more)
        mms([(e, a("idk"), s, False, False), (e, a("idm"), s, False, True)])

    def clause_part(t, F, ch):
        lo, hi = PH[ch]
        y, cl = Y0[ch], gl(t, 1, 1, ch)
        if t == 4:
            mm(y, a("k33"), a("hz", lo, hi), True, False)
            rows(y, a("tc", lo, hi), a("dd", lo, hi), cl, C0)
        else:
            act(a("hb", lo, hi), ind(a("tabb"), gl(t, 1, 0, ch)), AF.Identity, 8192.0, float(C0))
            if "tc%d" % ch in ONS:
                act(a("key", lo, hi), ind(a("skt"), cl), AF.Identity)
                mms([(y, a("idf"), a("hb", lo, hi), True, False), (y, a("idf"), a("key", lo, hi), False, True)])
                act(a("tc", lo, hi), y, AF.Identity)
            else:
                tt(a("tc", lo, hi), ind(a("skt"), cl), a("hb", lo, hi), OP.add)
                y = a("tc", lo, hi)
        act(a("sa", lo, hi), y, AF.Relu, -8.0, 16.0 * L)
        mms([(XP[ch], a("big", 0, 128, 1, 1), a("cv", 128 * (t == 4), 128 + 128 * (t == 4)), True, False),
             (XP[ch], a("idx"), a("zz", lo, hi), False, False) if t == 4 else (XP[ch], a("id2"), a(F, lo, hi), False, False)])
        mm(XP[ch], a("idb"), a("sa", lo, hi), False, False)

    def next_saved(sv, own, gs, cs):
        ts(a("s2"), a(sv), 8191, OP.bitwise_and)
        lin("s3", a("s3"), a("s2"), 1, -592)
        lin("t7", a("t7", *gs), a("s2", *cs), 1, -591)
        tt(a("t4", *gs), a("s3", *gs), a("s3", *cs), OP.mult)
        ts(a("t5", *gs), a("t4", *gs), 5, OP.arith_shift_right)
        tt(a("t6", *gs), a("t5", *gs), a("t7", *gs), OP.add)
        ts(a("t8", *gs), a("t6", *gs), 4095, OP.bitwise_and)
        tt(a("mx", *cs), a("t8", *gs), own, OP.add)

    lin("inf", a("inf"), a("ini"))
    lin("inb", a("inb"), a("ini", 128, 256))
    lin("id8", a("id8"), a("idf", 0, 16, 1, 16), 8192)
    mms([(a("xa1", 64 + 16 * (j // 2), 80 + 16 * (j // 2)), a("inf", 128 * j, 128 * j + 128), a("id8" if j == 1 else "idf", 0, 16, 1, 16), j != 1, j != 0) for j in range(3)])
    lin("sh", a("sh"), a("xa1", 64, 96))
    for ch in H:
        tt(a("lh", 256 * ch, 256 * ch + 256), ind(a("sh"), a("ek", 16 * ch, 16 * ch + 16)), a("mske"), OP.mult)
        mms([(a("xa1", 16 * ch + 8 * x, 16 * ch + 8 * x + 8), a("lh", 256 * ch + 128 * x, 256 * ch + 128 * x + 128), a("j8"), True, True) for x in H])
    cp(a("fi"), a("xa1", 0, 32))
    ts(a("wq", 0, 32), a("fi"), 8191, OP.bitwise_and)
    ts(a("wq", 32, 64), a("fi"), 13, OP.arith_shift_right)
    lin("g0", a("g0"), a("wq"))
    tt(a("sv"), a("iu"), a("xa1", 0, 32), OP.add)
    ts(a("frs"), a("fri"), 511 + (1 << 21), OP.bitwise_and)
    ts(a("pc"), a("fri"), 9, OP.arith_shift_right)
    lin("frs", a("xa0", 0, 256), a("frs"), 8192.0, float(O))
    tt(a("frm"), a("pc"), a("xa0", 0, 256), OP.add)
    ts(a("f0", *OWN), a("frm"), 2 * L, OP.min)
    act(a("zz"), a("frm"), AF.Sign, 1.0, -1.5 * L)

    def table(lo, hi, bank):
        h = a(bank, 0, hi - lo)
        act(a("sks", lo, hi), a("ski", lo, hi), AF.Sign, 1.0, -4095.5)
        mms([(h, a("idk"), a("sks", lo, hi), True, False), (h, a("idm"), a("sks", lo, hi), False, True)])
        tt(a("skt", lo + 592, hi + 592), a("ski", lo, hi), h, OP.add)

    for j, (lo, hi) in enumerate(SKP[:len(SKP) - DEF]):
        table(lo, hi, BANKS[j % len(BANKS)])
        for p in prog[-3:]:
            p["extra"] = 0.1 + 0.01 * j if j < EARLY else START + FILL
    for ch in H:
        clause_part(4, "f0", ch)
    fill(a("crow"), 0.0)
    iota(a("crow", 0, 128, 1, 1), [[0, 8], [-1, 16]], 16, 0)
    for r, m in ((0, 4080), (32, 15)):
        ts(a("thj", 0, 128, 1, r + 1, r), a("thi", 0, 128, 1, r + 1, r), m, OP.bitwise_and)
        for j, w in ((1, 1), (2, -1)):
            lin("crow", a("crow", 128 * j, 128 * j + 128, 1, r + 1, r), a("thj", 0, 128, 1, r + 1, r), 2, w * (r > 0))
    next_saved("sv", a("iu", 8, 32), (0, 24), (8, 32))
    for ch in H:
        if JOIN[ch]:
            lin("mx", a("mx", 16 * ch, 16 * ch + 8), a("sv", 16 * ch, 16 * ch + 8))

    def places(ch, raw, m, p, q, pr, r, u):
        lo, hi = PH[ch]
        if m == "ga" or not CQ[ch]:
            ts(a(m, lo, hi), a(raw, lo, hi), L - 1, OP.bitwise_and)
        c, d = (lo + x for x in SPLIT.get(u + str(ch), (128, 128)))
        for w in ((lo, c), (c, hi))[:1 + (c < hi)]:
            ts(a(q, *w), a(raw, *w), 13, OP.arith_shift_right, 1023, OP.bitwise_and)
            ts(a(p, *w), a(raw, *w), 8191, OP.bitwise_and)
        for w in ((lo, d), (d, hi))[:1 + (d < hi)]:
            if q + str(ch) in ONS:
                e = a("fa%d" % ch, 256 + 128 * (q == "qc") + w[0] - lo, 256 + 128 * (q == "qc") + w[1] - lo)
                act(e, a(q, *w), AF.Identity)
                tt(a(pr, *w), a(p, *w), e, OP.mult)
            else:
                tt(a(pr, *w), a(p, *w), a(q, *w), OP.mult)
            ts(a(r, *w), a(pr, *w), 4, OP.arith_shift_right, 4095, OP.bitwise_and)
            lin(u + str(ch), a(u, *w), a(r, *w))

    def outputs(ch):
        lo, hi = PH[ch]
        tt(a("w", ch, 32, 2), a("mx", ch, 32, 2), a("sum", 256 * ch + 15, 256 * ch + 256, 16), OP.max)
        if ch:
            mm(a("d0", 0, 128, 1, 64), a("svy"), a("idf"), True, False)
            if OUT:
                ts(a("fi"), a("w"), 8191, OP.bitwise_and)
                ts(a("flag", 16, 48), a("w"), 2 * U, OP.is_lt)
                ts(a("wq", 0, 32), a("w"), 13, OP.arith_shift_right, 511, OP.bitwise_and)
                lin("oa", a("flag", 0, 16), a("flag", 16, 32), 512)
                lin("ob", a("fia", 0, 32), a("fi"), 512, -512 * 592)
                tt(a("fim", 32, 64), a("old", 0, 32), a("flag", 16, 48), OP.mult)
                mm(a("d0", 0, 128, 1, 64), a("fim"), a("idf"), False, False)
                lin("oc", a("fib", 0, 32), a("wq", 0, 32))
                tt(a("fib", 32, 48), a("wq", 0, 16), a("flag", 16, 32), OP.mult)
                mm(a("d0", 0, 128, 1, 48), a("fib", 0, 48), a("idf"), False, False)
                tt(a("fia", 48, 64), a("fi", 16, 32), a("flag", 32, 48), OP.mult)
                tt(a("fia", 32, 48), a("fi", 0, 16), a("flag", 0, 16), OP.mult)
                mm(a("d0", 0, 128, 1, 64), a("fia"), a("idf"), False, True)
            else:
                ts(a("fi"), a("w"), 8191, OP.bitwise_and)
                ts(a("fq"), a("w"), 13, OP.arith_shift_right, 511, OP.bitwise_and)
                ts(a("w2"), a("w"), 2 * U, OP.is_lt)
                ts(a("s2"), a("fi"), 512, OP.mult, -512 * 592, OP.add)
                tt(a("sh", 0, 16), a("fq", 0, 16), a("svy", 32, 48), OP.subtract)
                tt(a("svs", 16, 32), a("fi", 16, 32), a("sg1", 16, 32), OP.subtract)
                tt(a("svs", 0, 16), a("s2", 0, 16), a("sh", 0, 16), OP.add)
                tt(a("fim", 0, 32), a("s2"), a("fq"), OP.add)
                tt(a("fim", 32, 64), a("svs"), a("w2"), OP.mult)
                mm(a("d0", 0, 128, 1, 64), a("fim"), a("idf"), False, True)
            cp(a("fot"), a("d0", 0, 128, 1, 64))
            for j, y in enumerate((T.yg, T.yc, T.ysg, T.yk)):
                dma("sy"[j % 2], ("!", y[:]), a("fot", 0, 128, 1, 16 * j + 16, 16 * j))
        e = a("fa%d" % ch, 128, 256)
        mm(e, a("idb"), a("zz", lo, hi), True, False)
        act(a("rs", lo, hi), ind(a("sum", 256 * ch, 256 * ch + 128), e15), AF.Sign, -1.0, 2.0 * U - 0.5)
        mm(e, a("rs", lo, hi), a("idn"), False, True)
        act(a("sa", lo, hi), e, AF.Relu, 0.5)
        ts(a("o2", lo, hi), a("oi", lo, hi), 8191, OP.bitwise_and)
        ts(a("oq", lo, hi), a("oi", lo, hi), 12, OP.arith_shift_right, 2046, OP.bitwise_and)
        act(a("o3", lo, hi), a("o2", lo, hi), AF.Identity, 1024.0, -1024.0 * 592)
        act(a("hb", lo, hi), a("oq", lo, hi), AF.Identity, 1.0, -32.0)
        e = XP[ch]
        mm(e, a("idf"), a("o3", lo, hi), True, False)
        mm(e, a("idf"), a("hb", lo, hi), False, False)
        mm(e, a("idb"), a("sa", lo, hi), False, True)
        ts(a("oz", lo, hi), e, -1, OP.max)
        dma("y", ("!", T.yf[:, lo:hi]), a("oz", lo, hi))

    def runs(js):
        out = []
        for j in js:
            if out and out[-1][1] == 32 * j and (out[-1][0] == 0 or (out[-1][0], j) == (64, 3)):
                out[-1] = (out[-1][0], 32 * j + 32)
            else:
                out.append((32 * j, 32 * j + 32))
        return out

    for t in range(RO):
        F, last, to = "f%d" % t, t == RO - 1, T.cores[(rank + 1 + t % 3) % N]
        B = "f%d" % max(t - 1, 0)
        for ch, (lo, hi) in enumerate(PH):
            up(t, "g%d" % ch)
            e = E0[ch]
            if t == 0:
                lin("fc%d" % ch, a("sm", lo, hi), ind(a(F, *OWN), gl(4, 0, 0, ch)))
                mm(e, a("e16", lo, hi), a("inb"), True, False)
                rows(e, a("tg", lo, hi), a("clx", lo, hi), gl(4, 0, 1, ch), 16 * 8192 + C0)
                tt(a("rawg", lo, hi), a("sm", lo, hi), e, OP.min)
            else:
                c, C = 32 * (2 * t - 2 + ch), a("r%d" % (t - 1))
                fr, sk = a("arr", c, c + 8), a("arr", c + 8 + 8 * JOIN[ch], c + 16 + 8 * JOIN[ch])
                up(t, "col%d" % ch)
                act(a(F, 256 + lo, 256 + hi), ind(C, fr), AF.Identity)
                up(t, "g%d" % ch)
                if TG[ch]:
                    act(a("tg", lo, hi), ind(a("skt"), sk), AF.Identity)
                    mms([(e, a("idf"), a("bg", lo, hi), True, False), (e, a("idf"), a("tg", lo, hi), False, True)])
                    if TG[ch] == 1:
                        tt(a("rawg", lo, hi), a(F, 256 + lo, 256 + hi), e, OP.min)
                    else:
                        act(a("sm", lo, hi), e, AF.Identity)
                        tt(a("rawg", lo, hi), ind(C, fr), a("sm", lo, hi), OP.min)
                else:
                    tt(a("tg", lo, hi), ind(a("skt"), sk), a("bg", lo, hi), OP.add)
                    tt(a("rawg", lo, hi), ind(C, fr), a("tg", lo, hi), OP.min)
            places(ch, "rawg", "ga", "pg", "qg", "prg", "rg", "ug")
        if not last:
            send(a("r%d" % t, *GH), a(F, *(GH if t else OWN)), to, "ag%d" % t)
        for j, (lo, hi) in enumerate(GCH):
            up(t, "u%d" % (lo // 1024), lo % 1024 / 730)
            act(a("ub" if lo or WAYS.get(t, WAY)[0] != "m" else "um", lo, hi), ind(a("xr"), a("ug", lo // 16, hi // 16)), AF.Identity)
        for ch, (lo, hi) in enumerate(PH):
            up(t, "x%d" % ch)
            lin("gaf%d" % ch, a("gaf", 2 * lo, 2 * lo + 128), a("ga", lo, hi), 1, -16 * 8192)
            mm(XP[ch], a("idf"), a("gaf", 2 * lo, 2 * lo + 128), False, True)
            tt(a(F, 512 + lo, 512 + hi), a(B, lo, hi), XP[ch], OP.min)
            up(t, "c%d" % ch)
            if t:
                tt(a("rawc", lo, hi), ind(a(F, 0, 512 + hi), gl(t - 1, 1, 0, ch)), a("tc", lo, hi), OP.min)
            else:
                tt(a("rawc", lo, hi), a(F, 512 + lo, 512 + hi), Y0[ch], OP.min)
            places(ch, "rawc", "ca", "pc", "qc", "prc", "rc", "uc")
        if t == 0:
            step[1] = None
            for c, bank in zip(SKP[len(SKP) - DEF:], PARK):
                table(c[0], c[1], bank)
                prog[-3]["extra"], prog[-2]["extra"], prog[-1]["extra"] = START + FILL, START + FILL, START + 10.5
        way = WAYS.get(t, WAY)
        pieces = [(w.lower(), 512 * j + c, 512 * j + c + (512 if w.islower() else 256)) for j, w in enumerate(way) for c in ((0,) if w.islower() else (0, 256))]
        for w, lo, hi in pieces:
            up(t, "w4" if hi == 4096 else "w%d" % (lo // 1024), lo % 1024 / 730)
            if w == "s":
                e = a("ea%d" % (lo // 2048), lo % 512, lo % 512 + hi - lo)
                act(a("df", lo, hi), ind(a("xr"), a("uc", lo // 16, hi // 16)), AF.Identity)
                mms([(e, a("idn"), a("ub", lo, hi), True, False), (e, a("idb"), a("df", lo, hi), False, True)])
                act(a("ab", lo, hi), e, AF.Abs)
            elif w == "m":
                act(a("df", lo, hi), ind(a("xr"), a("uc", lo // 16, hi // 16)), AF.Identity)
            elif lo // 512 not in WIDE:
                lo -= 512 * (lo // 512 - 1 in WIDE)
                tt(a("df", lo, hi), ind(a("xr"), a("uc", lo // 16, hi // 16)), a("ub", lo, hi), OP.subtract)
        for w, lo, hi in pieces:
            up(t, "a4" if hi == 4096 else "a%d" % (lo // 1024), lo % 1024 / 730)
            if w == "r":
                ts(a("ab", lo, hi), a("df", lo, hi), 0, OP.max)
            elif w == "b":
                act(a("ab", lo - 512, hi), a("df", lo - 512, hi), AF.Abs)
            elif w == "a" and way[hi // 512:hi // 512 + 1] != "b":
                act(a("ab", lo, hi), a("df", lo, hi), AF.Abs)
        for j, lo, hi in folds(t):
            up(t, "a%d" % ((hi - 1) // 1024), (hi - 1) % 1024 / 730)
            fold(a("ab", lo, hi), [a("df", lo, hi), a("um", 0, hi - lo) if way[j] == "m" and j == 0 else a("ub", lo, hi) if way[j] == "m" else a("um", 512, 512 + hi - lo)], "h%d" % j)
        for ch in H:
            up(t, "d%d" % ch)
            D = "d%d" % ch
            mm(a("fa%d" % ch, 0, 128), a("idu"), a("zz", *PH[ch]), True, False)
            mm(a(D, 0, 384), a("big"), a("crow"), True, False)
            for l0, h0 in LATE[ch]:
                todo = [(x, c) + r for x, c, ws in (("ub", 24, "m"), ("df", 24, "rRfgm"), ("ab", 48, "rR"[2 * ONCE:]), ("ab", 0, "aAbs"), ("ab", 48, "fgm" + "rR" * ONCE))
                        for r in runs([j for j in range(l0 // 32, h0 // 32) if way[4 * ch + j] in ws])]
                for x, c, lo, hi in todo:
                    x = "um" if (x, ch, lo) == ("ub", 0, 0) else x
                    for k0 in range(0, 16, MK):
                        mms([(a(D, k, 384, 16, hi, lo), a(x, 2048 * ch + 16 * lo + k, 2048 * ch + 16 * hi, 16), a("bw", c, c + 24), False,
                              k == 15 and x == "ab") for k in range(k0, k0 + MK)])
        for ch, (lo, hi) in enumerate(PH):
            D, FA, EA = "d%d" % ch, "fa%d" % ch, "ea%d" % ch
            s1, s2 = a("sg", 2 * lo, 2 * lo + 128), a("sg", 2 * lo + 128, 2 * lo + 256)
            gc = [(2 * lo + 128 * x, 2 * lo + 128 * x + 128) for x in H]
            EX = (a(EA, 0, 128), a("xa%d" % ch, 384, 512))
            up(t, "f%d" % ch)
            act(s1 if S2[ch] else a("sg", 2 * lo, 2 * lo + 256), a(D, 128, 256 if S2[ch] else 384), AF.Sign)
            scan(a("cnt", lo, hi), a("rstb"), s1, OP.mult, OP.add)
            act(a("clx", lo, hi), ind(a("cnt", lo, hi), e15), AF.Sign, -1.0, a("lim", ch, ch + 1), a("par", ch, ch + 1) if PAR and not last else None)
            mm(a(FA, 0, 128), a("clx", lo, hi), a("idu"), False, True)
            tt(a("oi", lo, hi) if last else a(F, lo, hi), a(F, 512 + lo, 512 + hi), a(FA, 0, 128), OP.max)
            if not last:
                send(a("r%d" % t, lo, hi), a(F, lo, hi), to, "ao%d" % (2 * t + ch))
            up(t, "m%d" % ch)
            key = a(KB[ch], 128, 256) if S2[ch] else a(D, 384, 512)
            cuts = ((0, 64), (64, 128)) if PS[ch] else ((0, 128),)

            def sub(o, c):
                return a(o[0], o[1] + c[0], o[1] + c[1])
            for c in cuts:
                tt(sub(key, c), sub(s1, c), a(D, *c), OP.mult)
            if S2[ch]:
                act(s2, a(D, 256, 384), AF.Sign)
            for c in cuts:
                scan(a("sm", lo + c[0], lo + c[1]), a("rsb", *c), sub(key, c), OP.add, OP.max)
            for c in cuts:
                tt(a("dd", lo + c[0], lo + c[1]), a("sm", lo + c[0], lo + c[1]), sub(key, c), OP.subtract)
            for x in H:
                up(t, "lj"[x] + str(ch))
                if x and CQ[ch]:
                    act(a("gaf", *gc[x]), a("qc", lo, hi), AF.Identity, 8192.0, -16.0 * 8192)
                    act(a("key", lo, hi), a("pc", lo, hi), AF.Identity)
                elif x:
                    lin("caf%d" % ch, a("gaf", *gc[x]), a("ca", lo, hi), 1, -16 * 8192)
                mm(EX[x], a("gaf", *gc[x]), a("idf"), True, False)
                if x and CQ[ch]:
                    mm(EX[x], a("key", lo, hi), a("idf"), False, False)
                mm(EX[x], a("idx"), a("clx", lo, hi), False, False)
                bare = BARE[ch] and not last and not x
                mm(EX[x], *((a("oneb"), a("cw")) if bare else (a("ids"), s2)), False, False)
                mm(EX[x], a("idn"), a("dd", lo, hi), False, True)
                scan(a("sum", *gc[x]), a("dd", lo, hi), EX[x], OP.min, OP.max)
                if last or (JOIN[ch] and not x):
                    continue
                if bare:
                    e, y, c, d = a("d0", 0, 128), a(EA, 384, 392), 40 * (2 * t + ch), 32 * (2 * t + ch)
                    up(t, "b%d" % ch)
                    act(a("key", 0, 128), ind(a("sv", 16 * ch, 16 * ch + 8), a("el", 0, 8)), AF.Identity)
                    mms([(e, a("key", 0, 128), a("idf"), True, False), (e, a("idb"), a("mko"), False, False)])
                    mm(e, a("idu"), a("clx", lo, hi), False, True)
                    act(a("key", 128, 256), e, AF.Relu)
                    mm(y, a("key", 128, 256), a("j8"), True, False)
                    up(t, "l%d" % ch)
                    tt(a("lh", *gc[0]), ind(a("sum", *gc[0]), e15), a("mske", 0, 128), OP.mult)
                    mm(y, a("lh", *gc[0]), a("j8"), False, True)
                    lin("gq", a("gl", c, c + 8), y, 1 / 8192, -591.5 / 8192)
                    send(a("arr", d, d + 8), a("gl", c, c + 8), to, "al%d" % (2 * t + ch))
                    up(t, "p%d" % ch)
                    lin("gw", a("w", 16 * ch, 16 * ch + 8), y)
                    ts(a("wq", 32 * ch + 8, 32 * ch + 16), a("w", 16 * ch, 16 * ch + 8), 8191, OP.bitwise_and)
                    lin("gp", a("gl", c + 8, c + 16), a("wq", 32 * ch + 8, 32 * ch + 16))
                    send(a("arr", d + 8, d + 16), a("gl", c + 8, c + 16), to, "ap%d" % (2 * t + ch))
                    continue
                xs = H if JOIN[ch] else (x,)
                c, n = gc[xs[0]][0], len(xs)
                tt(a("lh", c, c + 128 * n), ind(a("sum", c, c + 128 * n), a("el", 16, 16 + 8 * n)), a("mske", 0, 128 * n), OP.mult)
                mms([(a(EA, 384 + 8 * y, 392 + 8 * y), a("lh", *gc[y]), a("j8"), True, True) for y in xs])
                c = (16 * ch + 8 * xs[0], 16 * ch + 8 * x + 8)
                tt(a("w", *c), a("mx" if x else "sv", *c), a(EA, 384 + 8 * xs[0], 392 + 8 * x), OP.max)
                lists(t, ch, xs)
                if not xs[0]:
                    c, d = 40 * (2 * t + ch), 32 * (2 * t + ch)
                    send(a("arr", d, d + 8 + 8 * n), a("gl", c, c + 8 + 8 * n), to, "al%d" % (2 * t + ch))
            if last:
                up(t, "o%d" % ch)
                outputs(ch)
                continue
            up(t, "z%d" % ch)
            e = a(FA, 128, 256)
            act(a("rs", lo, hi), ind(a("sum", *gc[BARE[ch]]), e15), AF.Sign, -1.0, 2.0 * U - 0.5)
            mm(e, a("idu"), a("zz", lo, hi), True, False)
            mm(e, a("idf"), a(F, lo, hi), False, False)
            mm(e, a("rs", lo, hi), a("idx"), False, True)
            act(a("zz", lo, hi), e, AF.Sign, 1.0, -1.25 * L)

        if last:
            break
        up(t, "z1")
        dma("y", a("f%d" % (t + 1), *OWN), a(F, *OWN), 2.8)
        for ch in H:
            up(t, "k%d" % ch)
            clause_part(t, F, ch)
        up(t, "sv")
        if PAR:
            act(a("par", 2, 4), a("par", 0, 2), AF.Abs, 1.0 / 32)
            act(a("par", 4, 6), a("par", 2, 4), AF.Abs, 1.0, -2.0)
            act(a("par", 6, 8), a("par", 4, 6), AF.Abs, 2.0, -2.0)
            act(a("lim", 0, 2), a("par", 6, 8), AF.Identity, 1.0, -1.0)
        for ch, (lo, hi) in enumerate(() if PAR else PH):
            prod(a("lim", ch, ch + 1), a("clx", lo, hi, 16))
        for ch in H:
            if BARE[ch]:
                ts(a("wl"), a("w", 16 * ch + 8, 16 * ch + 16), 2 * U, OP.bitwise_and)
                tt(a("w", 16 * ch, 16 * ch + 8), a("w", 16 * ch, 16 * ch + 8), a("wl"), OP.add)
        ts(a("w2"), a("w"), 3 * U - 1, OP.bitwise_and)
        lin("sg2", a("sg1"), a("w"), -2048, 4096 * U)
        tt(a("sh"), a("sv"), a("sg1"), OP.max)
        tt(a("sv"), a("w2"), a("sh"), OP.min)
        if t < RO - 2:
            next_saved("sv", a("iu", 8, 32), (0, 24), (8, 32))
            for ch in H:
                if JOIN[ch]:
                    lin("mx", a("mx", 16 * ch, 16 * ch + 8), a("sv", 16 * ch, 16 * ch + 8))
            continue
        up(t, "sl")
        for ch in H:
            tt(a("lh", 256 * ch, 256 * ch + 256), ind(a("sv", 16 * ch, 16 * ch + 16), a("el", 0, 16)), a("mske"), OP.mult)
            for x in H:
                c = 256 * ch + 128 * x
                mm(a("fa1", 256 + 16 * x + ch, 272 + 16 * x, 2), a("lh", c, c + 128), a("j8"))
        lin("svs", a("svs"), a("fa1", 256, 288))
        next_saved("svs", a("il"), (0, 16), (16, 32))
        lin("mx", a("mx", 0, 16), a("svs", 0, 16))
        ts(a("fq"), a("svs"), 13, OP.arith_shift_right, 511, OP.bitwise_and)
        lin("fi", a("fi", 0, 16), a("s3", 0, 16), 512)
        tt(a("svy", 32, 48), a("fi", 0, 16), a("fq", 0, 16), OP.add)
        lin("svy", a("svy", 48, 64), a("s3", 16, 32))
        if OUT:
            lin("old", a("old", 0, 16), a("svy", 32, 48), -1, -512 * 592)
            lin("old", a("old", 16, 32), a("s2", 16, 32), -1)
            fill(a("fim", 0, 32), 0.0)
        else:
            lin("svy", a("sg1", 16, 32), a("s2", 16, 32))

    lg, n = {}, len(prog)
    dep = [[] for _ in range(n)]
    for i, p in enumerate(prog):
        ds, q = {}, p["q"] if p["kind"] == "c" else "#%d" % i
        for e in meets(q, p["acc"], lg):
            ds[e[3]] = WAKE.get(prog[e[3]]["q"] + p["q"], WAKE[prog[e[3]]["q"]])
        if p["kind"] == "n":
            ds[p["extra"][2]] = 0.0
        if p["kind"] != "f":
            note(q, p["acc"], lg, i)
        dep[i] = sorted(ds.items())
    dur, lat, qs = [p["dur"] for p in prog], [p["lat"] for p in prog], [p["q"] for p in prog]
    before, after = [[(d, w + lat[d]) for d, w in dep[i]] for i in range(n)], [[] for _ in range(n)]
    for i in range(2, len(LD)):
        before[i].append((i - 2, 0.0))
    above = [0] * n
    for i in range(n):
        before[i] = [(d, w) for d, w in before[i] if not any(above[e] >> d & 1 and w <= dur[e] + x for e, x in before[i])]
        for d, w in before[i]:
            after[d].append((i, w))
            above[i] |= above[d] | 1 << d

    def pack(order, needs, head):
        done, busy = [0.0] * n, {q: [] for q in Q}
        for i in order:
            t0 = max([head[i]] + [done[d] + w for d, w in needs[i]])
            if qs[i] != "net":
                b = busy[qs[i]]
                lo, hi = 0, len(b)
                while lo < hi:
                    m = (lo + hi) // 2
                    lo, hi = (m + 1, hi) if b[m][1] <= t0 else (lo, m)
                while lo < len(b) and b[lo][0] < t0 + dur[i] - 1e-9:
                    t0 = max(t0, b[lo][1])
                    lo += 1
                b.insert(lo, (t0, t0 + dur[i]))
            done[i] = t0 + dur[i]
        return done

    seed, tops = [SEED], []

    def rnd():
        seed[0] = (seed[0] * 1103515245 + 12345) % 2147483648
        return (seed[0] >> 8) / 8388608

    def search(du, qu, arcs, st, span, edge, turns):
        m = len(du)
        now, old, later, newer = ([[] for _ in range(m)] for _ in range(4))
        for i, j, w, s in arcs:
            if s < 2:
                (old if s else now)[j].append((i, w))
                (newer if s else later)[i].append((j, w))
        head, tail, ends = edge or ([-1e9] * m, [-99.0] * m, None)
        for _ in range(6):
            for j in range(m):
                st[j] = max([st[j]] + [st[i] + 1e-6 for i, w in now[j]])
        order, seq = sorted(range(m), key=lambda j: st[j]), {}
        for j in order:
            if qu[j] != "net" and (ends or qu[j] != "y"):
                seq.setdefault(qu[j], []).append(j)
        rest, hh, tl, prev, nxt, rests = [0.0] * m, [0.0] * m, [0.0] * m, [-1] * m, [-1] * (m + 1), [0] * m
        best, undo = (1e9, list(st), order), None
        for turn in range(turns):
            for q in seq.values():
                e = m
                for j in q:
                    prev[j], nxt[e], e = e, j, j
                prev[q[0]] = nxt[e] = -1
            if turn:
                deg = [len(now[j]) + (prev[j] >= 0) for j in range(m)]
                order = [j for j in range(m) if not deg[j]]
                for j in order:
                    for d, w in later[j]:
                        deg[d] -= 1
                        if not deg[d]:
                            order.append(d)
                    d = nxt[j]
                    if d >= 0:
                        deg[d] -= 1
                        if not deg[d]:
                            order.append(d)
                if len(order) < m:
                    seq[qu[undo[0]]] = undo[1]
                    continue
            for _ in range(1 if ends else 3 if turn else 8):
                was = sum(st)
                for j in order:
                    t0 = head[j]
                    for d, w in now[j]:
                        if st[d] + w > t0:
                            t0 = st[d] + w
                    for d, w in old[j]:
                        if st[d] + w - span > t0:
                            t0 = st[d] + w - span
                    hh[j] = t0
                    e = prev[j]
                    if e >= 0:
                        e = st[e] + du[e]
                    elif qu[j] in seq:
                        e = seq[qu[j]][-1]
                        e = ends[qu[j]][0] if ends else st[e] + du[e] - span
                    else:
                        e = t0
                    st[j] = t0 if t0 > e else e
                more = 0.0 if ends else (sum(st) - was) / m
                span += more
                if -1e-4 < more < 1e-4:
                    break
            for _ in range(1 if ends else 2 if turn else 8):
                for j in reversed(order):
                    t0 = tail[j]
                    for d, w in later[j]:
                        if rest[d] + w > t0:
                            t0 = rest[d] + w
                    for d, w in newer[j]:
                        if rest[d] + w - span > t0:
                            t0 = rest[d] + w - span
                    tl[j] = t0
                    e = nxt[j]
                    if e >= 0:
                        e = rest[e] + du[j]
                    elif qu[j] in seq:
                        e = du[j] + (ends[qu[j]][1] if ends else rest[seq[qu[j]][0]] - span)
                    else:
                        e = t0
                    rest[j] = t0 if t0 > e else e
            way = [st[j] + rest[j] for j in range(m)]
            top = max(way)
            if (top if ends else span) < best[0] - 1e-4 and abs(more) < 0.003:
                best = (top if ends else span, list(st), order)
            e = top - NEAR
            hot = [j for j in range(m) if way[j] > e and qu[j] in seq and rests[j] <= turn and
                   ((prev[j] >= 0 and st[prev[j]] + du[prev[j]] > st[j] - NEAR and way[prev[j]] > e) or (nxt[j] >= 0 and rest[nxt[j]] + du[j] > rest[j] - NEAR and way[nxt[j]] > e))]
            move = None
            for _ in range(min(SOME, len(hot))):
                j = hot.pop(int(rnd() * len(hot)))
                q = seq[qu[j]]
                p, k = q.index(j), len(q)
                for sign in (-1, 1):
                    for x in range(p + sign, min(max(p + sign * FAR, -1), k), sign):
                        if sign < 0:
                            if st[q[x]] + du[q[x]] <= hh[j]:
                                break
                            seg, lo, hi = [j] + q[x:p], x - 1, p + 1
                        else:
                            if rest[q[x]] <= tl[j]:
                                break
                            seg, lo, hi = q[p + 1:x + 1] + [j], p - 1, x + 1
                        t0 = st[q[lo]] + du[q[lo]] if lo >= 0 else ends[qu[j]][0] if ends else st[q[-1]] + du[q[-1]] - span
                        hs = []
                        for y in seg:
                            if hh[y] > t0:
                                t0 = hh[y]
                            hs.append(t0)
                            t0 += du[y]
                        t0 = rest[q[hi]] if hi < k else ends[qu[j]][1] if ends else rest[q[0]] - span
                        e = soft = 0.0
                        for y in reversed(seg):
                            t0 += du[y]
                            if tl[y] > t0:
                                t0 = tl[y]
                            f = hs.pop() + t0 - top
                            if f > e:
                                e = f
                            soft += math.exp(f / SOFT) - math.exp((way[y] - top) / SOFT)
                        e += WEIGH * soft + 0.01 * rnd()
                        if not move or e < move[0]:
                            move = (e, j, x)
            if move:
                e, j, x = move
                undo, q = (j, list(seq[qu[j]])), seq[qu[j]]
                q.remove(j)
                q.insert(x, j)
                rests[j] = turn + REST + int(2 * REST * rnd())
        return best, (span, st)

    if not PLAN:
        prio = [0.0] * n
        for i in range(n - 1, -1, -1):
            prio[i] = dur[i] + max([w + prio[j] for j, w in after[i]] + [lat[i]])
        due = pack(sorted(range(n), key=lambda i: (-prio[i], i)), before, [0.0] * n)
        for i, p in enumerate(prog):
            if p["id"]:
                due[i] = max([p["due"]] + [due[d] + w for d, w in before[i]]) + dur[i]
        ids = {prog[i]["id"]: i for i in range(n) if prog[i]["id"]}
        names = [k[1:] for k in ids if k[0] == 2]
        m, num, own = len(names), {k: j for j, k in enumerate(names)}, [ids[(2,) + k] for k in names]
        needs = [(num[prog[d]["id"][1:]], j, 2 - prog[d]["id"][0], w + dur[d]) for j in range(m) for d, w in before[own[j]] if prog[d]["id"] and prog[d]["id"][1:] in num]
        at, span, best, kept = [due[i] - dur[i] for i in own], PERIOD, (1e9,), (1e9,)
        for turn in range(CUTS):
            if turn % KICK == KICK - 1:
                kept = best if best[0] < kept[0] + LOOSE * rnd() else kept
                (span, at), best, c = kept, (1e9,), rnd() * kept[0]
                at = [x + SHAKE * rnd() * ((x - c) % span < STRETCH) for x in at]
                tops.append(kept)
            cut = min(at) + span * (1 + rnd())
            back = [math.ceil((x - cut) / span) for x in at]
            for _ in range(4):
                for i, j, s, w in needs:
                    back[j] = max(back[j], back[i] - s)
            arcs = [(i, j, w, s + back[j] - back[i]) for i, j, s, w in needs]
            good, now = search([dur[i] for i in own], [qs[i] for i in own], arcs, [x - b * span for x, b in zip(at, back)], span, None, ROUND)
            if good[0] < best[0]:
                best = (good[0], [x + b * good[0] for x, b in zip(good[1], back)])
            span, at = best if now[0] > best[0] + STRAY else (now[0], [x + b * now[0] for x, b in zip(now[1], back)])
        span, at = min(tops + [best])
        SPANS.append([round(x[0], 2) for x in tops])
        SPANS.append(round(span, 2))
        key, end = [0.0] * n, START + RO * span + TAIL
        for i in range(n - 1, -1, -1):
            k = prog[i]["id"]
            mine = at[num[k[1:]]] - at[num["u1", "sub0"]] + 1.5 + k[0] * span + START if k and k[1:] in num else prog[i]["extra"] if prog[i]["kind"] == "c" else None
            key[i] = min([key[j] - w - dur[i] for j, w in after[i]] + [mine or end - prio[i]])
        order, tries = sorted(range(n), key=lambda i: (key[i], i)), []
        for _ in range(3):
            due = pack(order, before, [0.0] * n)
            tries.append((max(due), sorted(range(n), key=lambda i: (due[i] - dur[i], i))))
            back = pack(sorted(range(n), key=lambda i: (-due[i], -i)), after, lat)
            order = sorted(range(n), key=lambda i: (-back[i], i))
        order = min(tries)[1]
        if MAP:
            due = pack(sorted(range(n), key=lambda i: (-prio[i], i)), before, [0.0] * n)
            for i, p in enumerate(prog):
                if not p["id"]:
                    due[i] = max([min(due[i], START)] + [due[d] + 1e-6 + dur[i] - dur[d] for d, w in before[i]])
                else:
                    e = at[num[p["id"][1:]]] - at[num["u1", "sub0"]] + 1.5 + p["id"][0] * span + START if p["id"][1:] in num else 0.0
                    due[i] = max([e] + [due[d] + w if e < START + GAP else due[d] - dur[d] + 1e-6 for d, w in before[i]]) + dur[i]
            key = [due[i] - dur[i] for i in range(n)]
            for i, p in enumerate(prog):
                key[i] = max([p["extra"] if p["kind"] == "c" and p["extra"] else key[i]] + [key[d] + 1e-6 for d, w in before[i]])
            cut = sorted(range(n), key=lambda i: key[i])
            some = [i for i in cut if key[i] < START + GAP]
            due = pack(some, before, [0.0] * n)
            order = sorted(some, key=lambda i: (due[i] - dur[i], key[i])) + cut[len(some):]
        for turn in range(STEPS + 1):
            st, rest, prev, nxt, last = [0.0] * n, [0.0] * n, [-1] * n, [-1] * n, {}
            for i in order:
                if qs[i] != "net" and qs[i] in last:
                    prev[i], nxt[last[qs[i]]] = last[qs[i]], i
                last[qs[i]] = i
                st[i] = max([st[d] + dur[d] + w for d, w in before[i]] + [st[prev[i]] + dur[prev[i]] if prev[i] >= 0 else 0.0])
            for i in reversed(order):
                rest[i] = dur[i] + max([lat[i], rest[nxt[i]] if nxt[i] >= 0 else 0.0] + [rest[d] + w for d, w in after[i]])
            order.sort(key=lambda i: st[i])
            if turn % 10 == 0:
                SPANS.append(round(max(rest), 1))
            if turn == STEPS:
                break
            part = TURNS[turn // PART]
            if turn % PART == 0:
                seed[0] = part[0]
            lo, hi, wide = part[1 + turn % (len(part) - 1)]
            first = int((n - wide) * (lo + (hi - lo) * rnd()))
            some = order[first:first + wide]
            loc = {i: j for j, i in enumerate(some)}
            arcs = [(loc[d], loc[i], w + dur[d], 0) for i in some for d, w in before[i] if d in loc]
            head = [max([0.0] + [st[d] + dur[d] + w for d, w in before[i] if d not in loc]) for i in some]
            tail = [dur[i] + max([lat[i]] + [rest[d] + w for d, w in after[i] if d not in loc]) for i in some]
            ends = {}
            for i in some:
                ends[qs[i]] = (ends[qs[i]][0] if qs[i] in ends else st[prev[i]] + dur[prev[i]] if prev[i] >= 0 else 0.0, rest[nxt[i]] if nxt[i] >= 0 else 0.0)
            c, e = st[some[int(rnd() * wide)]], SHAKE * rnd() * (turn % PART >= CALM)
            at = [st[i] + e * rnd() * (c - 2 < st[i] < c + 2) for i in some]
            good, now = search([dur[i] for i in some], [qs[i] for i in some], arcs, at, 0.0, (head, tail, ends), STAY)
            if good[0] < max(rest) + 1e-6:
                order[first:first + wide] = [some[j] for j in good[2]]
        PLAN.extend((max(rest), order, prog, before, dur, lat))

    def wait(q, sem, c):
        if know[q].get(sem, 0) < c:
            Q[q].wait_ge(T.sem[sem], c)
            for k, v in snap.get((sem, c), {}).items():
                know[q][k] = max(know[q].get(k, 0), v)
            know[q][sem] = c

    ref = {}
    for i in PLAN[1]:
        p = prog[i]
        q = p["q"]
        if p["kind"] != "n":
            want = {}
            for d, w in dep[i]:
                if w:
                    sem, c = ref[d]
                    want[sem] = max(want.get(sem, 0), c)
            for sem in sorted(want, key=lambda s: (s == SEM.get(q), s)):
                wait(q, sem, want[sem])
            inst = p["call"]()
        if p["kind"] == "c":
            sem = SEM[q]
            inst.then_inc(T.sem[sem], 1)
            cnt[sem] = cnt.get(sem, 0) + 1
        elif p["kind"] == "d":
            sem = "d%d" % nd[0]
            nd[0] += 1
            inst.then_inc(T.sem[sem], 16)
            cnt[sem] = 16
        elif p["kind"] in "rf":
            sem = "rl" if p["kind"] == "r" else "rf"
            cnt[sem] = cnt.get(sem, 0) + p["extra"][1]
        else:
            sem = p["extra"][0]
            cnt[sem] = cnt.get(sem, 0) + p["extra"][1]
        ref[i] = (sem, cnt[sem])
        if p["kind"] != "n":
            snap[ref[i]] = dict(know[q])
    for sem in sorted(cnt):
        g.wait_ge(T.sem[sem], cnt[sem])
